import numpy as np, ml_dtypes
CORES = [10,34,74,98]
N = 4
BF = ml_dtypes.bfloat16
W, M, H, L, CAP, RO = 2048, 4096, 2048, 256, 56, 4
def sums(w, x):
    return np.add.reduce(w[..., 0:1] * x, axis=2) & 4095, np.add.reduce(w[..., 1:2] * x, axis=2) & 4095
def probe(w, lm, tl, mo, m):
    u, v = sums(w, m); a = (u * v) >> 5
    c = (a[:, :, None] + w[..., 2:3] * u[:, :, None]) & (W - 1)
    x = np.take_along_axis(lm, c.reshape(N, 8, 1, 16 * L), 3).reshape(N, 8, 16, 16, L)
    ok = np.all(x <= m[:, :, :, None], axis=2); has = np.any(ok, axis=2)
    g = np.take_along_axis(c, np.argmax(ok, axis=2)[:, :, None], 2)
    tg = np.take_along_axis(tl, g, 3); q = m - np.take_along_axis(lm, g, 3)
    y = np.take_along_axis(mo, tg.reshape(N, 8, 1, 16 * L), 3).reshape(N, 8, 16, 16, L)
    p = np.minimum(q[:, :, :, None] + y, 255).reshape(N, 8, 16, 16 * L)
    e, f = sums(w, p); h = (((e * f) >> 5) + e) & (H - 1)
    return a, c[:, :, 0], has, tg, p, h
def seek(sn, has, p, h):
    new = np.any(np.take_along_axis(sn, h[:, :, None], 3) != p, axis=2).reshape(N, 8, 16, L) & has[:, :, None]
    return np.any(new, axis=2), np.argmax(new, axis=2)
def first(key):
    o = np.argsort(key, axis=2, kind="stable"); s = np.take_along_axis(key, o, 2)
    b = np.ones(key.shape, bool); b[..., 1:] = s[..., 1:] != s[..., :-1]
    win = np.zeros(key.shape, bool); np.put_along_axis(win, o, b, 2); return win
def turn(st, pr, fill):
    lm, tl, sn, m, ct, ci = st; a, c0, has, tg, p, h = pr
    child, i = seek(sn, has, p, h); j = i * L + np.arange(L)
    pc = np.take_along_axis(p, j[:, :, None], 3); hc = np.take_along_axis(h, j, 2)
    win = first(np.where(child, hc, np.where(has, 2 ** 15 + np.arange(L), 2 ** 14 + c0)))
    wt = np.where(np.arange(16)[:, None] == ci[:, :, None], (a & (M - 1))[:, :, None], ct)
    lm, tl, sn = lm.copy(), tl.copy(), sn.copy()
    for r in range(N):
        for g in range(8):
            b = win[r, g] & child[r, g]; sn[r, g][:, hc[r, g, b]] = pc[r, g][:, b]
            b = win[r, g] & ~has[r, g]; lm[r, g][:, c0[r, g, b]] = m[r, g][:, b]; tl[r, g][:, c0[r, g, b]] = wt[r, g][:, b]
    nm, nt, ni = fill.copy(), tl[..., :L].copy(), np.zeros((N, 8, L), np.int64)
    for d in range(N):
        f = child & ((hc & (N - 1)) == d); f = f & (np.add.accumulate(f.astype(np.int64), axis=2) <= CAP)
        for r in range(N):
            for g in range(8):
                b = np.flatnonzero(f[r, g]); z = r * CAP + np.arange(b.size)
                nm[d, g][:, z] = pc[r, g][:, b]; nt[d, g][:, z] = tg[r, g][:, b]; ni[d, g, z] = i[r, g, b]
    return lm, tl, sn, nm, nt, ni
def mono(rng, n, den, top):
    return ((rng.random((N, 8, 16, n), dtype=np.float32) < den) * rng.integers(1, top + 1, (N, 8, 16, n), dtype=np.int32)).astype(np.int32)
def uneven(rng, n, den):
    v = np.exp2(8 * rng.random((N, 8, 1, n), dtype=np.float32) * rng.random((N, 8, 16, n), dtype=np.float32))
    return ((rng.random((N, 8, 16, n), dtype=np.float32) < den) * np.minimum(v, 255).astype(np.int32)).astype(np.int32)
def base(rng):
    w = np.tile(rng.integers(0, 128, (1, 8, 16, 3), dtype=np.int32), (N, 1, 1, 1)); dens = np.array([0.15, 0.5, 0.8, 1.0, 1.0])
    lm = mono(rng, W, rng.choice(np.array([0.2, 0.3, 0.5]), (N, 8, 1, W)), 160); mo = mono(rng, M, rng.choice(np.array([0.2, 0.4]), (N, 8, 1, M)), 120)
    tl = rng.integers(0, M, (N, 8, 16, W), dtype=np.int32)
    sn = np.where(rng.random((N, 8, 1, H)) < 0.5, -1, mono(rng, H, 0.5, 255)).astype(np.int32)
    m = mono(rng, L, rng.choice(dens, (N, 8, 1, L)), 255); fr = mono(rng, RO * L, rng.choice(dens, (N, 8, 1, RO * L)), 255)
    old = np.take_along_axis(m, rng.integers(0, L, (N, 8, 1, RO * L)), 3)
    return w, lm, tl, mo, sn, m, np.where(rng.random((N, 8, 1, RO * L)) < 0.3, old, fr)
def plant(rng, w, lm, tl, mo, sn, m, fr, until=1, n=L - N * CAP - 8):
    pr = probe(w, lm, tl, mo, m); a, c0, has, tg, p, h = pr; used = np.zeros((N, 8, H), bool)
    cnt = rng.choice(np.array([0, 1, 2, 5, 15, 16]), (N, 8, L), p=[0.5, 0.2, 0.15, 0.05, 0.05, 0.05])
    for r in range(N):
        for g in range(8):
            for k in (1, 2, 5, 15, 16):
                x = np.flatnonzero(has[r, g] & (cnt[r, g] == k)); j = (np.arange(k)[:, None] * L + x).reshape(-1)
                sn[r, g][:, h[r, g, j]] = p[r, g][:, j]; used[r, g, h[r, g, j]] = True
    st = (lm, tl, sn, m, tl[..., :L], np.zeros((N, 8, L), np.int64))
    for t in range(until):
        was, row = st[1], st[5]; st = turn(st, pr, fr[..., t * L:(t + 1) * L])
        pr = probe(w, st[0], st[1], mo, st[3])
    own = pr[0] & (M - 1); came = np.any(st[3] != fr[..., (until - 1) * L:until * L], axis=2)
    stale = ~pr[2] & ~came & (row > 0)
    lone = ~pr[2] & came; anew = ~pr[2] & ~came & ~stale & np.any(st[1][..., :L] != was[..., :L], axis=2)
    used = used | np.any(st[2] != sn, axis=2)
    for r in range(N):
        for g in range(8):
            x = np.flatnonzero(lone[r, g]); v = np.flatnonzero(anew[r, g])[:4]
            s0 = np.flatnonzero(stale[r, g])[:4]
            if x.size + v.size + s0.size == 0: continue
            o = np.concatenate([s0, v, np.resize(x, n - v.size - s0.size)]) if x.size else np.concatenate([s0, v])
            fr[r, g][:, until * L + N * CAP:until * L + N * CAP + o.size] = st[3][r, g][:, o]
            half = rng.random(x.size) < 0.5
            col = np.concatenate([st[4][r, g][:, x][np.arange(16)[:, None] < st[5][r, g, x]],
                own[r, g, x[half]], own[r, g, v]])
            for part, cs in ((True, own[r, g, x[~half]]), (False, col)):
                y = mo[r, g][:, cs]
                e = np.add.reduce(w[r, g, :, 0:1] * y, axis=0) & 4095; f = np.add.reduce(w[r, g, :, 1:2] * y, axis=0) & 4095
                z = (((e * f) >> 5) + e) & (H - 1); b = ~used[r, g, z]
                if part: y = np.where((y == 0) & (rng.random(y.shape) < rng.choice(np.array([0.1, 0.5]), (1, y.shape[1]))), -1, y)
                sn[r, g][:, z[b]] = y[:, b]
def pack(w, lm, tl, mo, sn, m, fr):
    d = {"lm": lm, "tl": tl, "mo": mo, "sn": sn, "fm": m, "fr": fr, "wk": w}
    return {k: np.ascontiguousarray(x.reshape(N, 128, -1)).astype(np.int32) if k in ("tl", "wk") else np.ascontiguousarray(x.reshape(N, 128, -1)).astype(np.float32).astype(BF) for k, x in d.items()}
def setup_inputs(rng):
    s = base(rng); plant(rng, *s); return pack(*s)
def setup_inputs_again(rng):
    w, lm, tl, mo, sn, m, fr = base(rng); w[:, 2, :, 2] = 0; w[:, 3, :, 0] = 0; lm[:, 0] = 255; lm[:, 1] = 0; lm[N - 1, 3, :, 0] = 0; sn[:] = -1
    few = np.tile(rng.integers(0, M, (1, 8, 1, 5), dtype=np.int32), (N, 1, 1, 1))
    tl = np.take_along_axis(few, rng.integers(0, 5, (N, 8, 16, W)), 3); tl[:, :, 7] = rng.integers(0, M, (N, 8, W))
    fr = np.take_along_axis(m, rng.integers(0, 12, (N, 8, 1, RO * L)), 3); m = np.take_along_axis(m, rng.integers(0, 12, (N, 8, 1, L)), 3)
    return pack(w, lm, tl, mo, sn, m, fr)
def setup_inputs_corners(rng):
    w, lm, tl, mo, sn, m, fr = base(rng)
    lm[:, :, 0] = np.where(np.any(lm > 0, axis=2), lm[:, :, 0], 1); tl[:, 5] = rng.choice(np.array([0, M - 1]), (N, 16, W))
    fr[..., ::7] = 0; fr[..., 3::7] = 255
    pool, to = [], []
    for z in range(2):
        x = mono(rng, L, 0.9, 255); pr = probe(w, lm, tl, mo, x); child, i = seek(sn, pr[2], pr[4], pr[5])
        hc = np.take_along_axis(pr[5], i * L + np.arange(L), 2); pool.append(x); to.append(np.where(child, hc & (N - 1), -1))
    pool = np.concatenate(pool, axis=3); to = np.concatenate(to, axis=2)
    for r in range(N):
        for g in range(8):
            left = L; lanes = []
            for e in range(N):
                n = int(rng.choice(np.array([0, 1, CAP - 1, CAP, CAP + 1, 2 * CAP])))
                if r == 0 and e == 0: n = (CAP, CAP + 1, CAP - 1, 0, 1, CAP, CAP + 1, 2 * CAP)[g]
                if r == N - 1 and e == 0: n = CAP
                x = np.flatnonzero(to[r, g] == (r + 1 + e) % N)[:min(n, left)]; lanes.append(x); left -= x.size
            x = np.concatenate(lanes); m[r, g] = 0; m[r, g][:, rng.permutation(L)[:x.size]] = pool[r, g][:, x]
    return pack(w, lm, tl, mo, sn, m, fr)
def setup_inputs_ends(rng):
    def sub(n, den):
        return 255 * (rng.random((N, 8, 16, n)) < den).astype(np.int32)
    w = 127 * rng.integers(0, 2, (8, 16, 3)); w[6, :, 0:2] = 127; w[7, :, 0:2] = 0; w[:, 0, 2] = 0; w[:, 15, 2] = 127
    w[7, 0:4, 0] = 127; w[7, 4:8, 1] = 127; w[7, 13:16, 0] = (127, 127, 3); w[7, 10:13, 1] = (127, 127, 3)
    w = np.tile(w[None], (N, 1, 1, 1)).astype(np.int32); dens = np.array([0.0, 0.3, 0.6, 0.9, 1.0])
    lm = sub(W, 0.15); mo = sub(M, 0.3); tl = (M - 1) * rng.integers(0, 2, (N, 8, 16, W))
    t = rng.integers(0, 3, (N, 8, 1, H)); sn = np.where(t == 0, -1, np.where(t == 1, 255, 256 * rng.integers(0, 2, (N, 8, 16, H)) - 1))
    m = sub(L, rng.choice(dens, (N, 8, 1, L))); fr = sub(RO * L, rng.choice(dens, (N, 8, 1, RO * L)))
    for x in (m, fr):
        x[..., 0] = 255; x[..., -1] = 255
        z = rng.random(x.shape[-1]) < 0.3; z[0] = True; z[-1] = True
        x[:, 7, 0:8][:, :, z] = 0; x[:, 7, 10:16][:, :, z] = 255
    return pack(w, lm, tl, mo, sn, m, fr)
def setup_inputs_late(rng):
    w, lm, tl, mo, sn, m, fr = base(rng)
    lm = mono(rng, W, rng.choice(np.array([0.5, 0.6]), (N, 8, 1, W)), 160)
    pool = mono(rng, 8192, 0.5, 255); u, v = sums(w, pool)
    aim = np.where(np.arange(8) % 2 == 1, H - 1, 0)[:, None]
    k = np.argmax(((((u * v) >> 5) + u) & (H - 1)) == aim, axis=2)
    mo[..., M - 1:] = np.take_along_axis(pool, k[:, :, None, None], 3); sn[..., 0] = -1; sn[..., H - 1] = -1
    x = mono(rng, 4, 0.6, 255); u, v = sums(w, x); c0 = (((u * v) >> 5) + w[:, :, 0, 2:3] * u) & (W - 1)
    np.put_along_axis(lm, c0[:, :, None], x, 3); np.put_along_axis(tl[:, :, 0], c0, M - 1, 2)
    for t in (1, 2):
        fr[..., t * L + N * CAP + 24:t * L + N * CAP + 28] = x
    one = mono(rng, 1, 0.4, 255)
    for g in (3, 4):
        fr[:, g, :, :L] = one[:, g]
    s = (w, lm, tl, mo, sn, m, fr); plant(rng, *s, until=2, n=24); return pack(*s)
def setup_inputs_spread(rng):
    w = np.tile((np.exp2(7 * rng.random((1, 8, 16, 3))) - 1).astype(np.int32), (N, 1, 1, 1)); dens = np.array([0.3, 0.7, 1.0])
    lm = uneven(rng, W, rng.choice(np.array([0.2, 0.4]), (N, 8, 1, W))); mo = uneven(rng, M, 0.4)
    tl = np.minimum(M * rng.random((N, 8, 16, W)) ** 3, M - 1).astype(np.int32); sn = uneven(rng, H, 0.7) - 1
    m = uneven(rng, L, rng.choice(dens, (N, 8, 1, L))); fr = uneven(rng, RO * L, rng.choice(dens, (N, 8, 1, RO * L)))
    s = (w, lm, tl, mo, sn, m, fr); plant(rng, *s); return pack(*s)
def check_inputs(d):
    bad = []
    for k, lo, hi in (("lm", 0, 255), ("tl", 0, M - 1), ("mo", 0, 255), ("sn", -1, 255), ("fm", 0, 255), ("fr", 0, 255), ("wk", 0, 127)):
        x = np.asarray(d[k]).astype(np.float32)
        if not (np.all(x >= lo) and np.all(x <= hi)): bad.append("range of " + k)
        elif np.any(x != np.floor(x)): bad.append("whole numbers in " + k)
    if np.any(d["wk"] != d["wk"][:1]): bad.append("wk alike on all ranks")
    return bad
def reference(lm, tl, mo, sn, fm, fr, wk):
    lead, tail, mon, seen, front, fill, w = [x.astype(np.float32).astype(np.int32).reshape(N, 8, 16, -1) for x in (lm, tl, mo, sn, fm, fr, wk)]
    st = (lead, tail, seen, front, tail[..., :L], np.zeros((N, 8, L), np.int64))
    for t in range(RO):
        st = turn(st, probe(w, st[0], st[1], mon, st[3]), fill[..., t * L:(t + 1) * L])
    return {"yl": st[0].reshape(N, 128, W).astype(np.float32).astype(BF), "yf": st[3].reshape(N, 128, L).astype(np.float32).astype(BF)}

@@ -1,0 +1,715 @@
+from concourse.bass import DstId, RemoteDMATransfer
+from concourse.mybir import dt, AluOpType as A, AxisListType, ActivationFunctionType as F
+
+N, W, H, L, CAP, RO, SL = 4, 2048, 2048, 256, 56, 4, 224
+DUMP = 256
+SW = DUMP + N * 256
+_B, _F, _H, _I, _U = "bfloat16", "float32", "float16", "int32", "uint16"
+_SB = {
+    "xlm": (W + L, _B), "xtl": (W + L, _I), "xmo": (4096, _B), "xsn": (H + L, _B), "sn0": (H, _B), "fm0": (L, _B),
+    "fr0": (RO * L, _B), "wk0": (3, _I), "wkf": (3, _F), "frs": (N * SL, _B), "win0": (SW, _B), "win1": (SW, _B), "win2": (SW, _B), "win3": (SW, _B),
+    "wint0": (SW, _F), "wint1": (SW, _F),
+    "L0": (L, _B), "L1": (L, _B), "L2": (L, _B), "L3": (L, _B), "L4": (L, _B), "TR0": (L, _F), "TR1": (L, _F), "TR2": (L, _F), "yfo": (L, _B),
+    "mp": (L, _B), "mT": (L, _B), "qT": (L, _B), "au": (32, _I), "am": (32, _I), "up": (16, _I), "av": (48, _I), "ci": (L, _I),
+    "cj": (L, _I), "XV": (48, _H), "XA": (256, _H), "ti": (12, _F), "tj": (12, _F), "tk": (12, _F), "tbl": (2304, _B),
+    "CL": (L, _U), "X": (4096, _B), "E": (4096, _B), "Y": (4096, _B), "P": (4096, _B), "NE": (4096, _B), "SX": (4096, _B),
+    "SC": (272, _F), "gi": (16, _I), "gj": (16, _I), "GV": (16, _H), "XG": (256, _H), "GL": (16, _U), "TG": (L, _U), "xg": (L, _B),
+    "hi": (512, _I), "hp": (256, _I), "hq": (256, _I), "hs": (256, _I), "hh": (256, _I), "hf": (256, _H), "HL": (256, _U), "Kh": (256, _F),
+    "k2": (256, _F), "SC2": (256, _F), "ki": (16, _I), "kj": (16, _I), "IV": (16, _H), "XI": (256, _B), "CHL": (16, _U), "CH": (L, _B),
+    "has": (16, _F), "kh": (16, _I), "ch": (16, _I), "cd": (16, _I), "nc": (16, _I), "dd": (16, _I), "OH": (80, _B),
+    "w3": (80, _H), "rin": (N * SL, _B), "XS": (256, _H), "sf": (16, _F), "SLL": (16, _U),
+    "TGp": (L, _F), "mk": (L, _F), "YT": (L, _F), "CT": (L, _I), "CTm": (L, _I),
+    "nh": (16, _B), "nn": (16, _B), "lq": (16, _F), "sq": (16, _F),
+}
+for _z in "ls":
+    for _k, _v in {"y": (16, _F), "V2": (16, _H), "XW": (256, _H), "WA": (16, _U), "FT0": (L, _B), "FT1": (L, _B), "SCW": (1024, _B), "SCM": (1024, _B), "nd": (16, _F),
+                   "z": (16, _F), "V3": (16, _H), "XV": (256, _H), "WL": (16, _U)}.items():
+        _SB[_k + _z] = _v
+_CO = {
+    "one": (512, _B), "I": (128, _B), "nI": (128, _B), "Ih": (128, _H), "bo": (128, _B), "b8": (8, _B), "tmp": (128, _B), "tri": (128, _B),
+    "Rep": (512, _B), "RepN": (512, _B), "Sel": (144, _B), "Selh": (144, _H), "i4": (128, _B), "R8": (128, _B), "TR": (128, _B), "key": (128, _B),
+    "key18": (136, _B), "r16": (128, _F), "cC": (16, _B), "lane": (16, _F), "base": (80, _B),
+    "i5": (40, _B), "mkc": (256, _B), "EC17": (136, _H), "key17": (136, _B), "r17": (136, _F), "pc": (8, _F), "pi": (4, _I), "Wb": (128, _B), "Wt": (16, _B), "cT": (256, _F), "NB8": (8, _B), "PB8": (8, _B),
+    "c32": (32, _F), "duT": (16, _F), "dlT": (16, _F), "e0": (128, _F), "e1": (128, _F), "e2": (128, _F), "ek": (128, _F), "ea": (128, _F),
+    "EC": (128, _H), "EA": (128, _H),
+}
+_PACK, _POS = {}, {}
+for _k in list(_SB) + list(_CO):
+    _n, _t = (_SB.get(_k) or _CO.get(_k))
+    if _n <= 64:
+        _nn = max(32, (_n + 31) // 32 * 32)
+        _o = _PACK.get(_t, 0)
+        _POS[_k] = ("pk_" + _t, _o)
+        _PACK[_t] = _o + _nn
+    else:
+        _POS[_k] = ("t_" + _k, 0)
+SCRATCH = {}
+for _k in list(_SB) + list(_CO):
+    _n, _t = (_SB.get(_k) or _CO.get(_k))
+    if _n > 64:
+        SCRATCH["t_" + _k] = ("sbuf", [128, _n], _t)
+for _t, _n in _PACK.items():
+    SCRATCH["pk_" + _t] = ("sbuf", [128, _n], _t)
+for _k in range(8):
+    SCRATCH["ps%d" % _k] = ("psum", [128, 512], "float32")
+    _POS["ps%d" % _k] = ("ps%d" % _k, 0)
+_QUE = ("V", "S", "T", "G")
+SEMAPHORES = ["q" + e for e in _QUE] + ["ld%d" % i for i in range(12)] + ["rarr", "rloc", "st0", "st1"] + \
+    ["%s%d" % (p, t) for p in ("arr", "tarr", "loc", "tloc") for t in range(RO)]
+
+GB, EB = "VSSSVVSS", "VVVVSSVS"
+GD, ED = "SVSSVSSV", "VSSVSSSV"
+SE = "SSVSSVVV"
+BI = (-11.0, -8.0, -2.0, -1.0)
+
+
+def rank_program(g, core, T, topo):
+    me = T.rank_of(core)
+    if me is None:
+        return
+    others = [(me + 1 + k) % N for k in range(N - 1)]
+    ops = []
+    bias = [0.0]
+
+    def v(name, a=None, b=None, step=1, p0=0, p1=128):
+        buf, o = _POS[name]
+        n = (_SB.get(name) or _CO.get(name) or (512, _F))[0]
+        a = 0 if a is None else a
+        b = n if b is None else b
+        return (buf, p0, p1, o + a, o + b, step)
+
+    def ap(x):
+        if x[5] == 1:
+            return T[x[0]][x[1]:x[2], x[3]:x[4]]
+        return T[x[0]][x[1]:x[2], x[3]:x[4]:x[5]]
+
+    def ncol(x):
+        return len(range(x[3], x[4], x[5]))
+
+    def arg(s):
+        return ap(s) if isinstance(s, tuple) else s
+
+    def op(q, fn, rd, wr, cost, sem=None, val=0, lag=0.06, after=None, n=1):
+        ops.append({"q": q, "fn": fn, "rd": rd, "wr": wr, "cost": cost, "sem": sem, "val": val, "lag": lag, "after": after, "bias": bias[0]})
+        return len(ops) - 1
+
+    cyc = 0.00083 * 1.2
+
+    def vc(n, f=1.0):
+        return 0.03 + cyc * max(64, n * f)
+
+    two = ("pk_bfloat16", "pk_float16", "pk_uint16")
+
+    def is2(x):
+        return x[0] in two or SCRATCH[x[0]][2] in (_B, _H, _U)
+
+    def tc(out, x):
+        f = 0.5 if is2(out) and is2(x) else 1.0
+        return op("V", lambda: g.vector.tensor_copy(ap(out), ap(x)), [x], [out], vc(ncol(x), f))
+
+    def tt(out, x, y, o):
+        f = 1.0 if x[0][:2] == "ps" or y[0][:2] == "ps" else 2.0
+        return op("V", lambda: g.vector.tensor_tensor(ap(out), ap(x), ap(y), o), [x, y], [out], vc(ncol(x), f))
+
+    def ts(out, x, s1, o1, s2=None, o2=None):
+        f = 0.5 if is2(out) and is2(x) else 1.0
+        rd = [x] + [s for s in (s1, s2) if isinstance(s, tuple)]
+        if o2 is None:
+            return op("V", lambda: g.vector.tensor_scalar(ap(out), ap(x), arg(s1), None, o1), rd, [out], vc(ncol(x), f))
+        return op("V", lambda: g.vector.tensor_scalar(ap(out), ap(x), arg(s1), arg(s2), o1, o2), rd, [out], vc(ncol(x), f))
+
+    def scan(out, d0, d1):
+        return op("V", lambda: g.vector.tensor_tensor_scan(ap(out), ap(d0), ap(d1), 0.0, A.mult, A.max), [d0, d1], [out], vc(ncol(d1)))
+
+    def vset(out, c):
+        return op("V", lambda: g.vector.memset(ap(out), c), [], [out], vc(ncol(out), 0.5))
+
+    def act(out, x, fn=F.Copy, bias=0.0, scale=1.0):
+        return op("S", lambda: g.scalar.activation(ap(out), ap(x), fn, bias=arg(bias), scale=arg(scale)),
+                  [x] + [s for s in (bias, scale) if isinstance(s, tuple)], [out], 0.06 + cyc * ncol(x))
+
+    def copy(q, out, x):
+        return tc(out, x) if q == "V" else act(out, x)
+
+    def gather(q, out, win, off):
+        c = 0.06 + cyc * 1.5 * ncol(out)
+        if q == "V":
+            return op("V", lambda: g.vector.tensor_copy(ap(out), ap(win).indirect(ap(off))), [win, off], [out], c)
+        return op("S", lambda: g.scalar.activation(ap(out), ap(win).indirect(ap(off)), F.Copy), [win, off], [out], c)
+
+    def gatherop(out, win, off, y, o):
+        return op("V", lambda: g.vector.tensor_tensor(ap(out), ap(win).indirect(ap(off)), ap(y), o), [win, off, y], [out],
+                  0.06 + cyc * 1.5 * ncol(out))
+
+    def scatter(win, off, x):
+        return op("V", lambda: g.vector.tensor_copy(ap(win).indirect(ap(off)), ap(x)), [x, off], [win], 0.06 + cyc * 3 * ncol(x))
+
+    def mm(out, lhsT, rhs, start=True, stop=True):
+        m = ncol(lhsT)
+        return op("T", lambda: g.tensor.matmul(ap(out), ap(lhsT), ap(rhs), start, stop), [lhsT, rhs], [out],
+                  0.0005 * max(min(64, m), ncol(rhs)))
+
+    def pick(out, x, pattern, cmp, fill, base, cm):
+        n = ncol(out)
+        return op("G", lambda: g.affine_select(ap(out), ap(x), pattern, cmp, fill, base, cm), [x], [out, pool], 0.2 + cyc * 2 * n)
+
+    def iota(out, pattern, base, cm, small=True):
+        def fn():
+            if small:
+                return g.iota(ap(out), pattern, base, cm, allow_small_or_imprecise_dtypes=True)
+            return g.iota(ap(out), pattern, base, cm)
+        return op("G", fn, [], [out, pool], 0.15 + cyc * 2 * ncol(out))
+    pool = ("pool", 0, 128, 0, 1, 1)
+
+    nld = [0]
+
+    def load(q, out, src, cost):
+        s = "ld%d" % nld[0]
+        nld[0] += 1
+        eng = g.sync if q == "D" else g.scalar
+        return op(q, lambda: eng.dma_start(ap(out), src), [], [out, ("order", 0, 128, 0, 1, 2)], 0.08, sem=s, val=16, lag=2.0 + cost)
+
+    bank = [0]
+
+    def ps(a=0, b=512, step=1, p0=0, p1=128, k=None):
+        k = bank[0] if k is None else k
+        return ("ps%d" % k, p0, p1, a, b, step)
+
+    def nb(kind=0):
+        cnt[kind] += 1
+        return (cnt[kind] % 2, 2 + cnt[kind] % 4, 6 + cnt[kind] % 2)[kind]
+    cnt = {0: 0, 1: 0, 2: 0}
+
+
+    def fused(name, src, dst, sem, loc, t_lag, after=None):
+        eng = topo.engines(core, T.cores[others[0]])
+        for d in others:
+            eng = [e for e in eng if e in topo.engines(core, T.cores[d])]
+        parts, total = [eng[0:len(eng) // 4], eng[len(eng) // 4:len(eng) // 2], eng[len(eng) // 2:]], len(eng)
+
+        def fn():
+            tr = []
+            for d, es in zip(others, parts):
+                rid, pid, _ = topo.addr(T.cores[d])
+                m = 0
+                for e in es:
+                    m |= 1 << e
+                tr.append(RemoteDMATransfer(dst_ids=[DstId(rid=rid, pnc=pid)], dma_engine_mask=m, remote_sem=T.sem[sem],
+                                            srcs=[ap(src(d))], dsts=[ap(dst(d))], alu_op=0))
+            return g.remote_dma_fused(tr, local_sem=T.sem[loc])
+        return op("G", fn, [src(d) for d in others], [], 1.0, sem=loc, val=total, lag=1.5)
+
+    def got(sem, total, wr, after, lag):
+        return op("R", None, [], wr, 0.0, sem=sem, val=total, lag=lag, after=after)
+
+    def arrivals():
+        n = 0
+        for s in others:
+            od = [(s + 1 + k) % N for k in range(N - 1)]
+            eng = topo.engines(T.cores[s], T.cores[od[0]])
+            for d in od:
+                eng = [e for e in eng if e in topo.engines(T.cores[s], T.cores[d])]
+            parts = [eng[0:len(eng) // 4], eng[len(eng) // 4:len(eng) // 2], eng[len(eng) // 2:]]
+            n += len(parts[od.index(me)])
+        return n
+    narr = arrivals()
+
+    def slot(d, name, t):
+        return v("%s%d" % (name, t), DUMP + 256 * d, DUMP + 256 * d + CAP)
+
+    load("D", v("fm0"), T.fm[:], 0.5)
+    load("D", v("wk0"), T.wk[:], 0.2)
+    load("D", v("xlm", 0, W), T.lm[:], 2.0)
+    load("D", v("xtl", 0, W), T.tl[:], 5.0)
+    load("D", v("xmo"), T.mo[:], 8.0)
+    load("D", v("fr0"), T.fr[:], 9.0)
+    load("D", v("sn0"), T.sn[:], 11.0)
+    vset(v("one", 0, 128), 1.0)
+    vset(v("one", 128, 512), 1.0)
+    o128 = v("one", 0, 128)
+    pick(v("I"), o128, [[-1, 128]], A.is_equal, 0.0, 0, 1)
+    pick(v("tmp"), o128, [[-16, 8], [0, 16]], A.is_ge, 0.0, 0, 1)
+    pick(v("bo"), v("tmp"), [[16, 8], [0, 16]], A.is_ge, 0.0, 15, -1)
+    for k in range(3):
+        pick(v("e%d" % k, p1=24), v("one", 0, 128, p1=24), [[-1, 8], [0, 16]], A.is_equal, 0.0, -8 * k, 1)
+    pick(v("RepN", p1=32), v("one", 0, 512, p1=32), [[-1, 32], [0, 16]], A.is_equal, 0.0, 0, 1)
+    for a in range(4):
+        act(v("i4", 32 * a, 32 * a + 32, p1=32), v("I", 0, 32, p1=32))
+    b = nb(0)
+    mm(ps(k=b), v("i4", p1=32), v("RepN", p1=32))
+    act(v("Rep"), ps(k=b))
+    act(v("RepN"), ps(k=b), scale=-1.0)
+    ts(v("nI"), v("I"), -1.0, A.mult)
+    tc(v("Ih"), v("I"))
+    tc(v("b8"), v("bo", 0, 128, 16))
+    ts(v("NB8"), v("b8"), -8388608.0, A.mult)
+    ts(v("PB8"), v("b8"), 131072.0, A.mult)
+    iota(v("key"), [[0, 8], [-2048, 16]], 65536 + 32768, 0)
+    iota(v("pi", 0, 1), [[0, 1]], 0, 1, False)
+    ts(v("pi", 1, 2), v("pi", 0, 1), 15, A.bitwise_and)
+    tc(v("pc", 0, 1), v("pi", 1, 2))
+    ts(v("pc", 1, 2), v("pc", 0, 1), 0.0, A.is_gt)
+    ts(v("pc", 2, 3), v("pc", 0, 1), -16.0, A.add)
+    ts(v("pc", 4, 5), v("pc", 1, 2), 65536.0, A.mult)
+    ts(v("pi", 3, 4), v("pi", 0, 1), 4, A.arith_shift_right, 1, A.bitwise_and)
+    tc(v("pc", 6, 7), v("pi", 3, 4))
+    ts(v("pc", 5, 6), v("pc", 6, 7), -1.0, A.mult, 1.0, A.add)
+    tc(v("wkf"), v("wk0"))
+    ts(v("Wb"), v("bo"), v("wkf", 0, 1), A.mult)
+    ts(v("tri"), v("bo"), v("wkf", 1, 2), A.mult)
+    ts(v("tmp"), v("I"), v("wkf", 2, 3), A.mult)
+    b = nb(1)
+    mm(ps(0, 128, p1=24, k=b), v("one", 0, 24), v("tmp"))
+    tt(v("ek", p1=24), v("e1", p1=24), ps(0, 128, p1=24, k=b), A.mult)
+    tt(v("EC", p1=24), v("ek", p1=24), v("e0", p1=24), A.add)
+    ts(v("ea", p1=24), v("e2", p1=24), 2048.0, A.mult)
+    tt(v("EA", p1=24), v("ea", p1=24), v("e0", p1=24), A.add)
+    vset(v("r16"), 1.0)
+    vset(v("r16", 0, 128, 16), 0.0)
+    for x in range(2):
+        w = v("wkf", x, x + 1)
+        ts(v("Wt", 8 * x, 8 * x + 8), v("b8"), w, A.mult, -1.0, A.mult)
+        b = nb(1)
+        mm(ps(0, 128, k=b), o128, v("Wb") if x == 0 else v("tri"))
+        ts(v("cT", 128 * x, 128 * x + 128), ps(0, 128, k=b), 255.0, A.mult)
+    b = nb(1)
+    mm(ps(0, 16, k=b), o128, v("Wt"))
+    for h in range(2):
+        ts(v("c32", h, 32, 2), ps(0, 16, k=b), -255.0, A.mult)
+    for gr in range(8):
+        tc(v("EC17", 17 * gr, 17 * gr + 16, p1=24), v("EC", 16 * gr, 16 * gr + 16, p1=24))
+    tc(v("EC17", 16, 136, 17, p1=24), v("EC", 0, 128, 16, p1=24))
+    iota(v("key17"), [[0, 8], [-2048, 17]], 32768, 0)
+    ts(v("key18"), v("key17"), 128.0, A.mult)
+    vset(v("r17"), 1.0)
+    vset(v("r17", 0, 136, 17), 0.0)
+    pick(v("Sel", p1=8), v("one", 0, 144, p1=8), [[1, 144]], A.is_equal, 0.0, -16, -16)
+    for k in range(5):
+        act(v("i5", 8 * k, 8 * k + 8, p1=8), v("I", 0, 8, p1=8))
+    b = nb(1)
+    mm(ps(0, 144, p1=40, k=b), v("i5", p1=8), v("Sel", p1=8))
+    tc(v("Selh", p1=40), ps(0, 144, p1=40, k=b))
+    iota(v("duT"), [[0, 8], [128, 2]], 1024, 1)
+    ts(v("dlT"), v("duT"), 1024.0, A.add)
+    iota(v("ti"), [[1, 12]], 0, 0)
+    ts(v("tj"), v("ti"), v("pc", 0, 1), A.is_equal)
+    ts(v("tk"), v("tj"), 2.0, A.mult, -1.0, A.add)
+    vset(v("tbl", 0, 1), -1.0)
+    for k in range(12):
+        n = min(1 << k, 2304 - (1 << k))
+        ts(v("tbl", 1 << k, (1 << k) + n), v("tbl", 0, n), v("tk", k, k + 1), A.max)
+    iota(v("lane", 0, 16), [[16, 16]], 0, 0)
+    ts(v("lane", 0, 16), v("lane", 0, 16), v("pc", 0, 1), A.add)
+    for h in range(2):
+        ts(v("cC", 8 * h, 8 * h + 8), v("lane", 0, 8), 16.0, A.mult, 16.0, A.add)
+    iota(v("base"), [[256, 5], [0, 16]], 0, 0)
+    pick(v("R8", p1=8), v("one", 0, 128, p1=8), [[-1, 8], [0, 16]], A.is_equal, 0.0, 0, 1)
+    for t in range(RO - 1):
+        o = v("TR%d" % t, SL if t else 0, L)
+        act(o, v("one", 0, ncol(o)), F.Identity, 0.0, v("pc", 4, 5))
+        for d in range(N):
+            if t < RO - 2:
+                act(slot(d, "wint", t), v("one", 0, CAP), F.Identity, 0.0, v("pc", 4, 5))
+    pick(v("TR"), o128, [[1, 128]], A.is_gt, 0.0, 0, -1)
+    ts(v("mkc"), v("one", 0, 256), -7.5, A.mult)
+    for a in range(2):
+        x = v("mkc", p0=64 * a, p1=64 * a + 64)
+        pick(x, x, [[0, 4], [1, 64]], A.is_gt, -100.0, 0, -1)
+    TRI = v("TR")
+    ts(v("xsn", 0, H), v("sn0"), -1.0, A.mult, 255.0, A.add)
+
+    for s in others + [me]:
+        for t in range(RO):
+            o = v("frs", s * SL + t * CAP, s * SL + t * CAP + CAP)
+            if s == me:
+                o = slot(me, "win", t)
+            act(o, v("fr0", t * L + s * CAP, t * L + s * CAP + CAP), F.Identity, 255.0, -1.0)
+    for t in range(RO):
+        act(v("L%d" % (t + 1), SL, L), v("fr0", t * L + SL, t * L + L), F.Identity, 255.0, -1.0)
+    snd = fused("r", lambda d: v("frs", d * SL, d * SL + SL), lambda d: v("rin", me * SL, me * SL + SL), "rarr", "rloc", 0)
+    got("rarr", narr, [v("rin", s * SL, s * SL + SL) for s in others], snd, 8.0)
+    for t in range(RO):
+        for s in others:
+            act(slot(s, "win", t), v("rin", s * SL + t * CAP, s * SL + t * CAP + CAP))
+
+    ts(v("L0"), v("fm0"), -1.0, A.mult, 255.0, A.add)
+
+    def halves(name, h, n=128):
+        return v(name, h * n, h * n + n)
+
+    def todisk(b, c, X, x0, n, first, sel="Selh", rows=8):
+        for ll in range(16):
+            mm(ps(c, c + n, k=b), v(sel, 16 - ll, 144 - ll, p1=rows), v(X, x0 + ll, x0 + 16 * n, 16, p1=rows), first and ll == 0, ll == 15)
+
+    def tolist(src, xs, out, shift):
+        b = nb(2)
+        for h in range(2):
+            mm(ps(128 * h, 128 * h + 128, p1=8, k=b), ps8(src, h), v("Ih"))
+        tc(v(xs, p1=8), ps(0, 256, p1=8, k=b))
+        b = nb(2)
+        todisk(b, 0, xs, 0, 16, True)
+        ts(v(out), ps(0, 16, k=b), shift, A.add)
+
+    def ps8(src, h):
+        return v(src, h, 16, 2)
+
+    def lowest(z, places, q, valid):
+        for k in range(2):
+            x = v("FT%d%s" % (k, z))
+            op("S", lambda x=x, k=k: g.scalar.activation(ap(x), ap(v("tbl")).indirect(ap(v(places))), F.Copy, scale=ap(v("pc", 5 + k, 6 + k))),
+               [v("tbl"), v(places), v("pc", 5 + k, 6 + k)], [x], 0.06 + cyc * 1.5 * 256)
+        tt(v("y" + z), q, valid, A.mult)
+        for pair in range(4):
+            b, p = nb(2), 32 * pair
+            mm(ps(0, 256, k=b), v("I"), v("mkc"), True, False)
+            for odd in range(2):
+                for lc in range(2):
+                    for blk in range(2):
+                        c, o = lc * 128 + blk * 64, (odd * 2 + lc) * 64
+                        x = v("FT%d%s" % (odd, z), c, c + 64, p0=p, p1=p + 32)
+                        mm(ps(o, o + 64, p0=64 * blk, p1=64 * blk + 64, k=b), x, x, False, False)
+            mm(ps(0, 256, k=b), v("I"), v("mkc"), False, True)
+            act(v("SCW" + z, 256 * pair, 256 * pair + 256), ps(0, 256, k=b), F.Relu)
+        b = nb(2)
+        for k in range(16):
+            for blk in range(2):
+                p = 64 * blk
+                mm(ps(k, k + 1, p0=p, p1=p + 64, k=b), v("SCW" + z, 64 * k, 64 * k + 64, p0=p, p1=p + 64),
+                   (valid[0], p, p + 64, valid[3] + k, valid[3] + k + 1, 1))
+        ts(v("nd" + z), ps(0, 16, k=b), 0.5, A.is_lt)
+        tt(v("z" + z), v("y" + z), v("nd" + z), A.mult)
+        tt(v("V3" + z), v("z" + z), v("duT"), A.add)
+        tolist("V3" + z, "XV" + z, "WL" + z, 1024.0)
+
+    for t in range(RO):
+        last = t == RO - 1
+        Lt, Ln = "L%d" % t, "L%d" % (t + 1)
+        bias[0] = 0.0
+        b = nb(1)
+        for h in range(2):
+            mm(ps(h, 32, 2, k=b), halves(Lt, h), v("Wt"))
+        tt(v("au"), ps(0, 32, k=b), v("c32"), A.add)
+        ts(v("am"), v("au"), 4095, A.bitwise_and)
+        tt(v("up"), v("am", 0, 16), v("am", 16, 32), A.mult)
+        ts(v("av", 0, 16), v("up"), 5, A.arith_shift_right, 2047, A.bitwise_and)
+        ts(v("av", 16, 32), v("am", 0, 16), 2047, A.bitwise_and)
+        ts(v("av", 32, 48), v("up"), 16, A.arith_shift_right, 1, A.bitwise_and)
+        tc(v("XV"), v("av"))
+        for h in range(2):
+            act(halves("mp", h), halves(Lt, h), F.Identity, 255.0, -1.0)
+            b2 = nb(1)
+            mm(ps(0, 128, k=b2), halves("mp", h), v("I"))
+            act(halves("mT", h), ps(0, 128, k=b2))
+            b = nb(1)
+            mm(ps(0, 128, p1=24, k=b), v("XV", h, 48, 2), v("Ih"))
+            xa = v("XA", 128 * h, 128 * h + 128, p1=24)
+            tc(xa, ps(0, 128, p1=24, k=b))
+            b = nb(1)
+            mm(ps(0, 128, k=b), v("EC", p1=24), xa)
+            tc(halves("ci", h), ps(0, 128, k=b))
+            ts(halves("cj", h), halves("ci", h), 2047, A.bitwise_and)
+            tc(halves("CL", h), halves("cj", h))
+        for h in range(2):
+            for q in range(4 * h, 4 * h + 4):
+                a = q % 4
+                x, e, off = halves("X", q, 512), halves("E", q, 512), halves("CL", q, 32)
+                gather(GB[q], x, v("xlm", 0, W), off)
+                mt = v("mT", h * 128, h * 128 + 128, p0=32 * a, p1=32 * a + 32)
+                b = nb(0)
+                if EB[q] == "V":
+                    mm(ps(k=b), mt, v("Rep", p0=32 * a, p1=32 * a + 32))
+                    tt(e, x, ps(k=b), A.is_gt)
+                else:
+                    mm(ps(k=b), mt, v("RepN", p0=32 * a, p1=32 * a + 32), True, False)
+                    mm(ps(k=b), v("I"), x, False, True)
+                    act(e, ps(k=b), F.Relu)
+            b = nb(1)
+            mm(ps(0, 136, k=b), v("I"), v("key18"), True, False)
+            for i in range(16):
+                mm(ps(i, 136, 17, k=b), v("E", 2048 * h + i, 2048 * h + 2048, 16), v("NB8"), False, False)
+            mm(ps(0, 136, k=b), v("XA", 128 * h, 128 * h + 128, p1=24), v("EC17", p1=24), False, True)
+            scan(halves("SC", h, 136), v("r17"), ps(0, 136, k=b))
+            G8 = [v(z, 8 * h, 8 * h + 8) for z in ("gi", "gj", "GV", "GL")]
+            tc(G8[0], v("SC", 136 * h + 16, 136 * h + 136, 17))
+            ts(G8[1], G8[0], 2047, A.bitwise_and)
+            tc(G8[2], G8[1])
+            b = nb(1)
+            mm(ps(0, 128, p1=8, k=b), G8[2], v("Ih"))
+            tc(v("XG", 128 * h, 128 * h + 128, p1=8), ps(0, 128, p1=8, k=b))
+            b = nb(1)
+            todisk(b, 0, "XG", 128 * h, 8, True)
+            tc(G8[3], ps(0, 8, k=b))
+            gather("V", halves("TG", h), v("xtl", 0, W), G8[3])
+            gather("S", halves("xg", h), v("xlm", 0, W), G8[3])
+            b = nb(1)
+            mm(ps(0, 128, k=b), halves("xg", h), v("I"), True, False)
+            mm(ps(0, 128, k=b), halves("mp", h), v("nI"), False, True)
+            act(halves("qT", h), ps(0, 128, k=b))
+        if t < RO - 2:
+            ts(v("TGp"), v("TG"), 8192.0, A.add)
+        for h in range(2):
+            ts(v("has", h, 16, 2), v("SC", 136 * h + 16, 136 * h + 136, 17), 262144.0, A.is_ge)
+            tt(v("lq", h, 16, 2), v("gj", 8 * h, 8 * h + 8), v("dlT", h, 16, 2), A.subtract)
+        ts(v("nh"), v("has"), -1.0, A.mult, 1.0, A.add)
+        bias[0] = BI[0]
+        lowest("l", "GL", v("lq"), v("nh"))
+        bias[0] = BI[1]
+        if not last:
+            b = nb(2)
+            mm(ps(0, 256, k=b), v("EA", p1=24), v("XA", p1=24))
+            b2 = nb(2)
+            ts(ps(0, 256, k=b2), v("xtl", 0, L), 32768.0, A.add)
+            tt(v("YT"), v("TR%d" % t), ps(0, 256, k=b), A.max)
+            tt(v("CT"), v("YT"), ps(0, 256, k=b2), A.min)
+            ts(v("CTm"), v("CT"), 4095, A.bitwise_and)
+        for blk in range(3, -1, -1):
+            d = 64 * blk
+            wl = v("WLl", 4 * blk, 4 * blk + 4)
+            scatter(v("xlm"), wl, v("mp", d, d + 64))
+            if not last:
+                scatter(v("xtl"), wl, v("CTm", d, d + 64))
+        bias[0] = 0.0
+        for h in range(2):
+            for q in range(4 * h, 4 * h + 4):
+                a = q % 4
+                y, p = halves("Y", q, 512), halves("P", q, 512)
+                gather(GD[q], y, v("xmo"), halves("TG", q, 32))
+                b = nb(0)
+                mm(ps(k=b), v("qT", h * 128, h * 128 + 128, p0=32 * a, p1=32 * a + 32), v("Rep", p0=32 * a, p1=32 * a + 32), True, False)
+                mm(ps(k=b), v("nI"), y, False, True)
+                if ED[q] == "V":
+                    ts(p, ps(k=b), 255.0, A.add, 0.0, A.max)
+                else:
+                    act(p, ps(k=b), F.Relu, 255.0)
+            b = nb(1)
+            for i in range(16):
+                mm(ps(i, 256, 16, k=b), v("P", 2048 * h + i, 2048 * h + 2048, 16), v("Wt"))
+            u = halves("hi", h, 256)
+            tt(u, ps(0, 256, k=b), v("cT"), A.add)
+            ts(u, u, 4095, A.bitwise_and)
+            u0, u1 = v("hi", 256 * h, 256 * h + 128), v("hi", 256 * h + 128, 256 * h + 256)
+            tt(halves("hp", h), u0, u1, A.mult)
+            ts(halves("hq", h), halves("hp", h), 5, A.arith_shift_right)
+            tt(halves("hs", h), halves("hq", h), u0, A.add)
+            ts(halves("hh", h), halves("hs", h), 2047, A.bitwise_and)
+            tc(halves("hf", h), halves("hh", h))
+            b = nb(1)
+            mm(ps(0, 128, k=b), halves("hf", h), v("Ih"))
+            tc(halves("HL", h), ps(0, 128, k=b))
+            b = nb(1)
+            mm(ps(0, 128, k=b), v("I"), v("key"), True, False)
+            mm(ps(0, 128, k=b), v("Ih"), halves("hf", h), False, True)
+            act(halves("Kh", h), ps(0, 128, k=b))
+        bias[0] = BI[3]
+        for h in range(2):
+            for q in range(4 * h, 4 * h + 4):
+                ne, p, sx = halves("NE", q, 512), halves("P", q, 512), halves("SX", q, 512)
+                if SE[q] == "V":
+                    gatherop(ne, v("xsn", 0, H), halves("HL", q, 32), p, A.not_equal)
+                else:
+                    gather("S", sx, v("xsn", 0, H), halves("HL", q, 32))
+                    b = nb(0)
+                    mm(ps(k=b), v("nI"), p, True, False)
+                    mm(ps(k=b), v("I"), sx, False, True)
+                    act(ne, ps(k=b), F.Abs)
+            b = nb(1)
+            for i in range(16):
+                mm(ps(i, 128, 16, k=b), v("NE", 2048 * h + i, 2048 * h + 2048, 16), v("PB8"))
+            tt(halves("k2", h), ps(0, 128, k=b), halves("Kh", h), A.min)
+            scan(halves("SC2", h), v("r16"), halves("k2", h))
+            tt(v("kh", h, 16, 2), v("SC2", 128 * h + 15, 128 * h + 128, 16), v("has", h, 16, 2), A.mult)
+        bias[0] = 0.0
+        tc(v("ki"), v("SC2", 15, 256, 16))
+        ts(v("kj"), v("ki"), 11, A.arith_shift_right, 31, A.bitwise_and)
+        ts(v("IV"), v("kj"), 1.0, A.max, -1.0, A.mult)
+        b = nb(1)
+        for h in range(2):
+            mm(ps(128 * h, 128 * h + 128, p1=8, k=b), v("IV", 8 * h, 8 * h + 8), v("Ih"))
+        act(v("XI", p1=8), ps(0, 256, p1=8, k=b))
+        b = nb(1)
+        mm(ps(0, 16, k=b), v("I"), v("cC"), True, False)
+        todisk(b, 0, "XI", 0, 16, False, "Sel")
+        tc(v("CHL"), ps(0, 16, k=b))
+        for h in range(2):
+            gather("S", halves("CH", h), halves("P", h, 2048), v("CHL", 8 * h, 8 * h + 8))
+        ts(v("dd"), v("kh"), 65536 + 3, A.bitwise_and)
+        for d in range(N + 1):
+            ts(v("OH", 16 * d, 16 * d + 16), v("dd"), float(65536 + d - 1 if d else 0), A.is_equal)
+        b = nb(1)
+        mm(ps(0, 80, k=b), v("I"), v("base"), True, False)
+        mm(ps(1, 80, 2, k=b), o128, v("OH", 0, 80, 2), False, False)
+        mm(ps(0, 80, k=b), TRI, v("OH"), False, True)
+        tt(v("w3"), ps(0, 80, k=b), v("OH"), A.mult)
+        b = nb(1)
+        for h in range(2):
+            mm(ps(128 * h, 128 * h + 128, p1=40, k=b), v("w3", h, 80, 2), v("Ih"))
+        tc(v("XS", p1=40), ps(0, 256, p1=40, k=b))
+        b = nb(1)
+        todisk(b, 0, "XS", 0, 16, True, rows=40)
+        tc(v("SLL"), ps(0, 16, k=b))
+        wt = "win%d" % t
+        scatter(v(wt), v("SLL"), v("CH"))
+        mine = (me * CAP, me * CAP + CAP)
+        snd = fused("m", lambda d, t=t: slot(d, "win", t), lambda d, Ln=Ln: v(Ln, mine[0], mine[1]), "arr%d" % t, "loc%d" % t, 0)
+        act(v(Ln, mine[0], mine[1]), slot(me, "win", t))
+        got("arr%d" % t, narr, [v(Ln, s * CAP, s * CAP + CAP) for s in others], snd, 3.0)
+        if t < RO - 2:
+            TR = "TR%d" % (t + 1)
+            b = nb(2)
+            mm(ps(0, 256, k=b), v("R8", p1=8), v("XI", p1=8))
+            ts(v("mk"), ps(0, 256, k=b), v("pc", 2, 3), A.not_equal)
+            wv = v("wint%d" % t)
+            op("V", lambda wv=wv: g.vector.tensor_tensor(ap(wv).indirect(ap(v("SLL"))), ap(v("TGp")), ap(v("mk")), A.mult),
+               [v("SLL"), v("TGp"), v("mk")], [wv], 0.06 + cyc * 3 * 256)
+            snd = fused("t", lambda d, t=t: slot(d, "wint", t), lambda d, TR=TR: v(TR, mine[0], mine[1]), "tarr%d" % t, "tloc%d" % t, 0)
+            act(v(TR, mine[0], mine[1]), slot(me, "wint", t))
+            got("tarr%d" % t, narr, [v(TR, s * CAP, s * CAP + CAP) for s in others], snd, 4.0)
+        if not last:
+            ts(v("ch"), v("kh"), 2047, A.bitwise_and)
+            ts(v("nn"), v("kh"), 0.0, A.is_gt)
+            tt(v("sq"), v("ch"), v("dlT"), A.subtract)
+            bias[0] = BI[2]
+            tc(v("V2s"), v("ch"))
+            tolist("V2s", "XWs", "WAs", 0.0)
+            lowest("s", "WAs", v("sq"), v("nn"))
+            for blk in range(3, -1, -1):
+                scatter(v("xsn"), v("WLs", 4 * blk, 4 * blk + 4), v("CH", 64 * blk, 64 * blk + 64))
+    ts(v("yfo"), v("L4"), -1.0, A.mult, 255.0, A.add)
+    op("D", lambda: g.sync.dma_start(T.yf[:], ap(v("yfo"))), [v("yfo")], [], 0.08, sem="st0", val=16, lag=2.0)
+    op("D", lambda: g.sync.dma_start(T.yl[:], ap(v("xlm", 0, W))), [v("xlm", 0, W)], [], 0.08, sem="st1", val=16, lag=2.0)
+    _emit(g, T, ops)
+
+
+def _emit(g, T, ops):
+    nop = len(ops)
+    acc, deps = {}, [None] * nop
+
+    def mask(x):
+        if x[5] == 1:
+            return ((1 << (x[4] - x[3])) - 1) << x[3]
+        m = 0
+        for c in range(x[3], x[4], x[5]):
+            m |= 1 << c
+        return m
+    memo = {}
+    for i, o in enumerate(ops):
+        need = {}
+        mine = []
+        for wr, lst in ((0, o["rd"]), (1, o["wr"])):
+            for x in lst:
+                if x not in memo:
+                    memo[x] = mask(x)
+                mine.append((x[0], x[1], x[2], memo[x], wr))
+        for (bf, p0, p1, m, wr) in mine:
+            for (j, q0, q1, mj, wj) in acc.get(bf, ()):
+                if j == i:
+                    continue
+                same = ops[j]["q"] == o["q"]
+                if bf[:2] == "ps":
+                    hit = not same or ((wr or wj) and (m & mj) and p0 < q1 and q0 < p1)
+                else:
+                    hit = (wr or wj) and (m & mj) and p0 < q1 and q0 < p1
+                if not hit and bf[:2] == "ps":
+                    need[j] = max(need.get(j, 0), 1)
+                if hit:
+                    k = 2
+                    if same and (o["q"] == "T" or bf == "order"):
+                        k = 1
+                    need[j] = max(need.get(j, 0), k)
+        for (bf, p0, p1, m, wr) in mine:
+            old = acc.get(bf, [])
+            if bf[:2] == "ps":
+                old = [z for z in old if z[0] == i]
+            elif wr:
+                old = [z for z in old if not (z[0] != i and (z[3] | m) == m and p0 <= z[1] and z[2] <= p1)]
+            acc[bf] = old + [(i, p0, p1, m, wr)]
+        if o["after"] is not None:
+            need[o["after"]] = max(need.get(o["after"], 0), 1)
+        deps[i] = need
+    tail = [0.0] * nop
+    succ = [[] for _ in range(nop)]
+    for i in range(nop):
+        for j in deps[i]:
+            succ[j].append(i)
+    for i in range(nop - 1, -1, -1):
+        o = ops[i]
+        tail[i] = o["cost"] + max([tail[j] + o["lag"] for j in succ[i]] + [0.0])
+    left = [len(d) for d in deps]
+    est = [0.0] * nop
+    ready = {}
+    for i in range(nop):
+        if left[i] == 0:
+            ready.setdefault(ops[i]["q"], []).append(i)
+    clock, order, done = {}, [], 0
+    while done < nop:
+        best = None
+        for q, lst in ready.items():
+            if not lst:
+                continue
+            c = clock.get(q, 0.0)
+            s = max(c, min(est[i] for i in lst)) if q != "R" else min(est[i] for i in lst)
+            if best is None or s < best[0]:
+                best = (s, q)
+        s, q = best
+        i = max([z for z in ready[q] if est[z] <= s + 1e-9], key=lambda z: (tail[z] + ops[z]["bias"], -z))
+        ready[q].remove(i)
+        o = ops[i]
+        if q != "R":
+            clock[q] = s + o["cost"]
+        order.append(i)
+        done += 1
+        for j in succ[i]:
+            e = s + o["cost"] + (o["lag"] if q != "R" and (deps[j][i] == 2 or q == "G") else 0.0)
+            if ops[j]["q"] == "R":
+                e = s + o["cost"] + ops[j]["lag"]
+            est[j] = max(est[j], e)
+            left[j] -= 1
+            if left[j] == 0:
+                ready.setdefault(ops[j]["q"], []).append(j)
+    queue = {"V": g.vector, "S": g.scalar, "T": g.tensor, "G": g, "D": g.sync}
+    count = {}
+    know = {q: {} for q in queue}
+    tok, kn = [None] * nop, [None] * nop
+    for i in order:
+        o = ops[i]
+        q = o["q"]
+        if q == "R":
+            tok[i] = (o["sem"], o["val"])
+            kn[i] = {o["sem"]: o["val"]}
+            continue
+        k = know[q]
+        want = {}
+        for j, kind in deps[i].items():
+            if kind == 2:
+                s, val = tok[j]
+                if k.get(s, 0) < val and (s not in want or want[s][0] < val):
+                    want[s] = (val, j)
+        for s in list(want):
+            if any(z != s and kn[want[z][1]].get(s, 0) >= want[s][0] for z in want):
+                del want[s]
+        for s, (val, j) in want.items():
+            queue[q].wait_ge(T.sem[s], val)
+        for s, (val, j) in want.items():
+            for z, n in kn[j].items():
+                if k.get(z, 0) < n:
+                    k[z] = n
+        ins = o["fn"]()
+        if o["sem"] is None:
+            s = "q" + q
+            count[s] = count.get(s, 0) + 1
+            ins.then_inc(T.sem[s], 1)
+            tok[i] = (s, count[s])
+        else:
+            tok[i] = (o["sem"], o["val"])
+            if q == "D":
+                ins.then_inc(T.sem[o["sem"]], 16)
+        kn[i] = dict(k)
+        kn[i][tok[i][0]] = tok[i][1]
+    k = know["G"]
+    fin = {}
+    for i in range(nop):
+        if tok[i][1] > fin.get(tok[i][0], 0):
+            fin[tok[i][0]] = tok[i][1]
+    for s, n in fin.items():
+        if k.get(s, 0) < n:
+            g.wait_ge(T.sem[s], n)

@@ -4,34 +4,33 @@ from concourse.mybir import dt, AluOpType as A, AxisListType, ActivationFunction
 N, W, H, L, CAP, RO, SL = 4, 2048, 2048, 256, 56, 4, 224
 DUMP = 256
 SW = DUMP + N * 256
+PH = 2176
+BIG = 67108864.0
 _B, _F, _H, _I, _U = "bfloat16", "float32", "float16", "int32", "uint16"
 _SB = {
-    "xlm": (W + L, _B), "xtl": (W + L, _I), "xmo": (4096, _B), "xsn": (H + L, _B), "sn0": (H, _B), "fm0": (L, _B),
-    "fr0": (RO * L, _B), "wk0": (3, _I), "wkf": (3, _F), "frs": (N * SL, _B), "win0": (SW, _B), "win1": (SW, _B), "win2": (SW, _B), "win3": (SW, _B),
-    "wint0": (SW, _F), "wint1": (SW, _F),
-    "L0": (L, _B), "L1": (L, _B), "L2": (L, _B), "L3": (L, _B), "L4": (L, _B), "TR0": (L, _F), "TR1": (L, _F), "TR2": (L, _F), "yfo": (L, _B),
-    "mp": (L, _B), "mT": (L, _B), "qT": (L, _B), "au": (32, _I), "am": (32, _I), "up": (16, _I), "av": (48, _I), "ci": (L, _I),
-    "cj": (L, _I), "XV": (48, _H), "XA": (256, _H), "ti": (12, _F), "tj": (12, _F), "tk": (12, _F), "tbl": (2304, _B),
-    "CL": (L, _U), "X": (4096, _B), "E": (4096, _B), "Y": (4096, _B), "P": (4096, _B), "NE": (4096, _B), "SX": (4096, _B),
-    "SC": (272, _F), "gi": (16, _I), "gj": (16, _I), "GV": (16, _H), "XG": (256, _H), "GL": (16, _U), "TG": (L, _U), "xg": (L, _B),
-    "hi": (512, _I), "hp": (256, _I), "hq": (256, _I), "hs": (256, _I), "hh": (256, _I), "hf": (256, _H), "HL": (256, _U), "Kh": (256, _F),
-    "k2": (256, _F), "SC2": (256, _F), "ki": (16, _I), "kj": (16, _I), "IV": (16, _H), "XI": (256, _B), "CHL": (16, _U), "CH": (L, _B),
-    "has": (16, _F), "kh": (16, _I), "ch": (16, _I), "cd": (16, _I), "nc": (16, _I), "dd": (16, _I), "OH": (80, _B),
-    "w3": (80, _H), "rin": (N * SL, _B), "XS": (256, _H), "sf": (16, _F), "SLL": (16, _U),
-    "TGp": (L, _F), "mk": (L, _F), "YT": (L, _F), "CT": (L, _I), "CTm": (L, _I),
-    "nh": (16, _B), "nn": (16, _B), "lq": (16, _F), "sq": (16, _F),
+    "tab": (2 * H + W + L, _B), "xtl": (H + W + L, _I), "xmo": (4096, _B), "sn0": (H, _B), "fm0": (L, _B),
+    "fr0": (RO * L, _B), "wk0": (3, _I), "wkf": (3, _F), "frs": (N * SL, _B), "rin": (N * SL, _B),
+    "win0": (SW, _B), "win1": (SW, _B), "win2": (SW, _B), "win3": (SW, _B), "wint0": (SW, _F), "wint1": (SW, _F),
+    "L0": (L, _B), "L1": (L, _B), "L2": (L, _B), "L3": (L, _B), "L4": (L, _B), "TR0": (L, _F), "TR1": (L, _F), "TR2": (L, _F),
+    "mT": (L, _B), "qT": (L, _B), "au": (32, _I), "am": (32, _I), "up": (16, _I), "av": (48, _I), "cq": (L, _B),
+    "XV": (48, _H), "XA": (256, _H), "CL": (L, _U), "X": (4096, _B), "E": (4096, _B), "Y": (4096, _B), "P": (2 * PH, _B),
+    "NE": (4096, _B), "SX": (4096, _B), "SD": (272, _F), "GV": (272, _H), "GS": (128, _F), "GL": (16, _U), "TG": (L, _U), "xg": (L, _B),
+    "hi": (512, _I), "hm": (512, _I), "hp": (256, _I), "hq": (256, _I), "hs": (256, _I), "hh": (256, _I), "lo": (256, _F), "kf": (256, _F),
+    "kq": (512, _B), "Vs": (256, _F), "HL": (256, _U), "k2": (256, _F), "SC2": (256, _F), "key": (16, _I), "hb": (16, _F), "g2": (16, _F),
+    "cap": (16, _F), "kj": (16, _I), "IV": (16, _H), "XI": (256, _B), "fp": (16, _I), "XC": (16, _H), "CS": (128, _F), "CHL": (16, _U),
+    "CH": (L, _B), "dd": (16, _I), "OH": (80, _B), "S5": (80, _H), "SS": (128, _F), "SLL": (16, _U),
+    "TGp": (L, _F), "mk": (L, _F), "T2": (L, _F), "CT": (L, _I), "CTm": (L, _I),
+    "t1": (16, _I), "t2": (16, _I), "t3": (16, _F), "XT": (16, _H), "TS": (128, _F), "WA": (16, _U), "FT0": (L, _B), "FT1": (L, _B),
+    "SCW": (1024, _B), "cn": (16, _F), "XZ": (16, _H), "ZS": (128, _F), "zm": (16, _F), "WL": (16, _U),
 }
-for _z in "ls":
-    for _k, _v in {"y": (16, _F), "V2": (16, _H), "XW": (256, _H), "WA": (16, _U), "FT0": (L, _B), "FT1": (L, _B), "SCW": (1024, _B), "SCM": (1024, _B), "nd": (16, _F),
-                   "z": (16, _F), "V3": (16, _H), "XV": (256, _H), "WL": (16, _U)}.items():
-        _SB[_k + _z] = _v
 _CO = {
-    "one": (512, _B), "I": (128, _B), "nI": (128, _B), "Ih": (128, _H), "bo": (128, _B), "b8": (8, _B), "tmp": (128, _B), "tri": (128, _B),
-    "Rep": (512, _B), "RepN": (512, _B), "Sel": (144, _B), "Selh": (144, _H), "i4": (128, _B), "R8": (128, _B), "TR": (128, _B), "key": (128, _B),
-    "key18": (136, _B), "r16": (128, _F), "cC": (16, _B), "lane": (16, _F), "base": (80, _B),
-    "i5": (40, _B), "mkc": (256, _B), "EC17": (136, _H), "key17": (136, _B), "r17": (136, _F), "pc": (8, _F), "pi": (4, _I), "Wb": (128, _B), "Wt": (16, _B), "cT": (256, _F), "NB8": (8, _B), "PB8": (8, _B),
-    "c32": (32, _F), "duT": (16, _F), "dlT": (16, _F), "e0": (128, _F), "e1": (128, _F), "e2": (128, _F), "ek": (128, _F), "ea": (128, _F),
-    "EC": (128, _H), "EA": (128, _H),
+    "one": (512, _B), "zero": (128, _B), "I": (128, _B), "nI": (128, _B), "Ih": (128, _H), "If": (128, _F), "nIf": (128, _F), "qI": (128, _B),
+    "hI": (128, _B), "bo": (128, _B), "b8": (8, _B), "tmp": (128, _B), "Rep": (512, _B), "R32": (512, _B), "C8": (1024, _B), "i4": (128, _B),
+    "R8": (128, _B), "TR": (128, _B), "TRB": (128, _B), "JR": (272, _B), "JN": (272, _B), "K17": (272, _B), "Et": (48, _B), "KC": (128, _F),
+    "ZC": (128, _F), "base": (80, _B), "r5": (80, _B), "rm8": (128, _B), "rm16": (128, _B), "rm64": (256, _B), "Mk": (128, _B),
+    "mkc": (256, _B), "pc": (8, _F), "pi": (4, _I), "W3": (384, _B), "Wt": (24, _B), "NP": (16, _B), "PB8": (8, _B), "c128": (128, _B),
+    "c129": (384, _B), "c32": (32, _F), "ln": (16, _F), "lt": (16, _F), "dm": (16, _F), "LL": (16, _U), "EC": (128, _H), "EA": (128, _H),
+    "ER": (272, _H), "ti": (12, _F), "tj": (12, _F), "tk": (12, _F), "tbl": (4096 + 16, _B),
 }
 _PACK, _POS = {}, {}
 for _k in list(_SB) + list(_CO):
@@ -52,15 +51,19 @@ for _t, _n in _PACK.items():
     SCRATCH["pk_" + _t] = ("sbuf", [128, _n], _t)
 for _k in range(8):
     SCRATCH["ps%d" % _k] = ("psum", [128, 512], "float32")
-    _POS["ps%d" % _k] = ("ps%d" % _k, 0)
-_QUE = ("V", "S", "T", "G")
-SEMAPHORES = ["q" + e for e in _QUE] + ["ld%d" % i for i in range(12)] + ["rarr", "rloc", "st0", "st1"] + \
+SEMAPHORES = ["q" + e for e in "VSTG"] + ["ld%d" % i for i in range(12)] + ["rarr", "rloc", "st0", "st1"] + \
     ["%s%d" % (p, t) for p in ("arr", "tarr", "loc", "tloc") for t in range(RO)]
 
-GB, EB = "VSSSVVSS", "VVVVSSVS"
-GD, ED = "SVSSVSSV", "VSSVSSSV"
-SE = "SSVSSVVV"
-BI = (-11.0, -8.0, -2.0, -1.0)
+EB = "SSVVSSVV"
+SE = "SSSVSVVV"
+HS = "VV"
+CYC = 0.00087
+PE = 0.00028
+GAT = 1.15
+LAG = 0.2
+XLAG = 4.5
+LOOK = (0.2, 2.0)
+PASSES = 8
 
 
 def rank_program(g, core, T, topo):
@@ -68,20 +71,19 @@ def rank_program(g, core, T, topo):
     if me is None:
         return
     others = [(me + 1 + k) % N for k in range(N - 1)]
-    ops = []
-    bias = [0.0]
+    ops, bank = [], {}
+    main = [False]
 
     def v(name, a=None, b=None, step=1, p0=0, p1=128):
         buf, o = _POS[name]
-        n = (_SB.get(name) or _CO.get(name) or (512, _F))[0]
-        a = 0 if a is None else a
-        b = n if b is None else b
-        return (buf, p0, p1, o + a, o + b, step)
+        n = (_SB.get(name) or _CO.get(name))[0]
+        return (buf, p0, p1, o + (a or 0), o + (n if b is None else b), step)
 
     def ap(x):
+        buf = T[bank.get(x[0], x[0])]
         if x[5] == 1:
-            return T[x[0]][x[1]:x[2], x[3]:x[4]]
-        return T[x[0]][x[1]:x[2], x[3]:x[4]:x[5]]
+            return buf[x[1]:x[2], x[3]:x[4]]
+        return buf[x[1]:x[2], x[3]:x[4]:x[5]]
 
     def ncol(x):
         return len(range(x[3], x[4], x[5]))
@@ -89,26 +91,26 @@ def rank_program(g, core, T, topo):
     def arg(s):
         return ap(s) if isinstance(s, tuple) else s
 
-    def op(q, fn, rd, wr, cost, sem=None, val=0, lag=0.06, after=None, n=1):
-        ops.append({"q": q, "fn": fn, "rd": rd, "wr": wr, "cost": cost, "sem": sem, "val": val, "lag": lag, "after": after, "bias": bias[0]})
+    def op(q, fn, rd, wr, cost, sem=None, val=0, lag=LAG, after=None):
+        ops.append({"q": q, "fn": fn, "rd": rd, "wr": wr, "cost": cost, "sem": sem, "val": val, "lag": lag, "after": after,
+                    "main": main[0] and len(ops)})
         return len(ops) - 1
 
-    cyc = 0.00083 * 1.2
-
     def vc(n, f=1.0):
-        return 0.03 + cyc * max(64, n * f)
+        return 0.04 + CYC * max(64, n * f)
 
-    two = ("pk_bfloat16", "pk_float16", "pk_uint16")
+    def inps(x):
+        return x[0][:2] == "ps"
 
     def is2(x):
-        return x[0] in two or SCRATCH[x[0]][2] in (_B, _H, _U)
+        return not inps(x) and SCRATCH[x[0]][2] in (_B, _H, _U)
 
     def tc(out, x):
         f = 0.5 if is2(out) and is2(x) else 1.0
         return op("V", lambda: g.vector.tensor_copy(ap(out), ap(x)), [x], [out], vc(ncol(x), f))
 
     def tt(out, x, y, o):
-        f = 1.0 if x[0][:2] == "ps" or y[0][:2] == "ps" else 2.0
+        f = 1.0 if inps(x) or inps(y) else 2.0
         return op("V", lambda: g.vector.tensor_tensor(ap(out), ap(x), ap(y), o), [x, y], [out], vc(ncol(x), f))
 
     def ts(out, x, s1, o1, s2=None, o2=None):
@@ -118,469 +120,589 @@ def rank_program(g, core, T, topo):
             return op("V", lambda: g.vector.tensor_scalar(ap(out), ap(x), arg(s1), None, o1), rd, [out], vc(ncol(x), f))
         return op("V", lambda: g.vector.tensor_scalar(ap(out), ap(x), arg(s1), arg(s2), o1, o2), rd, [out], vc(ncol(x), f))
 
-    def scan(out, d0, d1):
-        return op("V", lambda: g.vector.tensor_tensor_scan(ap(out), ap(d0), ap(d1), 0.0, A.mult, A.max), [d0, d1], [out], vc(ncol(d1)))
+    def scan(out, d0, d1, o0, o1=A.max):
+        return op("V", lambda: g.vector.tensor_tensor_scan(ap(out), ap(d0), ap(d1), 0.0, o0, o1), [d0, d1], [out], vc(ncol(d1)))
 
     def vset(out, c):
         return op("V", lambda: g.vector.memset(ap(out), c), [], [out], vc(ncol(out), 0.5))
 
     def act(out, x, fn=F.Copy, bias=0.0, scale=1.0):
         return op("S", lambda: g.scalar.activation(ap(out), ap(x), fn, bias=arg(bias), scale=arg(scale)),
-                  [x] + [s for s in (bias, scale) if isinstance(s, tuple)], [out], 0.06 + cyc * ncol(x))
+                  [x] + [s for s in (bias, scale) if isinstance(s, tuple)], [out], (0.13 if inps(x) else 0.05) + CYC * ncol(x))
 
-    def copy(q, out, x):
-        return tc(out, x) if q == "V" else act(out, x)
+    def gather(q, out, win, off, turn=None):
+        fn = {"V": lambda: g.vector.tensor_copy(ap(out), ap(win).indirect(ap(off))),
+              "S": lambda: g.scalar.activation(ap(out), ap(win).indirect(ap(off)), F.Copy)}
+        if turn:
+            fn["S"] = lambda: g.scalar.activation(ap(out), ap(win).indirect(ap(off)), F.Identity, bias=turn[0], scale=turn[1])
+        return op(q, fn, [win, off], [out], 0.06 + CYC * GAT * ncol(out))
 
-    def gather(q, out, win, off):
-        c = 0.06 + cyc * 1.5 * ncol(out)
-        if q == "V":
-            return op("V", lambda: g.vector.tensor_copy(ap(out), ap(win).indirect(ap(off))), [win, off], [out], c)
-        return op("S", lambda: g.scalar.activation(ap(out), ap(win).indirect(ap(off)), F.Copy), [win, off], [out], c)
+    def relu(out, x, c):
+        return op("X", {"V": lambda: g.vector.tensor_scalar(ap(out), ap(x), c, 0.0, A.add, A.max),
+                        "S": lambda: g.scalar.activation(ap(out), ap(x), F.Relu, bias=c)}, [x], [out], 0.1 + CYC * ncol(x))
+
+    def times(out, x, s):
+        return op("X", {"V": lambda: g.vector.tensor_scalar(ap(out), ap(x), ap(s), None, A.mult),
+                        "S": lambda: g.scalar.activation(ap(out), ap(x), F.Identity, scale=ap(s))}, [x, s], [out], vc(ncol(x), 0.8))
 
     def gatherop(out, win, off, y, o):
         return op("V", lambda: g.vector.tensor_tensor(ap(out), ap(win).indirect(ap(off)), ap(y), o), [win, off, y], [out],
-                  0.06 + cyc * 1.5 * ncol(out))
+                  0.05 + CYC * GAT * ncol(out))
 
-    def scatter(win, off, x):
-        return op("V", lambda: g.vector.tensor_copy(ap(win).indirect(ap(off)), ap(x)), [x, off], [win], 0.06 + cyc * 3 * ncol(x))
+    def scatter(win, off, x, y=None):
+        c = 0.05 + CYC * 3.0 * ncol(x)
+        if y:
+            return op("V", lambda: g.vector.tensor_tensor(ap(win).indirect(ap(off)), ap(x), ap(y), A.mult), [x, y, off], [win], c)
+        return op("V", lambda: g.vector.tensor_copy(ap(win).indirect(ap(off)), ap(x)), [x, off], [win], c)
 
     def mm(out, lhsT, rhs, start=True, stop=True):
-        m = ncol(lhsT)
+        f = 4 if SCRATCH[rhs[0]][2] == _F else 1
         return op("T", lambda: g.tensor.matmul(ap(out), ap(lhsT), ap(rhs), start, stop), [lhsT, rhs], [out],
-                  0.0005 * max(min(64, m), ncol(rhs)))
+                  0.015 + PE * f * max(min(64, ncol(lhsT)), ncol(rhs)), lag=LAG + 0.1)
 
     def pick(out, x, pattern, cmp, fill, base, cm):
-        n = ncol(out)
-        return op("G", lambda: g.affine_select(ap(out), ap(x), pattern, cmp, fill, base, cm), [x], [out, pool], 0.2 + cyc * 2 * n)
+        return op("G", lambda: g.affine_select(ap(out), ap(x), pattern, cmp, fill, base, cm), [x], [out, pool], 0.17 + CYC * 2 * ncol(out))
 
     def iota(out, pattern, base, cm, small=True):
         def fn():
             if small:
                 return g.iota(ap(out), pattern, base, cm, allow_small_or_imprecise_dtypes=True)
             return g.iota(ap(out), pattern, base, cm)
-        return op("G", fn, [], [out, pool], 0.15 + cyc * 2 * ncol(out))
+        return op("G", fn, [], [out, pool], 0.13 + CYC * 2 * ncol(out))
     pool = ("pool", 0, 128, 0, 1, 1)
 
-    nld = [0]
+    nld, nps = [0], [0]
 
-    def load(q, out, src, cost):
+    def load(out, src, cost):
         s = "ld%d" % nld[0]
         nld[0] += 1
-        eng = g.sync if q == "D" else g.scalar
-        return op(q, lambda: eng.dma_start(ap(out), src), [], [out, ("order", 0, 128, 0, 1, 2)], 0.08, sem=s, val=16, lag=2.0 + cost)
+        return op("D", lambda: g.sync.dma_start(ap(out), src), [], [out, ("order", 0, 128, 0, 1, 2)], 0.08, sem=s, val=16, lag=2.0 + cost)
 
-    bank = [0]
-
-    def ps(a=0, b=512, step=1, p0=0, p1=128, k=None):
-        k = bank[0] if k is None else k
+    def ps(a, b, step=1, p0=0, p1=128, k=0):
         return ("ps%d" % k, p0, p1, a, b, step)
 
-    def nb(kind=0):
-        cnt[kind] += 1
-        return (cnt[kind] % 2, 2 + cnt[kind] % 4, 6 + cnt[kind] % 2)[kind]
-    cnt = {0: 0, 1: 0, 2: 0}
+    def nb():
+        nps[0] += 1
+        return nps[0]
 
+    def masks(s):
+        od = [(s + 1 + k) % N for k in range(N - 1)]
+        eng = topo.engines(T.cores[s], T.cores[od[0]])
+        for d in od:
+            eng = [e for e in eng if e in topo.engines(T.cores[s], T.cores[d])]
+        return dict(zip(od, [eng[0:len(eng) // 4], eng[len(eng) // 4:len(eng) // 2], eng[len(eng) // 2:]]))
 
-    def fused(name, src, dst, sem, loc, t_lag, after=None):
-        eng = topo.engines(core, T.cores[others[0]])
-        for d in others:
-            eng = [e for e in eng if e in topo.engines(core, T.cores[d])]
-        parts, total = [eng[0:len(eng) // 4], eng[len(eng) // 4:len(eng) // 2], eng[len(eng) // 2:]], len(eng)
+    def fused(src, dst, sem, loc):
+        parts = masks(me)
 
         def fn():
             tr = []
-            for d, es in zip(others, parts):
+            for d in others:
                 rid, pid, _ = topo.addr(T.cores[d])
-                m = 0
-                for e in es:
-                    m |= 1 << e
-                tr.append(RemoteDMATransfer(dst_ids=[DstId(rid=rid, pnc=pid)], dma_engine_mask=m, remote_sem=T.sem[sem],
+                tr.append(RemoteDMATransfer(dst_ids=[DstId(rid=rid, pnc=pid)], dma_engine_mask=sum(1 << e for e in parts[d]), remote_sem=T.sem[sem],
                                             srcs=[ap(src(d))], dsts=[ap(dst(d))], alu_op=0))
             return g.remote_dma_fused(tr, local_sem=T.sem[loc])
-        return op("G", fn, [src(d) for d in others], [], 1.0, sem=loc, val=total, lag=1.5)
+        return op("G", fn, [src(d) for d in others], [], 1.0, sem=loc, val=sum(len(x) for x in parts.values()), lag=1.5)
 
-    def got(sem, total, wr, after, lag):
-        return op("R", None, [], wr, 0.0, sem=sem, val=total, lag=lag, after=after)
-
-    def arrivals():
-        n = 0
-        for s in others:
-            od = [(s + 1 + k) % N for k in range(N - 1)]
-            eng = topo.engines(T.cores[s], T.cores[od[0]])
-            for d in od:
-                eng = [e for e in eng if e in topo.engines(T.cores[s], T.cores[d])]
-            parts = [eng[0:len(eng) // 4], eng[len(eng) // 4:len(eng) // 2], eng[len(eng) // 2:]]
-            n += len(parts[od.index(me)])
-        return n
-    narr = arrivals()
+    def got(sem, wr, after, lag):
+        return op("R", None, [], wr, 0.0, sem=sem, val=sum(len(masks(s)[me]) for s in others), lag=lag, after=after)
 
     def slot(d, name, t):
         return v("%s%d" % (name, t), DUMP + 256 * d, DUMP + 256 * d + CAP)
 
-    load("D", v("fm0"), T.fm[:], 0.5)
-    load("D", v("wk0"), T.wk[:], 0.2)
-    load("D", v("xlm", 0, W), T.lm[:], 2.0)
-    load("D", v("xtl", 0, W), T.tl[:], 5.0)
-    load("D", v("xmo"), T.mo[:], 8.0)
-    load("D", v("fr0"), T.fr[:], 9.0)
-    load("D", v("sn0"), T.sn[:], 11.0)
+    def halves(name, h, n=128):
+        return v(name, h * n, h * n + n)
+
+    def mp(h):
+        return v("P", PH * h + 2048, PH * h + PH)
+
+    def prod(q):
+        c = PH * (q // 4) + 512 * (q % 4)
+        return v("P", c, c + 512)
+    SN, LM, TL = v("tab", 0, 2 * H), v("tab", 2 * H, 2 * H + W), v("xtl", H, H + W)
+
+    def again():
+        for c in range(0, H, 512):
+            act(v("tab", c, c + 512), v("tab", H + c, H + c + 512))
+
+    load(v("fm0"), T.fm[:], 0.5)
+    load(v("wk0"), T.wk[:], 0.2)
+    load(LM, T.lm[:], 2.5)
+    load(v("fr0"), T.fr[:], 4.0)
+    load(TL, T.tl[:], 5.0)
+    load(v("xmo"), T.mo[:], 8.0)
+    load(v("sn0"), T.sn[:], 10.0)
     vset(v("one", 0, 128), 1.0)
     vset(v("one", 128, 512), 1.0)
+    vset(v("zero"), 0.0)
     o128 = v("one", 0, 128)
     pick(v("I"), o128, [[-1, 128]], A.is_equal, 0.0, 0, 1)
     pick(v("tmp"), o128, [[-16, 8], [0, 16]], A.is_ge, 0.0, 0, 1)
     pick(v("bo"), v("tmp"), [[16, 8], [0, 16]], A.is_ge, 0.0, 15, -1)
-    for k in range(3):
-        pick(v("e%d" % k, p1=24), v("one", 0, 128, p1=24), [[-1, 8], [0, 16]], A.is_equal, 0.0, -8 * k, 1)
-    pick(v("RepN", p1=32), v("one", 0, 512, p1=32), [[-1, 32], [0, 16]], A.is_equal, 0.0, 0, 1)
-    for a in range(4):
-        act(v("i4", 32 * a, 32 * a + 32, p1=32), v("I", 0, 32, p1=32))
-    b = nb(0)
-    mm(ps(k=b), v("i4", p1=32), v("RepN", p1=32))
-    act(v("Rep"), ps(k=b))
-    act(v("RepN"), ps(k=b), scale=-1.0)
-    ts(v("nI"), v("I"), -1.0, A.mult)
-    tc(v("Ih"), v("I"))
-    tc(v("b8"), v("bo", 0, 128, 16))
-    ts(v("NB8"), v("b8"), -8388608.0, A.mult)
-    ts(v("PB8"), v("b8"), 131072.0, A.mult)
-    iota(v("key"), [[0, 8], [-2048, 16]], 65536 + 32768, 0)
+    pick(v("R32", p1=32), v("one", 0, 512, p1=32), [[-1, 32], [0, 16]], A.is_equal, 0.0, 0, 1)
+    pick(v("JR"), v("one", 0, 272), [[0, 2], [-16, 8], [1, 17]], A.is_equal, 0.0, -16, 1)
+    for a in range(2):
+        pick(halves("C8", a, 512), v("one"), [[-16, 4], [0, 8], [-1, 16]], A.is_equal, 0.0, -64 * a, 1)
+    pick(v("Mk"), v("zero"), [[0, 16], [-16, 8]], A.is_ge, -BIG / 4, 0, 1)
+    pick(v("Mk"), v("Mk"), [[0, 16], [16, 8]], A.is_ge, -BIG / 4, 15, -1)
     iota(v("pi", 0, 1), [[0, 1]], 0, 1, False)
-    ts(v("pi", 1, 2), v("pi", 0, 1), 15, A.bitwise_and)
-    tc(v("pc", 0, 1), v("pi", 1, 2))
-    ts(v("pc", 1, 2), v("pc", 0, 1), 0.0, A.is_gt)
-    ts(v("pc", 2, 3), v("pc", 0, 1), -16.0, A.add)
-    ts(v("pc", 4, 5), v("pc", 1, 2), 65536.0, A.mult)
-    ts(v("pi", 3, 4), v("pi", 0, 1), 4, A.arith_shift_right, 1, A.bitwise_and)
-    tc(v("pc", 6, 7), v("pi", 3, 4))
-    ts(v("pc", 5, 6), v("pc", 6, 7), -1.0, A.mult, 1.0, A.add)
-    tc(v("wkf"), v("wk0"))
-    ts(v("Wb"), v("bo"), v("wkf", 0, 1), A.mult)
-    ts(v("tri"), v("bo"), v("wkf", 1, 2), A.mult)
-    ts(v("tmp"), v("I"), v("wkf", 2, 3), A.mult)
-    b = nb(1)
-    mm(ps(0, 128, p1=24, k=b), v("one", 0, 24), v("tmp"))
-    tt(v("ek", p1=24), v("e1", p1=24), ps(0, 128, p1=24, k=b), A.mult)
-    tt(v("EC", p1=24), v("ek", p1=24), v("e0", p1=24), A.add)
-    ts(v("ea", p1=24), v("e2", p1=24), 2048.0, A.mult)
-    tt(v("EA", p1=24), v("ea", p1=24), v("e0", p1=24), A.add)
-    vset(v("r16"), 1.0)
-    vset(v("r16", 0, 128, 16), 0.0)
-    for x in range(2):
-        w = v("wkf", x, x + 1)
-        ts(v("Wt", 8 * x, 8 * x + 8), v("b8"), w, A.mult, -1.0, A.mult)
-        b = nb(1)
-        mm(ps(0, 128, k=b), o128, v("Wb") if x == 0 else v("tri"))
-        ts(v("cT", 128 * x, 128 * x + 128), ps(0, 128, k=b), 255.0, A.mult)
-    b = nb(1)
-    mm(ps(0, 16, k=b), o128, v("Wt"))
-    for h in range(2):
-        ts(v("c32", h, 32, 2), ps(0, 16, k=b), -255.0, A.mult)
-    for gr in range(8):
-        tc(v("EC17", 17 * gr, 17 * gr + 16, p1=24), v("EC", 16 * gr, 16 * gr + 16, p1=24))
-    tc(v("EC17", 16, 136, 17, p1=24), v("EC", 0, 128, 16, p1=24))
-    iota(v("key17"), [[0, 8], [-2048, 17]], 32768, 0)
-    ts(v("key18"), v("key17"), 128.0, A.mult)
-    vset(v("r17"), 1.0)
-    vset(v("r17", 0, 136, 17), 0.0)
-    pick(v("Sel", p1=8), v("one", 0, 144, p1=8), [[1, 144]], A.is_equal, 0.0, -16, -16)
-    for k in range(5):
-        act(v("i5", 8 * k, 8 * k + 8, p1=8), v("I", 0, 8, p1=8))
-    b = nb(1)
-    mm(ps(0, 144, p1=40, k=b), v("i5", p1=8), v("Sel", p1=8))
-    tc(v("Selh", p1=40), ps(0, 144, p1=40, k=b))
-    iota(v("duT"), [[0, 8], [128, 2]], 1024, 1)
-    ts(v("dlT"), v("duT"), 1024.0, A.add)
-    iota(v("ti"), [[1, 12]], 0, 0)
-    ts(v("tj"), v("ti"), v("pc", 0, 1), A.is_equal)
-    ts(v("tk"), v("tj"), 2.0, A.mult, -1.0, A.add)
-    vset(v("tbl", 0, 1), -1.0)
-    for k in range(12):
-        n = min(1 << k, 2304 - (1 << k))
-        ts(v("tbl", 1 << k, (1 << k) + n), v("tbl", 0, n), v("tk", k, k + 1), A.max)
-    iota(v("lane", 0, 16), [[16, 16]], 0, 0)
-    ts(v("lane", 0, 16), v("lane", 0, 16), v("pc", 0, 1), A.add)
-    for h in range(2):
-        ts(v("cC", 8 * h, 8 * h + 8), v("lane", 0, 8), 16.0, A.mult, 16.0, A.add)
-    iota(v("base"), [[256, 5], [0, 16]], 0, 0)
-    pick(v("R8", p1=8), v("one", 0, 128, p1=8), [[-1, 8], [0, 16]], A.is_equal, 0.0, 0, 1)
-    for t in range(RO - 1):
-        o = v("TR%d" % t, SL if t else 0, L)
-        act(o, v("one", 0, ncol(o)), F.Identity, 0.0, v("pc", 4, 5))
-        for d in range(N):
-            if t < RO - 2:
-                act(slot(d, "wint", t), v("one", 0, CAP), F.Identity, 0.0, v("pc", 4, 5))
+    iota(v("KC"), [[0, 8], [-8192, 16]], 2047 * 8192, -16 * 8192)
+    iota(v("lt"), [[128, 2], [0, 8]], 0, 1)
+    iota(v("ln"), [[16, 16]], 2048, 0)
+    iota(v("base"), [[0, 16], [256, 5]], DUMP - 256 - 2048, 0)
     pick(v("TR"), o128, [[1, 128]], A.is_gt, 0.0, 0, -1)
-    ts(v("mkc"), v("one", 0, 256), -7.5, A.mult)
+    pick(v("R8", p1=8), v("one", 0, 128, p1=8), [[-1, 8], [0, 16]], A.is_equal, 0.0, 0, 1)
+    iota(v("ti"), [[1, 12]], 0, 0)
+    vset(v("mkc"), -7.5)
     for a in range(2):
         x = v("mkc", p0=64 * a, p1=64 * a + 64)
-        pick(x, x, [[0, 4], [1, 64]], A.is_gt, -100.0, 0, -1)
-    TRI = v("TR")
-    ts(v("xsn", 0, H), v("sn0"), -1.0, A.mult, 255.0, A.add)
+        pick(x, x, [[0, 4], [-1, 64]], A.is_gt, -100.0, 0, 1)
+    for a in range(4):
+        act(v("i4", 32 * a, 32 * a + 32, p1=32), v("I", 0, 32, p1=32))
+    b = nb()
+    mm(ps(0, 512, k=b), v("i4", p1=32), v("R32", p1=32))
+    act(v("Rep"), ps(0, 512, k=b))
+    act(v("nI"), v("I"), scale=-1.0)
+    tc(v("Ih"), v("I"))
+    act(v("If"), v("I"))
+    act(v("hI"), v("I"), scale=-2048.0)
+    tc(v("b8"), v("bo", 0, 128, 16))
+    act(v("NP", 0, 8), v("b8"), scale=-8192.0)
+    act(v("NP", 8, 16), v("b8"), scale=8192.0)
+    act(v("PB8"), v("b8"), scale=BIG / 2)
+    ts(v("pi", 1, 2), v("pi", 0, 1), 15, A.bitwise_and)
+    tc(v("pc", 0, 1), v("pi", 1, 2))
+    ts(v("pc", 1, 2), v("pc", 0, 1), 0.0, A.is_gt, 65536.0, A.mult)
+    ts(v("pc", 2, 3), v("pc", 0, 1), -1.0, A.mult, 15.0, A.add)
+    ts(v("pc", 3, 4), v("pi", 0, 1), -8192.0, A.mult, 4096.0 - 8192.0, A.add)
+    act(v("pc", 4, 5), v("pc", 3, 4), F.Identity, 2048.0)
+    act(v("ZC"), v("zero"), F.Identity, v("pc", 4, 5))
+    ts(v("pi", 3, 4), v("pi", 0, 1), 4, A.arith_shift_right, 1, A.bitwise_and)
+    tc(v("pc", 6, 7), v("pi", 3, 4))
+    tc(v("wkf"), v("wk0"))
+    for x in range(3 if "S" in HS else 2):
+        w = v("wkf", x % 2, x % 2 + 1)
+        ts(v("Wt", 8 * x, 8 * x + 8), v("b8"), w, A.mult, -1.0, A.mult)
+        act(halves("W3", x), v("bo"), F.Identity, 0.0, w)
+    vset(v("Et"), 0.0)
+    act(v("Et", 0, 8), v("b8"))
+    act(v("Et", 8, 16), v("b8"), F.Identity, 0.0, v("wkf", 2, 3))
+    act(v("Et", 24, 32), v("b8"))
+    act(v("Et", 40, 48), v("b8"), scale=2048.0)
+    for x in range(2):
+        act(v("JR", 136 * x, 136 * x + 136, 17), v("I", 0, 128, 16))
+    act(v("JN"), v("JR"), scale=-2048.0)
+    for name, x, y in (("EC", 0, "I"), ("ER", 0, "JR"), ("EA", 24, "I")):
+        b = nb()
+        mm(ps(0, ncol(v(y)), p1=24, k=b), v("Et", x, x + 24), v(y))
+        tc(v(name, p1=24), ps(0, ncol(v(y)), p1=24, k=b))
+    vset(v("K17"), 129.0 * 2048)
+    vset(v("K17", 0, 272, 17), 128.0 * 2048)
+    b = nb()
+    mm(ps(0, 16, k=b), o128, v("Wt", 0, 16))
+    for h in range(2):
+        act(v("c32", h, 32, 2), ps(0, 16, k=b), scale=-255.0)
+    for n in (8, 16, 64):
+        vset(v("rm%d" % n), BIG)
+        vset(v("rm%d" % n, 0, None, n), -BIG)
+    vset(v("c128"), 127.5)
+    if "S" in HS:
+        vset(v("c129"), 129.0 * 4096)
+        act(v("qI"), v("I"), scale=-4096.0)
+        act(v("nIf"), v("I"), scale=-1.0)
+    act(v("dm"), v("ln"), F.Identity, v("pc", 0, 1))
+    ts(v("LL"), v("dm"), -2048.0, A.add)
+    act(v("base", 0, 80, 5), v("lt"))
+    vset(v("r5"), 1.0)
+    vset(v("r5", 0, 80, 5), 0.0)
+    vset(v("OH"), 0.0)
+    act(v("tmp"), v("I"), scale=2048.0)
+    tt(v("TRB"), v("TR"), v("tmp"), A.add)
+    ts(v("tj"), v("ti"), v("pc", 0, 1), A.is_equal)
+    act(v("tk"), v("tj"), F.Identity, 1.0, -2.0)
+    vset(v("tbl", 0, 1), -1.0)
+    vset(v("tbl", 4096, 4112), 0.0)
+    for k in range(12):
+        for c in range(0, 1 << k, 512):
+            n = min(1 << k, 512)
+            times(v("tbl", (1 << k) + c, (1 << k) + c + n), v("tbl", c, c + n), v("tk", k, k + 1))
+    for t in range(RO - 1):
+        o = v("TR%d" % t, SL if t else 0, L)
+        act(o, v("one", 0, ncol(o)), F.Identity, 0.0, v("pc", 1, 2))
+        for d in range(N):
+            if t < RO - 2:
+                act(slot(d, "wint", t), v("one", 0, CAP), F.Identity, 0.0, v("pc", 1, 2))
+    for c in range(0, 2 * H, 1024):
+        ts(v("tab", c, c + 1024), v("sn0", c % H, c % H + 1024), -1.0, A.mult, 255.0, A.add)
 
+    def refill(o, t, a, b):
+        if t < RO - 1:
+            act(o, v("fr0", t * L + a, t * L + b), F.Identity, 255.0, -1.0)
+        else:
+            act(o, v("fr0", t * L + a, t * L + b))
     for s in others + [me]:
         for t in range(RO):
             o = v("frs", s * SL + t * CAP, s * SL + t * CAP + CAP)
-            if s == me:
-                o = slot(me, "win", t)
-            act(o, v("fr0", t * L + s * CAP, t * L + s * CAP + CAP), F.Identity, 255.0, -1.0)
+            refill(slot(me, "win", t) if s == me else o, t, s * CAP, s * CAP + CAP)
     for t in range(RO):
-        act(v("L%d" % (t + 1), SL, L), v("fr0", t * L + SL, t * L + L), F.Identity, 255.0, -1.0)
-    snd = fused("r", lambda d: v("frs", d * SL, d * SL + SL), lambda d: v("rin", me * SL, me * SL + SL), "rarr", "rloc", 0)
-    got("rarr", narr, [v("rin", s * SL, s * SL + SL) for s in others], snd, 8.0)
+        refill(v("L%d" % (t + 1), SL, L), t, SL, L)
+    snd = fused(lambda d: v("frs", d * SL, d * SL + SL), lambda d: v("rin", me * SL, me * SL + SL), "rarr", "rloc")
+    got("rarr", [v("rin", s * SL, s * SL + SL) for s in others], snd, 12.0)
     for t in range(RO):
         for s in others:
             act(slot(s, "win", t), v("rin", s * SL + t * CAP, s * SL + t * CAP + CAP))
 
     ts(v("L0"), v("fm0"), -1.0, A.mult, 255.0, A.add)
 
-    def halves(name, h, n=128):
-        return v(name, h * n, h * n + n)
+    def tolist(name, a, n, step, out):
+        b = nb()
+        mm(ps(0, 8 * n, k=b), v("I"), v("Mk", 0, 8 * n), True, False)
+        for c in range(8):
+            mm(ps(n * c, n * c + n, k=b), halves("C8", c), v(name, a, a + (n - 1) * step + 1, step), False, False)
+        mm(ps(0, 8 * n, k=b), v("I"), v("Mk", 0, 8 * n), False, True)
+        scan(out, v("rm8", 0, 8 * n), ps(0, 8 * n, k=b), A.min)
 
-    def todisk(b, c, X, x0, n, first, sel="Selh", rows=8):
-        for ll in range(16):
-            mm(ps(c, c + n, k=b), v(sel, 16 - ll, 144 - ll, p1=rows), v(X, x0 + ll, x0 + 16 * n, 16, p1=rows), first and ll == 0, ll == 15)
+    def ends(name, h):
+        return v(name, 8 * h + 7, 128, 16)
 
-    def tolist(src, xs, out, shift):
-        b = nb(2)
+    def sums(b, cols, name, c, w):
+        for i in range(16):
+            mm(ps(*cols(i), k=b), v(name, c + i, c + 2048, 16), w, False, False)
+
+    def lowest(shift, between=None):
+        tolist("XT", 0, 16, 1, v("TS"))
         for h in range(2):
-            mm(ps(128 * h, 128 * h + 128, p1=8, k=b), ps8(src, h), v("Ih"))
-        tc(v(xs, p1=8), ps(0, 256, p1=8, k=b))
-        b = nb(2)
-        todisk(b, 0, xs, 0, 16, True)
-        ts(v(out), ps(0, 16, k=b), shift, A.add)
-
-    def ps8(src, h):
-        return v(src, h, 16, 2)
-
-    def lowest(z, places, q, valid):
-        for k in range(2):
-            x = v("FT%d%s" % (k, z))
-            op("S", lambda x=x, k=k: g.scalar.activation(ap(x), ap(v("tbl")).indirect(ap(v(places))), F.Copy, scale=ap(v("pc", 5 + k, 6 + k))),
-               [v("tbl"), v(places), v("pc", 5 + k, 6 + k)], [x], 0.06 + cyc * 1.5 * 256)
-        tt(v("y" + z), q, valid, A.mult)
+            ts(halves("WA", h, 8), ends("TS", h), 2048.0, A.add, 4096.0, A.min)
+        gather("S", v("FT0"), v("tbl"), v("WA"))
+        act(v("FT1"), v("FT0"), F.Identity, 0.0, v("pc", 6, 7))
         for pair in range(4):
-            b, p = nb(2), 32 * pair
+            b, p = nb(), 32 * pair
             mm(ps(0, 256, k=b), v("I"), v("mkc"), True, False)
             for odd in range(2):
                 for lc in range(2):
                     for blk in range(2):
-                        c, o = lc * 128 + blk * 64, (odd * 2 + lc) * 64
-                        x = v("FT%d%s" % (odd, z), c, c + 64, p0=p, p1=p + 32)
-                        mm(ps(o, o + 64, p0=64 * blk, p1=64 * blk + 64, k=b), x, x, False, False)
+                        c, o, e = lc * 128 + blk * 64, (odd * 2 + lc) * 64, p + 16 + 16 * odd
+                        mm(ps(o, o + 64, p0=64 * blk, p1=64 * blk + 64, k=b), v("FT%d" % odd, c, c + 64, p0=p, p1=e),
+                           v("FT0", c, c + 64, p0=p, p1=e), False, False)
             mm(ps(0, 256, k=b), v("I"), v("mkc"), False, True)
-            act(v("SCW" + z, 256 * pair, 256 * pair + 256), ps(0, 256, k=b), F.Relu)
-        b = nb(2)
-        for k in range(16):
-            for blk in range(2):
-                p = 64 * blk
-                mm(ps(k, k + 1, p0=p, p1=p + 64, k=b), v("SCW" + z, 64 * k, 64 * k + 64, p0=p, p1=p + 64),
-                   (valid[0], p, p + 64, valid[3] + k, valid[3] + k + 1, 1))
-        ts(v("nd" + z), ps(0, 16, k=b), 0.5, A.is_lt)
-        tt(v("z" + z), v("y" + z), v("nd" + z), A.mult)
-        tt(v("V3" + z), v("z" + z), v("duT"), A.add)
-        tolist("V3" + z, "XV" + z, "WL" + z, 1024.0)
+            scan(halves("SCW", pair, 256), v("rm64"), ps(0, 256, k=b), A.min)
+        if between:
+            between()
+        ts(v("cn"), v("SCW", 63, 1024, 64), 0.5, A.is_gt, 6144.0, A.mult)
+        for h in range(2):
+            tt(halves("XZ", h, 8), v("cn", h, 16, 2), halves("XT", h, 8), A.add)
+        tolist("XZ", 0, 16, 1, v("ZS"))
+        for h in range(2):
+            tt(halves("zm", h, 8), ends("ZS", h), halves("dm", h, 8), A.min)
+        ts(v("WL"), v("zm"), shift, A.add)
 
     for t in range(RO):
         last = t == RO - 1
         Lt, Ln = "L%d" % t, "L%d" % (t + 1)
-        bias[0] = 0.0
-        b = nb(1)
+        main[0] = True
+        b = nb()
         for h in range(2):
-            mm(ps(h, 32, 2, k=b), halves(Lt, h), v("Wt"))
+            mm(ps(h, 32, 2, k=b), halves(Lt, h), v("Wt", 0, 16))
         tt(v("au"), ps(0, 32, k=b), v("c32"), A.add)
         ts(v("am"), v("au"), 4095, A.bitwise_and)
         tt(v("up"), v("am", 0, 16), v("am", 16, 32), A.mult)
+        ts(v("av", 16, 32), v("au", 0, 16), 2047, A.bitwise_and)
         ts(v("av", 0, 16), v("up"), 5, A.arith_shift_right, 2047, A.bitwise_and)
-        ts(v("av", 16, 32), v("am", 0, 16), 2047, A.bitwise_and)
-        ts(v("av", 32, 48), v("up"), 16, A.arith_shift_right, 1, A.bitwise_and)
-        tc(v("XV"), v("av"))
+        rows = 16 if last else 24
+        if not last:
+            ts(v("av", 32, 48), v("up"), 16, A.arith_shift_right, 1, A.bitwise_and)
+        tc(v("XV", 0, 2 * rows), v("av", 0, 2 * rows))
         for h in range(2):
-            act(halves("mp", h), halves(Lt, h), F.Identity, 255.0, -1.0)
-            b2 = nb(1)
-            mm(ps(0, 128, k=b2), halves("mp", h), v("I"))
-            act(halves("mT", h), ps(0, 128, k=b2))
-            b = nb(1)
-            mm(ps(0, 128, p1=24, k=b), v("XV", h, 48, 2), v("Ih"))
-            xa = v("XA", 128 * h, 128 * h + 128, p1=24)
-            tc(xa, ps(0, 128, p1=24, k=b))
-            b = nb(1)
-            mm(ps(0, 128, k=b), v("EC", p1=24), xa)
-            tc(halves("ci", h), ps(0, 128, k=b))
-            ts(halves("cj", h), halves("ci", h), 2047, A.bitwise_and)
-            tc(halves("CL", h), halves("cj", h))
+            act(mp(h), halves(Lt, h), F.Identity, 255.0, -1.0)
+            b = nb()
+            mm(ps(0, 128, k=b), mp(h), v("I"))
+            act(halves("mT", h), ps(0, 128, k=b))
+            b = nb()
+            mm(ps(0, 128, p1=rows, k=b), v("XV", h, 2 * rows, 2), v("Ih"))
+            tc(v("XA", 128 * h, 128 * h + 128, p1=rows), ps(0, 128, p1=rows, k=b))
+            xa = v("XA", 128 * h, 128 * h + 128, p1=16)
+            b, b2 = nb(), nb()
+            mm(ps(0, 128, k=b), v("EC", p1=16), xa)
+            act(halves("cq", h), ps(0, 128, k=b), F.Identity, 128.5 + 1.0 / 4096, 1.0 / 2048)
+            mm(ps(0, 128, k=b2), v("EC", p1=16), xa, True, False)
+            mm(ps(0, 128, k=b2), v("hI"), halves("cq", h), False, True)
+            ts(halves("CL", h), ps(0, 128, k=b2), 129.0 * 2048, A.add)
         for h in range(2):
             for q in range(4 * h, 4 * h + 4):
                 a = q % 4
                 x, e, off = halves("X", q, 512), halves("E", q, 512), halves("CL", q, 32)
-                gather(GB[q], x, v("xlm", 0, W), off)
+                gather("X", x, LM, off)
                 mt = v("mT", h * 128, h * 128 + 128, p0=32 * a, p1=32 * a + 32)
-                b = nb(0)
+                b = nb()
                 if EB[q] == "V":
-                    mm(ps(k=b), mt, v("Rep", p0=32 * a, p1=32 * a + 32))
-                    tt(e, x, ps(k=b), A.is_gt)
+                    mm(ps(0, 512, k=b), mt, v("Rep", p0=32 * a, p1=32 * a + 32))
+                    tt(e, x, ps(0, 512, k=b), A.is_gt)
                 else:
-                    mm(ps(k=b), mt, v("RepN", p0=32 * a, p1=32 * a + 32), True, False)
-                    mm(ps(k=b), v("I"), x, False, True)
-                    act(e, ps(k=b), F.Relu)
-            b = nb(1)
-            mm(ps(0, 136, k=b), v("I"), v("key18"), True, False)
-            for i in range(16):
-                mm(ps(i, 136, 17, k=b), v("E", 2048 * h + i, 2048 * h + 2048, 16), v("NB8"), False, False)
-            mm(ps(0, 136, k=b), v("XA", 128 * h, 128 * h + 128, p1=24), v("EC17", p1=24), False, True)
-            scan(halves("SC", h, 136), v("r17"), ps(0, 136, k=b))
-            G8 = [v(z, 8 * h, 8 * h + 8) for z in ("gi", "gj", "GV", "GL")]
-            tc(G8[0], v("SC", 136 * h + 16, 136 * h + 136, 17))
-            ts(G8[1], G8[0], 2047, A.bitwise_and)
-            tc(G8[2], G8[1])
-            b = nb(1)
-            mm(ps(0, 128, p1=8, k=b), G8[2], v("Ih"))
-            tc(v("XG", 128 * h, 128 * h + 128, p1=8), ps(0, 128, p1=8, k=b))
-            b = nb(1)
-            todisk(b, 0, "XG", 128 * h, 8, True)
-            tc(G8[3], ps(0, 8, k=b))
-            gather("V", halves("TG", h), v("xtl", 0, W), G8[3])
-            gather("S", halves("xg", h), v("xlm", 0, W), G8[3])
-            b = nb(1)
-            mm(ps(0, 128, k=b), halves("xg", h), v("I"), True, False)
-            mm(ps(0, 128, k=b), halves("mp", h), v("nI"), False, True)
+                    mm(ps(0, 512, k=b), mt, v("Rep", p0=32 * a, p1=32 * a + 32), True, False)
+                    mm(ps(0, 512, k=b), v("nI"), x, False, True)
+                    act(e, ps(0, 512, k=b), F.Relu, 0.0, -1.0)
+            b = nb()
+            mm(ps(0, 272, k=b), v("I"), v("K17"), True, False)
+            mm(ps(0, 272, k=b), v("XA", 128 * h, 128 * h + 128, p1=16), v("ER", p1=16), False, False)
+            sums(b, lambda i: (16 - i, 272, 17), "E", 2048 * h, v("NP"))
+            mm(ps(0, 272, k=b), halves("cq", h), v("JN"), False, True)
+            act(halves("SD", h, 136), ps(136, 272, k=b))
+            scan(halves("GV", h, 136), ps(0, 136, k=b), halves("SD", h, 136), A.max, A.min)
+            tolist("GV", 136 * h + 16, 8, 17, halves("GS", h, 64))
+            gl = halves("GL", h, 8)
+            ts(gl, v("GS", 64 * h + 7, 64 * h + 64, 8), 0.0, A.max)
+            gather("S", halves("xg", h), LM, gl)
+            gather("V", halves("TG", h), TL, gl)
+            b = nb()
+            mm(ps(0, 128, k=b), mp(h), v("nI"), True, False)
+            mm(ps(0, 128, k=b), halves("xg", h), v("I"), False, True)
             act(halves("qT", h), ps(0, 128, k=b))
-        if t < RO - 2:
-            ts(v("TGp"), v("TG"), 8192.0, A.add)
-        for h in range(2):
-            ts(v("has", h, 16, 2), v("SC", 136 * h + 16, 136 * h + 136, 17), 262144.0, A.is_ge)
-            tt(v("lq", h, 16, 2), v("gj", 8 * h, 8 * h + 8), v("dlT", h, 16, 2), A.subtract)
-        ts(v("nh"), v("has"), -1.0, A.mult, 1.0, A.add)
-        bias[0] = BI[0]
-        lowest("l", "GL", v("lq"), v("nh"))
-        bias[0] = BI[1]
-        if not last:
-            b = nb(2)
-            mm(ps(0, 256, k=b), v("EA", p1=24), v("XA", p1=24))
-            b2 = nb(2)
-            ts(ps(0, 256, k=b2), v("xtl", 0, L), 32768.0, A.add)
-            tt(v("YT"), v("TR%d" % t), ps(0, 256, k=b), A.max)
-            tt(v("CT"), v("YT"), ps(0, 256, k=b2), A.min)
-            ts(v("CTm"), v("CT"), 4095, A.bitwise_and)
-        for blk in range(3, -1, -1):
-            d = 64 * blk
-            wl = v("WLl", 4 * blk, 4 * blk + 4)
-            scatter(v("xlm"), wl, v("mp", d, d + 64))
-            if not last:
-                scatter(v("xtl"), wl, v("CTm", d, d + 64))
-        bias[0] = 0.0
+        main[0] = False
+        gv = v("GV", 16, 272, 17)
+        ts(v("hb"), gv, 0.0, A.is_ge, BIG / 2, A.mult)
+        ts(v("g2"), gv, v("pc", 3, 4), A.add)
+        tt(v("cap"), v("hb"), v("g2"), A.add)
+        if last:
+            tt(v("zm"), v("hb"), gv, A.add)
+            ts(v("XT"), v("zm"), 2048.0, A.add, 4096.0, A.min)
+            lowest(0.0)
+            for blk in range(3, -1, -1):
+                c = PH * (blk // 2) + 2048 + 64 * (blk % 2)
+                scatter(v("tab", 2 * H, 2 * H + W + L), halves("WL", blk, 4), v("P", c, c + 64))
+        main[0] = True
         for h in range(2):
             for q in range(4 * h, 4 * h + 4):
                 a = q % 4
-                y, p = halves("Y", q, 512), halves("P", q, 512)
-                gather(GD[q], y, v("xmo"), halves("TG", q, 32))
-                b = nb(0)
-                mm(ps(k=b), v("qT", h * 128, h * 128 + 128, p0=32 * a, p1=32 * a + 32), v("Rep", p0=32 * a, p1=32 * a + 32), True, False)
-                mm(ps(k=b), v("nI"), y, False, True)
-                if ED[q] == "V":
-                    ts(p, ps(k=b), 255.0, A.add, 0.0, A.max)
-                else:
-                    act(p, ps(k=b), F.Relu, 255.0)
-            b = nb(1)
-            for i in range(16):
-                mm(ps(i, 256, 16, k=b), v("P", 2048 * h + i, 2048 * h + 2048, 16), v("Wt"))
-            u = halves("hi", h, 256)
-            tt(u, ps(0, 256, k=b), v("cT"), A.add)
-            ts(u, u, 4095, A.bitwise_and)
-            u0, u1 = v("hi", 256 * h, 256 * h + 128), v("hi", 256 * h + 128, 256 * h + 256)
-            tt(halves("hp", h), u0, u1, A.mult)
-            ts(halves("hq", h), halves("hp", h), 5, A.arith_shift_right)
-            tt(halves("hs", h), halves("hq", h), u0, A.add)
-            ts(halves("hh", h), halves("hs", h), 2047, A.bitwise_and)
-            tc(halves("hf", h), halves("hh", h))
-            b = nb(1)
-            mm(ps(0, 128, k=b), halves("hf", h), v("Ih"))
-            tc(halves("HL", h), ps(0, 128, k=b))
-            b = nb(1)
-            mm(ps(0, 128, k=b), v("I"), v("key"), True, False)
-            mm(ps(0, 128, k=b), v("Ih"), halves("hf", h), False, True)
-            act(halves("Kh", h), ps(0, 128, k=b))
-        bias[0] = BI[3]
+                y, p = halves("Y", q, 512), prod(q)
+                gather("X", y, v("xmo"), halves("TG", q, 32))
+                b = nb()
+                mm(ps(0, 512, k=b), v("nI"), y, True, False)
+                mm(ps(0, 512, k=b), v("qT", h * 128, h * 128 + 128, p0=32 * a, p1=32 * a + 32), v("Rep", p0=32 * a, p1=32 * a + 32), False, True)
+                relu(p, ps(0, 512, k=b), 255.0)
+            hp, hq, hs, hh, kf = [halves(x, h) for x in ("hp", "hq", "hs", "hh", "kf")]
+            if HS[h] == "V":
+                b = nb()
+                mm(ps(0, 256, k=b), v("c128"), v("W3", 0, 256), True, False)
+                sums(b, lambda i: (i, 256, 16), "P", PH * h, v("Wt", 0, 16))
+                mm(ps(0, 256, k=b), v("c128"), v("W3", 0, 256), False, True)
+                tc(halves("hi", h, 256), ps(0, 256, k=b))
+                ts(halves("hm", h, 256), halves("hi", h, 256), 4095, A.bitwise_and)
+                tt(hp, halves("hm", 2 * h), halves("hm", 2 * h + 1), A.mult)
+                ts(hs, halves("hi", 2 * h), 2047, A.bitwise_and)
+                ts(hq, hp, 5, A.arith_shift_right, 2047, A.bitwise_and)
+                tt(halves("lo", h), hq, hs, A.add)
+                b = nb()
+                mm(ps(0, 128, k=b), halves("lo", h), v("If"))
+                tc(halves("HL", h), ps(0, 128, k=b))
+                tt(kf, halves("lo", h), v("KC"), A.add)
+            else:
+                b, b2, kq = nb(), nb(), halves("kq", h, 256)
+                for k, n in ((b, 16), (b2, 24)):
+                    mm(ps(0, 16 * n, k=k), v("c128"), v("W3", 0, 16 * n), True, False)
+                    mm(ps(0, 16 * n, k=k), v("I"), v("c129", 0, 16 * n), False, False)
+                    sums(k, lambda i: (i, 16 * n, 16), "P", PH * h, v("Wt", 0, n))
+                mm(ps(0, 256, k=b), v("c128"), v("W3", 0, 256), False, True)
+                act(kq, ps(0, 256, k=b), F.Identity, -0.5 + 1.0 / 8192, 1.0 / 4096)
+                mm(ps(0, 256, k=b2), v("qI"), kq, False, False)
+                mm(ps(256, 384, k=b2), v("qI"), v("kq", 256 * h, 256 * h + 128), False, False)
+                mm(ps(0, 384, k=b2), v("c128"), v("W3"), False, True)
+                act(halves("Vs", h), ps(128, 256, k=b2))
+                tt(hp, halves("Vs", h), ps(0, 128, k=b2), A.mult)
+                ts(hq, hp, 5, A.arith_shift_right, 2047, A.bitwise_and)
+                tt(hs, hq, ps(256, 384, k=b2), A.add)
+                ts(hh, hs, 2047, A.bitwise_and)
+                tc(halves("lo", h), hh)
+                b = nb()
+                mm(ps(0, 128, k=b), halves("lo", h), v("If"))
+                tc(halves("HL", h), ps(0, 128, k=b))
+                b = nb()
+                mm(ps(0, 128, k=b), v("If"), v("KC"), True, False)
+                mm(ps(0, 128, k=b), v("If"), halves("lo", h), False, True)
+                act(kf, ps(0, 128, k=b))
         for h in range(2):
             for q in range(4 * h, 4 * h + 4):
-                ne, p, sx = halves("NE", q, 512), halves("P", q, 512), halves("SX", q, 512)
+                ne, p, sx = halves("NE", q, 512), prod(q), halves("SX", q, 512)
                 if SE[q] == "V":
-                    gatherop(ne, v("xsn", 0, H), halves("HL", q, 32), p, A.not_equal)
+                    gatherop(ne, SN, halves("HL", q, 32), p, A.not_equal)
                 else:
-                    gather("S", sx, v("xsn", 0, H), halves("HL", q, 32))
-                    b = nb(0)
-                    mm(ps(k=b), v("nI"), p, True, False)
-                    mm(ps(k=b), v("I"), sx, False, True)
-                    act(ne, ps(k=b), F.Abs)
-            b = nb(1)
-            for i in range(16):
-                mm(ps(i, 128, 16, k=b), v("NE", 2048 * h + i, 2048 * h + 2048, 16), v("PB8"))
-            tt(halves("k2", h), ps(0, 128, k=b), halves("Kh", h), A.min)
-            scan(halves("SC2", h), v("r16"), halves("k2", h))
-            tt(v("kh", h, 16, 2), v("SC2", 128 * h + 15, 128 * h + 128, 16), v("has", h, 16, 2), A.mult)
-        bias[0] = 0.0
-        tc(v("ki"), v("SC2", 15, 256, 16))
-        ts(v("kj"), v("ki"), 11, A.arith_shift_right, 31, A.bitwise_and)
-        ts(v("IV"), v("kj"), 1.0, A.max, -1.0, A.mult)
-        b = nb(1)
-        for h in range(2):
-            mm(ps(128 * h, 128 * h + 128, p1=8, k=b), v("IV", 8 * h, 8 * h + 8), v("Ih"))
-        act(v("XI", p1=8), ps(0, 256, p1=8, k=b))
-        b = nb(1)
-        mm(ps(0, 16, k=b), v("I"), v("cC"), True, False)
-        todisk(b, 0, "XI", 0, 16, False, "Sel")
-        tc(v("CHL"), ps(0, 16, k=b))
-        for h in range(2):
-            gather("S", halves("CH", h), halves("P", h, 2048), v("CHL", 8 * h, 8 * h + 8))
-        ts(v("dd"), v("kh"), 65536 + 3, A.bitwise_and)
-        for d in range(N + 1):
-            ts(v("OH", 16 * d, 16 * d + 16), v("dd"), float(65536 + d - 1 if d else 0), A.is_equal)
-        b = nb(1)
+                    gather("S", sx, SN, halves("HL", q, 32))
+                    b = nb()
+                    mm(ps(0, 512, k=b), v("nI"), p, True, False)
+                    mm(ps(0, 512, k=b), v("I"), sx, False, True)
+                    act(ne, ps(0, 512, k=b), F.Abs)
+            b = nb()
+            mm(ps(0, 128, k=b), v("If"), v("ZC"), True, False)
+            sums(b, lambda i: (i, 128, 16), "NE", 2048 * h, v("PB8"))
+            mm(ps(0, 128, k=b), v("I"), v("zero"), False, True)
+            tt(halves("k2", h), ps(0, 128, k=b), halves("kf", h), A.min)
+            scan(halves("SC2", h), v("rm16"), halves("k2", h), A.min)
+        tt(v("key"), v("SC2", 15, 256, 16), v("cap"), A.min)
+        ts(v("dd"), v("key"), (1 << 24) + 3, A.bitwise_and)
+        for d in range(N):
+            ts(v("OH", 1 + d, 80, 5), v("dd"), float(d), A.is_equal)
+        b = nb()
         mm(ps(0, 80, k=b), v("I"), v("base"), True, False)
-        mm(ps(1, 80, 2, k=b), o128, v("OH", 0, 80, 2), False, False)
-        mm(ps(0, 80, k=b), TRI, v("OH"), False, True)
-        tt(v("w3"), ps(0, 80, k=b), v("OH"), A.mult)
-        b = nb(1)
+        mm(ps(40, 80, k=b), o128, v("OH", 0, 40), False, False)
+        mm(ps(0, 80, k=b), v("TRB"), v("OH"), False, True)
+        scan(v("S5"), v("r5"), ps(0, 80, k=b), A.mult)
+        tolist("S5", 4, 16, 5, v("SS"))
         for h in range(2):
-            mm(ps(128 * h, 128 * h + 128, p1=40, k=b), v("w3", h, 80, 2), v("Ih"))
-        tc(v("XS", p1=40), ps(0, 256, p1=40, k=b))
-        b = nb(1)
-        todisk(b, 0, "XS", 0, 16, True, rows=40)
-        tc(v("SLL"), ps(0, 16, k=b))
-        wt = "win%d" % t
-        scatter(v(wt), v("SLL"), v("CH"))
+            tc(halves("SLL", h, 8), ends("SS", h))
+        ts(v("fp"), v("key"), 13, A.arith_shift_right)
+        ts(v("XC"), v("fp"), -1.0, A.mult)
+        tolist("XC", 0, 16, 1, v("CS"))
+        for h in range(2):
+            ts(halves("CHL", h, 8), ends("CS", h), 2047.0, A.add)
+            gather("S", halves("CH", h), halves("P", h, PH), halves("CHL", h, 8), last and (255.0, -1.0))
+        scatter(v("win%d" % t), v("SLL"), v("CH"))
         mine = (me * CAP, me * CAP + CAP)
-        snd = fused("m", lambda d, t=t: slot(d, "win", t), lambda d, Ln=Ln: v(Ln, mine[0], mine[1]), "arr%d" % t, "loc%d" % t, 0)
+        snd = fused(lambda d, t=t: slot(d, "win", t), lambda d, Ln=Ln: v(Ln, mine[0], mine[1]), "arr%d" % t, "loc%d" % t)
         act(v(Ln, mine[0], mine[1]), slot(me, "win", t))
-        got("arr%d" % t, narr, [v(Ln, s * CAP, s * CAP + CAP) for s in others], snd, 3.0)
-        if t < RO - 2:
-            TR = "TR%d" % (t + 1)
-            b = nb(2)
-            mm(ps(0, 256, k=b), v("R8", p1=8), v("XI", p1=8))
-            ts(v("mk"), ps(0, 256, k=b), v("pc", 2, 3), A.not_equal)
-            wv = v("wint%d" % t)
-            op("V", lambda wv=wv: g.vector.tensor_tensor(ap(wv).indirect(ap(v("SLL"))), ap(v("TGp")), ap(v("mk")), A.mult),
-               [v("SLL"), v("TGp"), v("mk")], [wv], 0.06 + cyc * 3 * 256)
-            snd = fused("t", lambda d, t=t: slot(d, "wint", t), lambda d, TR=TR: v(TR, mine[0], mine[1]), "tarr%d" % t, "tloc%d" % t, 0)
-            act(v(TR, mine[0], mine[1]), slot(me, "wint", t))
-            got("tarr%d" % t, narr, [v(TR, s * CAP, s * CAP + CAP) for s in others], snd, 4.0)
+        got("arr%d" % t, [v(Ln, s * CAP, s * CAP + CAP) for s in others], snd, XLAG)
+
+        def tails():
+            if t < RO - 2:
+                TR = "TR%d" % (t + 1)
+                gather("S", v("TGp"), TL, v("GL"), (8192.0, 1.0))
+                ts(v("kj"), v("key"), 13, A.arith_shift_right, 15, A.bitwise_and)
+                tc(v("IV"), v("kj"))
+                b = nb()
+                for h in range(2):
+                    mm(ps(128 * h, 128 * h + 128, p1=8, k=b), halves("IV", h, 8), v("Ih"))
+                act(v("XI", p1=8), ps(0, 256, p1=8, k=b))
+                b = nb()
+                mm(ps(0, 256, k=b), v("R8", p1=8), v("XI", p1=8))
+                ts(v("mk"), ps(0, 256, k=b), v("pc", 2, 3), A.not_equal)
+                scatter(v("wint%d" % t), v("SLL"), v("TGp"), v("mk"))
+                snd = fused(lambda d, t=t: slot(d, "wint", t), lambda d, TR=TR: v(TR, mine[0], mine[1]), "tarr%d" % t, "tloc%d" % t)
+                act(v(TR, mine[0], mine[1]), slot(me, "wint", t))
+                got("tarr%d" % t, [v(TR, s * CAP, s * CAP + CAP) for s in others], snd, XLAG + 1.0)
+            b, b2 = nb(), nb()
+            mm(ps(0, 256, k=b), v("EA", p1=24), v("XA", p1=24))
+            gather("S", v("T2"), TL, v("LL"), (32768.0, 1.0))
+            tt(ps(0, 256, k=b2), v("TR%d" % t), ps(0, 256, k=b), A.max)
+            tt(v("CT"), v("T2"), ps(0, 256, k=b2), A.min)
+            ts(v("CTm"), v("CT"), 4095, A.bitwise_and)
         if not last:
-            ts(v("ch"), v("kh"), 2047, A.bitwise_and)
-            ts(v("nn"), v("kh"), 0.0, A.is_gt)
-            tt(v("sq"), v("ch"), v("dlT"), A.subtract)
-            bias[0] = BI[2]
-            tc(v("V2s"), v("ch"))
-            tolist("V2s", "XWs", "WAs", 0.0)
-            lowest("s", "WAs", v("sq"), v("nn"))
+            ts(v("t1"), v("key"), 2047, A.bitwise_and)
+            ts(v("t2"), v("key"), (1 << 24) + 6144, A.bitwise_and)
+            ts(v("t3"), v("t2"), -2048.0 - (1 << 24), A.add, -2048.0, A.max)
+            tt(v("XT"), v("t1"), v("t3"), A.add)
+            lowest(2048.0, tails)
             for blk in range(3, -1, -1):
-                scatter(v("xsn"), v("WLs", 4 * blk, 4 * blk + 4), v("CH", 64 * blk, 64 * blk + 64))
-    ts(v("yfo"), v("L4"), -1.0, A.mult, 255.0, A.add)
-    op("D", lambda: g.sync.dma_start(T.yf[:], ap(v("yfo"))), [v("yfo")], [], 0.08, sem="st0", val=16, lag=2.0)
-    op("D", lambda: g.sync.dma_start(T.yl[:], ap(v("xlm", 0, W))), [v("xlm", 0, W)], [], 0.08, sem="st1", val=16, lag=2.0)
-    _emit(g, T, ops)
+                scatter(v("tab", H, 2 * H + W + L), halves("WL", blk, 4), halves("CH", blk, 64))
+            main[0] = False
+            again()
+            for blk in range(3, -1, -1):
+                scatter(v("xtl"), halves("WL", blk, 4), halves("CTm", blk, 64))
+    op("D", lambda: g.sync.dma_start(T.yf[:], ap(v("L4"))), [v("L4")], [], 0.08, sem="st0", val=16, lag=2.0)
+    out = op("D", lambda: g.sync.dma_start(T.yl[:], ap(LM)), [LM], [], 0.08, sem="st1", val=16, lag=2.0)
+    op("R", None, [], [], 0.0, sem="st1", val=16, lag=4.0, after=out)
+    _emit(g, T, ops, bank)
 
 
-def _emit(g, T, ops):
+def _plan(ops, deps, bank):
+    nop = len(ops)
+    post = [[] for _ in ops]
+    for j in range(nop):
+        for i, kind in deps[j].items():
+            post[i].append((j, ops[j]["lag"] if ops[j]["q"] == "R" else ops[i]["lag"] if kind == 2 and ops[i]["q"] != "R" else 0.0))
+    key = [0.0] * nop
+    for i in range(nop - 1, -1, -1):
+        key[i] = min([key[j] - 1e-4 for j, _ in post[i]] + [ops[i]["main"] or nop + i])
+    uses = {}
+    for i, o in enumerate(ops):
+        for x in o["rd"] + o["wr"]:
+            if x[0][:2] == "ps" and i not in uses.setdefault(x[0], []):
+                uses[x[0]].append(i)
+    opens, closes, need = {}, {}, [len(d) for d in deps]
+    gate = [[] for _ in ops]
+    for u, lst in uses.items():
+        opens[lst[0]] = u
+        closes.setdefault(lst[-1], []).append(u)
+        for j in deps[lst[1]]:
+            if j != lst[0] and j not in deps[lst[0]]:
+                gate[j].append(lst[0])
+                need[lst[0]] += 1
+    cost = [o["cost"] for o in ops]
+
+    def forward(key):
+        left, est, end, on, banks, after = list(need), [0.0] * nop, [0.0] * nop, [o["q"] for o in ops], {}, {}
+        ready = {q: [] for q in "VSTGDRX"}
+        for i in range(nop):
+            if not left[i]:
+                ready[on[i]].append(i)
+        clock, free, order = {q: 0.0 for q in "VSTGDR"}, [(0.0, k, None) for k in range(8)], []
+
+        def when(i):
+            return max(est[i], min(free)[0] if free else 1e9) if i in opens else est[i]
+        while len(order) < nop:
+            best = None
+            for q in clock:
+                lst = ready[q] + ready["X"] if q in "VS" else ready[q]
+                if lst:
+                    s = max(clock[q], min(when(i) for i in lst))
+                    if best is None or s < best[0]:
+                        best = (s, q, lst)
+            s, q, lst = best
+            i = min((z for z in lst if when(z) <= s), key=lambda z: key[z] + (LOOK[1] if q == "V" and on[z] == "X" else 0))
+            soon = [when(z) for z in lst if key[z] < key[i] and s < when(z) < s + min(LOOK[0], cost[i])]
+            if soon and q != "R":
+                clock[q] = min(soon)
+                continue
+            ready[on[i]].remove(i)
+            on[i] = q
+            if i in opens:
+                f = min(free)
+                free.remove(f)
+                banks[opens[i]], after[i] = f[1], f[2]
+            end[i] = s + cost[i]
+            for u in closes.get(i, ()):
+                free.append((end[i] + LAG, banks[u], i))
+            if q != "R":
+                clock[q] = end[i]
+            order.append(i)
+            for j, lag in post[i]:
+                est[j] = max(est[j], end[i] + lag)
+            for j in [j for j, _ in post[i]] + gate[i]:
+                left[j] -= 1
+                if not left[j]:
+                    ready[on[j]].append(j)
+        return max(end), order, on, banks, after, end
+
+    def backward(order, on, end):
+        late, busy, at = [0.0] * nop, {}, {i: n for n, i in enumerate(order)}
+        for i in sorted(order, key=lambda i: (-end[i], -at[i])):
+            s = max([late[j] + lag for j, lag in post[i]] + [0.0])
+            if on[i] != "R":
+                row = busy.setdefault(on[i], [])
+                lo = len(row)
+                while lo and row[lo - 1][1] > s:
+                    lo -= 1
+                while lo < len(row) and row[lo][0] < s + cost[i]:
+                    s = max(s, row[lo][1])
+                    lo += 1
+                row.insert(lo, (s, s + cost[i]))
+            late[i] = s + cost[i]
+        return [-x for x in late]
+    best = None
+    for _ in range(PASSES):
+        plan = forward(key)
+        if best is None or plan[0] < best[0]:
+            best = plan
+        key = backward(plan[1], plan[2], plan[5])
+    _, order, on, banks, after, _ = best
+    for i in range(nop):
+        ops[i]["q"] = on[i]
+    for i, j in after.items():
+        if j is not None:
+            deps[i][j] = 2
+    for u, k in banks.items():
+        bank[u] = "ps%d" % k
+    return order
+
+
+def _emit(g, T, ops, bank):
     nop = len(ops)
     acc, deps = {}, [None] * nop
 
@@ -604,18 +726,13 @@ def _emit(g, T, ops):
             for (j, q0, q1, mj, wj) in acc.get(bf, ()):
                 if j == i:
                     continue
-                same = ops[j]["q"] == o["q"]
+                same = ops[j]["q"] == o["q"] != "X"
+                hit = (wr or wj) and (m & mj) and p0 < q1 and q0 < p1
                 if bf[:2] == "ps":
-                    hit = not same or ((wr or wj) and (m & mj) and p0 < q1 and q0 < p1)
-                else:
-                    hit = (wr or wj) and (m & mj) and p0 < q1 and q0 < p1
-                if not hit and bf[:2] == "ps":
+                    hit = hit or not same
                     need[j] = max(need.get(j, 0), 1)
                 if hit:
-                    k = 2
-                    if same and (o["q"] == "T" or bf == "order"):
-                        k = 1
-                    need[j] = max(need.get(j, 0), k)
+                    need[j] = max(need.get(j, 0), 1 if same and (o["q"] == "T" or bf == "order") else 2)
         for (bf, p0, p1, m, wr) in mine:
             old = acc.get(bf, [])
             if bf[:2] == "ps":
@@ -626,46 +743,7 @@ def _emit(g, T, ops):
         if o["after"] is not None:
             need[o["after"]] = max(need.get(o["after"], 0), 1)
         deps[i] = need
-    tail = [0.0] * nop
-    succ = [[] for _ in range(nop)]
-    for i in range(nop):
-        for j in deps[i]:
-            succ[j].append(i)
-    for i in range(nop - 1, -1, -1):
-        o = ops[i]
-        tail[i] = o["cost"] + max([tail[j] + o["lag"] for j in succ[i]] + [0.0])
-    left = [len(d) for d in deps]
-    est = [0.0] * nop
-    ready = {}
-    for i in range(nop):
-        if left[i] == 0:
-            ready.setdefault(ops[i]["q"], []).append(i)
-    clock, order, done = {}, [], 0
-    while done < nop:
-        best = None
-        for q, lst in ready.items():
-            if not lst:
-                continue
-            c = clock.get(q, 0.0)
-            s = max(c, min(est[i] for i in lst)) if q != "R" else min(est[i] for i in lst)
-            if best is None or s < best[0]:
-                best = (s, q)
-        s, q = best
-        i = max([z for z in ready[q] if est[z] <= s + 1e-9], key=lambda z: (tail[z] + ops[z]["bias"], -z))
-        ready[q].remove(i)
-        o = ops[i]
-        if q != "R":
-            clock[q] = s + o["cost"]
-        order.append(i)
-        done += 1
-        for j in succ[i]:
-            e = s + o["cost"] + (o["lag"] if q != "R" and (deps[j][i] == 2 or q == "G") else 0.0)
-            if ops[j]["q"] == "R":
-                e = s + o["cost"] + ops[j]["lag"]
-            est[j] = max(est[j], e)
-            left[j] -= 1
-            if left[j] == 0:
-                ready.setdefault(ops[j]["q"], []).append(j)
+    order = _plan(ops, deps, bank)
     queue = {"V": g.vector, "S": g.scalar, "T": g.tensor, "G": g, "D": g.sync}
     count = {}
     know = {q: {} for q in queue}
@@ -693,7 +771,7 @@ def _emit(g, T, ops):
             for z, n in kn[j].items():
                 if k.get(z, 0) < n:
                     k[z] = n
-        ins = o["fn"]()
+        ins = o["fn"][q]() if isinstance(o["fn"], dict) else o["fn"]()
         if o["sem"] is None:
             s = "q" + q
             count[s] = count.get(s, 0) + 1

@@ -8,28 +8,28 @@ PH = 2176
 BIG = 67108864.0
 _B, _F, _H, _I, _U = "bfloat16", "float32", "float16", "int32", "uint16"
 _SB = {
-    "tab": (2 * H + W + L, _B), "xtl": (H + W + L, _I), "xmo": (4096, _B), "sn0": (H, _B), "fm0": (L, _B),
-    "fr0": (RO * L, _B), "wk0": (3, _I), "wkf": (3, _F), "frs": (N * SL, _B), "rin": (N * SL, _B),
+    "tab": (3 * H + W + L, _B), "xtl": (H + W + L, _I), "xmo": (4096, _B), "sn0": (H, _B), "fm0": (L, _B),
+    "fr0": (RO * L, _B), "wk0": (3, _I), "wkf": (3, _F), "frc": (3 * L, _B),
     "win0": (SW, _B), "win1": (SW, _B), "win2": (SW, _B), "win3": (SW, _B), "wint0": (SW, _F), "wint1": (SW, _F),
-    "L0": (L, _B), "L1": (L, _B), "L2": (L, _B), "L3": (L, _B), "L4": (L, _B), "TR0": (L, _F), "TR1": (L, _F), "TR2": (L, _F),
+    "L1": (L, _B), "L2": (L, _B), "L3": (L, _B), "L4": (L, _B), "TR0": (L, _F), "TR1": (L, _F), "TR2": (L, _F),
     "mT": (L, _B), "qT": (L, _B), "au": (32, _I), "am": (32, _I), "up": (16, _I), "av": (48, _I), "cq": (L, _B),
     "XV": (48, _H), "XA": (256, _H), "CL": (L, _U), "X": (4096, _B), "E": (4096, _B), "Y": (4096, _B), "P": (2 * PH, _B),
     "NE": (4096, _B), "SX": (4096, _B), "SD": (272, _F), "GV": (272, _H), "GS": (128, _F), "GL": (16, _U), "TG": (L, _U), "xg": (L, _B),
-    "hi": (512, _I), "hm": (512, _I), "hp": (256, _I), "hq": (256, _I), "hs": (256, _I), "hh": (256, _I), "lo": (256, _F), "kf": (256, _F),
-    "kq": (512, _B), "Vs": (256, _F), "HL": (256, _U), "k2": (256, _F), "SC2": (256, _F), "key": (16, _I), "hb": (16, _F), "g2": (16, _F),
+    "hi": (512, _I), "hm": (512, _I), "hp": (256, _I), "hq": (256, _I), "lo": (256, _F), "kf": (256, _F),
+    "HL": (256, _U), "k2": (256, _F), "SC2": (256, _F), "key": (16, _I), "hb": (16, _F), "g2": (16, _F),
     "cap": (16, _F), "kj": (16, _I), "IV": (16, _H), "XI": (256, _B), "fp": (16, _I), "XC": (16, _H), "CS": (128, _F), "CHL": (16, _U),
     "CH": (L, _B), "dd": (16, _I), "OH": (80, _B), "S5": (80, _H), "SS": (128, _F), "SLL": (16, _U),
     "TGp": (L, _F), "mk": (L, _F), "T2": (L, _F), "CT": (L, _I), "CTm": (L, _I),
     "t1": (16, _I), "t2": (16, _I), "t3": (16, _F), "XT": (16, _H), "TS": (128, _F), "WA": (16, _U), "FT0": (L, _B), "FT1": (L, _B),
-    "SCW": (1024, _B), "cn": (16, _F), "XZ": (16, _H), "ZS": (128, _F), "zm": (16, _F), "WL": (16, _U),
+    "SCW": (1024, _F), "XZ": (16, _H), "ZS": (128, _F), "zm": (16, _F), "WL": (16, _U),
 }
 _CO = {
-    "one": (512, _B), "zero": (128, _B), "I": (128, _B), "nI": (128, _B), "Ih": (128, _H), "If": (128, _F), "nIf": (128, _F), "qI": (128, _B),
+    "one": (512, _B), "zero": (128, _B), "I": (128, _B), "nI": (128, _B), "Ih": (128, _H), "If": (128, _F),
     "hI": (128, _B), "bo": (128, _B), "b8": (8, _B), "tmp": (128, _B), "Rep": (512, _B), "R32": (512, _B), "C8": (1024, _B), "i4": (128, _B),
     "R8": (128, _B), "TR": (128, _B), "TRB": (128, _B), "JR": (272, _B), "JN": (272, _B), "K17": (272, _B), "Et": (48, _B), "KC": (128, _F),
-    "ZC": (128, _F), "base": (80, _B), "r5": (80, _B), "rm8": (128, _B), "rm16": (128, _B), "rm64": (256, _B), "Mk": (128, _B),
-    "mkc": (256, _B), "pc": (8, _F), "pi": (4, _I), "W3": (384, _B), "Wt": (24, _B), "NP": (16, _B), "PB8": (8, _B), "c128": (128, _B),
-    "c129": (384, _B), "c32": (32, _F), "ln": (16, _F), "lt": (16, _F), "dm": (16, _F), "LL": (16, _U), "EC": (128, _H), "EA": (128, _H),
+    "ZC": (128, _F), "base": (80, _B), "r5": (80, _B), "rm8": (128, _B), "rm16": (128, _B), "rm64": (256, _F), "Mk": (128, _B),
+    "mkc": (256, _B), "pc": (8, _F), "pi": (4, _I), "W3": (256, _B), "Wt": (16, _B), "Wp": (16, _B), "NP": (16, _B), "PB8": (8, _B), "cT": (256, _F),
+    "c32": (32, _F), "ln": (16, _F), "lt": (16, _F), "LL": (16, _U), "EC": (128, _H), "EA": (128, _H),
     "ER": (272, _H), "ti": (12, _F), "tj": (12, _F), "tk": (12, _F), "tbl": (4096 + 16, _B),
 }
 _PACK, _POS = {}, {}
@@ -51,19 +51,20 @@ for _t, _n in _PACK.items():
     SCRATCH["pk_" + _t] = ("sbuf", [128, _n], _t)
 for _k in range(8):
     SCRATCH["ps%d" % _k] = ("psum", [128, 512], "float32")
-SEMAPHORES = ["q" + e for e in "VSTG"] + ["ld%d" % i for i in range(12)] + ["rarr", "rloc", "st0", "st1"] + \
-    ["%s%d" % (p, t) for p in ("arr", "tarr", "loc", "tloc") for t in range(RO)]
+SEMAPHORES = ["q" + e for e in "VSTG"] + ["ld%d" % i for i in range(39)] + ["st0", "st1"] + \
+    ["%s%d" % (p, t) for p in ("arr", "tarr", "rarr", "loc", "tloc", "rloc") for t in range(RO)]
 
-EB = "SSVVSSVV"
+EB = "SSVVSVSV"
 SE = "SSSVSVVV"
-HS = "VV"
-CYC = 0.00087
-PE = 0.00028
-GAT = 1.15
-LAG = 0.2
-XLAG = 4.5
-LOOK = (0.2, 2.0)
-PASSES = 8
+GB = "XXVXXXXX"
+GD = "XXSXVXXS"
+ED = "XXSXXSVX"
+SETS = ({"e": 0.00085, "g": 0.00095, "s": 0.0021, "t": 0.00030}, {"e": 0.00120, "g": 0.00220, "s": 0.0055, "t": 0.00045})
+LAG = 0.17
+XLAG = 3.5
+LOOKS = ((0.2, 2.0, 0.0), (0.2, 2.0, 2.0), (0.25, 1.0, 1.0))
+MIX = (0.25,)
+PASSES = 6
 
 
 def rank_program(g, core, T, topo):
@@ -73,6 +74,7 @@ def rank_program(g, core, T, topo):
     others = [(me + 1 + k) % N for k in range(N - 1)]
     ops, bank = [], {}
     main = [False]
+    setup = [True]
 
     def v(name, a=None, b=None, step=1, p0=0, p1=128):
         buf, o = _POS[name]
@@ -92,12 +94,12 @@ def rank_program(g, core, T, topo):
         return ap(s) if isinstance(s, tuple) else s
 
     def op(q, fn, rd, wr, cost, sem=None, val=0, lag=LAG, after=None):
-        ops.append({"q": q, "fn": fn, "rd": rd, "wr": wr, "cost": cost, "sem": sem, "val": val, "lag": lag, "after": after,
-                    "main": main[0] and len(ops)})
+        ops.append({"q": q, "fn": fn, "rd": rd, "wr": wr, "cost": cost if isinstance(cost, tuple) else (cost, 0, "e"),
+                    "sem": sem, "val": val, "lag": lag, "after": after, "main": main[0] and len(ops)})
         return len(ops) - 1
 
     def vc(n, f=1.0):
-        return 0.04 + CYC * max(64, n * f)
+        return (0.04, max(64, n * f), "e")
 
     def inps(x):
         return x[0][:2] == "ps"
@@ -127,19 +129,28 @@ def rank_program(g, core, T, topo):
         return op("V", lambda: g.vector.memset(ap(out), c), [], [out], vc(ncol(out), 0.5))
 
     def act(out, x, fn=F.Copy, bias=0.0, scale=1.0):
+        if setup[0]:
+            return move(out, x, bias, scale)
         return op("S", lambda: g.scalar.activation(ap(out), ap(x), fn, bias=arg(bias), scale=arg(scale)),
-                  [x] + [s for s in (bias, scale) if isinstance(s, tuple)], [out], (0.13 if inps(x) else 0.05) + CYC * ncol(x))
+                  [x] + [s for s in (bias, scale) if isinstance(s, tuple)], [out], (0.13 if inps(x) else 0.05, ncol(x), "e"))
 
     def gather(q, out, win, off, turn=None):
         fn = {"V": lambda: g.vector.tensor_copy(ap(out), ap(win).indirect(ap(off))),
               "S": lambda: g.scalar.activation(ap(out), ap(win).indirect(ap(off)), F.Copy)}
         if turn:
-            fn["S"] = lambda: g.scalar.activation(ap(out), ap(win).indirect(ap(off)), F.Identity, bias=turn[0], scale=turn[1])
-        return op(q, fn, [win, off], [out], 0.06 + CYC * GAT * ncol(out))
+            fn = {"V": lambda: g.vector.tensor_scalar(ap(out), ap(win).indirect(ap(off)), turn[1], turn[0], A.mult, A.add),
+                  "S": lambda: g.scalar.activation(ap(out), ap(win).indirect(ap(off)), F.Identity, bias=turn[0], scale=turn[1])}
+        return op(q, fn, [win, off], [out], (0.06, ncol(out), "g"))
 
-    def relu(out, x, c):
-        return op("X", {"V": lambda: g.vector.tensor_scalar(ap(out), ap(x), c, 0.0, A.add, A.max),
-                        "S": lambda: g.scalar.activation(ap(out), ap(x), F.Relu, bias=c)}, [x], [out], 0.1 + CYC * ncol(x))
+    def relu(out, x, c, q):
+        return op(q, {"V": lambda: g.vector.tensor_scalar(ap(out), ap(x), c, 0.0, A.add, A.max),
+                        "S": lambda: g.scalar.activation(ap(out), ap(x), F.Relu, bias=c)}, [x], [out], (0.1, ncol(x), "e"))
+
+    def move(out, x, bias=0.0, scale=1.0):
+        return op("X", {"V": lambda: g.vector.tensor_scalar(ap(out), ap(x), arg(scale), arg(bias), A.mult, A.add),
+                        "S": lambda: g.scalar.activation(ap(out), ap(x), F.Identity, bias=arg(bias), scale=arg(scale))},
+                  [x] + [s for s in (bias, scale) if isinstance(s, tuple)], [out],
+                  (0.1 if inps(x) else 0.05, max(64, ncol(x)), "e"))
 
     def times(out, x, s):
         return op("X", {"V": lambda: g.vector.tensor_scalar(ap(out), ap(x), ap(s), None, A.mult),
@@ -147,10 +158,10 @@ def rank_program(g, core, T, topo):
 
     def gatherop(out, win, off, y, o):
         return op("V", lambda: g.vector.tensor_tensor(ap(out), ap(win).indirect(ap(off)), ap(y), o), [win, off, y], [out],
-                  0.05 + CYC * GAT * ncol(out))
+                  (0.05, ncol(out), "g"))
 
     def scatter(win, off, x, y=None):
-        c = 0.05 + CYC * 3.0 * ncol(x)
+        c = (0.05, ncol(x), "s")
         if y:
             return op("V", lambda: g.vector.tensor_tensor(ap(win).indirect(ap(off)), ap(x), ap(y), A.mult), [x, y, off], [win], c)
         return op("V", lambda: g.vector.tensor_copy(ap(win).indirect(ap(off)), ap(x)), [x, off], [win], c)
@@ -158,25 +169,29 @@ def rank_program(g, core, T, topo):
     def mm(out, lhsT, rhs, start=True, stop=True):
         f = 4 if SCRATCH[rhs[0]][2] == _F else 1
         return op("T", lambda: g.tensor.matmul(ap(out), ap(lhsT), ap(rhs), start, stop), [lhsT, rhs], [out],
-                  0.015 + PE * f * max(min(64, ncol(lhsT)), ncol(rhs)), lag=LAG + 0.1)
+                  (0.015, f * max(min(64, ncol(lhsT)), ncol(rhs)), "t"), lag=LAG + 0.1)
 
     def pick(out, x, pattern, cmp, fill, base, cm):
-        return op("G", lambda: g.affine_select(ap(out), ap(x), pattern, cmp, fill, base, cm), [x], [out, pool], 0.17 + CYC * 2 * ncol(out))
+        return op("G", lambda: g.affine_select(ap(out), ap(x), pattern, cmp, fill, base, cm), [x], [out, pool], (0.17, 2 * ncol(out), "e"))
 
     def iota(out, pattern, base, cm, small=True):
         def fn():
             if small:
                 return g.iota(ap(out), pattern, base, cm, allow_small_or_imprecise_dtypes=True)
             return g.iota(ap(out), pattern, base, cm)
-        return op("G", fn, [], [out, pool], 0.13 + CYC * 2 * ncol(out))
+        return op("G", fn, [], [out, pool], (0.13, 2 * ncol(out), "e"))
     pool = ("pool", 0, 128, 0, 1, 1)
 
     nld, nps = [0], [0]
 
-    def load(out, src, cost):
+    def load(out, src, cost, rows=None):
         s = "ld%d" % nld[0]
         nld[0] += 1
-        return op("D", lambda: g.sync.dma_start(ap(out), src), [], [out, ("order", 0, 128, 0, 1, 2)], 0.08, sem=s, val=16, lag=2.0 + cost)
+        rd, wr = ([src, v("sn0", 0, 1)], [out]) if isinstance(src, tuple) else ([], [out, ("order", 0, 128, 0, 1, 2)])
+        if rows:
+            return op("D", lambda: g.sync.dma_start(T[out[0]][rows[0]::16, out[3]:out[4]], T[src[0]][rows[1]::16, src[3]:src[4]]),
+                      rd, wr, 0.08, sem=s, val=16, lag=2.0 + cost)
+        return op("D", lambda: g.sync.dma_start(ap(out), arg(src)), rd, wr, 0.08, sem=s, val=16, lag=2.0 + cost)
 
     def ps(a, b, step=1, p0=0, p1=128, k=0):
         return ("ps%d" % k, p0, p1, a, b, step)
@@ -185,27 +200,30 @@ def rank_program(g, core, T, topo):
         nps[0] += 1
         return nps[0]
 
-    def masks(s):
+    def masks(s, two):
         od = [(s + 1 + k) % N for k in range(N - 1)]
         eng = topo.engines(T.cores[s], T.cores[od[0]])
         for d in od:
             eng = [e for e in eng if e in topo.engines(T.cores[s], T.cores[d])]
-        return dict(zip(od, [eng[0:len(eng) // 4], eng[len(eng) // 4:len(eng) // 2], eng[len(eng) // 2:]]))
+        n = len(eng)
+        return dict(zip(od, [eng[:n // 2], eng[n // 2:], eng] if two else [eng[:n // 4], eng[n // 4:n // 2], eng[n // 2:]]))
 
-    def fused(src, dst, sem, loc):
-        parts = masks(me)
+    def fused(src, dst, sem, loc, two=False):
+        parts = masks(me, two)
 
         def fn():
-            tr = []
-            for d in others:
-                rid, pid, _ = topo.addr(T.cores[d])
-                tr.append(RemoteDMATransfer(dst_ids=[DstId(rid=rid, pnc=pid)], dma_engine_mask=sum(1 << e for e in parts[d]), remote_sem=T.sem[sem],
-                                            srcs=[ap(src(d))], dsts=[ap(dst(d))], alu_op=0))
-            return g.remote_dma_fused(tr, local_sem=T.sem[loc])
+            for call in ([others[:2], others[2:]] if two else [others]):
+                tr = []
+                for d in call:
+                    rid, pid, _ = topo.addr(T.cores[d])
+                    tr.append(RemoteDMATransfer(dst_ids=[DstId(rid=rid, pnc=pid)], dma_engine_mask=sum(1 << e for e in parts[d]),
+                                                remote_sem=T.sem[sem], srcs=[ap(src(d))], dsts=[ap(dst(d))], alu_op=0))
+                ins = g.remote_dma_fused(tr, local_sem=T.sem[loc])
+            return ins
         return op("G", fn, [src(d) for d in others], [], 1.0, sem=loc, val=sum(len(x) for x in parts.values()), lag=1.5)
 
-    def got(sem, wr, after, lag):
-        return op("R", None, [], wr, 0.0, sem=sem, val=sum(len(masks(s)[me]) for s in others), lag=lag, after=after)
+    def got(sem, wr, after, lag, two=False):
+        return op("R", None, [], wr, 0.0, sem=sem, val=sum(len(masks(s, two)[me]) for s in others), lag=lag, after=after)
 
     def slot(d, name, t):
         return v("%s%d" % (name, t), DUMP + 256 * d, DUMP + 256 * d + CAP)
@@ -219,44 +237,44 @@ def rank_program(g, core, T, topo):
     def prod(q):
         c = PH * (q // 4) + 512 * (q % 4)
         return v("P", c, c + 512)
-    SN, LM, TL = v("tab", 0, 2 * H), v("tab", 2 * H, 2 * H + W), v("xtl", H, H + W)
+    SN, LM, TL = v("tab", 0, 3 * H), v("tab", 3 * H, 3 * H + W), v("xtl", H, H + W)
 
     def again():
-        for c in range(0, H, 512):
-            act(v("tab", c, c + 512), v("tab", H + c, H + c + 512))
+        for c in range(2):
+            load(v("tab", c * H, c * H + H), v("tab", 2 * H, 3 * H), 3.0)
 
     load(v("fm0"), T.fm[:], 0.5)
     load(v("wk0"), T.wk[:], 0.2)
     load(LM, T.lm[:], 2.5)
-    load(v("fr0"), T.fr[:], 4.0)
     load(TL, T.tl[:], 5.0)
     load(v("xmo"), T.mo[:], 8.0)
-    load(v("sn0"), T.sn[:], 10.0)
+    load(v("sn0"), T.sn[:], 9.5)
+    load(v("fr0"), T.fr[:], 10.5)
     vset(v("one", 0, 128), 1.0)
     vset(v("one", 128, 512), 1.0)
     vset(v("zero"), 0.0)
     o128 = v("one", 0, 128)
-    pick(v("I"), o128, [[-1, 128]], A.is_equal, 0.0, 0, 1)
+    iota(v("pi", 0, 1), [[0, 1]], 0, 1, False)
+    iota(v("ti"), [[1, 12]], 0, 0)
     pick(v("tmp"), o128, [[-16, 8], [0, 16]], A.is_ge, 0.0, 0, 1)
     pick(v("bo"), v("tmp"), [[16, 8], [0, 16]], A.is_ge, 0.0, 15, -1)
+    pick(v("I"), o128, [[-1, 128]], A.is_equal, 0.0, 0, 1)
     pick(v("R32", p1=32), v("one", 0, 512, p1=32), [[-1, 32], [0, 16]], A.is_equal, 0.0, 0, 1)
     pick(v("JR"), v("one", 0, 272), [[0, 2], [-16, 8], [1, 17]], A.is_equal, 0.0, -16, 1)
     for a in range(2):
         pick(halves("C8", a, 512), v("one"), [[-16, 4], [0, 8], [-1, 16]], A.is_equal, 0.0, -64 * a, 1)
     pick(v("Mk"), v("zero"), [[0, 16], [-16, 8]], A.is_ge, -BIG / 4, 0, 1)
     pick(v("Mk"), v("Mk"), [[0, 16], [16, 8]], A.is_ge, -BIG / 4, 15, -1)
-    iota(v("pi", 0, 1), [[0, 1]], 0, 1, False)
     iota(v("KC"), [[0, 8], [-8192, 16]], 2047 * 8192, -16 * 8192)
     iota(v("lt"), [[128, 2], [0, 8]], 0, 1)
-    iota(v("ln"), [[16, 16]], 2048, 0)
+    iota(v("ln"), [[16, 16]], 0, 0)
     iota(v("base"), [[0, 16], [256, 5]], DUMP - 256 - 2048, 0)
     pick(v("TR"), o128, [[1, 128]], A.is_gt, 0.0, 0, -1)
     pick(v("R8", p1=8), v("one", 0, 128, p1=8), [[-1, 8], [0, 16]], A.is_equal, 0.0, 0, 1)
-    iota(v("ti"), [[1, 12]], 0, 0)
-    vset(v("mkc"), -7.5)
+    vset(v("mkc"), -7.5 * 4096)
     for a in range(2):
         x = v("mkc", p0=64 * a, p1=64 * a + 64)
-        pick(x, x, [[0, 4], [-1, 64]], A.is_gt, -100.0, 0, 1)
+        pick(x, x, [[0, 4], [-1, 64]], A.is_gt, -BIG, 0, 1)
     for a in range(4):
         act(v("i4", 32 * a, 32 * a + 32, p1=32), v("I", 0, 32, p1=32))
     b = nb()
@@ -275,14 +293,17 @@ def rank_program(g, core, T, topo):
     ts(v("pc", 1, 2), v("pc", 0, 1), 0.0, A.is_gt, 65536.0, A.mult)
     ts(v("pc", 2, 3), v("pc", 0, 1), -1.0, A.mult, 15.0, A.add)
     ts(v("pc", 3, 4), v("pi", 0, 1), -8192.0, A.mult, 4096.0 - 8192.0, A.add)
-    act(v("pc", 4, 5), v("pc", 3, 4), F.Identity, 2048.0)
+    ts(v("pi", 2, 3), v("pi", 0, 1), 63, A.bitwise_and)
+    ts(v("pc", 5, 6), v("pi", 2, 3), 2.0, A.mult, 2048.0, A.add)
+    ts(v("pc", 4, 5), v("pc", 3, 4), v("pc", 5, 6), A.add, -2048.0, A.add)
     act(v("ZC"), v("zero"), F.Identity, v("pc", 4, 5))
     ts(v("pi", 3, 4), v("pi", 0, 1), 4, A.arith_shift_right, 1, A.bitwise_and)
     tc(v("pc", 6, 7), v("pi", 3, 4))
     tc(v("wkf"), v("wk0"))
-    for x in range(3 if "S" in HS else 2):
-        w = v("wkf", x % 2, x % 2 + 1)
+    for x in range(2):
+        w = v("wkf", x, x + 1)
         ts(v("Wt", 8 * x, 8 * x + 8), v("b8"), w, A.mult, -1.0, A.mult)
+        act(v("Wp", 8 * x, 8 * x + 8), v("b8"), F.Identity, 0.0, w)
         act(halves("W3", x), v("bo"), F.Identity, 0.0, w)
     vset(v("Et"), 0.0)
     act(v("Et", 0, 8), v("b8"))
@@ -298,20 +319,16 @@ def rank_program(g, core, T, topo):
         tc(v(name, p1=24), ps(0, ncol(v(y)), p1=24, k=b))
     vset(v("K17"), 129.0 * 2048)
     vset(v("K17", 0, 272, 17), 128.0 * 2048)
-    b = nb()
-    mm(ps(0, 16, k=b), o128, v("Wt", 0, 16))
-    for h in range(2):
-        act(v("c32", h, 32, 2), ps(0, 16, k=b), scale=-255.0)
     for n in (8, 16, 64):
-        vset(v("rm%d" % n), BIG)
+        if n < 64:
+            vset(v("rm%d" % n), BIG)
+        else:
+            act(v("rm64"), v("one", 0, 256), F.Identity, 0.0, v("pc", 5, 6))
         vset(v("rm%d" % n, 0, None, n), -BIG)
-    vset(v("c128"), 127.5)
-    if "S" in HS:
-        vset(v("c129"), 129.0 * 4096)
-        act(v("qI"), v("I"), scale=-4096.0)
-        act(v("nIf"), v("I"), scale=-1.0)
-    act(v("dm"), v("ln"), F.Identity, v("pc", 0, 1))
-    ts(v("LL"), v("dm"), -2048.0, A.add)
+    b = nb()
+    mm(ps(0, 256, k=b), o128, v("W3"))
+    act(v("cT"), ps(0, 256, k=b), scale=255.0)
+    ts(v("LL"), v("ln"), v("pc", 0, 1), A.add)
     act(v("base", 0, 80, 5), v("lt"))
     vset(v("r5"), 1.0)
     vset(v("r5", 0, 80, 5), 0.0)
@@ -320,39 +337,36 @@ def rank_program(g, core, T, topo):
     tt(v("TRB"), v("TR"), v("tmp"), A.add)
     ts(v("tj"), v("ti"), v("pc", 0, 1), A.is_equal)
     act(v("tk"), v("tj"), F.Identity, 1.0, -2.0)
-    vset(v("tbl", 0, 1), -1.0)
+    ts(v("tbl", 0, 1), v("pc", 0, 1), 11.5, A.is_lt, 128.0, A.mult)
+    ts(v("tbl", 0, 1), v("tbl", 0, 1), -64.0, A.add)
     vset(v("tbl", 4096, 4112), 0.0)
     for k in range(12):
+        if k >= 10:
+            load(v("tbl", 1 << k, 2 << k), v("tbl", 0, 1 << k), 1.5)
+            load(v("tbl", 1 << k, 2 << k), v("tbl", 0, 1 << k), 0.5, (k, 12))
+            continue
         for c in range(0, 1 << k, 512):
             n = min(1 << k, 512)
             times(v("tbl", (1 << k) + c, (1 << k) + c + n), v("tbl", c, c + n), v("tk", k, k + 1))
-    for t in range(RO - 1):
-        o = v("TR%d" % t, SL if t else 0, L)
-        act(o, v("one", 0, ncol(o)), F.Identity, 0.0, v("pc", 1, 2))
+    act(v("TR0"), v("one", 0, L), F.Identity, 0.0, v("pc", 1, 2))
+    for t in range(RO - 2):
+        load(v("TR%d" % (t + 1), SL, L), v("TR0", SL, L), 1.0)
         for d in range(N):
-            if t < RO - 2:
-                act(slot(d, "wint", t), v("one", 0, CAP), F.Identity, 0.0, v("pc", 1, 2))
-    for c in range(0, 2 * H, 1024):
-        ts(v("tab", c, c + 1024), v("sn0", c % H, c % H + 1024), -1.0, A.mult, 255.0, A.add)
+            load(slot(d, "wint", t), v("TR0", 0, CAP), 1.0)
+    for c in range(0, H, 1024):
+        ts(v("tab", 2 * H + c, 2 * H + c + 1024), v("sn0", c, c + 1024), -1.0, A.mult, 255.0, A.add)
+    again()
 
-    def refill(o, t, a, b):
-        if t < RO - 1:
-            act(o, v("fr0", t * L + a, t * L + b), F.Identity, 255.0, -1.0)
-        else:
-            act(o, v("fr0", t * L + a, t * L + b))
-    for s in others + [me]:
-        for t in range(RO):
-            o = v("frs", s * SL + t * CAP, s * SL + t * CAP + CAP)
-            refill(slot(me, "win", t) if s == me else o, t, s * CAP, s * CAP + CAP)
+    ts(v("frc"), v("fr0", 0, 3 * L), -1.0, A.mult, 255.0, A.add)
     for t in range(RO):
-        refill(v("L%d" % (t + 1), SL, L), t, SL, L)
-    snd = fused(lambda d: v("frs", d * SL, d * SL + SL), lambda d: v("rin", me * SL, me * SL + SL), "rarr", "rloc")
-    got("rarr", [v("rin", s * SL, s * SL + SL) for s in others], snd, 12.0)
-    for t in range(RO):
-        for s in others:
-            act(slot(s, "win", t), v("rin", s * SL + t * CAP, s * SL + t * CAP + CAP))
+        def fill(a, b, t=t):
+            return v("frc" if t < RO - 1 else "fr0", t * L + a, t * L + b)
+        load(slot(me, "win", t), fill(me * CAP, me * CAP + CAP), 1.0)
+        load(v("L%d" % (t + 1), SL, L), fill(SL, L), 1.0)
+        snd = fused(lambda d, fill=fill: fill(d * CAP, d * CAP + CAP), lambda d, t=t: slot(me, "win", t), "rarr%d" % t, "rloc%d" % t)
+        got("rarr%d" % t, [slot(s, "win", t) for s in others], snd, 12.0)
 
-    ts(v("L0"), v("fm0"), -1.0, A.mult, 255.0, A.add)
+    setup[0] = False
 
     def tolist(name, a, n, step, out):
         b = nb()
@@ -365,16 +379,18 @@ def rank_program(g, core, T, topo):
     def ends(name, h):
         return v(name, 8 * h + 7, 128, 16)
 
-    def sums(b, cols, name, c, w):
+    def sums(b, cols, name, c, w, alone=False):
         for i in range(16):
-            mm(ps(*cols(i), k=b), v(name, c + i, c + 2048, 16), w, False, False)
+            mm(ps(*cols(i), k=b), v(name, c + i, c + 2048, 16), w, alone, alone)
 
-    def lowest(shift, between=None):
+    def targets():
         tolist("XT", 0, 16, 1, v("TS"))
         for h in range(2):
             ts(halves("WA", h, 8), ends("TS", h), 2048.0, A.add, 4096.0, A.min)
-        gather("S", v("FT0"), v("tbl"), v("WA"))
-        act(v("FT1"), v("FT0"), F.Identity, 0.0, v("pc", 6, 7))
+
+    def lowest(shift):
+        gather("X", v("FT0"), v("tbl"), v("WA"))
+        times(v("FT1"), v("FT0"), v("pc", 6, 7))
         for pair in range(4):
             b, p = nb(), 32 * pair
             mm(ps(0, 256, k=b), v("I"), v("mkc"), True, False)
@@ -386,24 +402,23 @@ def rank_program(g, core, T, topo):
                            v("FT0", c, c + 64, p0=p, p1=e), False, False)
             mm(ps(0, 256, k=b), v("I"), v("mkc"), False, True)
             scan(halves("SCW", pair, 256), v("rm64"), ps(0, 256, k=b), A.min)
-        if between:
-            between()
-        ts(v("cn"), v("SCW", 63, 1024, 64), 0.5, A.is_gt, 6144.0, A.mult)
         for h in range(2):
-            tt(halves("XZ", h, 8), v("cn", h, 16, 2), halves("XT", h, 8), A.add)
+            tt(halves("XZ", h, 8), v("SCW", 63 + 64 * h, 1024, 128), halves("XT", h, 8), A.max)
         tolist("XZ", 0, 16, 1, v("ZS"))
         for h in range(2):
-            tt(halves("zm", h, 8), ends("ZS", h), halves("dm", h, 8), A.min)
-        ts(v("WL"), v("zm"), shift, A.add)
+            ts(halves("WL", h, 8), ends("ZS", h), shift, A.add)
 
     for t in range(RO):
         last = t == RO - 1
-        Lt, Ln = "L%d" % t, "L%d" % (t + 1)
+        Lt, Ln = "L%d" % t if t else "fm0", "L%d" % (t + 1)
         main[0] = True
         b = nb()
         for h in range(2):
-            mm(ps(h, 32, 2, k=b), halves(Lt, h), v("Wt", 0, 16))
-        tt(v("au"), ps(0, 32, k=b), v("c32"), A.add)
+            mm(ps(h, 32, 2, k=b), halves(Lt, h), v("Wt" if t else "Wp"))
+        if t:
+            tt(v("au"), ps(0, 32, k=b), v("cT", 0, 256, 8), A.add)
+        else:
+            tc(v("au"), ps(0, 32, k=b))
         ts(v("am"), v("au"), 4095, A.bitwise_and)
         tt(v("up"), v("am", 0, 16), v("am", 16, 32), A.mult)
         ts(v("av", 16, 32), v("au", 0, 16), 2047, A.bitwise_and)
@@ -413,17 +428,17 @@ def rank_program(g, core, T, topo):
             ts(v("av", 32, 48), v("up"), 16, A.arith_shift_right, 1, A.bitwise_and)
         tc(v("XV", 0, 2 * rows), v("av", 0, 2 * rows))
         for h in range(2):
-            act(mp(h), halves(Lt, h), F.Identity, 255.0, -1.0)
+            move(mp(h), halves(Lt, h), *((255.0, -1.0) if t else ()))
             b = nb()
             mm(ps(0, 128, k=b), mp(h), v("I"))
-            act(halves("mT", h), ps(0, 128, k=b))
+            move(halves("mT", h), ps(0, 128, k=b))
             b = nb()
             mm(ps(0, 128, p1=rows, k=b), v("XV", h, 2 * rows, 2), v("Ih"))
             tc(v("XA", 128 * h, 128 * h + 128, p1=rows), ps(0, 128, p1=rows, k=b))
             xa = v("XA", 128 * h, 128 * h + 128, p1=16)
             b, b2 = nb(), nb()
             mm(ps(0, 128, k=b), v("EC", p1=16), xa)
-            act(halves("cq", h), ps(0, 128, k=b), F.Identity, 128.5 + 1.0 / 4096, 1.0 / 2048)
+            move(halves("cq", h), ps(0, 128, k=b), 128.5 + 1.0 / 4096, 1.0 / 2048)
             mm(ps(0, 128, k=b2), v("EC", p1=16), xa, True, False)
             mm(ps(0, 128, k=b2), v("hI"), halves("cq", h), False, True)
             ts(halves("CL", h), ps(0, 128, k=b2), 129.0 * 2048, A.add)
@@ -431,7 +446,7 @@ def rank_program(g, core, T, topo):
             for q in range(4 * h, 4 * h + 4):
                 a = q % 4
                 x, e, off = halves("X", q, 512), halves("E", q, 512), halves("CL", q, 32)
-                gather("X", x, LM, off)
+                gather(GB[q], x, LM, off)
                 mt = v("mT", h * 128, h * 128 + 128, p0=32 * a, p1=32 * a + 32)
                 b = nb()
                 if EB[q] == "V":
@@ -446,17 +461,17 @@ def rank_program(g, core, T, topo):
             mm(ps(0, 272, k=b), v("XA", 128 * h, 128 * h + 128, p1=16), v("ER", p1=16), False, False)
             sums(b, lambda i: (16 - i, 272, 17), "E", 2048 * h, v("NP"))
             mm(ps(0, 272, k=b), halves("cq", h), v("JN"), False, True)
-            act(halves("SD", h, 136), ps(136, 272, k=b))
+            move(halves("SD", h, 136), ps(136, 272, k=b))
             scan(halves("GV", h, 136), ps(0, 136, k=b), halves("SD", h, 136), A.max, A.min)
             tolist("GV", 136 * h + 16, 8, 17, halves("GS", h, 64))
             gl = halves("GL", h, 8)
             ts(gl, v("GS", 64 * h + 7, 64 * h + 64, 8), 0.0, A.max)
-            gather("S", halves("xg", h), LM, gl)
+            gather("X", halves("xg", h), LM, gl)
             gather("V", halves("TG", h), TL, gl)
             b = nb()
             mm(ps(0, 128, k=b), mp(h), v("nI"), True, False)
             mm(ps(0, 128, k=b), halves("xg", h), v("I"), False, True)
-            act(halves("qT", h), ps(0, 128, k=b))
+            move(halves("qT", h), ps(0, 128, k=b))
         main[0] = False
         gv = v("GV", 16, 272, 17)
         ts(v("hb"), gv, 0.0, A.is_ge, BIG / 2, A.mult)
@@ -464,61 +479,36 @@ def rank_program(g, core, T, topo):
         tt(v("cap"), v("hb"), v("g2"), A.add)
         if last:
             tt(v("zm"), v("hb"), gv, A.add)
-            ts(v("XT"), v("zm"), 2048.0, A.add, 4096.0, A.min)
+            ts(v("XT"), v("zm"), 2048.0, A.add, v("pc", 5, 6), A.min)
+            targets()
             lowest(0.0)
             for blk in range(3, -1, -1):
                 c = PH * (blk // 2) + 2048 + 64 * (blk % 2)
-                scatter(v("tab", 2 * H, 2 * H + W + L), halves("WL", blk, 4), v("P", c, c + 64))
+                scatter(v("tab", 3 * H, 3 * H + W + L), halves("WL", blk, 4), v("P", c, c + 64))
         main[0] = True
         for h in range(2):
             for q in range(4 * h, 4 * h + 4):
                 a = q % 4
                 y, p = halves("Y", q, 512), prod(q)
-                gather("X", y, v("xmo"), halves("TG", q, 32))
+                gather(GD[q], y, v("xmo"), halves("TG", q, 32))
                 b = nb()
                 mm(ps(0, 512, k=b), v("nI"), y, True, False)
                 mm(ps(0, 512, k=b), v("qT", h * 128, h * 128 + 128, p0=32 * a, p1=32 * a + 32), v("Rep", p0=32 * a, p1=32 * a + 32), False, True)
-                relu(p, ps(0, 512, k=b), 255.0)
-            hp, hq, hs, hh, kf = [halves(x, h) for x in ("hp", "hq", "hs", "hh", "kf")]
-            if HS[h] == "V":
-                b = nb()
-                mm(ps(0, 256, k=b), v("c128"), v("W3", 0, 256), True, False)
-                sums(b, lambda i: (i, 256, 16), "P", PH * h, v("Wt", 0, 16))
-                mm(ps(0, 256, k=b), v("c128"), v("W3", 0, 256), False, True)
-                tc(halves("hi", h, 256), ps(0, 256, k=b))
-                ts(halves("hm", h, 256), halves("hi", h, 256), 4095, A.bitwise_and)
-                tt(hp, halves("hm", 2 * h), halves("hm", 2 * h + 1), A.mult)
-                ts(hs, halves("hi", 2 * h), 2047, A.bitwise_and)
-                ts(hq, hp, 5, A.arith_shift_right, 2047, A.bitwise_and)
-                tt(halves("lo", h), hq, hs, A.add)
-                b = nb()
-                mm(ps(0, 128, k=b), halves("lo", h), v("If"))
-                tc(halves("HL", h), ps(0, 128, k=b))
-                tt(kf, halves("lo", h), v("KC"), A.add)
-            else:
-                b, b2, kq = nb(), nb(), halves("kq", h, 256)
-                for k, n in ((b, 16), (b2, 24)):
-                    mm(ps(0, 16 * n, k=k), v("c128"), v("W3", 0, 16 * n), True, False)
-                    mm(ps(0, 16 * n, k=k), v("I"), v("c129", 0, 16 * n), False, False)
-                    sums(k, lambda i: (i, 16 * n, 16), "P", PH * h, v("Wt", 0, n))
-                mm(ps(0, 256, k=b), v("c128"), v("W3", 0, 256), False, True)
-                act(kq, ps(0, 256, k=b), F.Identity, -0.5 + 1.0 / 8192, 1.0 / 4096)
-                mm(ps(0, 256, k=b2), v("qI"), kq, False, False)
-                mm(ps(256, 384, k=b2), v("qI"), v("kq", 256 * h, 256 * h + 128), False, False)
-                mm(ps(0, 384, k=b2), v("c128"), v("W3"), False, True)
-                act(halves("Vs", h), ps(128, 256, k=b2))
-                tt(hp, halves("Vs", h), ps(0, 128, k=b2), A.mult)
-                ts(hq, hp, 5, A.arith_shift_right, 2047, A.bitwise_and)
-                tt(hs, hq, ps(256, 384, k=b2), A.add)
-                ts(hh, hs, 2047, A.bitwise_and)
-                tc(halves("lo", h), hh)
-                b = nb()
-                mm(ps(0, 128, k=b), halves("lo", h), v("If"))
-                tc(halves("HL", h), ps(0, 128, k=b))
-                b = nb()
-                mm(ps(0, 128, k=b), v("If"), v("KC"), True, False)
-                mm(ps(0, 128, k=b), v("If"), halves("lo", h), False, True)
-                act(kf, ps(0, 128, k=b))
+                relu(p, ps(0, 512, k=b), 255.0, ED[q])
+            b = nb()
+            sums(b, lambda i: (i, 256, 16), "P", PH * h, v("Wt"), True)
+            tt(halves("hi", h, 256), ps(0, 256, k=b), v("cT"), A.add)
+            ts(halves("hm", h, 256), halves("hi", h, 256), 4095, A.bitwise_and)
+            tt(halves("hp", h), halves("hm", 2 * h), halves("hm", 2 * h + 1), A.mult)
+            ts(halves("hq", h), halves("hp", h), 5, A.arith_shift_right, 2047, A.bitwise_and)
+            tt(halves("lo", h), halves("hq", h), halves("hm", 2 * h), A.add)
+            b = nb()
+            mm(ps(0, 128, k=b), halves("lo", h), v("If"))
+            tc(halves("HL", h), ps(0, 128, k=b))
+            b = nb()
+            mm(ps(0, 128, k=b), v("If"), v("KC"), True, False)
+            mm(ps(0, 128, k=b), v("If"), halves("lo", h), False, True)
+            move(halves("kf", h), ps(0, 128, k=b))
         for h in range(2):
             for q in range(4 * h, 4 * h + 4):
                 ne, p, sx = halves("NE", q, 512), prod(q), halves("SX", q, 512)
@@ -553,11 +543,17 @@ def rank_program(g, core, T, topo):
         tolist("XC", 0, 16, 1, v("CS"))
         for h in range(2):
             ts(halves("CHL", h, 8), ends("CS", h), 2047.0, A.add)
-            gather("S", halves("CH", h), halves("P", h, PH), halves("CHL", h, 8), last and (255.0, -1.0))
+            gather("X", halves("CH", h), halves("P", h, PH), halves("CHL", h, 8), last and (255.0, -1.0))
+        if not last:
+            ts(v("t1"), v("key"), 2047, A.bitwise_and)
+            ts(v("t2"), v("key"), (1 << 24) + 6144, A.bitwise_and)
+            ts(v("t3"), v("t2"), -2048.0 - (1 << 24), A.add, -2048.0, A.max)
+            tt(v("XT"), v("t1"), v("t3"), A.add)
+            targets()
         scatter(v("win%d" % t), v("SLL"), v("CH"))
         mine = (me * CAP, me * CAP + CAP)
         snd = fused(lambda d, t=t: slot(d, "win", t), lambda d, Ln=Ln: v(Ln, mine[0], mine[1]), "arr%d" % t, "loc%d" % t)
-        act(v(Ln, mine[0], mine[1]), slot(me, "win", t))
+        move(v(Ln, mine[0], mine[1]), slot(me, "win", t))
         got("arr%d" % t, [v(Ln, s * CAP, s * CAP + CAP) for s in others], snd, XLAG)
 
         def tails():
@@ -569,7 +565,7 @@ def rank_program(g, core, T, topo):
                 b = nb()
                 for h in range(2):
                     mm(ps(128 * h, 128 * h + 128, p1=8, k=b), halves("IV", h, 8), v("Ih"))
-                act(v("XI", p1=8), ps(0, 256, p1=8, k=b))
+                move(v("XI", p1=8), ps(0, 256, p1=8, k=b))
                 b = nb()
                 mm(ps(0, 256, k=b), v("R8", p1=8), v("XI", p1=8))
                 ts(v("mk"), ps(0, 256, k=b), v("pc", 2, 3), A.not_equal)
@@ -584,20 +580,17 @@ def rank_program(g, core, T, topo):
             tt(v("CT"), v("T2"), ps(0, 256, k=b2), A.min)
             ts(v("CTm"), v("CT"), 4095, A.bitwise_and)
         if not last:
-            ts(v("t1"), v("key"), 2047, A.bitwise_and)
-            ts(v("t2"), v("key"), (1 << 24) + 6144, A.bitwise_and)
-            ts(v("t3"), v("t2"), -2048.0 - (1 << 24), A.add, -2048.0, A.max)
-            tt(v("XT"), v("t1"), v("t3"), A.add)
-            lowest(2048.0, tails)
+            lowest(2048.0)
             for blk in range(3, -1, -1):
-                scatter(v("tab", H, 2 * H + W + L), halves("WL", blk, 4), halves("CH", blk, 64))
+                scatter(v("tab", 2 * H, 3 * H + W + L), halves("WL", blk, 4), halves("CH", blk, 64))
             main[0] = False
+            tails()
             again()
             for blk in range(3, -1, -1):
                 scatter(v("xtl"), halves("WL", blk, 4), halves("CTm", blk, 64))
     op("D", lambda: g.sync.dma_start(T.yf[:], ap(v("L4"))), [v("L4")], [], 0.08, sem="st0", val=16, lag=2.0)
     out = op("D", lambda: g.sync.dma_start(T.yl[:], ap(LM)), [LM], [], 0.08, sem="st1", val=16, lag=2.0)
-    op("R", None, [], [], 0.0, sem="st1", val=16, lag=4.0, after=out)
+    op("R", None, [], [], 0.0, sem="st1", val=16, lag=4.5, after=out)
     _emit(g, T, ops, bank)
 
 
@@ -624,9 +617,9 @@ def _plan(ops, deps, bank):
             if j != lst[0] and j not in deps[lst[0]]:
                 gate[j].append(lst[0])
                 need[lst[0]] += 1
-    cost = [o["cost"] for o in ops]
+    costs = [[o["cost"][0] + o["cost"][1] * z[o["cost"][2]] for o in ops] for z in SETS]
 
-    def forward(key):
+    def forward(key, cost, LOOK):
         left, est, end, on, banks, after = list(need), [0.0] * nop, [0.0] * nop, [o["q"] for o in ops], {}, {}
         ready = {q: [] for q in "VSTGDRX"}
         for i in range(nop):
@@ -645,7 +638,7 @@ def _plan(ops, deps, bank):
                     if best is None or s < best[0]:
                         best = (s, q, lst)
             s, q, lst = best
-            i = min((z for z in lst if when(z) <= s), key=lambda z: key[z] + (LOOK[1] if q == "V" and on[z] == "X" else 0))
+            i = min((z for z in lst if when(z) <= s), key=lambda z: key[z] + (LOOK[1 + (ops[z]["cost"][2] == "e")] if q == "V" and on[z] == "X" else 0))
             soon = [when(z) for z in lst if key[z] < key[i] and s < when(z) < s + min(LOOK[0], cost[i])]
             if soon and q != "R":
                 clock[q] = min(soon)
@@ -670,7 +663,7 @@ def _plan(ops, deps, bank):
                     ready[on[j]].append(j)
         return max(end), order, on, banks, after, end
 
-    def backward(order, on, end):
+    def backward(order, on, end, cost):
         late, busy, at = [0.0] * nop, {}, {i: n for n, i in enumerate(order)}
         for i in sorted(order, key=lambda i: (-end[i], -at[i])):
             s = max([late[j] + lag for j, lag in post[i]] + [0.0])
@@ -685,12 +678,28 @@ def _plan(ops, deps, bank):
                 row.insert(lo, (s, s + cost[i]))
             late[i] = s + cost[i]
         return [-x for x in late]
-    best = None
-    for _ in range(PASSES):
-        plan = forward(key)
-        if best is None or plan[0] < best[0]:
-            best = plan
-        key = backward(plan[1], plan[2], plan[5])
+
+    def replay(plan, cost):
+        est, clock, end = [0.0] * nop, {}, [0.0] * nop
+        for i in plan[1]:
+            s = max(est[i], clock.get(plan[2][i], 0.0) if plan[2][i] != "R" else 0.0)
+            if plan[4].get(i) is not None:
+                s = max(s, end[plan[4][i]] + LAG)
+            end[i] = clock[plan[2][i]] = s + cost[i]
+            for j, lag in post[i]:
+                est[j] = max(est[j], end[i] + lag)
+        return max(end)
+    best, first = None, key
+    for mix in MIX:
+        cost = [a + mix * (b - a) for a, b in zip(*costs)]
+        for look in LOOKS:
+            key = first
+            for _ in range(PASSES):
+                plan = forward(key, cost, look)
+                mark = replay(plan, costs[0]) * 1.5 + replay(plan, costs[1])
+                if best is None or mark < best[0]:
+                    best = (mark,) + plan[1:]
+                key = backward(plan[1], plan[2], plan[5], cost)
     _, order, on, banks, after, _ = best
     for i in range(nop):
         ops[i]["q"] = on[i]

@@ -8,29 +8,30 @@ PH = 2176
 BIG = 67108864.0
 _B, _F, _H, _I, _U = "bfloat16", "float32", "float16", "int32", "uint16"
 _SB = {
-    "tab": (3 * H + W + L, _B), "xtl": (H + W + L, _I), "xmo": (4096, _B), "sn0": (H, _B), "fm0": (L, _B),
+    "tab": (3 * H + W, _B), "xtl": (H + W + L, _I), "xmo": (4096, _B), "sn0": (H, _B), "fm0": (L, _B),
     "fr0": (RO * L, _B), "wk0": (3, _I), "wkf": (3, _F), "frc": (3 * L, _B),
     "win0": (SW, _B), "win1": (SW, _B), "win2": (SW, _B), "win3": (SW, _B), "wint0": (SW, _F), "wint1": (SW, _F),
     "L1": (L, _B), "L2": (L, _B), "L3": (L, _B), "L4": (L, _B), "TR0": (L, _F), "TR1": (L, _F), "TR2": (L, _F),
-    "mT": (L, _B), "qT": (L, _B), "au": (32, _I), "am": (32, _I), "up": (16, _I), "av": (48, _I), "cq": (L, _B),
-    "XV": (48, _H), "XA": (256, _H), "CL": (L, _U), "X": (4096, _B), "E": (4096, _B), "Y": (4096, _B), "P": (2 * PH, _B),
+    "L0": (L, _B), "mT": (L, _B), "mE": (L, _B), "qT": (L, _B), "au": (128, _I), "am": (128, _I), "up": (64, _F), "ui": (64, _I), "uj": (64, _I),
+    "a12": (64, _F), "ci": (L, _I), "cj": (L, _I), "cf": (L, _H), "MR": (4096, _B), "CL": (L, _U), "X": (4096, _B), "E": (4096, _B), "Y": (4096, _B), "P": (2 * PH + 16, _B),
     "NE": (4096, _B), "SX": (4096, _B), "SD": (272, _F), "GV": (272, _H), "GS": (128, _F), "GL": (16, _U), "TG": (L, _U), "xg": (L, _B),
-    "hi": (512, _I), "hm": (512, _I), "hp": (256, _I), "hq": (256, _I), "lo": (256, _F), "kf": (256, _F),
-    "HL": (256, _U), "k2": (256, _F), "SC2": (256, _F), "key": (16, _I), "hb": (16, _F), "g2": (16, _F),
+    "hi": (512, _I), "hm": (512, _I), "hp": (256, _I), "hq": (256, _I), "lo": (256, _F), "hQ": (512, _B), "hV": (256, _F),
+    "HL": (256, _U), "LO": (W + L, _B), "SC2": (256, _F), "key": (16, _I), "hb": (16, _F), "g2": (16, _F),
     "cap": (16, _F), "kj": (16, _I), "IV": (16, _H), "XI": (256, _B), "fp": (16, _I), "XC": (16, _H), "CS": (128, _F), "CHL": (16, _U),
     "CH": (L, _B), "dd": (16, _I), "OH": (80, _B), "S5": (80, _H), "SS": (128, _F), "SLL": (16, _U),
     "TGp": (L, _F), "mk": (L, _F), "T2": (L, _F), "CT": (L, _I), "CTm": (L, _I),
     "t1": (16, _I), "t2": (16, _I), "t3": (16, _F), "XT": (16, _H), "TS": (128, _F), "WA": (16, _U), "FT0": (L, _B), "FT1": (L, _B),
-    "SCW": (1024, _F), "XZ": (16, _H), "ZS": (128, _F), "zm": (16, _F), "WL": (16, _U),
+    "SCW": (1024, _F), "zn": (16, _F), "capT": (16, _F), "XZ": (16, _H), "ZS": (128, _F), "zm": (16, _F), "WL": (16, _U),
 }
 _CO = {
-    "one": (512, _B), "zero": (128, _B), "I": (128, _B), "nI": (128, _B), "Ih": (128, _H), "If": (128, _F),
-    "hI": (128, _B), "bo": (128, _B), "b8": (8, _B), "tmp": (128, _B), "Rep": (512, _B), "R32": (512, _B), "C8": (1024, _B), "i4": (128, _B),
-    "R8": (128, _B), "TR": (128, _B), "TRB": (128, _B), "JR": (272, _B), "JN": (272, _B), "K17": (272, _B), "Et": (48, _B), "KC": (128, _F),
-    "ZC": (128, _F), "base": (80, _B), "r5": (80, _B), "rm8": (128, _B), "rm16": (128, _B), "rm64": (256, _F), "Mk": (128, _B),
-    "mkc": (256, _B), "pc": (8, _F), "pi": (4, _I), "W3": (256, _B), "Wt": (16, _B), "Wp": (16, _B), "NP": (16, _B), "PB8": (8, _B), "cT": (256, _F),
-    "c32": (32, _F), "ln": (16, _F), "lt": (16, _F), "LL": (16, _U), "EC": (128, _H), "EA": (128, _H),
-    "ER": (272, _H), "ti": (12, _F), "tj": (12, _F), "tk": (12, _F), "tbl": (4096 + 16, _B),
+    "one": (512, _B), "zero": (272, _B), "I": (128, _B), "nI": (128, _B), "Ih": (128, _H), "If": (128, _F),
+    "bo": (128, _B), "b8": (8, _B), "tmp": (128, _B), "Rep": (512, _B), "R32": (512, _B), "C8": (1024, _B), "i4": (128, _B),
+    "R8": (128, _B), "TR": (128, _B), "TRB": (128, _B), "JR": (272, _B), "K17": (16, _B), "Et": (96, _B), "ZU": (96, _B), "ZV": (96, _B),
+    "cA": (128, _F), "EX": (512, _F), "cB": (256, _B), "o32": (128, _B),
+    "base": (80, _B), "r5": (80, _B), "rm8": (128, _B), "k8": (128, _B), "Mk": (128, _B),
+    "mkc": (256, _B), "pc": (12, _F), "pi": (4, _I), "W3": (256, _B), "Wt": (16, _B), "NP": (16, _B), "PB8": (8, _B), "cT": (256, _F),
+    "c32": (32, _F), "ln": (16, _F), "lt": (16, _F), "LL": (16, _U),
+    "ti": (12, _F), "tj": (12, _F), "tk": (12, _F), "tbl": (4096 + 16, _B),
 }
 _PACK, _POS = {}, {}
 for _k in list(_SB) + list(_CO):
@@ -51,19 +52,28 @@ for _t, _n in _PACK.items():
     SCRATCH["pk_" + _t] = ("sbuf", [128, _n], _t)
 for _k in range(8):
     SCRATCH["ps%d" % _k] = ("psum", [128, 512], "float32")
-SEMAPHORES = ["q" + e for e in "VSTG"] + ["ld%d" % i for i in range(39)] + ["st0", "st1"] + \
+SEMAPHORES = ["q" + e for e in "VSTG"] + ["ld%d" % i for i in range(40)] + ["st0", "st1"] + \
     ["%s%d" % (p, t) for p in ("arr", "tarr", "rarr", "loc", "tloc", "rloc") for t in range(RO)]
 
-EB = "SSVVSVSV"
+EB = "AAASAASS"
 SE = "SSSVSVVV"
-GB = "XXVXXXXX"
-GD = "XXSXVXXS"
-ED = "XXSXXSVX"
-SETS = ({"e": 0.00085, "g": 0.00095, "s": 0.0021, "t": 0.00030}, {"e": 0.00120, "g": 0.00220, "s": 0.0055, "t": 0.00045})
-LAG = 0.17
+GB = "SSSSSSSS"
+GD = "XXXXXXXX"
+ED = "XXXXXXXX"
+SETS = ({"e": 0.00085, "g": 0.00095, "s": 0.0021, "t": 0.00032}, {"e": 0.00120, "g": 0.00220, "s": 0.0055, "t": 0.00048})
+LOOSE = True
+SHUT, SHUT2 = False, True
+HS = ""
+SLOW = 1.2
+EARLY = False
+BY = ((128, 128), (128, 128), (128, 128))
+LAG = 0.18
 XLAG = 3.5
 LOOKS = ((0.2, 2.0, 0.0), (0.2, 2.0, 2.0), (0.25, 1.0, 1.0))
 MIX = (0.25,)
+SHAKES, SHAKE, SPAN, SEED, SHARE = 2400, (0.3, 0.6, 1.2), (2.0, 4.0, 3.0, 7.0), 12345, True
+TIE, SKIP = 2, 1
+NOTE = {}
 PASSES = 6
 
 
@@ -85,7 +95,7 @@ def rank_program(g, core, T, topo):
         buf = T[bank.get(x[0], x[0])]
         if x[5] == 1:
             return buf[x[1]:x[2], x[3]:x[4]]
-        return buf[x[1]:x[2], x[3]:x[4]:x[5]]
+        return buf[x[1]:x[2], x[3]:(x[4] if x[4] >= 0 else None):x[5]]
 
     def ncol(x):
         return len(range(x[3], x[4], x[5]))
@@ -94,7 +104,11 @@ def rank_program(g, core, T, topo):
         return ap(s) if isinstance(s, tuple) else s
 
     def op(q, fn, rd, wr, cost, sem=None, val=0, lag=LAG, after=None):
-        ops.append({"q": q, "fn": fn, "rd": rd, "wr": wr, "cost": cost if isinstance(cost, tuple) else (cost, 0, "e"),
+        cost = cost if isinstance(cost, tuple) else (cost, 0, "e")
+        if isinstance(fn, dict) and cost[2] == "e":
+            n = ncol(rd[0])
+            cost = vc(n, 0.5 if is2(rd[0]) and is2(wr[0]) else 1.0) + (0.13 if inps(rd[0]) else 0.05, n, "e")
+        ops.append({"q": q, "fn": fn, "rd": rd, "wr": wr, "cost": cost[:3], "costs": cost[-3:],
                     "sem": sem, "val": val, "lag": lag, "after": after, "main": main[0] and len(ops)})
         return len(ops) - 1
 
@@ -146,8 +160,8 @@ def rank_program(g, core, T, topo):
         return op(q, {"V": lambda: g.vector.tensor_scalar(ap(out), ap(x), c, 0.0, A.add, A.max),
                         "S": lambda: g.scalar.activation(ap(out), ap(x), F.Relu, bias=c)}, [x], [out], (0.1, ncol(x), "e"))
 
-    def move(out, x, bias=0.0, scale=1.0):
-        return op("X", {"V": lambda: g.vector.tensor_scalar(ap(out), ap(x), arg(scale), arg(bias), A.mult, A.add),
+    def move(out, x, bias=0.0, scale=1.0, q="X"):
+        return op(q, {"V": lambda: g.vector.tensor_scalar(ap(out), ap(x), arg(scale), arg(bias), A.mult, A.add),
                         "S": lambda: g.scalar.activation(ap(out), ap(x), F.Identity, bias=arg(bias), scale=arg(scale))},
                   [x] + [s for s in (bias, scale) if isinstance(s, tuple)], [out],
                   (0.1 if inps(x) else 0.05, max(64, ncol(x)), "e"))
@@ -163,13 +177,19 @@ def rank_program(g, core, T, topo):
     def scatter(win, off, x, y=None):
         c = (0.05, ncol(x), "s")
         if y:
-            return op("V", lambda: g.vector.tensor_tensor(ap(win).indirect(ap(off)), ap(x), ap(y), A.mult), [x, y, off], [win], c)
+            return op("V", lambda: g.vector.tensor_tensor(ap(win).indirect(ap(off)), ap(x), ap(y), A.add), [x, y, off], [win], c)
         return op("V", lambda: g.vector.tensor_copy(ap(win).indirect(ap(off)), ap(x)), [x, off], [win], c)
 
+    def mms(calls):
+        def fn():
+            for out, lhsT, rhs, start, stop in calls:
+                ins = g.tensor.matmul(ap(out), ap(lhsT), ap(rhs), start, stop)
+            return ins
+        n = sum((4 if SCRATCH[x[2][0]][2] == _F else 1) * max(min(64, ncol(x[1])), ncol(x[2])) for x in calls)
+        return op("T", fn, [y for x in calls for y in x[1:3]], [x[0] for x in calls], (0.015 * len(calls), n, "t"), lag=LAG + 0.1)
+
     def mm(out, lhsT, rhs, start=True, stop=True):
-        f = 4 if SCRATCH[rhs[0]][2] == _F else 1
-        return op("T", lambda: g.tensor.matmul(ap(out), ap(lhsT), ap(rhs), start, stop), [lhsT, rhs], [out],
-                  (0.015, f * max(min(64, ncol(lhsT)), ncol(rhs)), "t"), lag=LAG + 0.1)
+        return mms([(out, lhsT, rhs, start, stop)])
 
     def pick(out, x, pattern, cmp, fill, base, cm):
         return op("G", lambda: g.affine_select(ap(out), ap(x), pattern, cmp, fill, base, cm), [x], [out, pool], (0.17, 2 * ncol(out), "e"))
@@ -232,24 +252,27 @@ def rank_program(g, core, T, topo):
         return v(name, h * n, h * n + n)
 
     def mp(h):
-        return v("P", PH * h + 2048, PH * h + PH)
+        return v("P", PH * h, PH * h + 128)
 
     def prod(q):
-        c = PH * (q // 4) + 512 * (q % 4)
+        c = PH * (q // 4) + 128 + 512 * (q % 4)
         return v("P", c, c + 512)
-    SN, LM, TL = v("tab", 0, 3 * H), v("tab", 3 * H, 3 * H + W), v("xtl", H, H + W)
+
+    def back(x):
+        return x[:3] + (x[4] - 1, x[3] - 1, -1)
+    SN, LM, TL = v("tab", W, W + 3 * H), v("tab", 0, W), v("xtl", 0, W)
 
     def again():
-        for c in range(2):
-            load(v("tab", c * H, c * H + H), v("tab", 2 * H, 3 * H), 3.0)
+        for c in range(1, 3):
+            load(v("tab", W + c * H, W + c * H + H), v("tab", W, W + H), 3.0)
 
     load(v("fm0"), T.fm[:], 0.5)
     load(v("wk0"), T.wk[:], 0.2)
-    load(LM, T.lm[:], 2.5)
-    load(TL, T.tl[:], 5.0)
-    load(v("xmo"), T.mo[:], 8.0)
-    load(v("sn0"), T.sn[:], 9.5)
-    load(v("fr0"), T.fr[:], 10.5)
+    load(LM, T.lm[:], 2.5 * SLOW)
+    load(TL, T.tl[:], 5.0 * SLOW)
+    load(v("xmo"), T.mo[:], 8.0 * SLOW)
+    load(v("sn0"), T.sn[:], 9.5 * SLOW)
+    load(v("fr0"), T.fr[:], 10.5 * SLOW)
     vset(v("one", 0, 128), 1.0)
     vset(v("one", 128, 512), 1.0)
     vset(v("zero"), 0.0)
@@ -263,18 +286,16 @@ def rank_program(g, core, T, topo):
     pick(v("JR"), v("one", 0, 272), [[0, 2], [-16, 8], [1, 17]], A.is_equal, 0.0, -16, 1)
     for a in range(2):
         pick(halves("C8", a, 512), v("one"), [[-16, 4], [0, 8], [-1, 16]], A.is_equal, 0.0, -64 * a, 1)
-    pick(v("Mk"), v("zero"), [[0, 16], [-16, 8]], A.is_ge, -BIG / 4, 0, 1)
-    pick(v("Mk"), v("Mk"), [[0, 16], [16, 8]], A.is_ge, -BIG / 4, 15, -1)
-    iota(v("KC"), [[0, 8], [-8192, 16]], 2047 * 8192, -16 * 8192)
+    pick(v("Mk"), v("zero", 0, 128), [[0, 16], [-16, 8]], A.is_ge, -BIG / 2, 0, 1)
+    pick(v("Mk"), v("Mk"), [[0, 16], [16, 8]], A.is_ge, -BIG / 2, 15, -1)
     iota(v("lt"), [[128, 2], [0, 8]], 0, 1)
-    iota(v("ln"), [[16, 16]], 0, 0)
     iota(v("base"), [[0, 16], [256, 5]], DUMP - 256 - 2048, 0)
     pick(v("TR"), o128, [[1, 128]], A.is_gt, 0.0, 0, -1)
     pick(v("R8", p1=8), v("one", 0, 128, p1=8), [[-1, 8], [0, 16]], A.is_equal, 0.0, 0, 1)
-    vset(v("mkc"), -7.5 * 4096)
     for a in range(2):
-        x = v("mkc", p0=64 * a, p1=64 * a + 64)
-        pick(x, x, [[0, 4], [-1, 64]], A.is_gt, -BIG, 0, 1)
+        pick(v("mkc", p0=64 * a, p1=64 * a + 64), v("zero", 0, 256, p0=64 * a, p1=64 * a + 64), [[0, 4], [-1, 64]],
+             A.not_equal, float(1 << 20), 0, 1)
+    vset(v("mkc", 0, 256, 64), -BIG)
     for a in range(4):
         act(v("i4", 32 * a, 32 * a + 32, p1=32), v("I", 0, 32, p1=32))
     b = nb()
@@ -283,52 +304,63 @@ def rank_program(g, core, T, topo):
     act(v("nI"), v("I"), scale=-1.0)
     tc(v("Ih"), v("I"))
     act(v("If"), v("I"))
-    act(v("hI"), v("I"), scale=-2048.0)
     tc(v("b8"), v("bo", 0, 128, 16))
     act(v("NP", 0, 8), v("b8"), scale=-8192.0)
     act(v("NP", 8, 16), v("b8"), scale=8192.0)
-    act(v("PB8"), v("b8"), scale=BIG / 2)
+    act(v("PB8"), v("b8"), scale=-BIG / 2)
     ts(v("pi", 1, 2), v("pi", 0, 1), 15, A.bitwise_and)
     tc(v("pc", 0, 1), v("pi", 1, 2))
-    ts(v("pc", 1, 2), v("pc", 0, 1), 0.0, A.is_gt, 65536.0, A.mult)
-    ts(v("pc", 2, 3), v("pc", 0, 1), -1.0, A.mult, 15.0, A.add)
-    ts(v("pc", 3, 4), v("pi", 0, 1), -8192.0, A.mult, 4096.0 - 8192.0, A.add)
+    ts(v("pc", 1, 2), v("pc", 0, 1), 0.0, A.is_gt, 131072.0, A.mult)
+    ts(v("pc", 2, 3), v("pi", 0, 1), 16.0, A.mult, 128.0 - 2048, A.add)
+    ts(v("pc", 3, 4), v("pi", 0, 1), -15.0 * 8192, A.mult, 2048.0 - 128 * 8192, A.add)
     ts(v("pi", 2, 3), v("pi", 0, 1), 63, A.bitwise_and)
     ts(v("pc", 5, 6), v("pi", 2, 3), 2.0, A.mult, 2048.0, A.add)
-    ts(v("pc", 4, 5), v("pc", 3, 4), v("pc", 5, 6), A.add, -2048.0, A.add)
-    act(v("ZC"), v("zero"), F.Identity, v("pc", 4, 5))
+    ts(v("pc", 8, 9), v("pi", 2, 3), 0.0, A.is_equal, -BIG, A.mult)
+    tt(v("pc", 7, 8), v("pc", 8, 9), v("pc", 5, 6), A.add)
     ts(v("pi", 3, 4), v("pi", 0, 1), 4, A.arith_shift_right, 1, A.bitwise_and)
     tc(v("pc", 6, 7), v("pi", 3, 4))
     tc(v("wkf"), v("wk0"))
     for x in range(2):
         w = v("wkf", x, x + 1)
         ts(v("Wt", 8 * x, 8 * x + 8), v("b8"), w, A.mult, -1.0, A.mult)
-        act(v("Wp", 8 * x, 8 * x + 8), v("b8"), F.Identity, 0.0, w)
         act(halves("W3", x), v("bo"), F.Identity, 0.0, w)
-    vset(v("Et"), 0.0)
-    act(v("Et", 0, 8), v("b8"))
-    act(v("Et", 8, 16), v("b8"), F.Identity, 0.0, v("wkf", 2, 3))
+    for name in ("ZU", "ZV", "Et"):
+        vset(v(name), 0.0)
+    act(v("ZU", 24, 32), v("Wt", 0, 8))
+    act(v("ZU", 56, 64), v("Wt", 0, 8), scale=-1.0)
+    act(v("ZV", 24, 32), v("Wt", 8, 16))
     act(v("Et", 24, 32), v("b8"))
-    act(v("Et", 40, 48), v("b8"), scale=2048.0)
+    ts(v("Et", 56, 64), v("b8"), v("wkf", 2, 3), A.mult, -32.0, A.mult)
+
+    def lanesums(b, x):
+        mms([(ps(64 * n, 64 * n + 64, p1=64, k=b), v(name, 24 - 8 * blk, 88 - 8 * blk), x(blk), blk == 0, blk == 3)
+             for n, name in enumerate(("ZU", "ZV")) for blk in range(4)])
+    b = nb()
+    lanesums(b, lambda blk: v("one", 0, 64))
+    act(v("cA", p1=64), ps(0, 128, p1=64, k=b), scale=-255.0)
+    vset(v("cA", 64, 128, p0=32, p1=64), 1.0)
+    b = nb()
+    for blk in range(4):
+        mm(ps(128 * blk, 128 * blk + 128, p1=64, k=b), v("Et", 24 - 8 * blk, 88 - 8 * blk), v("I"))
+    act(v("EX", p1=64), ps(0, 512, p1=64, k=b))
     for x in range(2):
         act(v("JR", 136 * x, 136 * x + 136, 17), v("I", 0, 128, 16))
-    act(v("JN"), v("JR"), scale=-2048.0)
-    for name, x, y in (("EC", 0, "I"), ("ER", 0, "JR"), ("EA", 24, "I")):
-        b = nb()
-        mm(ps(0, ncol(v(y)), p1=24, k=b), v("Et", x, x + 24), v(y))
-        tc(v(name, p1=24), ps(0, ncol(v(y)), p1=24, k=b))
-    vset(v("K17"), 129.0 * 2048)
-    vset(v("K17", 0, 272, 17), 128.0 * 2048)
-    for n in (8, 16, 64):
-        if n < 64:
-            vset(v("rm%d" % n), BIG)
-        else:
-            act(v("rm64"), v("one", 0, 256), F.Identity, 0.0, v("pc", 5, 6))
-        vset(v("rm%d" % n, 0, None, n), -BIG)
+    vset(v("K17"), -2048.0)
+    ts(v("L0"), v("fm0"), -1.0, A.mult, 255.0, A.add)
+    vset(v("rm8"), BIG)
+    vset(v("rm8", 0, None, 8), -BIG)
+    vset(v("k8"), 8192.0)
     b = nb()
     mm(ps(0, 256, k=b), o128, v("W3"))
-    act(v("cT"), ps(0, 256, k=b), scale=255.0)
-    ts(v("LL"), v("ln"), v("pc", 0, 1), A.add)
+    if HS:
+        ts(v("hi", 0, 256, p1=64), ps(0, 256, p1=64, k=b), 255.0, A.mult)
+        ts(v("hm", 0, 256, p1=32), v("hi", 0, 256, p1=32), 3840, A.bitwise_and)
+        ts(v("hm", 0, 256, p0=32, p1=64), v("hi", 0, 256, p0=32, p1=64), 255, A.bitwise_and)
+        tc(v("cB", p1=64), v("hm", 0, 256, p1=64))
+        vset(v("cB", p0=64), 255.0 * 2048)
+        vset(v("o32"), 1.0 / 32)
+    else:
+        act(v("cT"), ps(0, 256, k=b), scale=255.0)
     act(v("base", 0, 80, 5), v("lt"))
     vset(v("r5"), 1.0)
     vset(v("r5", 0, 80, 5), 0.0)
@@ -339,7 +371,8 @@ def rank_program(g, core, T, topo):
     act(v("tk"), v("tj"), F.Identity, 1.0, -2.0)
     ts(v("tbl", 0, 1), v("pc", 0, 1), 11.5, A.is_lt, 128.0, A.mult)
     ts(v("tbl", 0, 1), v("tbl", 0, 1), -64.0, A.add)
-    vset(v("tbl", 4096, 4112), 0.0)
+    vset(v("tbl", 4096, 4112), 64.0)
+    vset(v("P", 2 * PH, 2 * PH + 16), 0.0)
     for k in range(12):
         if k >= 10:
             load(v("tbl", 1 << k, 2 << k), v("tbl", 0, 1 << k), 1.5)
@@ -348,13 +381,13 @@ def rank_program(g, core, T, topo):
         for c in range(0, 1 << k, 512):
             n = min(1 << k, 512)
             times(v("tbl", (1 << k) + c, (1 << k) + c + n), v("tbl", c, c + n), v("tk", k, k + 1))
-    act(v("TR0"), v("one", 0, L), F.Identity, 0.0, v("pc", 1, 2))
+    act(v("TR0"), v("one", 0, L), F.Identity, -65536.0, v("pc", 1, 2))
     for t in range(RO - 2):
         load(v("TR%d" % (t + 1), SL, L), v("TR0", SL, L), 1.0)
         for d in range(N):
             load(slot(d, "wint", t), v("TR0", 0, CAP), 1.0)
     for c in range(0, H, 1024):
-        ts(v("tab", 2 * H + c, 2 * H + c + 1024), v("sn0", c, c + 1024), -1.0, A.mult, 255.0, A.add)
+        ts(v("tab", W + c, W + c + 1024), v("sn0", c, c + 1024), -1.0, A.mult, 255.0, A.add)
     again()
 
     ts(v("frc"), v("fr0", 0, 3 * L), -1.0, A.mult, 255.0, A.add)
@@ -368,20 +401,29 @@ def rank_program(g, core, T, topo):
 
     setup[0] = False
 
+    def group(out, lhsT, rhs, parts, by=0):
+        if not by:
+            return mms([x + (n == 0, False) for n, x in enumerate(parts)] + [(out, lhsT, rhs, False, True)])
+        mm(out, lhsT, rhs, True, False)
+        k = len(parts) % by
+        if k:
+            mms([x + (False, False) for x in parts[:k]])
+        for n in range(k, len(parts), by):
+            mms([x + (False, False) for x in parts[n:n + by]] +
+                [(out, v("I"), v("zero", 0, ncol(out)), False, True)] * (n + by == len(parts)))
+
     def tolist(name, a, n, step, out):
         b = nb()
-        mm(ps(0, 8 * n, k=b), v("I"), v("Mk", 0, 8 * n), True, False)
-        for c in range(8):
-            mm(ps(n * c, n * c + n, k=b), halves("C8", c), v(name, a, a + (n - 1) * step + 1, step), False, False)
-        mm(ps(0, 8 * n, k=b), v("I"), v("Mk", 0, 8 * n), False, True)
+        group(ps(0, 8 * n, k=b), v("I"), v("Mk", 0, 8 * n),
+              [(ps(n * c, n * c + n, k=b), halves("C8", c), v(name, a, a + (n - 1) * step + 1, step)) for c in range(8)])
         scan(out, v("rm8", 0, 8 * n), ps(0, 8 * n, k=b), A.min)
 
     def ends(name, h):
         return v(name, 8 * h + 7, 128, 16)
 
-    def sums(b, cols, name, c, w, alone=False):
-        for i in range(16):
-            mm(ps(*cols(i), k=b), v(name, c + i, c + 2048, 16), w, alone, alone)
+    def sums(b, cols, name, c, w, n=128):
+        return [(ps(*cols(i), p0=a, p1=a + n, k=b), v(name, c + 16 * a + i, c + 16 * (a + n), 16), w)
+                for a in range(0, 128, n) for i in range(16)]
 
     def targets():
         tolist("XT", 0, 16, 1, v("TS"))
@@ -393,62 +435,60 @@ def rank_program(g, core, T, topo):
         times(v("FT1"), v("FT0"), v("pc", 6, 7))
         for pair in range(4):
             b, p = nb(), 32 * pair
-            mm(ps(0, 256, k=b), v("I"), v("mkc"), True, False)
+            parts = []
             for odd in range(2):
                 for lc in range(2):
                     for blk in range(2):
                         c, o, e = lc * 128 + blk * 64, (odd * 2 + lc) * 64, p + 16 + 16 * odd
-                        mm(ps(o, o + 64, p0=64 * blk, p1=64 * blk + 64, k=b), v("FT%d" % odd, c, c + 64, p0=p, p1=e),
-                           v("FT0", c, c + 64, p0=p, p1=e), False, False)
-            mm(ps(0, 256, k=b), v("I"), v("mkc"), False, True)
-            scan(halves("SCW", pair, 256), v("rm64"), ps(0, 256, k=b), A.min)
+                        parts.append((ps(o, o + 64, p0=64 * blk, p1=64 * blk + 64, k=b), v("FT%d" % odd, c, c + 64, p0=p, p1=e),
+                                      v("FT0", c, c + 64, p0=p, p1=e)))
+            mms([x + (True, True) for x in parts])
+            scan(halves("SCW", pair, 256), v("mkc"), ps(0, 256, k=b), A.add)
+        ts(v("zn"), v("SCW", 63, 1024, 64), -(1 << 20) - 15.0 * 4096, A.add, v("pc", 7, 8), A.min)
         for h in range(2):
-            tt(halves("XZ", h, 8), v("SCW", 63 + 64 * h, 1024, 128), halves("XT", h, 8), A.max)
+            tt(halves("XZ", h, 8), v("zn", h, 16, 2), halves("XT", h, 8), A.max)
         tolist("XZ", 0, 16, 1, v("ZS"))
         for h in range(2):
             ts(halves("WL", h, 8), ends("ZS", h), shift, A.add)
 
     for t in range(RO):
         last = t == RO - 1
-        Lt, Ln = "L%d" % t if t else "fm0", "L%d" % (t + 1)
+        Lt, Ln = "L%d" % t, "L%d" % (t + 1)
         main[0] = True
+        early = (7, -(-me * CAP // 32)) if t and EARLY else ()
+        for q in early:
+            b, p = nb(), 32 * (q % 4)
+            mm(ps(0, 128, p0=p, p1=p + 32, k=b), halves(Lt, q, 32), v("nI"))
+            move(v("mE", q // 4 * 128, q // 4 * 128 + 128, p0=p, p1=p + 32), ps(0, 128, p0=p, p1=p + 32, k=b), 255.0)
         b = nb()
+        lanesums(b, lambda blk: halves(Lt, blk, 64))
+        tt(v("au", p1=64), ps(0, 128, p1=64, k=b), v("cA", p1=64), A.add)
+        ts(v("am", p1=64), v("au", p1=64), 4095, A.bitwise_and)
+        tt(v("up", p1=64), v("am", 0, 64, p1=64), v("am", 64, 128, p1=64), A.mult)
         for h in range(2):
-            mm(ps(h, 32, 2, k=b), halves(Lt, h), v("Wt" if t else "Wp"))
-        if t:
-            tt(v("au"), ps(0, 32, k=b), v("cT", 0, 256, 8), A.add)
-        else:
-            tc(v("au"), ps(0, 32, k=b))
-        ts(v("am"), v("au"), 4095, A.bitwise_and)
-        tt(v("up"), v("am", 0, 16), v("am", 16, 32), A.mult)
-        ts(v("av", 16, 32), v("au", 0, 16), 2047, A.bitwise_and)
-        ts(v("av", 0, 16), v("up"), 5, A.arith_shift_right, 2047, A.bitwise_and)
-        rows = 16 if last else 24
-        if not last:
-            ts(v("av", 32, 48), v("up"), 16, A.arith_shift_right, 1, A.bitwise_and)
-        tc(v("XV", 0, 2 * rows), v("av", 0, 2 * rows))
-        for h in range(2):
-            move(mp(h), halves(Lt, h), *((255.0, -1.0) if t else ()))
             b = nb()
-            mm(ps(0, 128, k=b), mp(h), v("I"))
-            move(halves("mT", h), ps(0, 128, k=b))
+            mm(ps(0, 128, k=b), halves(Lt, h), v("nI"))
+            move(halves("mT", h), ps(0, 128, k=b), 255.0)
             b = nb()
-            mm(ps(0, 128, p1=rows, k=b), v("XV", h, 2 * rows, 2), v("Ih"))
-            tc(v("XA", 128 * h, 128 * h + 128, p1=rows), ps(0, 128, p1=rows, k=b))
-            xa = v("XA", 128 * h, 128 * h + 128, p1=16)
-            b, b2 = nb(), nb()
-            mm(ps(0, 128, k=b), v("EC", p1=16), xa)
-            move(halves("cq", h), ps(0, 128, k=b), 128.5 + 1.0 / 4096, 1.0 / 2048)
-            mm(ps(0, 128, k=b2), v("EC", p1=16), xa, True, False)
-            mm(ps(0, 128, k=b2), v("hI"), halves("cq", h), False, True)
-            ts(halves("CL", h), ps(0, 128, k=b2), 129.0 * 2048, A.add)
+            mms([(ps(64 * blk, 64 * blk + 64, k=b), v("EX", 128 * (2 * h + blk), 128 * (2 * h + blk + 1), p1=64), v("up", p1=64),
+                  True, True) for blk in range(2)])
+            tc(halves("ci", h), ps(0, 128, k=b))
+            ts(halves("cj", h), halves("ci", h), 5, A.arith_shift_right, 2047, A.bitwise_and)
+            tc(halves("CL", h), halves("cj", h))
+            ts(halves("cf", h), halves("CL", h), 0.0, A.add)
+            move(mp(h), halves(Lt, h), 255.0, -1.0)
         for h in range(2):
             for q in range(4 * h, 4 * h + 4):
                 a = q % 4
                 x, e, off = halves("X", q, 512), halves("E", q, 512), halves("CL", q, 32)
-                gather(GB[q], x, LM, off)
-                mt = v("mT", h * 128, h * 128 + 128, p0=32 * a, p1=32 * a + 32)
+                mt = v("mE" if q in early else "mT", h * 128, h * 128 + 128, p0=32 * a, p1=32 * a + 32)
                 b = nb()
+                if EB[q] == "A":
+                    mm(ps(0, 512, k=b), mt, v("Rep", p0=32 * a, p1=32 * a + 32))
+                    move(halves("MR", q, 512), ps(0, 512, k=b), q=GB[q])
+                    gatherop(e, LM, off, halves("MR", q, 512), A.is_gt)
+                    continue
+                gather(GB[q], x, LM, off)
                 if EB[q] == "V":
                     mm(ps(0, 512, k=b), mt, v("Rep", p0=32 * a, p1=32 * a + 32))
                     tt(e, x, ps(0, 512, k=b), A.is_gt)
@@ -457,10 +497,9 @@ def rank_program(g, core, T, topo):
                     mm(ps(0, 512, k=b), v("nI"), x, False, True)
                     act(e, ps(0, 512, k=b), F.Relu, 0.0, -1.0)
             b = nb()
-            mm(ps(0, 272, k=b), v("I"), v("K17"), True, False)
-            mm(ps(0, 272, k=b), v("XA", 128 * h, 128 * h + 128, p1=16), v("ER", p1=16), False, False)
-            sums(b, lambda i: (16 - i, 272, 17), "E", 2048 * h, v("NP"))
-            mm(ps(0, 272, k=b), halves("cq", h), v("JN"), False, True)
+            group(ps(0, 272, k=b), halves("cf", h), v("JR"),
+                  [(ps(0, 272, 17, k=b), v("I"), v("K17"))] + sums(b, lambda i: (16 - i, 272, 17), "E", 2048 * h, v("NP"), BY[0][h]),
+                  16 * (BY[0][h] < 128))
             move(halves("SD", h, 136), ps(136, 272, k=b))
             scan(halves("GV", h, 136), ps(0, 136, k=b), halves("SD", h, 136), A.max, A.min)
             tolist("GV", 136 * h + 16, 8, 17, halves("GS", h, 64))
@@ -474,17 +513,18 @@ def rank_program(g, core, T, topo):
             move(halves("qT", h), ps(0, 128, k=b))
         main[0] = False
         gv = v("GV", 16, 272, 17)
-        ts(v("hb"), gv, 0.0, A.is_ge, BIG / 2, A.mult)
-        ts(v("g2"), gv, v("pc", 3, 4), A.add)
-        tt(v("cap"), v("hb"), v("g2"), A.add)
+        ts(v("hb"), gv, 0.0, A.is_ge, BIG, A.mult)
+        tt(v("zm"), v("hb"), gv, A.add)
+        ts(v("cap"), v("zm"), v("pc", 3, 4), A.add, 131072.0, A.min)
+        if not last:
+            ts(v("capT"), v("zm"), 2048.0, A.min)
         if last:
-            tt(v("zm"), v("hb"), gv, A.add)
             ts(v("XT"), v("zm"), 2048.0, A.add, v("pc", 5, 6), A.min)
             targets()
             lowest(0.0)
             for blk in range(3, -1, -1):
-                c = PH * (blk // 2) + 2048 + 64 * (blk % 2)
-                scatter(v("tab", 3 * H, 3 * H + W + L), halves("WL", blk, 4), v("P", c, c + 64))
+                c = PH * (blk // 2) + 64 * (blk % 2)
+                scatter(v("LO"), halves("WL", blk, 4), v("P", c, c + 64))
         main[0] = True
         for h in range(2):
             for q in range(4 * h, 4 * h + 4):
@@ -496,19 +536,27 @@ def rank_program(g, core, T, topo):
                 mm(ps(0, 512, k=b), v("qT", h * 128, h * 128 + 128, p0=32 * a, p1=32 * a + 32), v("Rep", p0=32 * a, p1=32 * a + 32), False, True)
                 relu(p, ps(0, 512, k=b), 255.0, ED[q])
             b = nb()
-            sums(b, lambda i: (i, 256, 16), "P", PH * h, v("Wt"), True)
-            tt(halves("hi", h, 256), ps(0, 256, k=b), v("cT"), A.add)
-            ts(halves("hm", h, 256), halves("hi", h, 256), 4095, A.bitwise_and)
-            tt(halves("hp", h), halves("hm", 2 * h), halves("hm", 2 * h + 1), A.mult)
+            if HS:
+                group(ps(0, 256, k=b), v("o32"), v("cB"), sums(b, lambda i: (i, 256, 16), "P", PH * h + 128, v("Wt"), BY[1][h]),
+                      16 * (BY[1][h] < 128))
+                move(halves("hQ", h, 256), ps(0, 256, k=b), -2047.5, q=HS)
+                u = ps(0, 128, k=nb())
+                tt(halves("hV", h), ps(128, 256, k=b), halves("hQ", 2 * h + 1), A.subtract)
+                tt(u, ps(0, 128, k=b), halves("hQ", 2 * h), A.subtract)
+                tt(halves("hp", h), u, halves("hV", h), A.mult)
+            else:
+                parts = sums(b, lambda i: (i, 256, 16), "P", PH * h + 128, v("Wt"), BY[1][h])
+                for n in range(0, len(parts), 16):
+                    mms([x + (True, True) for x in parts[n:n + 16]])
+                tt(halves("hi", h, 256), ps(0, 256, k=b), v("cT"), A.add)
+                ts(halves("hm", h, 256), halves("hi", h, 256), 4095, A.bitwise_and)
+                u = halves("hm", 2 * h)
+                tt(halves("hp", h), u, halves("hm", 2 * h + 1), A.mult)
             ts(halves("hq", h), halves("hp", h), 5, A.arith_shift_right, 2047, A.bitwise_and)
-            tt(halves("lo", h), halves("hq", h), halves("hm", 2 * h), A.add)
+            tt(halves("lo", h), u, halves("hq", h), A.add)
             b = nb()
             mm(ps(0, 128, k=b), halves("lo", h), v("If"))
             tc(halves("HL", h), ps(0, 128, k=b))
-            b = nb()
-            mm(ps(0, 128, k=b), v("If"), v("KC"), True, False)
-            mm(ps(0, 128, k=b), v("If"), halves("lo", h), False, True)
-            move(halves("kf", h), ps(0, 128, k=b))
         for h in range(2):
             for q in range(4 * h, 4 * h + 4):
                 ne, p, sx = halves("NE", q, 512), prod(q), halves("SX", q, 512)
@@ -521,13 +569,11 @@ def rank_program(g, core, T, topo):
                     mm(ps(0, 512, k=b), v("I"), sx, False, True)
                     act(ne, ps(0, 512, k=b), F.Abs)
             b = nb()
-            mm(ps(0, 128, k=b), v("If"), v("ZC"), True, False)
-            sums(b, lambda i: (i, 128, 16), "NE", 2048 * h, v("PB8"))
-            mm(ps(0, 128, k=b), v("I"), v("zero"), False, True)
-            tt(halves("k2", h), ps(0, 128, k=b), halves("kf", h), A.min)
-            scan(halves("SC2", h), v("rm16"), halves("k2", h), A.min)
-        tt(v("key"), v("SC2", 15, 256, 16), v("cap"), A.min)
-        ts(v("dd"), v("key"), (1 << 24) + 3, A.bitwise_and)
+            group(ps(0, 128, k=b), v("I"), v("k8"), sums(b, lambda i: (i, 128, 16), "NE", 2048 * h, v("PB8"), BY[2][h]),
+                  16 * (BY[2][h] < 128))
+            scan(back(halves("SC2", h)), back(ps(0, 128, k=b)), back(halves("lo", h)), A.add)
+        tt(v("key"), v("SC2", 0, 256, 16), v("cap"), A.min)
+        ts(v("dd"), v("key"), (1 << 24) + (1 << 17) + 3, A.bitwise_and)
         for d in range(N):
             ts(v("OH", 1 + d, 80, 5), v("dd"), float(d), A.is_equal)
         b = nb()
@@ -539,16 +585,14 @@ def rank_program(g, core, T, topo):
         for h in range(2):
             tc(halves("SLL", h, 8), ends("SS", h))
         ts(v("fp"), v("key"), 13, A.arith_shift_right)
-        ts(v("XC"), v("fp"), -1.0, A.mult)
+        ts(v("XC"), v("fp"), v("pc", 2, 3), A.add)
         tolist("XC", 0, 16, 1, v("CS"))
         for h in range(2):
-            ts(halves("CHL", h, 8), ends("CS", h), 2047.0, A.add)
-            gather("X", halves("CH", h), halves("P", h, PH), halves("CHL", h, 8), last and (255.0, -1.0))
+            ts(halves("CHL", h, 8), ends("CS", h), 2048.0, A.add)
+            gather("X", halves("CH", h), v("P", PH * h, PH * h + PH + 16), halves("CHL", h, 8), last and (255.0, -1.0))
         if not last:
-            ts(v("t1"), v("key"), 2047, A.bitwise_and)
-            ts(v("t2"), v("key"), (1 << 24) + 6144, A.bitwise_and)
-            ts(v("t3"), v("t2"), -2048.0 - (1 << 24), A.add, -2048.0, A.max)
-            tt(v("XT"), v("t1"), v("t3"), A.add)
+            ts(v("t1"), v("key"), (1 << 17) + 2047, A.bitwise_and)
+            tt(v("XT"), v("t1"), v("capT"), A.min)
             targets()
         scatter(v("win%d" % t), v("SLL"), v("CH"))
         mine = (me * CAP, me * CAP + CAP)
@@ -559,7 +603,7 @@ def rank_program(g, core, T, topo):
         def tails():
             if t < RO - 2:
                 TR = "TR%d" % (t + 1)
-                gather("S", v("TGp"), TL, v("GL"), (8192.0, 1.0))
+                gather("X", v("TGp"), TL, v("GL"), (-8192.0, 1.0))
                 ts(v("kj"), v("key"), 13, A.arith_shift_right, 15, A.bitwise_and)
                 tc(v("IV"), v("kj"))
                 b = nb()
@@ -568,28 +612,33 @@ def rank_program(g, core, T, topo):
                 move(v("XI", p1=8), ps(0, 256, p1=8, k=b))
                 b = nb()
                 mm(ps(0, 256, k=b), v("R8", p1=8), v("XI", p1=8))
-                ts(v("mk"), ps(0, 256, k=b), v("pc", 2, 3), A.not_equal)
+                ts(v("mk"), ps(0, 256, k=b), v("pc", 0, 1), A.is_equal, -65536.0, A.mult)
                 scatter(v("wint%d" % t), v("SLL"), v("TGp"), v("mk"))
                 snd = fused(lambda d, t=t: slot(d, "wint", t), lambda d, TR=TR: v(TR, mine[0], mine[1]), "tarr%d" % t, "tloc%d" % t)
                 act(v(TR, mine[0], mine[1]), slot(me, "wint", t))
                 got("tarr%d" % t, [v(TR, s * CAP, s * CAP + CAP) for s in others], snd, XLAG + 1.0)
             b, b2 = nb(), nb()
-            mm(ps(0, 256, k=b), v("EA", p1=24), v("XA", p1=24))
-            gather("S", v("T2"), TL, v("LL"), (32768.0, 1.0))
+            tc(v("ui", p1=32), v("up", p1=32))
+            ts(v("uj", p1=32), v("ui", p1=32), 5, A.arith_shift_right, 4095, A.bitwise_and)
+            ts(v("a12", p1=32), v("uj", p1=32), -16384.0, A.add)
+            for blk in range(4):
+                mm(ps(64 * blk, 64 * blk + 64, k=b), v("EX", 128 * blk, 128 * blk + 128, p1=32), v("a12", p1=32))
             tt(ps(0, 256, k=b2), v("TR%d" % t), ps(0, 256, k=b), A.max)
-            tt(v("CT"), v("T2"), ps(0, 256, k=b2), A.min)
+            tt(v("CT"), v("xtl", 0, L), ps(0, 256, k=b2), A.min)
             ts(v("CTm"), v("CT"), 4095, A.bitwise_and)
         if not last:
             lowest(2048.0)
             for blk in range(3, -1, -1):
-                scatter(v("tab", 2 * H, 3 * H + W + L), halves("WL", blk, 4), halves("CH", blk, 64))
+                scatter(v("tab", 0, W + H + L), halves("WL", blk, 4), halves("CH", blk, 64))
             main[0] = False
             tails()
             again()
+            if t == RO - 2:
+                load(v("LO", 0, W), LM, 3.0)
             for blk in range(3, -1, -1):
                 scatter(v("xtl"), halves("WL", blk, 4), halves("CTm", blk, 64))
     op("D", lambda: g.sync.dma_start(T.yf[:], ap(v("L4"))), [v("L4")], [], 0.08, sem="st0", val=16, lag=2.0)
-    out = op("D", lambda: g.sync.dma_start(T.yl[:], ap(LM)), [LM], [], 0.08, sem="st1", val=16, lag=2.0)
+    out = op("D", lambda: g.sync.dma_start(T.yl[:], ap(v("LO", 0, W))), [v("LO", 0, W)], [], 0.08, sem="st1", val=16, lag=2.0)
     op("R", None, [], [], 0.0, sem="st1", val=16, lag=4.5, after=out)
     _emit(g, T, ops, bank)
 
@@ -599,7 +648,7 @@ def _plan(ops, deps, bank):
     post = [[] for _ in ops]
     for j in range(nop):
         for i, kind in deps[j].items():
-            post[i].append((j, ops[j]["lag"] if ops[j]["q"] == "R" else ops[i]["lag"] if kind == 2 and ops[i]["q"] != "R" else 0.0))
+            post[i].append((j, ops[j]["lag"] if ops[j]["q"] == "R" else ops[i]["lag"] if kind > 1 and ops[i]["q"] != "R" else 0.0))
     key = [0.0] * nop
     for i in range(nop - 1, -1, -1):
         key[i] = min([key[j] - 1e-4 for j, _ in post[i]] + [ops[i]["main"] or nop + i])
@@ -617,10 +666,13 @@ def _plan(ops, deps, bank):
             if j != lst[0] and j not in deps[lst[0]]:
                 gate[j].append(lst[0])
                 need[lst[0]] += 1
-    costs = [[o["cost"][0] + o["cost"][1] * z[o["cost"][2]] for o in ops] for z in SETS]
+    costs = [[o["cost"][0] + o["cost"][1] * z[o["cost"][2]] for o in ops] +
+             [o["costs"][0] + o["costs"][1] * z[o["costs"][2]] for o in ops] for z in SETS]
 
-    def forward(key, cost, LOOK):
-        left, est, end, on, banks, after = list(need), [0.0] * nop, [0.0] * nop, [o["q"] for o in ops], {}, {}
+    free_q = [o["q"] for o in ops]
+
+    def forward(key, cost, LOOK, pins=free_q):
+        left, est, end, on, banks, after = list(need), [0.0] * nop, [0.0] * nop, list(pins), {}, {}
         ready = {q: [] for q in "VSTGDRX"}
         for i in range(nop):
             if not left[i]:
@@ -649,7 +701,7 @@ def _plan(ops, deps, bank):
                 f = min(free)
                 free.remove(f)
                 banks[opens[i]], after[i] = f[1], f[2]
-            end[i] = s + cost[i]
+            end[i] = s + cost[i + nop * (q == "S")]
             for u in closes.get(i, ()):
                 free.append((end[i] + LAG, banks[u], i))
             if q != "R":
@@ -685,7 +737,7 @@ def _plan(ops, deps, bank):
             s = max(est[i], clock.get(plan[2][i], 0.0) if plan[2][i] != "R" else 0.0)
             if plan[4].get(i) is not None:
                 s = max(s, end[plan[4][i]] + LAG)
-            end[i] = clock[plan[2][i]] = s + cost[i]
+            end[i] = clock[plan[2][i]] = s + cost[i + nop * (plan[2][i] == "S")]
             for j, lag in post[i]:
                 est[j] = max(est[j], end[i] + lag)
         return max(end)
@@ -698,9 +750,42 @@ def _plan(ops, deps, bank):
                 plan = forward(key, cost, look)
                 mark = replay(plan, costs[0]) * 1.5 + replay(plan, costs[1])
                 if best is None or mark < best[0]:
-                    best = (mark,) + plan[1:]
+                    best = (mark,) + plan[1:] + (key, look, free_q)
                 key = backward(plan[1], plan[2], plan[5], cost)
-    _, order, on, banks, after, _ = best
+    z = SEED
+    cost = [a + MIX[0] * (b - a) for a, b in zip(*costs)]
+    shakes = SHAKES
+    site, alike = [], {}
+    for i, o in enumerate(ops):
+        site.append((o["q"],) + tuple((x[0].rstrip("0123456789"), x[1], x[3]) for x in o["wr"][:1] + o["rd"][:2]))
+        alike.setdefault(site[i], []).append(i)
+    if "key" in NOTE and SHARE:
+        key, look, pins = NOTE["key"]
+        plan = forward(key, cost, look, pins)
+        mark = replay(plan, costs[0]) * 1.5 + replay(plan, costs[1])
+        if mark < best[0]:
+            best, shakes = (mark,) + plan[1:] + (key, look, pins), SHAKES // 8
+    for n in range(shakes):
+        z = (z * 1103515245 + 12345) % 2147483648
+        lo, key, pins = z / 2147483648 * max(best[5]), list(best[6]), list(best[8])
+        seen = set()
+        for i in range(nop):
+            if lo <= best[5][i] < lo + SPAN[n % len(SPAN)] and site[i] not in seen:
+                seen.add(site[i])
+                z = (z * 1103515245 + 12345) % 2147483648
+                if z // 4096 % 4 < SKIP:
+                    continue
+                for j in (alike[site[i]] if n % 5 < TIE else [i]):
+                    key[j] += SHAKE[n % len(SHAKE)] * (z / 2147483648 - 0.5)
+                    if free_q[j] == "X" and z // 64 % 8 == 0:
+                        pins[j] = "VSX"[z // 512 % 3]
+        plan = forward(key, cost, best[7], pins)
+        mark = replay(plan, costs[0]) * 1.5 + replay(plan, costs[1])
+        if mark <= best[0]:
+            best = (mark,) + plan[1:] + (key, best[7], pins)
+    NOTE["key"] = best[6:9]
+    order, on, banks, after = best[1:5]
+    NOTE["mark"] = best[0]
     for i in range(nop):
         ops[i]["q"] = on[i]
     for i, j in after.items():
@@ -741,7 +826,10 @@ def _emit(g, T, ops, bank):
                     hit = hit or not same
                     need[j] = max(need.get(j, 0), 1)
                 if hit:
-                    need[j] = max(need.get(j, 0), 1 if same and (o["q"] == "T" or bf == "order") else 2)
+                    kind = 1 if same and (o["q"] == "T" or bf == "order") else 2
+                    if kind == 2 and wr and not wj and LOOSE and o["q"] in "VSX" and ops[j]["q"] in "VSX":
+                        kind = 1 if same else 1.5
+                    need[j] = max(need.get(j, 0), kind)
         for (bf, p0, p1, m, wr) in mine:
             old = acc.get(bf, [])
             if bf[:2] == "ps":
@@ -767,7 +855,7 @@ def _emit(g, T, ops, bank):
         k = know[q]
         want = {}
         for j, kind in deps[i].items():
-            if kind == 2:
+            if kind == 2 or kind == 1.5 and ops[j]["q"] != q:
                 s, val = tok[j]
                 if k.get(s, 0) < val and (s not in want or want[s][0] < val):
                     want[s] = (val, j)

@@ -6,32 +6,33 @@ DUMP = 256
 SW = DUMP + N * 256
 PH = 2176
 BIG = 67108864.0
+NONE = 127 << 17
 _B, _F, _H, _I, _U = "bfloat16", "float32", "float16", "int32", "uint16"
 _SB = {
-    "tab": (3 * H + W, _B), "xtl": (H + W + L, _I), "xmo": (4096, _B), "sn0": (H, _B), "fm0": (L, _B),
+    "tab": (3 * H + W, _B), "xtl": (W + H + L, _I), "xmo": (4096, _B), "sn0": (H, _B), "fm0": (L, _B),
     "fr0": (RO * L, _B), "wk0": (3, _I), "wkf": (3, _F), "frc": (3 * L, _B),
     "win0": (SW, _B), "win1": (SW, _B), "win2": (SW, _B), "win3": (SW, _B), "wint0": (SW, _F), "wint1": (SW, _F),
     "L1": (L, _B), "L2": (L, _B), "L3": (L, _B), "L4": (L, _B), "TR0": (L, _F), "TR1": (L, _F), "TR2": (L, _F),
-    "L0": (L, _B), "mT": (L, _B), "mE": (L, _B), "qT": (L, _B), "au": (128, _I), "am": (128, _I), "up": (64, _F), "ui": (64, _I), "uj": (64, _I),
+    "L0": (L, _B), "mT": (384, _B), "qT": (L, _B), "au": (128, _I), "am": (128, _I), "up": (64, _F), "ui": (64, _I), "uj": (64, _I),
+    "hb": (16, _F), "zm": (16, _F), "capT": (16, _F), "capU": (16, _F), "LO": (W + L, _B), "cT": (256, _F),
     "a12": (64, _F), "ci": (L, _I), "cj": (L, _I), "cf": (L, _H), "MR": (4096, _B), "CL": (L, _U), "X": (4096, _B), "E": (4096, _B), "Y": (4096, _B), "P": (2 * PH + 16, _B),
     "NE": (4096, _B), "SX": (4096, _B), "SD": (272, _F), "GV": (272, _H), "GS": (128, _F), "GL": (16, _U), "TG": (L, _U), "xg": (L, _B),
-    "hi": (512, _I), "hm": (512, _I), "hp": (256, _I), "hq": (256, _I), "lo": (256, _F), "hQ": (512, _B), "hV": (256, _F),
-    "HL": (256, _U), "LO": (W + L, _B), "SC2": (256, _F), "key": (16, _I), "hb": (16, _F), "g2": (16, _F),
-    "cap": (16, _F), "kj": (16, _I), "IV": (16, _H), "XI": (256, _B), "fp": (16, _I), "XC": (16, _H), "CS": (128, _F), "CHL": (16, _U),
+    "hi": (512, _I), "hm": (512, _I), "hV": (256, _F), "hp": (256, _I), "hq": (256, _I), "lo": (256, _F),
+    "HL": (256, _U), "SC2": (256, _F), "key": (16, _I),
+    "IV": (16, _H), "XI": (256, _B), "fp": (16, _I), "XC": (32, _H), "CS": (256, _F), "CHL": (16, _U),
     "CH": (L, _B), "dd": (16, _I), "OH": (80, _B), "S5": (80, _H), "SS": (128, _F), "SLL": (16, _U),
-    "TGp": (L, _F), "mk": (L, _F), "T2": (L, _F), "CT": (L, _I), "CTm": (L, _I),
-    "t1": (16, _I), "t2": (16, _I), "t3": (16, _F), "XT": (16, _H), "TS": (128, _F), "WA": (16, _U), "FT0": (L, _B), "FT1": (L, _B),
-    "SCW": (1024, _F), "zn": (16, _F), "capT": (16, _F), "XZ": (16, _H), "ZS": (128, _F), "zm": (16, _F), "WL": (16, _U),
+    "TGp": (L, _F), "mk": (L, _F), "CT": (L, _I), "CTm": (L, _I), "t1": (16, _I), "TS": (128, _F),
 }
+_SB.update({"WA": (16, _U), "FT0": (L, _B), "FT1": (L, _B), "SCW": (1024, _F), "zn": (16, _F), "XZ": (16, _H), "ZS": (128, _F),
+            "WL": (16, _U), "kj": (16, _I)})
 _CO = {
     "one": (512, _B), "zero": (272, _B), "I": (128, _B), "nI": (128, _B), "Ih": (128, _H), "If": (128, _F),
     "bo": (128, _B), "b8": (8, _B), "tmp": (128, _B), "Rep": (512, _B), "R32": (512, _B), "C8": (1024, _B), "i4": (128, _B),
     "R8": (128, _B), "TR": (128, _B), "TRB": (128, _B), "JR": (272, _B), "K17": (16, _B), "Et": (96, _B), "ZU": (96, _B), "ZV": (96, _B),
-    "cA": (128, _F), "EX": (512, _F), "cB": (256, _B), "o32": (128, _B),
-    "base": (80, _B), "r5": (80, _B), "rm8": (128, _B), "k8": (128, _B), "Mk": (128, _B),
-    "mkc": (256, _B), "pc": (12, _F), "pi": (4, _I), "W3": (256, _B), "Wt": (16, _B), "NP": (16, _B), "PB8": (8, _B), "cT": (256, _F),
-    "c32": (32, _F), "ln": (16, _F), "lt": (16, _F), "LL": (16, _U),
-    "ti": (12, _F), "tj": (12, _F), "tk": (12, _F), "tbl": (4096 + 16, _B),
+    "cA": (128, _F), "EX": (512, _F),
+    "base": (80, _B), "r5": (80, _B), "rm8": (256, _B), "k8": (128, _B), "Mk": (256, _B),
+    "mkc": (256, _B), "pc": (12, _F), "pi": (4, _I), "W3": (256, _B), "Wt": (16, _B), "NP": (16, _B), "PB8": (8, _B), "Wp": (16, _B),
+    "lt": (16, _F), "ti": (12, _F), "tj": (12, _F), "tk": (12, _F), "tbl": (4096 + 16, _B),
 }
 _PACK, _POS = {}, {}
 for _k in list(_SB) + list(_CO):
@@ -52,10 +53,12 @@ for _t, _n in _PACK.items():
     SCRATCH["pk_" + _t] = ("sbuf", [128, _n], _t)
 for _k in range(8):
     SCRATCH["ps%d" % _k] = ("psum", [128, 512], "float32")
-SEMAPHORES = ["q" + e for e in "VSTG"] + ["ld%d" % i for i in range(40)] + ["st0", "st1"] + \
+SEMAPHORES = ["q" + e for e in "VSTG"] + ["ld%d" % i for i in range(42)] + ["st0", "st1"] + \
     ["%s%d" % (p, t) for p in ("arr", "tarr", "rarr", "loc", "tloc", "rloc") for t in range(RO)]
 
-EB = "AAASAASS"
+EB, LITE = "AAASSASA", 1
+FIRST, YQ, MOD0 = True, "YYQQYQQQ", True
+PAR = True
 SE = "SSSVSVVV"
 GB = "SSSSSSSS"
 GD = "XXXXXXXX"
@@ -65,14 +68,15 @@ LOOSE = True
 SHUT, SHUT2 = False, True
 HS = ""
 SLOW = 1.2
-EARLY = False
+EARLY, TWO, JOIN, MRQ = False, True, True, "X"
 BY = ((128, 128), (128, 128), (128, 128))
 LAG = 0.18
 XLAG = 3.5
 LOOKS = ((0.2, 2.0, 0.0), (0.2, 2.0, 2.0), (0.25, 1.0, 1.0))
 MIX = (0.25,)
-SHAKES, SHAKE, SPAN, SEED, SHARE = 2400, (0.3, 0.6, 1.2), (2.0, 4.0, 3.0, 7.0), 12345, True
+SHAKES, SHAKE, SPAN, SEED, SHARE = 50, (0.3, 0.6, 1.2), (2.0, 4.0, 3.0, 7.0), 12345, True
 TIE, SKIP = 2, 1
+MENDS, HEAT, WIDE, FAR = 2500, (0.9, 0.8, 0.7, 0.6, 0.5, 0.4, 0.3, 0.2, 0.1), 200, (0, 0, 1, 2, 4)
 NOTE = {}
 PASSES = 6
 
@@ -85,6 +89,7 @@ def rank_program(g, core, T, topo):
     ops, bank = [], {}
     main = [False]
     setup = [True]
+    turn = [-9]
 
     def v(name, a=None, b=None, step=1, p0=0, p1=128):
         buf, o = _POS[name]
@@ -109,7 +114,7 @@ def rank_program(g, core, T, topo):
             n = ncol(rd[0])
             cost = vc(n, 0.5 if is2(rd[0]) and is2(wr[0]) else 1.0) + (0.13 if inps(rd[0]) else 0.05, n, "e")
         ops.append({"q": q, "fn": fn, "rd": rd, "wr": wr, "cost": cost[:3], "costs": cost[-3:],
-                    "sem": sem, "val": val, "lag": lag, "after": after, "main": main[0] and len(ops)})
+                    "sem": sem, "val": val, "lag": lag, "after": after, "main": main[0] and len(ops), "round": turn[0]})
         return len(ops) - 1
 
     def vc(n, f=1.0):
@@ -152,9 +157,9 @@ def rank_program(g, core, T, topo):
         fn = {"V": lambda: g.vector.tensor_copy(ap(out), ap(win).indirect(ap(off))),
               "S": lambda: g.scalar.activation(ap(out), ap(win).indirect(ap(off)), F.Copy)}
         if turn:
-            fn = {"V": lambda: g.vector.tensor_scalar(ap(out), ap(win).indirect(ap(off)), turn[1], turn[0], A.mult, A.add),
-                  "S": lambda: g.scalar.activation(ap(out), ap(win).indirect(ap(off)), F.Identity, bias=turn[0], scale=turn[1])}
-        return op(q, fn, [win, off], [out], (0.06, ncol(out), "g"))
+            fn = {"V": lambda: g.vector.tensor_scalar(ap(out), ap(win).indirect(ap(off)), arg(turn[1]), turn[0], A.mult, A.add),
+                  "S": lambda: g.scalar.activation(ap(out), ap(win).indirect(ap(off)), F.Identity, bias=turn[0], scale=arg(turn[1]))}
+        return op(q, fn, [win, off] + [x for x in turn or () if isinstance(x, tuple)], [out], (0.06, ncol(out), "g"))
 
     def relu(out, x, c, q):
         return op(q, {"V": lambda: g.vector.tensor_scalar(ap(out), ap(x), c, 0.0, A.add, A.max),
@@ -226,7 +231,7 @@ def rank_program(g, core, T, topo):
         for d in od:
             eng = [e for e in eng if e in topo.engines(T.cores[s], T.cores[d])]
         n = len(eng)
-        return dict(zip(od, [eng[:n // 2], eng[n // 2:], eng] if two else [eng[:n // 4], eng[n // 4:n // 2], eng[n // 2:]]))
+        return dict(zip(od, [eng[:n // 2], eng[n // 2:], eng] if two else [eng[:n // 2:2], eng[n // 2::2], eng[1::2]]))
 
     def fused(src, dst, sem, loc, two=False):
         parts = masks(me, two)
@@ -260,19 +265,20 @@ def rank_program(g, core, T, topo):
 
     def back(x):
         return x[:3] + (x[4] - 1, x[3] - 1, -1)
-    SN, LM, TL = v("tab", W, W + 3 * H), v("tab", 0, W), v("xtl", 0, W)
+    SN, LM, TL = v("tab", W), v("tab", 0, W), v("xtl", 0, W)
 
     def again():
         for c in range(1, 3):
             load(v("tab", W + c * H, W + c * H + H), v("tab", W, W + H), 3.0)
 
-    load(v("fm0"), T.fm[:], 0.5)
     load(v("wk0"), T.wk[:], 0.2)
+    load(v("fm0"), T.fm[:], 0.5)
     load(LM, T.lm[:], 2.5 * SLOW)
-    load(TL, T.tl[:], 5.0 * SLOW)
-    load(v("xmo"), T.mo[:], 8.0 * SLOW)
-    load(v("sn0"), T.sn[:], 9.5 * SLOW)
-    load(v("fr0"), T.fr[:], 10.5 * SLOW)
+    load(v("fr0", 0, L), T.fr[:, 0:L], 2.7 * SLOW)
+    load(TL, T.tl[:], 5.2 * SLOW)
+    load(v("xmo"), T.mo[:], 8.2 * SLOW)
+    load(v("sn0"), T.sn[:], 9.7 * SLOW)
+    load(v("fr0", L), T.fr[:, L:RO * L], 10.5 * SLOW)
     vset(v("one", 0, 128), 1.0)
     vset(v("one", 128, 512), 1.0)
     vset(v("zero"), 0.0)
@@ -286,8 +292,9 @@ def rank_program(g, core, T, topo):
     pick(v("JR"), v("one", 0, 272), [[0, 2], [-16, 8], [1, 17]], A.is_equal, 0.0, -16, 1)
     for a in range(2):
         pick(halves("C8", a, 512), v("one"), [[-16, 4], [0, 8], [-1, 16]], A.is_equal, 0.0, -64 * a, 1)
-    pick(v("Mk"), v("zero", 0, 128), [[0, 16], [-16, 8]], A.is_ge, -BIG / 2, 0, 1)
-    pick(v("Mk"), v("Mk"), [[0, 16], [16, 8]], A.is_ge, -BIG / 2, 15, -1)
+    pick(v("Mk", 0, 128), v("zero", 0, 128), [[0, 16], [-16, 8]], A.is_ge, -BIG / 2, 0, 1)
+    pick(v("Mk", 0, 128), v("Mk", 0, 128), [[0, 16], [16, 8]], A.is_ge, -BIG / 2, 15, -1)
+    act(v("Mk", 128, 256), v("Mk", 0, 128))
     iota(v("lt"), [[128, 2], [0, 8]], 0, 1)
     iota(v("base"), [[0, 16], [256, 5]], DUMP - 256 - 2048, 0)
     pick(v("TR"), o128, [[1, 128]], A.is_gt, 0.0, 0, -1)
@@ -326,39 +333,38 @@ def rank_program(g, core, T, topo):
         act(halves("W3", x), v("bo"), F.Identity, 0.0, w)
     for name in ("ZU", "ZV", "Et"):
         vset(v(name), 0.0)
-    act(v("ZU", 24, 32), v("Wt", 0, 8))
-    act(v("ZU", 56, 64), v("Wt", 0, 8), scale=-1.0)
-    act(v("ZV", 24, 32), v("Wt", 8, 16))
+    ts(v("ZU", 24, 32), v("b8"), v("wkf", 0, 1), A.mult, -1.0, A.mult)
+    act(v("ZU", 56, 64), v("b8"), F.Identity, 0.0, v("wkf", 0, 1))
+    ts(v("ZV", 24, 32), v("b8"), v("wkf", 1, 2), A.mult, -1.0, A.mult)
+    ts(v("pc", 4, 5), v("pi", 0, 1), 31.5, A.is_gt)
     act(v("Et", 24, 32), v("b8"))
     ts(v("Et", 56, 64), v("b8"), v("wkf", 2, 3), A.mult, -32.0, A.mult)
 
-    def lanesums(b, x):
-        mms([(ps(64 * n, 64 * n + 64, p1=64, k=b), v(name, 24 - 8 * blk, 88 - 8 * blk), x(blk), blk == 0, blk == 3)
-             for n, name in enumerate(("ZU", "ZV")) for blk in range(4)])
+    def lanesums(b, xs):
+        w = ncol(xs[0])
+        mms([(ps(w * n, w * n + ncol(x), p1=64, k=b), v(name, 24 - 8 * blk, 88 - 8 * blk), x, blk == len(xs) - 1, blk == 0)
+             for n, name in enumerate(("ZU", "ZV")) for blk, x in list(enumerate(xs))[::-1]])
     b = nb()
-    lanesums(b, lambda blk: v("one", 0, 64))
+    lanesums(b, [v("one", 0, 64)] * 4)
     act(v("cA", p1=64), ps(0, 128, p1=64, k=b), scale=-255.0)
     vset(v("cA", 64, 128, p0=32, p1=64), 1.0)
     b = nb()
     for blk in range(4):
         mm(ps(128 * blk, 128 * blk + 128, p1=64, k=b), v("Et", 24 - 8 * blk, 88 - 8 * blk), v("I"))
-    act(v("EX", p1=64), ps(0, 512, p1=64, k=b))
+    for x in range(2):
+        act(v("EX", 256 * x, 256 * x + 256, p1=64), ps(256 * x, 256 * x + 256, p1=64, k=b))
     for x in range(2):
         act(v("JR", 136 * x, 136 * x + 136, 17), v("I", 0, 128, 16))
     vset(v("K17"), -2048.0)
-    ts(v("L0"), v("fm0"), -1.0, A.mult, 255.0, A.add)
     vset(v("rm8"), BIG)
     vset(v("rm8", 0, None, 8), -BIG)
     vset(v("k8"), 8192.0)
     b = nb()
     mm(ps(0, 256, k=b), o128, v("W3"))
-    if HS:
-        ts(v("hi", 0, 256, p1=64), ps(0, 256, p1=64, k=b), 255.0, A.mult)
-        ts(v("hm", 0, 256, p1=32), v("hi", 0, 256, p1=32), 3840, A.bitwise_and)
-        ts(v("hm", 0, 256, p0=32, p1=64), v("hi", 0, 256, p0=32, p1=64), 255, A.bitwise_and)
-        tc(v("cB", p1=64), v("hm", 0, 256, p1=64))
-        vset(v("cB", p0=64), 255.0 * 2048)
-        vset(v("o32"), 1.0 / 32)
+    if TWO:
+        for x, y in enumerate((0, 2, 1, 3)):
+            act(halves("cT", x, 64), ps(64 * y, 64 * y + 64, k=b), scale=255.0)
+            act(halves("Wp", x, 4), halves("Wt", y, 4))
     else:
         act(v("cT"), ps(0, 256, k=b), scale=255.0)
     act(v("base", 0, 80, 5), v("lt"))
@@ -387,10 +393,14 @@ def rank_program(g, core, T, topo):
         for d in range(N):
             load(slot(d, "wint", t), v("TR0", 0, CAP), 1.0)
     for c in range(0, H, 1024):
-        ts(v("tab", W + c, W + c + 1024), v("sn0", c, c + 1024), -1.0, A.mult, 255.0, A.add)
-    again()
+        move(v("tab", W + c, W + c + 1024), v("sn0", c, c + 1024), 255.0, -1.0)
+    if MOD0:
+        vset(v("tab", W + H, W + H + L), 0.0)
+    else:
+        again()
 
-    ts(v("frc"), v("fr0", 0, 3 * L), -1.0, A.mult, 255.0, A.add)
+    move(v("frc", 0, L), v("fr0", 0, L), 255.0, -1.0)
+    move(v("frc", L), v("fr0", L, 3 * L), 255.0, -1.0)
     for t in range(RO):
         def fill(a, b, t=t):
             return v("frc" if t < RO - 1 else "fr0", t * L + a, t * L + b)
@@ -402,6 +412,12 @@ def rank_program(g, core, T, topo):
     setup[0] = False
 
     def group(out, lhsT, rhs, parts, by=0):
+        if FIRST:
+            mm(out, lhsT, rhs, True, False)
+            if by:
+                mms([x + (False, False) for x in parts[:1]])
+                parts = parts[1:]
+            return mms([x + (False, n == len(parts) - 1) for n, x in enumerate(parts)])
         if not by:
             return mms([x + (n == 0, False) for n, x in enumerate(parts)] + [(out, lhsT, rhs, False, True)])
         mm(out, lhsT, rhs, True, False)
@@ -425,14 +441,12 @@ def rank_program(g, core, T, topo):
         return [(ps(*cols(i), p0=a, p1=a + n, k=b), v(name, c + 16 * a + i, c + 16 * (a + n), 16), w)
                 for a in range(0, 128, n) for i in range(16)]
 
-    def targets():
-        tolist("XT", 0, 16, 1, v("TS"))
-        for h in range(2):
-            ts(halves("WA", h, 8), ends("TS", h), 2048.0, A.add, 4096.0, A.min)
-
-    def lowest(shift):
-        gather("X", v("FT0"), v("tbl"), v("WA"))
-        times(v("FT1"), v("FT0"), v("pc", 6, 7))
+    def lowest(shift, k=""):
+        gather("X", v("FT0" + k), v("tbl"), v("WA" + k))
+        if PAR:
+            gather("X", v("FT1" + k), v("tbl"), v("WA" + k), (0.0, v("pc", 6, 7)))
+        else:
+            times(v("FT1" + k), v("FT0" + k), v("pc", 6, 7))
         for pair in range(4):
             b, p = nb(), 32 * pair
             parts = []
@@ -440,66 +454,68 @@ def rank_program(g, core, T, topo):
                 for lc in range(2):
                     for blk in range(2):
                         c, o, e = lc * 128 + blk * 64, (odd * 2 + lc) * 64, p + 16 + 16 * odd
-                        parts.append((ps(o, o + 64, p0=64 * blk, p1=64 * blk + 64, k=b), v("FT%d" % odd, c, c + 64, p0=p, p1=e),
-                                      v("FT0", c, c + 64, p0=p, p1=e)))
+                        parts.append((ps(o, o + 64, p0=64 * blk, p1=64 * blk + 64, k=b), v("FT%d" % odd + k, c, c + 64, p0=p, p1=e),
+                                      v("FT0" + k, c, c + 64, p0=p, p1=e)))
             mms([x + (True, True) for x in parts])
-            scan(halves("SCW", pair, 256), v("mkc"), ps(0, 256, k=b), A.add)
-        ts(v("zn"), v("SCW", 63, 1024, 64), -(1 << 20) - 15.0 * 4096, A.add, v("pc", 7, 8), A.min)
+            scan(halves("SCW" + k, pair, 256), v("mkc"), ps(0, 256, k=b), A.add)
+        ts(v("zn" + k), v("SCW" + k, 63, 1024, 64), -(1 << 20) - 15.0 * 4096, A.add, v("pc", 7, 8), A.min)
         for h in range(2):
-            tt(halves("XZ", h, 8), v("zn", h, 16, 2), halves("XT", h, 8), A.max)
-        tolist("XZ", 0, 16, 1, v("ZS"))
+            tt(halves("XZ" + k, h, 8), v("zn" + k, h, 16, 2), halves("XC", 2 + h, 8), A.max)
+        tolist("XZ" + k, 0, 16, 1, v("ZS" + k))
         for h in range(2):
-            ts(halves("WL", h, 8), ends("ZS", h), shift, A.add)
+            ts(halves("WL" + k, h, 8), ends("ZS" + k, h), shift, A.add)
 
+    mine = (me * CAP, me * CAP + CAP)
+    order = (0, 1)
     for t in range(RO):
         last = t == RO - 1
-        Lt, Ln = "L%d" % t, "L%d" % (t + 1)
-        main[0] = True
-        early = (7, -(-me * CAP // 32)) if t and EARLY else ()
-        for q in early:
-            b, p = nb(), 32 * (q % 4)
-            mm(ps(0, 128, p0=p, p1=p + 32, k=b), halves(Lt, q, 32), v("nI"))
-            move(v("mE", q // 4 * 128, q // 4 * 128 + 128, p0=p, p1=p + 32), ps(0, 128, p0=p, p1=p + 32, k=b), 255.0)
+        Lt, Ln = "L%d" % t if t else "fm0", "L%d" % (t + 1)
+        main[0], turn[0] = True, t
+        soon = t and LITE
+        if soon:
+            b = nb()
+            mm(ps(0, 128, p1=32, k=b), halves(Lt, 7, 32), v("nI"))
+            move(v("mT", 256, 384, p1=32), ps(0, 128, p1=32, k=b), 255.0)
         b = nb()
-        lanesums(b, lambda blk: halves(Lt, blk, 64))
-        tt(v("au", p1=64), ps(0, 128, p1=64, k=b), v("cA", p1=64), A.add)
+        lanesums(b, [halves(Lt, blk, 64) for blk in range(4)])
+        if t:
+            tt(v("au", p1=64), ps(0, 128, p1=64, k=b), v("cA", p1=64), A.add)
+        else:
+            ts(v("au", 0, 64, p1=64), ps(0, 64, p1=64, k=b), -1.0, A.mult)
+            ts(v("au", 64, 128, p1=64), ps(64, 128, p1=64, k=b), -1.0, A.mult, v("pc", 4, 5, p1=64), A.add)
         ts(v("am", p1=64), v("au", p1=64), 4095, A.bitwise_and)
         tt(v("up", p1=64), v("am", 0, 64, p1=64), v("am", 64, 128, p1=64), A.mult)
-        for h in range(2):
+        for h in order:
             b = nb()
-            mm(ps(0, 128, k=b), halves(Lt, h), v("nI"))
-            move(halves("mT", h), ps(0, 128, k=b), 255.0)
+            mm(ps(0, 128, k=b), halves(Lt, h), v("nI" if t else "I"))
+            move(halves("mT", h), ps(0, 128, k=b), 255.0 if t else 0.0)
             b = nb()
-            mms([(ps(64 * blk, 64 * blk + 64, k=b), v("EX", 128 * (2 * h + blk), 128 * (2 * h + blk + 1), p1=64), v("up", p1=64),
+            mms([(ps(64 * blk, 64 * blk + 64, k=b), v("EX", 256 * h + 128 * blk, 256 * h + 128 * blk + 128, p1=64), v("up", p1=64),
                   True, True) for blk in range(2)])
             tc(halves("ci", h), ps(0, 128, k=b))
             ts(halves("cj", h), halves("ci", h), 5, A.arith_shift_right, 2047, A.bitwise_and)
             tc(halves("CL", h), halves("cj", h))
             ts(halves("cf", h), halves("CL", h), 0.0, A.add)
-            move(mp(h), halves(Lt, h), 255.0, -1.0)
-        for h in range(2):
+            move(mp(h), halves(Lt, h), *((255.0, -1.0) if t else ()))
+        for h in order:
             for q in range(4 * h, 4 * h + 4):
-                a = q % 4
-                x, e, off = halves("X", q, 512), halves("E", q, 512), halves("CL", q, 32)
-                mt = v("mE" if q in early else "mT", h * 128, h * 128 + 128, p0=32 * a, p1=32 * a + 32)
+                a, c = (0, 256) if soon and q == 7 else (q % 4, q // 4 * 128)
+                x, e, mr, off = halves("X", q, 512), halves("E", q, 512), halves("MR", q, 512), halves("CL", q, 32)
+                mt, rp = v("mT", c, c + 128, p0=32 * a, p1=32 * a + 32), v("Rep", p0=32 * a, p1=32 * a + 32)
                 b = nb()
                 if EB[q] == "A":
-                    mm(ps(0, 512, k=b), mt, v("Rep", p0=32 * a, p1=32 * a + 32))
-                    move(halves("MR", q, 512), ps(0, 512, k=b), q=GB[q])
-                    gatherop(e, LM, off, halves("MR", q, 512), A.is_gt)
-                    continue
-                gather(GB[q], x, LM, off)
-                if EB[q] == "V":
-                    mm(ps(0, 512, k=b), mt, v("Rep", p0=32 * a, p1=32 * a + 32))
-                    tt(e, x, ps(0, 512, k=b), A.is_gt)
+                    mm(ps(0, 512, k=b), mt, rp)
+                    move(mr, ps(0, 512, k=b), q=MRQ)
+                    gatherop(e, LM, off, mr, A.is_gt)
                 else:
-                    mm(ps(0, 512, k=b), mt, v("Rep", p0=32 * a, p1=32 * a + 32), True, False)
+                    gather("S", x, LM, off)
+                    mm(ps(0, 512, k=b), mt, rp, True, False)
                     mm(ps(0, 512, k=b), v("nI"), x, False, True)
                     act(e, ps(0, 512, k=b), F.Relu, 0.0, -1.0)
             b = nb()
             group(ps(0, 272, k=b), halves("cf", h), v("JR"),
                   [(ps(0, 272, 17, k=b), v("I"), v("K17"))] + sums(b, lambda i: (16 - i, 272, 17), "E", 2048 * h, v("NP"), BY[0][h]),
-                  16 * (BY[0][h] < 128))
+                  int(FIRST))
             move(halves("SD", h, 136), ps(136, 272, k=b))
             scan(halves("GV", h, 136), ps(0, 136, k=b), halves("SD", h, 136), A.max, A.min)
             tolist("GV", 136 * h + 16, 8, 17, halves("GS", h, 64))
@@ -515,52 +531,72 @@ def rank_program(g, core, T, topo):
         gv = v("GV", 16, 272, 17)
         ts(v("hb"), gv, 0.0, A.is_ge, BIG, A.mult)
         tt(v("zm"), v("hb"), gv, A.add)
-        ts(v("cap"), v("zm"), v("pc", 3, 4), A.add, 131072.0, A.min)
+        ts(v("capU"), v("zm"), v("pc", 3, 4), A.add, 131072.0, A.min)
         if not last:
             ts(v("capT"), v("zm"), 2048.0, A.min)
-        if last:
-            ts(v("XT"), v("zm"), 2048.0, A.add, v("pc", 5, 6), A.min)
-            targets()
+        else:
+            ts(v("XC", 16, 32), gv, 2048.0, A.add, 2048.0, A.min)
+            for h in order:
+                ts(halves("WA", h, 8), v("GS", 64 * h + 7, 64 * h + 64, 8), 2048.0, A.add, 2048.0, A.min)
             lowest(0.0)
             for blk in range(3, -1, -1):
                 c = PH * (blk // 2) + 64 * (blk % 2)
                 scatter(v("LO"), halves("WL", blk, 4), v("P", c, c + 64))
+        if t < RO - 2:
+            gather("X", v("TGp"), TL, v("GL"), (-8192.0, 1.0))
+        if not last:
+            b, b2 = nb(), nb()
+            tc(v("ui", p1=32), v("up", p1=32))
+            ts(v("uj", p1=32), v("ui", p1=32), 5, A.arith_shift_right, 4095, A.bitwise_and)
+            ts(v("a12", p1=32), v("uj", p1=32), -16384.0, A.add)
+            mms([(ps(64 * blk, 64 * blk + 64, k=b), v("EX", 128 * blk, 128 * blk + 128, p1=32), v("a12", p1=32), True, True)
+                 for blk in range(4)])
+            tt(ps(0, 256, k=b2), v("TR%d" % t), ps(0, 256, k=b), A.max)
+            tt(v("CT"), v("xtl", 0, L), ps(0, 256, k=b2), A.min)
+            ts(v("CTm"), v("CT"), 4095, A.bitwise_and)
         main[0] = True
-        for h in range(2):
+        for h in order:
             for q in range(4 * h, 4 * h + 4):
                 a = q % 4
                 y, p = halves("Y", q, 512), prod(q)
                 gather(GD[q], y, v("xmo"), halves("TG", q, 32))
                 b = nb()
-                mm(ps(0, 512, k=b), v("nI"), y, True, False)
-                mm(ps(0, 512, k=b), v("qT", h * 128, h * 128 + 128, p0=32 * a, p1=32 * a + 32), v("Rep", p0=32 * a, p1=32 * a + 32), False, True)
+                two = [(v("nI"), y), (v("qT", h * 128, h * 128 + 128, p0=32 * a, p1=32 * a + 32), v("Rep", p0=32 * a, p1=32 * a + 32))]
+                for n, x in enumerate(two if YQ[q] == "Y" else two[::-1]):
+                    mm(ps(0, 512, k=b), x[0], x[1], n == 0, n == 1)
                 relu(p, ps(0, 512, k=b), 255.0, ED[q])
             b = nb()
-            if HS:
-                group(ps(0, 256, k=b), v("o32"), v("cB"), sums(b, lambda i: (i, 256, 16), "P", PH * h + 128, v("Wt"), BY[1][h]),
-                      16 * (BY[1][h] < 128))
-                move(halves("hQ", h, 256), ps(0, 256, k=b), -2047.5, q=HS)
-                u = ps(0, 128, k=nb())
-                tt(halves("hV", h), ps(128, 256, k=b), halves("hQ", 2 * h + 1), A.subtract)
-                tt(u, ps(0, 128, k=b), halves("hQ", 2 * h), A.subtract)
-                tt(halves("hp", h), u, halves("hV", h), A.mult)
+            if TWO:
+                mms([x + (True, True) for x in sums(b, lambda i: (i, 256, 16), "P", PH * h + 128, v("Wp"))])
+                for z in range(2):
+                    c = 256 * h + 128 * z
+                    tt(v("hi", c, c + 128), ps(128 * z, 128 * z + 128, k=b), halves("cT", z), A.add)
+                    ts(v("hm", c, c + 128), v("hi", c, c + 128), 4095, A.bitwise_and)
+                    c, u = 2 * h + z, v("hm", c, c + 64)
+                    tt(halves("hp", c, 64), u, halves("hm", 2 * c + 1, 64), A.mult)
+                    ts(halves("hq", c, 64), halves("hp", c, 64), 5, A.arith_shift_right, 2047, A.bitwise_and)
+                    if t or not MOD0:
+                        tt(halves("lo", c, 64), u, halves("hq", c, 64), A.add)
+                    else:
+                        tt(halves("hp", c, 64), u, halves("hq", c, 64), A.add)
+                        ts(halves("hq", c, 64), halves("hp", c, 64), 2047, A.bitwise_and)
+                        tc(halves("lo", c, 64), halves("hq", c, 64))
             else:
-                parts = sums(b, lambda i: (i, 256, 16), "P", PH * h + 128, v("Wt"), BY[1][h])
-                for n in range(0, len(parts), 16):
-                    mms([x + (True, True) for x in parts[n:n + 16]])
+                mms([x + (True, True) for x in sums(b, lambda i: (i, 256, 16), "P", PH * h + 128, v("Wt"))])
                 tt(halves("hi", h, 256), ps(0, 256, k=b), v("cT"), A.add)
                 ts(halves("hm", h, 256), halves("hi", h, 256), 4095, A.bitwise_and)
                 u = halves("hm", 2 * h)
                 tt(halves("hp", h), u, halves("hm", 2 * h + 1), A.mult)
-            ts(halves("hq", h), halves("hp", h), 5, A.arith_shift_right, 2047, A.bitwise_and)
-            tt(halves("lo", h), u, halves("hq", h), A.add)
+                ts(halves("hq", h), halves("hp", h), 5, A.arith_shift_right, 2047, A.bitwise_and)
+                tt(halves("lo", h), u, halves("hq", h), A.add)
             b = nb()
             mm(ps(0, 128, k=b), halves("lo", h), v("If"))
             tc(halves("HL", h), ps(0, 128, k=b))
-        for h in range(2):
+        for h in order:
             for q in range(4 * h, 4 * h + 4):
                 ne, p, sx = halves("NE", q, 512), prod(q), halves("SX", q, 512)
-                if SE[q] == "V":
+                SN = v("tab", W) if t or not MOD0 else v("tab", W, W + H)
+                if SE[q ^ 4 * order[0]] == "V":
                     gatherop(ne, SN, halves("HL", q, 32), p, A.not_equal)
                 else:
                     gather("S", sx, SN, halves("HL", q, 32))
@@ -569,10 +605,9 @@ def rank_program(g, core, T, topo):
                     mm(ps(0, 512, k=b), v("I"), sx, False, True)
                     act(ne, ps(0, 512, k=b), F.Abs)
             b = nb()
-            group(ps(0, 128, k=b), v("I"), v("k8"), sums(b, lambda i: (i, 128, 16), "NE", 2048 * h, v("PB8"), BY[2][h]),
-                  16 * (BY[2][h] < 128))
+            group(ps(0, 128, k=b), v("I"), v("k8"), sums(b, lambda i: (i, 128, 16), "NE", 2048 * h, v("PB8"), BY[2][h]))
             scan(back(halves("SC2", h)), back(ps(0, 128, k=b)), back(halves("lo", h)), A.add)
-        tt(v("key"), v("SC2", 0, 256, 16), v("cap"), A.min)
+        tt(v("key"), v("SC2", 0, 256, 16), v("capU"), A.min)
         ts(v("dd"), v("key"), (1 << 24) + (1 << 17) + 3, A.bitwise_and)
         for d in range(N):
             ts(v("OH", 1 + d, 80, 5), v("dd"), float(d), A.is_equal)
@@ -585,53 +620,45 @@ def rank_program(g, core, T, topo):
         for h in range(2):
             tc(halves("SLL", h, 8), ends("SS", h))
         ts(v("fp"), v("key"), 13, A.arith_shift_right)
-        ts(v("XC"), v("fp"), v("pc", 2, 3), A.add)
-        tolist("XC", 0, 16, 1, v("CS"))
-        for h in range(2):
-            ts(halves("CHL", h, 8), ends("CS", h), 2048.0, A.add)
-            gather("X", halves("CH", h), v("P", PH * h, PH * h + PH + 16), halves("CHL", h, 8), last and (255.0, -1.0))
+        ts(v("XC", 0, 16), v("fp"), v("pc", 2, 3), A.add)
+        n = 16 if last or not JOIN else 32
         if not last:
             ts(v("t1"), v("key"), (1 << 17) + 2047, A.bitwise_and)
-            tt(v("XT"), v("t1"), v("capT"), A.min)
-            targets()
+            tt(v("XC", 16, 32), v("t1"), v("capT"), A.min)
+        tolist("XC", 0, n, 1, v("CS", 0, 8 * n))
+        for h in range(2):
+            ts(halves("CHL", h, 8), v("CS", 8 * h + 7, 8 * n, n), 2048.0, A.add)
+            gather("X", halves("CH", h), v("P", PH * h, PH * h + PH + 16), halves("CHL", h, 8), last and (255.0, -1.0))
+        if not last:
+            if not JOIN:
+                tolist("XC", 16, 16, 1, v("TS"))
+            for h in range(2):
+                ts(halves("WA", h, 8), v("CS", 8 * h + 23, 256, 32) if JOIN else ends("TS", h), 2048.0, A.add, 4096.0, A.min)
         scatter(v("win%d" % t), v("SLL"), v("CH"))
-        mine = (me * CAP, me * CAP + CAP)
         snd = fused(lambda d, t=t: slot(d, "win", t), lambda d, Ln=Ln: v(Ln, mine[0], mine[1]), "arr%d" % t, "loc%d" % t)
         move(v(Ln, mine[0], mine[1]), slot(me, "win", t))
         got("arr%d" % t, [v(Ln, s * CAP, s * CAP + CAP) for s in others], snd, XLAG)
-
-        def tails():
-            if t < RO - 2:
-                TR = "TR%d" % (t + 1)
-                gather("X", v("TGp"), TL, v("GL"), (-8192.0, 1.0))
-                ts(v("kj"), v("key"), 13, A.arith_shift_right, 15, A.bitwise_and)
-                tc(v("IV"), v("kj"))
-                b = nb()
-                for h in range(2):
-                    mm(ps(128 * h, 128 * h + 128, p1=8, k=b), halves("IV", h, 8), v("Ih"))
-                move(v("XI", p1=8), ps(0, 256, p1=8, k=b))
-                b = nb()
-                mm(ps(0, 256, k=b), v("R8", p1=8), v("XI", p1=8))
-                ts(v("mk"), ps(0, 256, k=b), v("pc", 0, 1), A.is_equal, -65536.0, A.mult)
-                scatter(v("wint%d" % t), v("SLL"), v("TGp"), v("mk"))
-                snd = fused(lambda d, t=t: slot(d, "wint", t), lambda d, TR=TR: v(TR, mine[0], mine[1]), "tarr%d" % t, "tloc%d" % t)
-                act(v(TR, mine[0], mine[1]), slot(me, "wint", t))
-                got("tarr%d" % t, [v(TR, s * CAP, s * CAP + CAP) for s in others], snd, XLAG + 1.0)
-            b, b2 = nb(), nb()
-            tc(v("ui", p1=32), v("up", p1=32))
-            ts(v("uj", p1=32), v("ui", p1=32), 5, A.arith_shift_right, 4095, A.bitwise_and)
-            ts(v("a12", p1=32), v("uj", p1=32), -16384.0, A.add)
-            for blk in range(4):
-                mm(ps(64 * blk, 64 * blk + 64, k=b), v("EX", 128 * blk, 128 * blk + 128, p1=32), v("a12", p1=32))
-            tt(ps(0, 256, k=b2), v("TR%d" % t), ps(0, 256, k=b), A.max)
-            tt(v("CT"), v("xtl", 0, L), ps(0, 256, k=b2), A.min)
-            ts(v("CTm"), v("CT"), 4095, A.bitwise_and)
+        main[0] = False
+        if t < RO - 2:
+            TR = "TR%d" % (t + 1)
+            ts(v("IV"), v("fp"), 0.0, A.add)
+            b = nb()
+            for h in range(2):
+                mm(ps(128 * h, 128 * h + 128, p1=8, k=b), halves("IV", h, 8), v("Ih"))
+            move(v("XI", p1=8), ps(0, 256, p1=8, k=b))
+            b = nb()
+            mm(ps(0, 256, k=b), v("R8", p1=8), v("XI", p1=8))
+            ts(v("mk"), ps(0, 256, k=b), v("pc", 0, 1), A.is_equal, -65536.0, A.mult)
+            scatter(v("wint%d" % t), v("SLL"), v("TGp"), v("mk"))
+            snd = fused(lambda d, t=t: slot(d, "wint", t), lambda d, TR=TR: v(TR, mine[0], mine[1]), "tarr%d" % t, "tloc%d" % t)
+            act(v(TR, mine[0], mine[1]), slot(me, "wint", t))
+            got("tarr%d" % t, [v(TR, s * CAP, s * CAP + CAP) for s in others], snd, XLAG + 1.0)
         if not last:
+            main[0] = True
             lowest(2048.0)
             for blk in range(3, -1, -1):
                 scatter(v("tab", 0, W + H + L), halves("WL", blk, 4), halves("CH", blk, 64))
             main[0] = False
-            tails()
             again()
             if t == RO - 2:
                 load(v("LO", 0, W), LM, 3.0)
@@ -759,13 +786,8 @@ def _plan(ops, deps, bank):
     for i, o in enumerate(ops):
         site.append((o["q"],) + tuple((x[0].rstrip("0123456789"), x[1], x[3]) for x in o["wr"][:1] + o["rd"][:2]))
         alike.setdefault(site[i], []).append(i)
-    if "key" in NOTE and SHARE:
-        key, look, pins = NOTE["key"]
-        plan = forward(key, cost, look, pins)
-        mark = replay(plan, costs[0]) * 1.5 + replay(plan, costs[1])
-        if mark < best[0]:
-            best, shakes = (mark,) + plan[1:] + (key, look, pins), SHAKES // 8
-    for n in range(shakes):
+    shared = "plan" in NOTE and SHARE
+    for n in range(0 if shared else shakes):
         z = (z * 1103515245 + 12345) % 2147483648
         lo, key, pins = z / 2147483648 * max(best[5]), list(best[6]), list(best[8])
         seen = set()
@@ -784,6 +806,200 @@ def _plan(ops, deps, bank):
         if mark <= best[0]:
             best = (mark,) + plan[1:] + (key, best[7], pins)
     NOTE["key"] = best[6:9]
+    pre = [[] for _ in ops]
+    for i in range(nop):
+        for j, lag in post[i]:
+            pre[j].append((i, lag, deps[j][i] == 1.5))
+    c0, c1 = costs
+    opn = [opens.get(i) for i in range(nop)]
+    cls = [closes.get(i) for i in range(nop)]
+
+    def play(order, on, head=None, tail=None):
+        if head:
+            (e0, e1), (w0, w1), (last, free), banks, after = [[x.copy() for x in y] for y in head[5:8]] + [head[3].copy(), {}]
+        else:
+            e0, e1, w0, w1 = [0.0] * nop, [0.0] * nop, [None] * nop, [None] * nop
+            last, free, banks, after = {}, [(0.0, k, None) for k in range(8)], {}, {}
+        for i in order:
+            q = on[i]
+            s0 = s1 = 0.0
+            a = b = None
+            if q != "R":
+                j = last.get(q)
+                if j is not None:
+                    s0, s1, a, b = e0[j], e1[j], j, j
+                last[q] = i
+            for j, lag, soft in pre[i]:
+                if soft and on[j] == q:
+                    continue
+                x = e0[j] + lag
+                if x > s0:
+                    s0, a = x, j
+                x = e1[j] + lag
+                if x > s1:
+                    s1, b = x, j
+            if opn[i] is not None:
+                if not free:
+                    return None
+                f = min(free)
+                free.remove(f)
+                banks[opn[i]], after[i] = f[1], f[2]
+                j = f[2]
+                if j is not None:
+                    if e0[j] + LAG > s0:
+                        s0, a = e0[j] + LAG, j
+                    if e1[j] + LAG > s1:
+                        s1, b = e1[j] + LAG, j
+            k = i + nop if q == "S" else i
+            e0[i], e1[i], w0[i], w1[i] = s0 + c0[k], s1 + c1[k], a, b
+            if cls[i]:
+                for u in cls[i]:
+                    free.append((e0[i] + e1[i], banks[u], i))
+        ends = []
+        for k, e in enumerate((e0, e1)):
+            if tail:
+                out = [(e[i] + x[k], i) for i, x in tail[0]] + [(e[last[q]] + x[k], last[q]) for q, x in tail[1] if q in last]
+                out += [(e[f[2]] + LAG + x[k], f[2]) for f, x in zip(sorted(free), tail[2]) if f[2] is not None]
+                ends.append(max(out))
+            else:
+                ends.append(max((e[i], i) for i in order[-60:]) if order else (0.0, 0))
+        return 1.5 * ends[0][0] + ends[1][0], order, on, banks, after, (e0, e1), (w0, w1), (last, free), ends
+
+    def rest(p, hi):
+        order, on, after = p[1], p[2], p[4]
+        t, nxt, takers, later = {}, {}, [], set(order[hi:])
+        for i in reversed(order[hi:]):
+            q, k = on[i], i + nop * (on[i] == "S")
+            x, y = nxt.get(q, (0.0, 0.0)) if q != "R" else (0.0, 0.0), t.pop(i, (0.0, 0.0))
+            x = nxt[q] = (max(x[0], y[0]) + c0[k], max(x[1], y[1]) + c1[k])
+            arcs = [(j, lag) for j, lag, soft in pre[i] if not (soft and on[j] == q)]
+            if after.get(i) in later:
+                arcs.append((after[i], LAG))
+            elif opn[i] is not None:
+                takers.append(x)
+            for j, lag in arcs:
+                y = t.get(j, (0.0, 0.0))
+                t[j] = (max(y[0], x[0] + lag), max(y[1], x[1] + lag))
+        nxt.pop("R", None)
+        return list(t.items()), list(nxt.items()), takers[::-1]
+
+    def chain(p, k, inside):
+        w = p[6][k]
+        i, out = p[8][k][1], []
+        while w[i] in inside:
+            if all(x[0] != w[i] or x[2] and p[2][i] == p[2][w[i]] for x in pre[i]):
+                out.append((w[i], i))
+            i = w[i]
+        return out
+    preset = [{x[0] for x in p} for p in pre]
+    now = top = play(best[1], best[2])
+    twin, count = {}, {}
+    for i, o in enumerate(ops):
+        k = (site[i], o["round"])
+        count[k] = count.get(k, 0) + 1
+        site[i] = (site[i], count[k])
+        twin[site[i], o["round"]] = i
+
+    def ahead(order, j, i):
+        lo, hi = order.index(i), order.index(j)
+        if lo > hi:
+            return order
+        take, keep, need = [j], [], set(preset[j])
+        for x in reversed(order[lo:hi]):
+            if x in need:
+                take.append(x)
+                need |= preset[x]
+            else:
+                keep.append(x)
+        return order[:lo] + take[::-1] + keep[::-1] + order[hi + 1:]
+
+    def behind(order, i, j):
+        lo, hi = order.index(i), order.index(j)
+        if lo > hi:
+            return order
+        take, keep, gone = [i], [], {i}
+        for x in order[lo + 1:hi + 1]:
+            if preset[x] & gone:
+                take.append(x)
+                gone.add(x)
+            else:
+                keep.append(x)
+        return order[:lo] + keep + take + order[hi + 1:]
+
+    def mend(whole, lo, hi, heat, z):
+        head, tail = play(whole[1][:lo], whole[2]), rest(whole, hi) if hi < nop else None
+        now = top = play(whole[1][lo:hi], whole[2], head, tail)
+        arcs, inside = None, set(now[1])
+        for n in range(MENDS):
+            if arcs is None:
+                row = {}
+                for i in now[1]:
+                    row.setdefault(now[2][i], []).append(i)
+                at = {i: k for r in row.values() for k, i in enumerate(r)}
+                arcs = chain(now, 0, inside) + chain(now, 1, inside)
+                if not arcs:
+                    break
+            z = (z * 1103515245 + 12345) % 2147483648
+            i, j = arcs[(z >> 8) % len(arcs)]
+            z = (z * 1103515245 + 12345) % 2147483648
+            how, far, order, on = (z >> 8) % 8, FAR[(z >> 14) % len(FAR)], now[1], now[2]
+            if how >= 6 and "X" in (free_q[i], free_q[j]):
+                i = i if free_q[i] == "X" and (free_q[j] != "X" or how == 6) else j
+                on = list(on)
+                on[i] = "S" if on[i] == "V" else "V"
+            elif how % 2:
+                order = ahead(order, j, row[on[i]][max(0, at[i] - far)])
+            else:
+                order = behind(order, i, row[on[j]][min(len(row[on[j]]) - 1, at[j] + far)])
+            p = play(order, on, head, tail)
+            z = (z * 1103515245 + 12345) % 2147483648
+            if p and p[0] <= now[0] + heat * (1 - n / MENDS) * (z / 2147483648) ** 2:
+                now, arcs = p, None
+                if p[0] < top[0]:
+                    top = p
+        return play(whole[1][:lo] + top[1] + whole[1][hi:], top[2])
+
+    def timed(p):
+        pos = {i: k for k, i in enumerate(p[1])}
+        x = play(sorted(p[1], key=lambda i: (round(p[5][0][i] - c0[i + nop * (p[2][i] == "S")], 6), pos[i])), p[2])
+        return x if x and x[0] <= p[0] + 0.2 else p
+
+    def like(p, a, b):
+        start = [p[5][0][i] - c0[i + nop * (p[2][i] == "S")] for i in range(nop)]
+        pairs = [(i, twin[site[i], a]) for i in range(nop) if ops[i]["round"] == b and (site[i], a) in twin]
+        shift = sorted(start[i] - start[j] for i, j in pairs)[len(pairs) // 2]
+        key, on = list(start), list(p[2])
+        for i, j in pairs:
+            key[i], on[i] = start[j] + shift, p[2][j]
+        return keyed(key, on)
+
+    def keyed(key, on):
+        left, order = [len(x) for x in preset], []
+        ready = [i for i in range(nop) if not left[i]]
+        while ready:
+            i = min(ready, key=lambda z: key[z])
+            ready.remove(i)
+            order.append(i)
+            for j, _ in post[i]:
+                left[j] -= 1
+                if not left[j]:
+                    ready.append(j)
+        return play(order, on)
+    if shared:
+        top = keyed(*NOTE["plan"])
+    for sweep, heat in enumerate(() if shared else HEAT):
+        for lo in range(-(sweep % 2) * WIDE // 4, nop - WIDE // 2, WIDE // 2):
+            z = (z * 1103515245 + 12345) % 2147483648
+            p = mend(top, max(lo, 0), min(lo + WIDE, nop), heat, z)
+            if p and p[0] <= top[0]:
+                top = timed(p)
+        for a in range(RO):
+            for b in range(1, RO):
+                p = like(top, a, b) if a != b else None
+                if p and p[0] < top[0]:
+                    top = p
+    best = top[:5] + best[5:]
+    NOTE["plan"] = ({i: k for k, i in enumerate(top[1])}, top[2])
     order, on, banks, after = best[1:5]
     NOTE["mark"] = best[0]
     for i in range(nop):

@@ -9,29 +9,30 @@ BIG = 67108864.0
 NONE = 127 << 17
 _B, _F, _H, _I, _U = "bfloat16", "float32", "float16", "int32", "uint16"
 _SB = {
-    "tab": (3 * H + W, _B), "xtl": (W + H + L, _I), "xmo": (4096, _B), "sn0": (H, _B), "fm0": (L, _B),
-    "fr0": (RO * L, _B), "wk0": (3, _I), "wkf": (3, _F), "frc": (3 * L, _B),
+    "tab": (3 * H + W + 1024, _B), "xtl": (W + H + L, _I), "xmo": (4096, _B), "sn0": (H, _B), "fm0": (L, _B),
+    "fr0": (RO * L, _B), "wk0": (3, _I), "wkf": (4, _F), "frc": (3 * L, _B),
     "win0": (SW, _B), "win1": (SW, _B), "win2": (SW, _B), "win3": (SW, _B), "wint0": (SW, _F), "wint1": (SW, _F),
     "L1": (L, _B), "L2": (L, _B), "L3": (L, _B), "L4": (L, _B), "TR0": (L, _F), "TR1": (L, _F), "TR2": (L, _F),
-    "L0": (L, _B), "mT": (384, _B), "qT": (L, _B), "au": (128, _I), "am": (128, _I), "up": (64, _F), "ui": (64, _I), "uj": (64, _I),
+    "mT": (384, _B), "qT": (L, _B), "au": (64, _I), "am": (64, _I), "up": (64, _F), "ui": (64, _I), "uj": (64, _I),
     "hb": (16, _F), "zm": (16, _F), "capT": (16, _F), "capU": (16, _F), "LO": (W + L, _B), "cT": (256, _F),
-    "a12": (64, _F), "ci": (L, _I), "cj": (L, _I), "cf": (L, _H), "MR": (4096, _B), "CL": (L, _U), "X": (4096, _B), "E": (4096, _B), "Y": (4096, _B), "P": (2 * PH + 16, _B),
+    "a12": (64, _H), "ci": (L, _I), "cj": (L, _I), "cf": (L, _H), "MR": (4096, _B), "CL": (L, _U),
+    "X": (4096, _B), "E": (4096, _B), "Y": (4096, _B), "P": (2 * PH + 16, _B),
     "NE": (4096, _B), "SX": (4096, _B), "SD": (272, _F), "GV": (272, _H), "GS": (128, _F), "GL": (16, _U), "TG": (L, _U), "xg": (L, _B),
-    "hi": (512, _I), "hm": (512, _I), "hV": (256, _F), "hp": (256, _I), "hq": (256, _I), "lo": (256, _F),
-    "HL": (256, _U), "SC2": (256, _F), "key": (16, _I),
-    "IV": (16, _H), "XI": (256, _B), "fp": (16, _I), "XC": (32, _H), "CS": (256, _F), "CHL": (16, _U),
+    "hi": (512, _I), "hm": (512, _I), "hp": (256, _I), "hq": (256, _I), "lo": (256, _F), "hh": (256, _H), "uf": (256, _H),
+    "hf": (256, _F), "hn": (256, _B), "hr": (256, _I), "hs": (256, _I), "HL": (256, _U), "SC2": (256, _F), "key": (16, _I), "T1": (128, _B),
+    "IV": (32, _H), "fp": (16, _I), "XC": (32, _H), "CS": (256, _H), "CHL": (16, _U),
     "CH": (L, _B), "dd": (16, _I), "OH": (80, _B), "S5": (80, _H), "SS": (128, _F), "SLL": (16, _U),
     "TGp": (L, _F), "mk": (L, _F), "CT": (L, _I), "CTm": (L, _I), "t1": (16, _I), "TS": (128, _F),
+    "WA": (16, _U), "FT0": (L, _B), "FT1": (L, _B), "EW": (1024, _B), "WL": (16, _U), "WO": (16, _H),
 }
-_SB.update({"WA": (16, _U), "FT0": (L, _B), "FT1": (L, _B), "SCW": (1024, _F), "zn": (16, _F), "XZ": (16, _H), "ZS": (128, _F),
-            "WL": (16, _U), "kj": (16, _I)})
 _CO = {
-    "one": (512, _B), "zero": (272, _B), "I": (128, _B), "nI": (128, _B), "Ih": (128, _H), "If": (128, _F),
-    "bo": (128, _B), "b8": (8, _B), "tmp": (128, _B), "Rep": (512, _B), "R32": (512, _B), "C8": (1024, _B), "i4": (128, _B),
-    "R8": (128, _B), "TR": (128, _B), "TRB": (128, _B), "JR": (272, _B), "K17": (16, _B), "Et": (96, _B), "ZU": (96, _B), "ZV": (96, _B),
-    "cA": (128, _F), "EX": (512, _F),
-    "base": (80, _B), "r5": (80, _B), "rm8": (256, _B), "k8": (128, _B), "Mk": (256, _B),
-    "mkc": (256, _B), "pc": (12, _F), "pi": (4, _I), "W3": (256, _B), "Wt": (16, _B), "NP": (16, _B), "PB8": (8, _B), "Wp": (16, _B),
+    "one": (512, _B), "zero": (272, _B), "I": (128, _B), "nI": (128, _B), "n8": (8, _B), "n32": (128, _B), "If": (128, _F),
+    "b8": (8, _B), "t8": (8, _B), "Rep": (512, _B), "R32": (512, _B), "C8": (1024, _B), "i4": (128, _B),
+    "TR": (128, _B), "TRB": (128, _B), "JR": (272, _B), "K17": (16, _B), "Et": (96, _B), "Z": (160, _B),
+    "EX": (512, _F), "EM": (256, _B), "EA": (512, _B), "Eq": (40, _B),
+    "base": (80, _B), "r5": (80, _B), "rm8": (256, _B), "k8": (128, _B), "Mk": (256, _B), "C8p": (1024, _B),
+    "mkw": (256, _B), "mki": (128, _B), "sel": (2, _B), "pc": (20, _F), "pi": (8, _I),
+    "NP": (16, _B), "PB8": (8, _B), "Wp": (16, _B),
     "lt": (16, _F), "ti": (12, _F), "tj": (12, _F), "tk": (12, _F), "tbl": (4096 + 16, _B),
 }
 _PACK, _POS = {}, {}
@@ -53,30 +54,34 @@ for _t, _n in _PACK.items():
     SCRATCH["pk_" + _t] = ("sbuf", [128, _n], _t)
 for _k in range(8):
     SCRATCH["ps%d" % _k] = ("psum", [128, 512], "float32")
-SEMAPHORES = ["q" + e for e in "VSTG"] + ["ld%d" % i for i in range(42)] + ["st0", "st1"] + \
+SEMAPHORES = ["q" + e for e in "VSTG"] + ["ld%d" % i for i in range(54)] + ["st0", "st1"] + \
     ["%s%d" % (p, t) for p in ("arr", "tarr", "rarr", "loc", "tloc", "rloc") for t in range(RO)]
 
-EB, LITE = "AAASSASA", 1
-FIRST, YQ, MOD0 = True, "YYQQYQQQ", True
-PAR = True
-SE = "SSSVSVVV"
-GB = "SSSSSSSS"
+EB0, EB = "AAAXXAXA", "AAAXXAXA"
+YQ = "YYQQYQQQ"
+SE = "XXVVxVVV"
 GD = "XXXXXXXX"
-ED = "XXXXXXXX"
-SETS = ({"e": 0.00085, "g": 0.00095, "s": 0.0021, "t": 0.00032}, {"e": 0.00120, "g": 0.00220, "s": 0.0055, "t": 0.00048})
-LOOSE = True
-SHUT, SHUT2 = False, True
-HS = ""
+MAGIC = 12582912.0
+AOFF = 262144.0
+SETS = ({"e": 0.00084, "g": 0.00100, "s": 0.0020, "t": 0.00037}, {"e": 0.00110, "g": 0.00160, "s": 0.0060, "t": 0.00052})
+FIX = (0.0, 0.0, 0.0, 0.0)
+LOOSE = False
 SLOW = 1.2
-EARLY, TWO, JOIN, MRQ = False, True, True, "X"
-BY = ((128, 128), (128, 128), (128, 128))
-LAG = 0.18
-XLAG = 3.5
+LAG, TLAG, LAG1, LONGER = 0.26, 0.0, 0.26, 1.3
+WEIGH = 1.3
+XLAG, CALL, RLAG, FLAG, FCALL = 1.8, 0.6, 5.0, 7.0, 4.0
+HF = True
+PAR = False
+DIRECT = ""
+HT = True
+CUTS = ((), (96,), (), (96,), (), (96,))
+QUART = (True, True)
+TWOCALL = True
 LOOKS = ((0.2, 2.0, 0.0), (0.2, 2.0, 2.0), (0.25, 1.0, 1.0))
 MIX = (0.25,)
 SHAKES, SHAKE, SPAN, SEED, SHARE = 50, (0.3, 0.6, 1.2), (2.0, 4.0, 3.0, 7.0), 12345, True
 TIE, SKIP = 2, 1
-MENDS, HEAT, WIDE, FAR = 2500, (0.9, 0.8, 0.7, 0.6, 0.5, 0.4, 0.3, 0.2, 0.1), 200, (0, 0, 1, 2, 4)
+MENDS, HEAT, WIDE, FAR = 6500, (0.9, 0.8, 0.7, 0.6, 0.5, 0.4, 0.3, 0.2, 0.1), 200, (0, 0, 1, 2, 4)
 NOTE = {}
 PASSES = 6
 
@@ -112,13 +117,13 @@ def rank_program(g, core, T, topo):
         cost = cost if isinstance(cost, tuple) else (cost, 0, "e")
         if isinstance(fn, dict) and cost[2] == "e":
             n = ncol(rd[0])
-            cost = vc(n, 0.5 if is2(rd[0]) and is2(wr[0]) else 1.0) + (0.13 if inps(rd[0]) else 0.05, n, "e")
+            cost = vc(n, 0.5 if is2(rd[0]) and is2(wr[0]) else 1.0) + (FIX[2] if inps(rd[0]) else FIX[1], max(64, n), "e")
         ops.append({"q": q, "fn": fn, "rd": rd, "wr": wr, "cost": cost[:3], "costs": cost[-3:],
                     "sem": sem, "val": val, "lag": lag, "after": after, "main": main[0] and len(ops), "round": turn[0]})
         return len(ops) - 1
 
     def vc(n, f=1.0):
-        return (0.04, max(64, n * f), "e")
+        return (FIX[0], max(64, n * f), "e")
 
     def inps(x):
         return x[0][:2] == "ps"
@@ -151,7 +156,8 @@ def rank_program(g, core, T, topo):
         if setup[0]:
             return move(out, x, bias, scale)
         return op("S", lambda: g.scalar.activation(ap(out), ap(x), fn, bias=arg(bias), scale=arg(scale)),
-                  [x] + [s for s in (bias, scale) if isinstance(s, tuple)], [out], (0.13 if inps(x) else 0.05, ncol(x), "e"))
+                  [x] + [s for s in (bias, scale) if isinstance(s, tuple)], [out],
+                  (FIX[2] if inps(x) else FIX[1], max(64, ncol(x)), "e"))
 
     def gather(q, out, win, off, turn=None):
         fn = {"V": lambda: g.vector.tensor_copy(ap(out), ap(win).indirect(ap(off))),
@@ -164,6 +170,14 @@ def rank_program(g, core, T, topo):
     def relu(out, x, c, q):
         return op(q, {"V": lambda: g.vector.tensor_scalar(ap(out), ap(x), c, 0.0, A.add, A.max),
                         "S": lambda: g.scalar.activation(ap(out), ap(x), F.Relu, bias=c)}, [x], [out], (0.1, ncol(x), "e"))
+
+    def under(out, x, q):
+        return op(q, {"V": lambda: g.vector.tensor_scalar(ap(out), ap(x), -1.0, 0.0, A.mult, A.max),
+                        "S": lambda: g.scalar.activation(ap(out), ap(x), F.Relu, scale=-1.0)}, [x], [out], (0.1, ncol(x), "e"))
+
+    def differs(out, x, q):
+        return op(q, {"V": lambda: g.vector.tensor_scalar(ap(out), ap(x), 0.0, None, A.not_equal),
+                        "S": lambda: g.scalar.activation(ap(out), ap(x), F.Abs)}, [x], [out], (0.1, ncol(x), "e"))
 
     def move(out, x, bias=0.0, scale=1.0, q="X"):
         return op(q, {"V": lambda: g.vector.tensor_scalar(ap(out), ap(x), arg(scale), arg(bias), A.mult, A.add),
@@ -179,10 +193,10 @@ def rank_program(g, core, T, topo):
         return op("V", lambda: g.vector.tensor_tensor(ap(out), ap(win).indirect(ap(off)), ap(y), o), [win, off, y], [out],
                   (0.05, ncol(out), "g"))
 
-    def scatter(win, off, x, y=None):
+    def scatter(win, off, x, y=None, o=A.add):
         c = (0.05, ncol(x), "s")
         if y:
-            return op("V", lambda: g.vector.tensor_tensor(ap(win).indirect(ap(off)), ap(x), ap(y), A.add), [x, y, off], [win], c)
+            return op("V", lambda: g.vector.tensor_tensor(ap(win).indirect(ap(off)), ap(x), ap(y), o), [x, y, off], [win], c)
         return op("V", lambda: g.vector.tensor_copy(ap(win).indirect(ap(off)), ap(x)), [x, off], [win], c)
 
     def mms(calls):
@@ -191,7 +205,7 @@ def rank_program(g, core, T, topo):
                 ins = g.tensor.matmul(ap(out), ap(lhsT), ap(rhs), start, stop)
             return ins
         n = sum((4 if SCRATCH[x[2][0]][2] == _F else 1) * max(min(64, ncol(x[1])), ncol(x[2])) for x in calls)
-        return op("T", fn, [y for x in calls for y in x[1:3]], [x[0] for x in calls], (0.015 * len(calls), n, "t"), lag=LAG + 0.1)
+        return op("T", fn, [y for x in calls for y in x[1:3]], [x[0] for x in calls], (FIX[3] * len(calls), n, "t"), lag=LAG + TLAG)
 
     def mm(out, lhsT, rhs, start=True, stop=True):
         return mms([(out, lhsT, rhs, start, stop)])
@@ -214,7 +228,7 @@ def rank_program(g, core, T, topo):
         nld[0] += 1
         rd, wr = ([src, v("sn0", 0, 1)], [out]) if isinstance(src, tuple) else ([], [out, ("order", 0, 128, 0, 1, 2)])
         if rows:
-            return op("D", lambda: g.sync.dma_start(T[out[0]][rows[0]::16, out[3]:out[4]], T[src[0]][rows[1]::16, src[3]:src[4]]),
+            return op("D", lambda: g.sync.dma_start(T[out[0]][rows[0], out[3]:out[4]], T[src[0]][rows[1], src[3]:src[4]]),
                       rd, wr, 0.08, sem=s, val=16, lag=2.0 + cost)
         return op("D", lambda: g.sync.dma_start(ap(out), arg(src)), rd, wr, 0.08, sem=s, val=16, lag=2.0 + cost)
 
@@ -233,7 +247,7 @@ def rank_program(g, core, T, topo):
         n = len(eng)
         return dict(zip(od, [eng[:n // 2], eng[n // 2:], eng] if two else [eng[:n // 2:2], eng[n // 2::2], eng[1::2]]))
 
-    def fused(src, dst, sem, loc, two=False):
+    def fused(src, dst, sem, loc, two=False, after=None, behind=()):
         parts = masks(me, two)
 
         def fn():
@@ -245,10 +259,11 @@ def rank_program(g, core, T, topo):
                                                 remote_sem=T.sem[sem], srcs=[ap(src(d))], dsts=[ap(dst(d))], alu_op=0))
                 ins = g.remote_dma_fused(tr, local_sem=T.sem[loc])
             return ins
-        return op("G", fn, [src(d) for d in others], [], 1.0, sem=loc, val=sum(len(x) for x in parts.values()), lag=1.5)
+        return op("G", fn, [src(d) for d in others] + list(behind), [], CALL, sem=loc, val=sum(len(x) for x in parts.values()), lag=1.5,
+                  after=after)
 
-    def got(sem, wr, after, lag, two=False):
-        return op("R", None, [], wr, 0.0, sem=sem, val=sum(len(masks(s, two)[me]) for s in others), lag=lag, after=after)
+    def got(sem, wr, after, lag, two=False, rd=()):
+        return op("R", None, list(rd), wr, 0.0, sem=sem, val=sum(len(masks(s, two)[me]) for s in others), lag=lag, after=after)
 
     def slot(d, name, t):
         return v("%s%d" % (name, t), DUMP + 256 * d, DUMP + 256 * d + CAP)
@@ -259,24 +274,37 @@ def rank_program(g, core, T, topo):
     def mp(h):
         return v("P", PH * h, PH * h + 128)
 
-    def prod(q):
-        c = PH * (q // 4) + 128 + 512 * (q % 4)
-        return v("P", c, c + 512)
+    def prod(a, n):
+        c = PH * (a // 128) + 128 + 16 * (a % 128)
+        return v("P", c, c + 16 * n)
+
+    def chunks(kinds, h):
+        return [(kinds[q].upper(), q, 32 * q + a, n) for q in range(4 * h, 4 * h + 4)
+                for a, n in (((0, 16), (16, 16)) if kinds[q].islower() else ((0, 32),))]
+
+    def wide(name, a, n):
+        return v(name, 16 * a, 16 * (a + n))
+
+    def rep(p, a, n):
+        return v("Rep", 16 * (a % 32), 16 * (a % 32 + n), p0=p, p1=p + 32)
 
     def back(x):
         return x[:3] + (x[4] - 1, x[3] - 1, -1)
-    SN, LM, TL = v("tab", W), v("tab", 0, W), v("xtl", 0, W)
+    LM, TL = v("tab", 0, W), v("xtl", 0, W)
+    copies = (1, 3, 3, 3)
 
-    def again():
-        for c in range(1, 3):
+    def again(n):
+        for c in range(1, n):
             load(v("tab", W + c * H, W + c * H + H), v("tab", W, W + H), 3.0)
+        if HF:
+            load(v("tab", W + 3 * H, W + 3 * H + 1024), v("tab", W, W + 1024), 3.5)
 
     load(v("wk0"), T.wk[:], 0.2)
     load(v("fm0"), T.fm[:], 0.5)
     load(LM, T.lm[:], 2.5 * SLOW)
-    load(v("fr0", 0, L), T.fr[:, 0:L], 2.7 * SLOW)
-    load(TL, T.tl[:], 5.2 * SLOW)
-    load(v("xmo"), T.mo[:], 8.2 * SLOW)
+    load(TL, T.tl[:], 5.0 * SLOW)
+    load(v("xmo"), T.mo[:], 8.0 * SLOW)
+    load(v("fr0", 0, L), T.fr[:, 0:L], 8.2 * SLOW)
     load(v("sn0"), T.sn[:], 9.7 * SLOW)
     load(v("fr0", L), T.fr[:, L:RO * L], 10.5 * SLOW)
     vset(v("one", 0, 128), 1.0)
@@ -285,74 +313,88 @@ def rank_program(g, core, T, topo):
     o128 = v("one", 0, 128)
     iota(v("pi", 0, 1), [[0, 1]], 0, 1, False)
     iota(v("ti"), [[1, 12]], 0, 0)
-    pick(v("tmp"), o128, [[-16, 8], [0, 16]], A.is_ge, 0.0, 0, 1)
-    pick(v("bo"), v("tmp"), [[16, 8], [0, 16]], A.is_ge, 0.0, 15, -1)
+    pick(v("t8"), v("one", 0, 8), [[-16, 8]], A.is_ge, 0.0, 0, 1)
+    pick(v("b8"), v("t8"), [[16, 8]], A.is_ge, 0.0, 15, -1)
     pick(v("I"), o128, [[-1, 128]], A.is_equal, 0.0, 0, 1)
     pick(v("R32", p1=32), v("one", 0, 512, p1=32), [[-1, 32], [0, 16]], A.is_equal, 0.0, 0, 1)
     pick(v("JR"), v("one", 0, 272), [[0, 2], [-16, 8], [1, 17]], A.is_equal, 0.0, -16, 1)
     for a in range(2):
         pick(halves("C8", a, 512), v("one"), [[-16, 4], [0, 8], [-1, 16]], A.is_equal, 0.0, -64 * a, 1)
-    pick(v("Mk", 0, 128), v("zero", 0, 128), [[0, 16], [-16, 8]], A.is_ge, -BIG / 2, 0, 1)
-    pick(v("Mk", 0, 128), v("Mk", 0, 128), [[0, 16], [16, 8]], A.is_ge, -BIG / 2, 15, -1)
+    pick(v("Mk", 0, 128), v("zero", 0, 128), [[0, 16], [-16, 8]], A.is_ge, -16384.0, 0, 1)
+    pick(v("Mk", 0, 128), v("Mk", 0, 128), [[0, 16], [16, 8]], A.is_ge, -16384.0, 15, -1)
     act(v("Mk", 128, 256), v("Mk", 0, 128))
     iota(v("lt"), [[128, 2], [0, 8]], 0, 1)
     iota(v("base"), [[0, 16], [256, 5]], DUMP - 256 - 2048, 0)
     pick(v("TR"), o128, [[1, 128]], A.is_gt, 0.0, 0, -1)
-    pick(v("R8", p1=8), v("one", 0, 128, p1=8), [[-1, 8], [0, 16]], A.is_equal, 0.0, 0, 1)
-    for a in range(2):
-        pick(v("mkc", p0=64 * a, p1=64 * a + 64), v("zero", 0, 256, p0=64 * a, p1=64 * a + 64), [[0, 4], [-1, 64]],
-             A.not_equal, float(1 << 20), 0, 1)
-    vset(v("mkc", 0, 256, 64), -BIG)
+    for c in range(8):
+        p = 64 * (c // 4)
+        load(v("C8p", p0=16 * c, p1=16 * c + 16), v("C8"), 0.5, (slice(16 * c, 16 * c + 16), slice(p + c % 4, p + 64, 4)))
+    iota(v("mki"), [[1, 16], [16, 4], [0, 2]], 0, 0)
+    for x in range(2):
+        for y in range(2):
+            vset(v("sel", x, x + 1, p0=64 * y, p1=64 * y + 64), float(x == y))
     for a in range(4):
         act(v("i4", 32 * a, 32 * a + 32, p1=32), v("I", 0, 32, p1=32))
     b = nb()
     mm(ps(0, 512, k=b), v("i4", p1=32), v("R32", p1=32))
     act(v("Rep"), ps(0, 512, k=b))
     act(v("nI"), v("I"), scale=-1.0)
-    tc(v("Ih"), v("I"))
-    act(v("If"), v("I"))
-    tc(v("b8"), v("bo", 0, 128, 16))
+    act(v("If"), v("I"), scale=1 / 32 if HF else 1.0)
+    act(v("n32"), v("I"), scale=-1 / 32)
+    act(v("n8"), v("b8"), scale=-1.0)
     act(v("NP", 0, 8), v("b8"), scale=-8192.0)
     act(v("NP", 8, 16), v("b8"), scale=8192.0)
     act(v("PB8"), v("b8"), scale=-BIG / 2)
     ts(v("pi", 1, 2), v("pi", 0, 1), 15, A.bitwise_and)
     tc(v("pc", 0, 1), v("pi", 1, 2))
-    ts(v("pc", 1, 2), v("pc", 0, 1), 0.0, A.is_gt, 131072.0, A.mult)
-    ts(v("pc", 2, 3), v("pi", 0, 1), 16.0, A.mult, 128.0 - 2048, A.add)
-    ts(v("pc", 3, 4), v("pi", 0, 1), -15.0 * 8192, A.mult, 2048.0 - 128 * 8192, A.add)
-    ts(v("pi", 2, 3), v("pi", 0, 1), 63, A.bitwise_and)
-    ts(v("pc", 5, 6), v("pi", 2, 3), 2.0, A.mult, 2048.0, A.add)
-    ts(v("pc", 8, 9), v("pi", 2, 3), 0.0, A.is_equal, -BIG, A.mult)
-    tt(v("pc", 7, 8), v("pc", 8, 9), v("pc", 5, 6), A.add)
+    ts(v("tj"), v("ti"), v("pc", 0, 1), A.is_equal)
+    act(v("pc", 1, 2), v("tj", 0, 1), F.Identity, 65536.0 + 2 * AOFF, -65536.0 - 2 * AOFF)
+    act(v("pc", 2, 3), v("lt", 0, 1), F.Identity, 128.0 - 2048, 16.0)
+    act(v("pc", 3, 4), v("lt", 0, 1), F.Identity, 2048.0 - 128 * 8192, -15.0 * 8192)
+    b = nb()
+    mms([(ps(0, 1, p0=64 * x, p1=64 * x + 64, k=b), v("mki", 0, 128, 2, p1=1), v("one", 0, 1, p1=1), True, True) for x in range(2)])
+    ts(halves("mkw", 0), v("mki"), ps(0, 1, k=b), A.is_le, -131072.0, A.mult)
+    act(halves("mkw", 1), halves("mkw", 0))
+    for c in range(4):
+        act(v("pc", 8 + c, 9 + c), v("pc", 0, 1), F.Identity, 2049.0 + 16 * c)
+    vset(v("pc", 4, 5, p1=96), 0.0)
+    vset(v("pc", 4, 5, p0=96), 32.0)
+    times(v("pc", 13, 14), v("pc", 0, 1), v("pc", 0, 1))
+    act(v("pc", 14, 15), v("pc", 13, 14), F.Identity, 2 * AOFF, -2 * AOFF)
+    act(v("pc", 15, 16), v("pc", 0, 1), F.Identity, 0.0, 2.0)
     ts(v("pi", 3, 4), v("pi", 0, 1), 4, A.arith_shift_right, 1, A.bitwise_and)
     tc(v("pc", 6, 7), v("pi", 3, 4))
-    tc(v("wkf"), v("wk0"))
-    for x in range(2):
-        w = v("wkf", x, x + 1)
-        ts(v("Wt", 8 * x, 8 * x + 8), v("b8"), w, A.mult, -1.0, A.mult)
-        act(halves("W3", x), v("bo"), F.Identity, 0.0, w)
-    for name in ("ZU", "ZV", "Et"):
+    tc(v("wkf", 0, 3), v("wk0"))
+    vset(v("Eq"), 0.0)
+    times(v("Eq", 8, 16), v("b8"), v("pc", 15, 16))
+    act(v("Eq", 24, 32), v("n8"))
+    b = nb()
+    for h in range(2):
+        mm(ps(128 * h, 128 * h + 128, p1=32, k=b), v("Eq", 8 - 8 * h, 40 - 8 * h), v("I"))
+    act(v("EM", p1=32), ps(0, 256, p1=32, k=b))
+    for x in range(4):
+        times(halves("Wp", x, 4), halves("n8", x // 2, 4), v("wkf", x % 2, x % 2 + 1))
+    for name in ("Z", "Et"):
         vset(v(name), 0.0)
-    ts(v("ZU", 24, 32), v("b8"), v("wkf", 0, 1), A.mult, -1.0, A.mult)
-    act(v("ZU", 56, 64), v("b8"), F.Identity, 0.0, v("wkf", 0, 1))
-    ts(v("ZV", 24, 32), v("b8"), v("wkf", 1, 2), A.mult, -1.0, A.mult)
-    ts(v("pc", 4, 5), v("pi", 0, 1), 31.5, A.is_gt)
+    times(v("Z", 24, 32), v("n8"), v("wkf", 0, 1))
+    times(v("Z", 56, 64), v("b8"), v("wkf", 0, 1))
+    times(v("Z", 88, 96), v("n8"), v("wkf", 1, 2))
     act(v("Et", 24, 32), v("b8"))
-    ts(v("Et", 56, 64), v("b8"), v("wkf", 2, 3), A.mult, -32.0, A.mult)
+    times(v("Et", 56, 64), v("n8"), v("wkf", 2, 3))
 
     def lanesums(b, xs):
-        w = ncol(xs[0])
-        mms([(ps(w * n, w * n + ncol(x), p1=64, k=b), v(name, 24 - 8 * blk, 88 - 8 * blk), x, blk == len(xs) - 1, blk == 0)
-             for n, name in enumerate(("ZU", "ZV")) for blk, x in list(enumerate(xs))[::-1]])
+        mms([(ps(0, ncol(x), k=b), v("Z", 24 - 8 * blk, 152 - 8 * blk), x, blk == 0, blk == 3) for blk, x in enumerate(xs)])
     b = nb()
-    lanesums(b, [v("one", 0, 64)] * 4)
-    act(v("cA", p1=64), ps(0, 128, p1=64, k=b), scale=-255.0)
-    vset(v("cA", 64, 128, p0=32, p1=64), 1.0)
+    lanesums(b, [v("one", 0, 2)] * 4)
+    act(v("pc", 12, 13), ps(0, 1, k=b), F.Identity, v("pc", 4, 5), -255.0)
     b = nb()
     for blk in range(4):
         mm(ps(128 * blk, 128 * blk + 128, p1=64, k=b), v("Et", 24 - 8 * blk, 88 - 8 * blk), v("I"))
     for x in range(2):
         act(v("EX", 256 * x, 256 * x + 256, p1=64), ps(256 * x, 256 * x + 256, p1=64, k=b))
+    pick(v("EA", p1=32), v("one", p1=32), [[-8, 4], [-1, 8], [0, 16]], A.is_equal, 0.0, 0, 1)
+    vset(v("EA", p0=32, p1=33), 2048 - AOFF)
+    tc(v("a12", p0=32, p1=33), v("one", 0, 64, p0=32, p1=33))
     for x in range(2):
         act(v("JR", 136 * x, 136 * x + 136, 17), v("I", 0, 128, 16))
     vset(v("K17"), -2048.0)
@@ -360,20 +402,13 @@ def rank_program(g, core, T, topo):
     vset(v("rm8", 0, None, 8), -BIG)
     vset(v("k8"), 8192.0)
     b = nb()
-    mm(ps(0, 256, k=b), o128, v("W3"))
-    if TWO:
-        for x, y in enumerate((0, 2, 1, 3)):
-            act(halves("cT", x, 64), ps(64 * y, 64 * y + 64, k=b), scale=255.0)
-            act(halves("Wp", x, 4), halves("Wt", y, 4))
-    else:
-        act(v("cT"), ps(0, 256, k=b), scale=255.0)
+    mms([(ps(i, 256, 16, k=b), o128, v("Wp"), True, True) for i in range(16)])
+    act(v("cT"), ps(0, 256, k=b), scale=-255.0)
     act(v("base", 0, 80, 5), v("lt"))
     vset(v("r5"), 1.0)
     vset(v("r5", 0, 80, 5), 0.0)
     vset(v("OH"), 0.0)
-    act(v("tmp"), v("I"), scale=2048.0)
-    tt(v("TRB"), v("TR"), v("tmp"), A.add)
-    ts(v("tj"), v("ti"), v("pc", 0, 1), A.is_equal)
+    pick(v("TRB"), v("TR"), [[-1, 128]], A.not_equal, 2048.0, 0, 1)
     act(v("tk"), v("tj"), F.Identity, 1.0, -2.0)
     ts(v("tbl", 0, 1), v("pc", 0, 1), 11.5, A.is_lt, 128.0, A.mult)
     ts(v("tbl", 0, 1), v("tbl", 0, 1), -64.0, A.add)
@@ -382,88 +417,88 @@ def rank_program(g, core, T, topo):
     for k in range(12):
         if k >= 10:
             load(v("tbl", 1 << k, 2 << k), v("tbl", 0, 1 << k), 1.5)
-            load(v("tbl", 1 << k, 2 << k), v("tbl", 0, 1 << k), 0.5, (k, 12))
+            load(v("tbl", 1 << k, 2 << k), v("tbl", 0, 1 << k), 0.5, (slice(k, 128, 16), slice(12, 128, 16)))
             continue
         for c in range(0, 1 << k, 512):
             n = min(1 << k, 512)
             times(v("tbl", (1 << k) + c, (1 << k) + c + n), v("tbl", c, c + n), v("tk", k, k + 1))
-    act(v("TR0"), v("one", 0, L), F.Identity, -65536.0, v("pc", 1, 2))
+    act(v("TR0"), v("one", 0, L), F.Identity, -2 * AOFF, v("pc", 1, 2))
     for t in range(RO - 2):
         load(v("TR%d" % (t + 1), SL, L), v("TR0", SL, L), 1.0)
         for d in range(N):
             load(slot(d, "wint", t), v("TR0", 0, CAP), 1.0)
     for c in range(0, H, 1024):
         move(v("tab", W + c, W + c + 1024), v("sn0", c, c + 1024), 255.0, -1.0)
-    if MOD0:
-        vset(v("tab", W + H, W + H + L), 0.0)
-    else:
-        again()
 
     move(v("frc", 0, L), v("fr0", 0, L), 255.0, -1.0)
     move(v("frc", L), v("fr0", L, 3 * L), 255.0, -1.0)
+    later = {}
     for t in range(RO):
         def fill(a, b, t=t):
             return v("frc" if t < RO - 1 else "fr0", t * L + a, t * L + b)
         load(slot(me, "win", t), fill(me * CAP, me * CAP + CAP), 1.0)
         load(v("L%d" % (t + 1), SL, L), fill(SL, L), 1.0)
-        snd = fused(lambda d, fill=fill: fill(d * CAP, d * CAP + CAP), lambda d, t=t: slot(me, "win", t), "rarr%d" % t, "rloc%d" % t)
-        got("rarr%d" % t, [slot(s, "win", t) for s in others], snd, 12.0)
+
+        def refills(snd, behind=(), t=t, fill=fill):
+            snd = fused(lambda d: fill(d * CAP, d * CAP + CAP), lambda d: slot(me, "win", t), "rarr%d" % t, "rloc%d" % t,
+                        after=snd, behind=behind)
+            if not t:
+                ops[snd]["cost"] = (FCALL, 0, "e")
+            got("rarr%d" % t, [slot(s, "win", t) for s in others], snd, RLAG if t else FLAG)
+        if not t:
+            refills(None)
+        else:
+            later[t - 1] = refills
 
     setup[0] = False
 
-    def group(out, lhsT, rhs, parts, by=0):
-        if FIRST:
-            mm(out, lhsT, rhs, True, False)
-            if by:
-                mms([x + (False, False) for x in parts[:1]])
-                parts = parts[1:]
-            return mms([x + (False, n == len(parts) - 1) for n, x in enumerate(parts)])
-        if not by:
-            return mms([x + (n == 0, False) for n, x in enumerate(parts)] + [(out, lhsT, rhs, False, True)])
+    def group(out, lhsT, rhs, parts, by=()):
         mm(out, lhsT, rhs, True, False)
-        k = len(parts) % by
-        if k:
-            mms([x + (False, False) for x in parts[:k]])
-        for n in range(k, len(parts), by):
-            mms([x + (False, False) for x in parts[n:n + by]] +
-                [(out, v("I"), v("zero", 0, ncol(out)), False, True)] * (n + by == len(parts)))
+        for n in by:
+            mms([x + (False, False) for x in parts[:n]])
+            parts = parts[n:]
+        if parts[-1][0][2] - parts[-1][0][1] < 128:
+            parts = parts + [(out[:4] + (out[3] + 2, 1), v("I"), v("zero", 0, 2))]
+        return mms([x + (False, n == len(parts) - 1) for n, x in enumerate(parts)])
 
-    def tolist(name, a, n, step, out):
+    def tolist(name, a, n, step, out, by="C8"):
         b = nb()
         group(ps(0, 8 * n, k=b), v("I"), v("Mk", 0, 8 * n),
-              [(ps(n * c, n * c + n, k=b), halves("C8", c), v(name, a, a + (n - 1) * step + 1, step)) for c in range(8)])
+              [(ps(n * c, n * c + n, k=b), halves(by, c), v(name, a, a + (n - 1) * step + 1, step)) for c in range(8)])
         scan(out, v("rm8", 0, 8 * n), ps(0, 8 * n, k=b), A.min)
 
     def ends(name, h):
         return v(name, 8 * h + 7, 128, 16)
 
-    def sums(b, cols, name, c, w, n=128):
-        return [(ps(*cols(i), p0=a, p1=a + n, k=b), v(name, c + 16 * a + i, c + 16 * (a + n), 16), w)
-                for a in range(0, 128, n) for i in range(16)]
+    def sums(b, cols, name, c, w, cuts):
+        return [(ps(*cols(i), p0=a, p1=e, k=b), v(name, c + 16 * a + i, c + 16 * e, 16), w)
+                for a, e in zip((0,) + cuts, cuts + (128,)) for i in range(16)]
 
-    def lowest(shift, k=""):
-        gather("X", v("FT0" + k), v("tbl"), v("WA" + k))
+    def lowest(shift, own):
+        tolist("XC", 16, 16, 1, v("TS"), "C8p")
+        for h in range(2):
+            ts(halves("WA", h, 8), ends("TS", h), shift, A.add, 4096.0, A.min)
+        gather("X", v("FT0"), v("tbl"), v("WA"))
         if PAR:
-            gather("X", v("FT1" + k), v("tbl"), v("WA" + k), (0.0, v("pc", 6, 7)))
+            gather("X", v("FT1"), v("tbl"), v("WA"), (0.0, v("pc", 6, 7)))
         else:
-            times(v("FT1" + k), v("FT0" + k), v("pc", 6, 7))
+            times(v("FT1"), v("FT0"), v("pc", 6, 7))
         for pair in range(4):
             b, p = nb(), 32 * pair
             parts = []
             for odd in range(2):
                 for lc in range(2):
                     for blk in range(2):
-                        c, o, e = lc * 128 + blk * 64, (odd * 2 + lc) * 64, p + 16 + 16 * odd
-                        parts.append((ps(o, o + 64, p0=64 * blk, p1=64 * blk + 64, k=b), v("FT%d" % odd + k, c, c + 64, p0=p, p1=e),
-                                      v("FT0" + k, c, c + 64, p0=p, p1=e)))
-            mms([x + (True, True) for x in parts])
-            scan(halves("SCW" + k, pair, 256), v("mkc"), ps(0, 256, k=b), A.add)
-        ts(v("zn" + k), v("SCW" + k, 63, 1024, 64), -(1 << 20) - 15.0 * 4096, A.add, v("pc", 7, 8), A.min)
-        for h in range(2):
-            tt(halves("XZ" + k, h, 8), v("zn" + k, h, 16, 2), halves("XC", 2 + h, 8), A.max)
-        tolist("XZ" + k, 0, 16, 1, v("ZS" + k))
-        for h in range(2):
-            ts(halves("WL" + k, h, 8), ends("ZS" + k, h), shift, A.add)
+                        c, o, e = lc * 128 + blk * 64, odd * 128, p + 16 + 16 * odd
+                        parts.append((ps(o + lc, o + 128, 2, p0=64 * blk, p1=64 * blk + 64, k=b), v("FT%d" % odd, c, c + 64, p0=p, p1=e),
+                                      v("FT0", c, c + 64, p0=p, p1=e)))
+            group(ps(0, 256, k=b), v("I"), v("mkw"), parts, () if PAR else (4,))
+            relu(halves("EW", pair, 256), ps(0, 256, k=b), -57344.0, "X")
+        b = nb()
+        group(ps(0, 16, k=b), v("I"), v("zero", 0, 16), [(ps(8 * h, 8 * h + 8, k=b), v("I"), own(h)) for h in range(2)] +
+              [(ps(8 * lc + c, 8 * lc + 8, 4, k=b), v("EW", 2 * c + lc, 1024, 8), v("sel")) for lc in range(2) for c in range(4)], (2,))
+        for c in range(4):
+            ts(v("WL", c, 16, 4), ps(c, 16, 4, k=b), v("pc", 8 + c, 9 + c), A.min, shift, A.add)
 
     mine = (me * CAP, me * CAP + CAP)
     order = (0, 1)
@@ -471,51 +506,56 @@ def rank_program(g, core, T, topo):
         last = t == RO - 1
         Lt, Ln = "L%d" % t if t else "fm0", "L%d" % (t + 1)
         main[0], turn[0] = True, t
-        soon = t and LITE
-        if soon:
+        if t:
             b = nb()
             mm(ps(0, 128, p1=32, k=b), halves(Lt, 7, 32), v("nI"))
             move(v("mT", 256, 384, p1=32), ps(0, 128, p1=32, k=b), 255.0)
         b = nb()
         lanesums(b, [halves(Lt, blk, 64) for blk in range(4)])
         if t:
-            tt(v("au", p1=64), ps(0, 128, p1=64, k=b), v("cA", p1=64), A.add)
+            ts(v("au"), ps(0, 64, k=b), v("pc", 12, 13), A.add)
         else:
-            ts(v("au", 0, 64, p1=64), ps(0, 64, p1=64, k=b), -1.0, A.mult)
-            ts(v("au", 64, 128, p1=64), ps(64, 128, p1=64, k=b), -1.0, A.mult, v("pc", 4, 5, p1=64), A.add)
-        ts(v("am", p1=64), v("au", p1=64), 4095, A.bitwise_and)
-        tt(v("up", p1=64), v("am", 0, 64, p1=64), v("am", 64, 128, p1=64), A.mult)
+            ts(v("au"), ps(0, 64, k=b), -1.0, A.mult, v("pc", 4, 5), A.add)
+        ts(v("am"), v("au"), 4095, A.bitwise_and)
+        o = ops[tt(v("up", p1=64), v("am", p1=64), v("am", p0=64), A.mult)]
+        o.update(drain=True, lag=0.01, cost=(LAG,) + o["cost"][1:])
         for h in order:
             b = nb()
             mm(ps(0, 128, k=b), halves(Lt, h), v("nI" if t else "I"))
             move(halves("mT", h), ps(0, 128, k=b), 255.0 if t else 0.0)
-            b = nb()
-            mms([(ps(64 * blk, 64 * blk + 64, k=b), v("EX", 256 * h + 128 * blk, 256 * h + 128 * blk + 128, p1=64), v("up", p1=64),
-                  True, True) for blk in range(2)])
-            tc(halves("ci", h), ps(0, 128, k=b))
-            ts(halves("cj", h), halves("ci", h), 5, A.arith_shift_right, 2047, A.bitwise_and)
-            tc(halves("CL", h), halves("cj", h))
+            for blks in ((0,), (1,)) if QUART[h] else ((0, 1),):
+                b, a, n = nb(), 128 * h + 64 * blks[0], 64 * len(blks)
+                mms([(ps(64 * k, 64 * k + 64, k=b), v("EX", 256 * h + 128 * blk, 256 * h + 128 * blk + 128, p1=64), v("up", p1=64),
+                      True, True) for k, blk in enumerate(blks)])
+                tc(v("ci", a, a + n), ps(0, n, k=b))
+                ts(v("cj", a, a + n), v("ci", a, a + n), 5, A.arith_shift_right, 2047, A.bitwise_and)
+                tc(v("CL", a, a + n), v("cj", a, a + n))
             ts(halves("cf", h), halves("CL", h), 0.0, A.add)
             move(mp(h), halves(Lt, h), *((255.0, -1.0) if t else ()))
         for h in order:
-            for q in range(4 * h, 4 * h + 4):
-                a, c = (0, 256) if soon and q == 7 else (q % 4, q // 4 * 128)
-                x, e, mr, off = halves("X", q, 512), halves("E", q, 512), halves("MR", q, 512), halves("CL", q, 32)
-                mt, rp = v("mT", c, c + 128, p0=32 * a, p1=32 * a + 32), v("Rep", p0=32 * a, p1=32 * a + 32)
+            for kind, q, a, n in chunks(EB if t else EB0, h):
+                p, c = (0, 256) if t and q == 7 else (32 * (q % 4), q // 4 * 128)
+                x, e, mr, off = wide("X", a, n), wide("E", a, n), wide("MR", a, n), v("CL", a, a + n)
+                mt, rp = v("mT", c, c + 128, p0=p, p1=p + 32), rep(p, a, n)
                 b = nb()
-                if EB[q] == "A":
-                    mm(ps(0, 512, k=b), mt, rp)
-                    move(mr, ps(0, 512, k=b), q=MRQ)
+                out = ps(0, 16 * n, k=b)
+                if kind == "A" and t and str(q) in DIRECT:
+                    mms([(ps(j, 16 * n, 16, k=b), v("nI"), v(Lt, a, a + n), True, True) for j in range(16)])
+                    move(mr, out, 255.0)
+                    gatherop(e, LM, off, mr, A.is_gt)
+                elif kind == "A":
+                    mm(out, mt, rp)
+                    move(mr, out)
                     gatherop(e, LM, off, mr, A.is_gt)
                 else:
-                    gather("S", x, LM, off)
-                    mm(ps(0, 512, k=b), mt, rp, True, False)
-                    mm(ps(0, 512, k=b), v("nI"), x, False, True)
-                    act(e, ps(0, 512, k=b), F.Relu, 0.0, -1.0)
+                    gather(kind, x, LM, off)
+                    mm(out, mt, rp, True, False)
+                    mm(out, v("nI"), x, False, True)
+                    under(e, out, kind)
             b = nb()
             group(ps(0, 272, k=b), halves("cf", h), v("JR"),
-                  [(ps(0, 272, 17, k=b), v("I"), v("K17"))] + sums(b, lambda i: (16 - i, 272, 17), "E", 2048 * h, v("NP"), BY[0][h]),
-                  int(FIRST))
+                  [(ps(0, 272, 17, k=b), v("I"), v("K17"))] + sums(b, lambda i: (16 - i, 272, 17), "E", 2048 * h, v("NP"), CUTS[h]),
+                  (1,) + (16,) * len(CUTS[h]))
             move(halves("SD", h, 136), ps(136, 272, k=b))
             scan(halves("GV", h, 136), ps(0, 136, k=b), halves("SD", h, 136), A.max, A.min)
             tolist("GV", 136 * h + 16, 8, 17, halves("GS", h, 64))
@@ -524,7 +564,7 @@ def rank_program(g, core, T, topo):
             gather("X", halves("xg", h), LM, gl)
             gather("V", halves("TG", h), TL, gl)
             b = nb()
-            mm(ps(0, 128, k=b), mp(h), v("nI"), True, False)
+            mm(ps(0, 128, k=b), v("nI"), halves("mT", h), True, False)
             mm(ps(0, 128, k=b), halves("xg", h), v("I"), False, True)
             move(halves("qT", h), ps(0, 128, k=b))
         main[0] = False
@@ -537,76 +577,94 @@ def rank_program(g, core, T, topo):
         else:
             ts(v("XC", 16, 32), gv, 2048.0, A.add, 2048.0, A.min)
             for h in order:
-                ts(halves("WA", h, 8), v("GS", 64 * h + 7, 64 * h + 64, 8), 2048.0, A.add, 2048.0, A.min)
-            lowest(0.0)
+                ts(halves("WO", h, 8), v("GS", 64 * h + 7, 64 * h + 64, 8), 2048.0, A.add, 2048.0, A.min)
+            lowest(0.0, lambda h: halves("WO", h, 8))
             for blk in range(3, -1, -1):
                 c = PH * (blk // 2) + 64 * (blk % 2)
                 scatter(v("LO"), halves("WL", blk, 4), v("P", c, c + 64))
         if t < RO - 2:
-            gather("X", v("TGp"), TL, v("GL"), (-8192.0, 1.0))
+            gather("X", v("TGp"), TL, v("GL"), (-16384.0, 1.0))
         if not last:
             b, b2 = nb(), nb()
             tc(v("ui", p1=32), v("up", p1=32))
             ts(v("uj", p1=32), v("ui", p1=32), 5, A.arith_shift_right, 4095, A.bitwise_and)
-            ts(v("a12", p1=32), v("uj", p1=32), -16384.0, A.add)
-            mms([(ps(64 * blk, 64 * blk + 64, k=b), v("EX", 128 * blk, 128 * blk + 128, p1=32), v("a12", p1=32), True, True)
+            ts(v("a12", p1=32), v("uj", p1=32), -2048.0, A.add)
+            mms([(ps(64 * blk, 64 * blk + 64, k=b), v("EA", 128 * blk, 128 * blk + 128, p1=33), v("a12", p1=33), True, True)
                  for blk in range(4)])
             tt(ps(0, 256, k=b2), v("TR%d" % t), ps(0, 256, k=b), A.max)
             tt(v("CT"), v("xtl", 0, L), ps(0, 256, k=b2), A.min)
             ts(v("CTm"), v("CT"), 4095, A.bitwise_and)
         main[0] = True
         for h in order:
-            for q in range(4 * h, 4 * h + 4):
-                a = q % 4
-                y, p = halves("Y", q, 512), prod(q)
-                gather(GD[q], y, v("xmo"), halves("TG", q, 32))
+            for kind, q, a, n in chunks(GD, h):
+                y, p, r = wide("Y", a, n), prod(a, n), 32 * (q % 4)
+                gather(kind, y, v("xmo"), v("TG", a, a + n))
                 b = nb()
-                two = [(v("nI"), y), (v("qT", h * 128, h * 128 + 128, p0=32 * a, p1=32 * a + 32), v("Rep", p0=32 * a, p1=32 * a + 32))]
-                for n, x in enumerate(two if YQ[q] == "Y" else two[::-1]):
-                    mm(ps(0, 512, k=b), x[0], x[1], n == 0, n == 1)
-                relu(p, ps(0, 512, k=b), 255.0, ED[q])
+                two = [(v("nI"), y), (v("qT", h * 128, h * 128 + 128, p0=r, p1=r + 32), rep(r, a, n))]
+                for k, x in enumerate(two if YQ[q] == "Y" else two[::-1]):
+                    mm(ps(0, 16 * n, k=b), x[0], x[1], k == 0, k == 1)
+                relu(p, ps(0, 16 * n, k=b), 255.0, kind)
             b = nb()
-            if TWO:
-                mms([x + (True, True) for x in sums(b, lambda i: (i, 256, 16), "P", PH * h + 128, v("Wp"))])
-                for z in range(2):
-                    c = 256 * h + 128 * z
-                    tt(v("hi", c, c + 128), ps(128 * z, 128 * z + 128, k=b), halves("cT", z), A.add)
-                    ts(v("hm", c, c + 128), v("hi", c, c + 128), 4095, A.bitwise_and)
-                    c, u = 2 * h + z, v("hm", c, c + 64)
-                    tt(halves("hp", c, 64), u, halves("hm", 2 * c + 1, 64), A.mult)
-                    ts(halves("hq", c, 64), halves("hp", c, 64), 5, A.arith_shift_right, 2047, A.bitwise_and)
-                    if t or not MOD0:
-                        tt(halves("lo", c, 64), u, halves("hq", c, 64), A.add)
-                    else:
-                        tt(halves("hp", c, 64), u, halves("hq", c, 64), A.add)
-                        ts(halves("hq", c, 64), halves("hp", c, 64), 2047, A.bitwise_and)
-                        tc(halves("lo", c, 64), halves("hq", c, 64))
-            else:
-                mms([x + (True, True) for x in sums(b, lambda i: (i, 256, 16), "P", PH * h + 128, v("Wt"))])
-                tt(halves("hi", h, 256), ps(0, 256, k=b), v("cT"), A.add)
-                ts(halves("hm", h, 256), halves("hi", h, 256), 4095, A.bitwise_and)
-                u = halves("hm", 2 * h)
-                tt(halves("hp", h), u, halves("hm", 2 * h + 1), A.mult)
-                ts(halves("hq", h), halves("hp", h), 5, A.arith_shift_right, 2047, A.bitwise_and)
-                tt(halves("lo", h), u, halves("hq", h), A.add)
-            b = nb()
-            mm(ps(0, 128, k=b), halves("lo", h), v("If"))
-            tc(halves("HL", h), ps(0, 128, k=b))
-        for h in order:
-            for q in range(4 * h, 4 * h + 4):
-                ne, p, sx = halves("NE", q, 512), prod(q), halves("SX", q, 512)
-                SN = v("tab", W) if t or not MOD0 else v("tab", W, W + H)
-                if SE[q ^ 4 * order[0]] == "V":
-                    gatherop(ne, SN, halves("HL", q, 32), p, A.not_equal)
+            parts = sums(b, lambda i: (i, 256, 16), "P", PH * h + 128, v("Wp"), CUTS[2 + h])
+            for n in range(0, len(parts), 16):
+                mms([x + (True, True) for x in parts[n:n + 16]])
+            for z in range(2):
+                c = 256 * h + 128 * z
+                tt(v("hi", c, c + 128), ps(128 * z, 128 * z + 128, k=b), halves("cT", z), A.add)
+                ts(v("hm", c, c + 128), v("hi", c, c + 128), 4095, A.bitwise_and)
+                c, u = 2 * h + z, v("hm", c, c + 64)
+                if t and HF:
+                    tt(halves("hf", c, 64), u, halves("hm", 2 * c + 1, 64), A.mult)
+                    ts(halves("hn", c, 64), halves("hf", c, 64), MAGIC * 65536, A.add, -MAGIC * 65536, A.add)
+                    ts(halves("uf", c, 64), u, -2048.0, A.add)
+                    continue
+                tt(halves("hp", c, 64), u, halves("hm", 2 * c + 1, 64), A.mult)
+                ts(halves("hq", c, 64), halves("hp", c, 64), 5, A.arith_shift_right, 2047, A.bitwise_and)
+                if not t:
+                    tt(halves("hr", c, 64), u, halves("hq", c, 64), A.add)
+                    ts(halves("hs", c, 64), halves("hr", c, 64), 2047, A.bitwise_and)
+                    tc(halves("hh", c, 64), halves("hs", c, 64))
+                elif HT:
+                    tc(halves("hh", c, 64), halves("hq", c, 64))
+                    ts(halves("uf", c, 64), u, -2048.0, A.add)
                 else:
-                    gather("S", sx, SN, halves("HL", q, 32))
-                    b = nb()
-                    mm(ps(0, 512, k=b), v("nI"), p, True, False)
-                    mm(ps(0, 512, k=b), v("I"), sx, False, True)
-                    act(ne, ps(0, 512, k=b), F.Abs)
+                    tt(halves("lo", c, 64), u, halves("hq", c, 64), A.add)
             b = nb()
-            group(ps(0, 128, k=b), v("I"), v("k8"), sums(b, lambda i: (i, 128, 16), "NE", 2048 * h, v("PB8"), BY[2][h]))
-            scan(back(halves("SC2", h)), back(ps(0, 128, k=b)), back(halves("lo", h)), A.add)
+            if t and HF:
+                three = (("hf", "If"), ("hn", "n32"), ("uf", "I"))
+                mm(ps(0, 128, k=b), halves("hf", h), v("If"), True, False)
+                mms([(ps(0, 128, k=b), halves(x, h), v(y), False, x == "uf") for x, y in three[1:]])
+                ts(halves("HL", h), ps(0, 128, k=b), 3072 - 15.5 / 32, A.add)
+                b = nb()
+                mms([(ps(0, 128, k=b), v(y), halves(x, h), x == "hf", x == "uf") for x, y in three])
+                move(halves("lo", h), ps(0, 128, k=b), 4096 - 15.5 / 32)
+            elif t and HT:
+                mm(ps(0, 128, k=b), halves("uf", h), v("I"), True, False)
+                mm(ps(0, 128, k=b), halves("hh", h), v("I"), False, True)
+                ts(halves("HL", h), ps(0, 128, k=b), 2048.0, A.add)
+                b = nb()
+                mm(ps(0, 128, k=b), v("I"), halves("uf", h), True, False)
+                mm(ps(0, 128, k=b), v("I"), halves("hh", h), False, True)
+                move(halves("lo", h), ps(0, 128, k=b), 2048.0)
+            else:
+                mm(ps(0, 128, k=b), halves("lo" if t else "hh", h), v("If" if t else "I"))
+                tc(halves("HL", h), ps(0, 128, k=b))
+        SN = v("tab", W + 1024, W + 7168) if t and HF else v("tab", W, W + copies[t] * H)
+        for h in order:
+            for kind, q, a, n in chunks(SE, h):
+                ne, p, sx, off = wide("NE", a, n), prod(a, n), wide("SX", a, n), v("HL", a, a + n)
+                if kind == "V":
+                    gatherop(ne, SN, off, p, A.not_equal)
+                else:
+                    gather(kind, sx, SN, off)
+                    b = nb()
+                    mm(ps(0, 16 * n, k=b), v("nI"), p, True, False)
+                    mm(ps(0, 16 * n, k=b), v("I"), sx, False, True)
+                    differs(ne, ps(0, 16 * n, k=b), kind)
+            b = nb()
+            group(ps(0, 128, k=b), v("I"), v("k8"), sums(b, lambda i: (i, 128, 16), "NE", 2048 * h, v("PB8"), CUTS[4 + h]),
+                  (16,) * len(CUTS[4 + h]))
+            scan(back(halves("SC2", h)), back(ps(0, 128, k=b)), back(halves("lo" if t else "hh", h)), A.add)
         tt(v("key"), v("SC2", 0, 256, 16), v("capU"), A.min)
         ts(v("dd"), v("key"), (1 << 24) + (1 << 17) + 3, A.bitwise_and)
         for d in range(N):
@@ -621,7 +679,7 @@ def rank_program(g, core, T, topo):
             tc(halves("SLL", h, 8), ends("SS", h))
         ts(v("fp"), v("key"), 13, A.arith_shift_right)
         ts(v("XC", 0, 16), v("fp"), v("pc", 2, 3), A.add)
-        n = 16 if last or not JOIN else 32
+        n = 16 if last else 32
         if not last:
             ts(v("t1"), v("key"), (1 << 17) + 2047, A.bitwise_and)
             tt(v("XC", 16, 32), v("t1"), v("capT"), A.min)
@@ -629,37 +687,35 @@ def rank_program(g, core, T, topo):
         for h in range(2):
             ts(halves("CHL", h, 8), v("CS", 8 * h + 7, 8 * n, n), 2048.0, A.add)
             gather("X", halves("CH", h), v("P", PH * h, PH * h + PH + 16), halves("CHL", h, 8), last and (255.0, -1.0))
-        if not last:
-            if not JOIN:
-                tolist("XC", 16, 16, 1, v("TS"))
-            for h in range(2):
-                ts(halves("WA", h, 8), v("CS", 8 * h + 23, 256, 32) if JOIN else ends("TS", h), 2048.0, A.add, 4096.0, A.min)
         scatter(v("win%d" % t), v("SLL"), v("CH"))
-        snd = fused(lambda d, t=t: slot(d, "win", t), lambda d, Ln=Ln: v(Ln, mine[0], mine[1]), "arr%d" % t, "loc%d" % t)
+        snd = fused(lambda d, t=t: slot(d, "win", t), lambda d, Ln=Ln: v(Ln, mine[0], mine[1]), "arr%d" % t, "loc%d" % t, TWOCALL)
         move(v(Ln, mine[0], mine[1]), slot(me, "win", t))
-        got("arr%d" % t, [v(Ln, s * CAP, s * CAP + CAP) for s in others], snd, XLAG)
+        here = [("here%d" % t, 0, 128, 0, 1, 1)]
+        got("arr%d" % t, [v(Ln, s * CAP, s * CAP + CAP) for s in others] + here, snd, XLAG, TWOCALL)
         main[0] = False
         if t < RO - 2:
             TR = "TR%d" % (t + 1)
-            ts(v("IV"), v("fp"), 0.0, A.add)
+            ts(halves("IV", 0, 16), v("fp"), 0.0, A.max, 16.0, A.min)
+            tt(halves("IV", 1, 16), halves("IV", 0, 16), halves("IV", 0, 16), A.mult)
             b = nb()
-            for h in range(2):
-                mm(ps(128 * h, 128 * h + 128, p1=8, k=b), halves("IV", h, 8), v("Ih"))
-            move(v("XI", p1=8), ps(0, 256, p1=8, k=b))
+            mm(ps(0, 128, p1=32, k=b), v("IV"), v("I"))
+            move(v("T1", p1=32), ps(0, 128, p1=32, k=b))
             b = nb()
-            mm(ps(0, 256, k=b), v("R8", p1=8), v("XI", p1=8))
-            ts(v("mk"), ps(0, 256, k=b), v("pc", 0, 1), A.is_equal, -65536.0, A.mult)
-            scatter(v("wint%d" % t), v("SLL"), v("TGp"), v("mk"))
-            snd = fused(lambda d, t=t: slot(d, "wint", t), lambda d, TR=TR: v(TR, mine[0], mine[1]), "tarr%d" % t, "tloc%d" % t)
+            mms([(ps(128 * h, 128 * h + 128, k=b), v("EM", 128 * h, 128 * h + 128, p1=32), v("T1", p1=32), True, True) for h in range(2)])
+            act(v("mk"), ps(0, 256, k=b), F.Relu, v("pc", 14, 15), 2 * AOFF)
+            scatter(v("wint%d" % t), v("SLL"), v("TGp"), v("mk"), A.subtract)
+            snd = fused(lambda d, t=t: slot(d, "wint", t), lambda d, TR=TR: v(TR, mine[0], mine[1]), "tarr%d" % t, "tloc%d" % t,
+                        behind=here)
             act(v(TR, mine[0], mine[1]), slot(me, "wint", t))
             got("tarr%d" % t, [v(TR, s * CAP, s * CAP + CAP) for s in others], snd, XLAG + 1.0)
         if not last:
+            later[t](snd, here)
             main[0] = True
-            lowest(2048.0)
+            lowest(2048.0, lambda h: v("CS", 8 * h + 23, 256, 32))
             for blk in range(3, -1, -1):
                 scatter(v("tab", 0, W + H + L), halves("WL", blk, 4), halves("CH", blk, 64))
             main[0] = False
-            again()
+            again(copies[t + 1])
             if t == RO - 2:
                 load(v("LO", 0, W), LM, 3.0)
             for blk in range(3, -1, -1):
@@ -673,6 +729,9 @@ def rank_program(g, core, T, topo):
 def _plan(ops, deps, bank):
     nop = len(ops)
     post = [[] for _ in ops]
+
+    def more(lag):
+        return lag + LAG1 - LAG if 0 < lag < 1 else lag * LONGER
     for j in range(nop):
         for i, kind in deps[j].items():
             post[i].append((j, ops[j]["lag"] if ops[j]["q"] == "R" else ops[i]["lag"] if kind > 1 and ops[i]["q"] != "R" else 0.0))
@@ -809,18 +868,32 @@ def _plan(ops, deps, bank):
     pre = [[] for _ in ops]
     for i in range(nop):
         for j, lag in post[i]:
-            pre[j].append((i, lag, deps[j][i] == 1.5))
+            pre[j].append((i, lag, deps[j][i] == 1.5, more(lag)))
+    above = [0] * nop
+    for j in range(nop):
+        for x in pre[j]:
+            above[j] |= above[x[0]] | 1 << x[0]
+        pre[j] = [x for x in pre[j] if x[1] > 1 or not any(above[y[0]] >> x[0] & 1 and not y[2] and y[1] >= x[1] for y in pre[j])]
     c0, c1 = costs
     opn = [opens.get(i) for i in range(nop)]
     cls = [closes.get(i) for i in range(nop)]
 
-    def play(order, on, head=None, tail=None):
-        if head:
+    def play(order, on, head=None, tail=None, same=0):
+        snaps = []
+        if same:
+            same -= same % 16
+            snaps = head[9][:same // 16]
+            (e0, e1), (w0, w1), (last, free) = [[x.copy() for x in y] for y in (head[5], head[6], head[9][same // 16])]
+            banks, after = head[3].copy(), head[4].copy()
+        elif head:
             (e0, e1), (w0, w1), (last, free), banks, after = [[x.copy() for x in y] for y in head[5:8]] + [head[3].copy(), {}]
         else:
             e0, e1, w0, w1 = [0.0] * nop, [0.0] * nop, [None] * nop, [None] * nop
             last, free, banks, after = {}, [(0.0, k, None) for k in range(8)], {}, {}
-        for i in order:
+        for n in range(same, len(order)):
+            i = order[n]
+            if not n & 15:
+                snaps.append((last.copy(), free.copy()))
             q = on[i]
             s0 = s1 = 0.0
             a = b = None
@@ -829,13 +902,13 @@ def _plan(ops, deps, bank):
                 if j is not None:
                     s0, s1, a, b = e0[j], e1[j], j, j
                 last[q] = i
-            for j, lag, soft in pre[i]:
-                if soft and on[j] == q:
+            for j, lag, soft, lag1 in pre[i]:
+                if soft and on[j] == q == "V":
                     continue
                 x = e0[j] + lag
                 if x > s0:
                     s0, a = x, j
-                x = e1[j] + lag
+                x = e1[j] + lag1
                 if x > s1:
                     s1, b = x, j
             if opn[i] is not None:
@@ -848,8 +921,8 @@ def _plan(ops, deps, bank):
                 if j is not None:
                     if e0[j] + LAG > s0:
                         s0, a = e0[j] + LAG, j
-                    if e1[j] + LAG > s1:
-                        s1, b = e1[j] + LAG, j
+                    if e1[j] + LAG1 > s1:
+                        s1, b = e1[j] + LAG1, j
             k = i + nop if q == "S" else i
             e0[i], e1[i], w0[i], w1[i] = s0 + c0[k], s1 + c1[k], a, b
             if cls[i]:
@@ -859,11 +932,11 @@ def _plan(ops, deps, bank):
         for k, e in enumerate((e0, e1)):
             if tail:
                 out = [(e[i] + x[k], i) for i, x in tail[0]] + [(e[last[q]] + x[k], last[q]) for q, x in tail[1] if q in last]
-                out += [(e[f[2]] + LAG + x[k], f[2]) for f, x in zip(sorted(free), tail[2]) if f[2] is not None]
+                out += [(e[f[2]] + (LAG, LAG1)[k] + x[k], f[2]) for f, x in zip(sorted(free), tail[2]) if f[2] is not None]
                 ends.append(max(out))
             else:
                 ends.append(max((e[i], i) for i in order[-60:]) if order else (0.0, 0))
-        return 1.5 * ends[0][0] + ends[1][0], order, on, banks, after, (e0, e1), (w0, w1), (last, free), ends
+        return WEIGH * ends[0][0] + ends[1][0], order, on, banks, after, (e0, e1), (w0, w1), (last, free), ends, snaps
 
     def rest(p, hi):
         order, on, after = p[1], p[2], p[4]
@@ -872,14 +945,14 @@ def _plan(ops, deps, bank):
             q, k = on[i], i + nop * (on[i] == "S")
             x, y = nxt.get(q, (0.0, 0.0)) if q != "R" else (0.0, 0.0), t.pop(i, (0.0, 0.0))
             x = nxt[q] = (max(x[0], y[0]) + c0[k], max(x[1], y[1]) + c1[k])
-            arcs = [(j, lag) for j, lag, soft in pre[i] if not (soft and on[j] == q)]
+            arcs = [(j, lag, lag1) for j, lag, soft, lag1 in pre[i] if not (soft and on[j] == q == "V")]
             if after.get(i) in later:
-                arcs.append((after[i], LAG))
+                arcs.append((after[i], LAG, LAG1))
             elif opn[i] is not None:
                 takers.append(x)
-            for j, lag in arcs:
+            for j, lag, lag1 in arcs:
                 y = t.get(j, (0.0, 0.0))
-                t[j] = (max(y[0], x[0] + lag), max(y[1], x[1] + lag))
+                t[j] = (max(y[0], x[0] + lag), max(y[1], x[1] + lag1))
         nxt.pop("R", None)
         return list(t.items()), list(nxt.items()), takers[::-1]
 
@@ -887,7 +960,7 @@ def _plan(ops, deps, bank):
         w = p[6][k]
         i, out = p[8][k][1], []
         while w[i] in inside:
-            if all(x[0] != w[i] or x[2] and p[2][i] == p[2][w[i]] for x in pre[i]):
+            if all(x[0] != w[i] or x[2] and p[2][i] == p[2][w[i]] == "V" for x in pre[i]):
                 out.append((w[i], i))
             i = w[i]
         return out
@@ -948,10 +1021,14 @@ def _plan(ops, deps, bank):
                 on = list(on)
                 on[i] = "S" if on[i] == "V" else "V"
             elif how % 2:
-                order = ahead(order, j, row[on[i]][max(0, at[i] - far)])
+                i = row[on[i]][max(0, at[i] - far)]
+                order = ahead(order, j, i)
             else:
                 order = behind(order, i, row[on[j]][min(len(row[on[j]]) - 1, at[j] + far)])
-            p = play(order, on, head, tail)
+            if order is now[1] and on is now[2]:
+                continue
+            same = now[1].index(i)
+            p = play(order, on, now, tail, same) if same >= 16 else play(order, on, head, tail)
             z = (z * 1103515245 + 12345) % 2147483648
             if p and p[0] <= now[0] + heat * (1 - n / MENDS) * (z / 2147483648) ** 2:
                 now, arcs = p, None
@@ -974,7 +1051,7 @@ def _plan(ops, deps, bank):
         return keyed(key, on)
 
     def keyed(key, on):
-        left, order = [len(x) for x in preset], []
+        left, order = [len(x) for x in deps], []
         ready = [i for i in range(nop) if not left[i]]
         while ready:
             i = min(ready, key=lambda z: key[z])
@@ -1044,7 +1121,7 @@ def _emit(g, T, ops, bank):
                 if hit:
                     kind = 1 if same and (o["q"] == "T" or bf == "order") else 2
                     if kind == 2 and wr and not wj and LOOSE and o["q"] in "VSX" and ops[j]["q"] in "VSX":
-                        kind = 1 if same else 1.5
+                        kind = 1 if same and o["q"] == "V" else 1.5
                     need[j] = max(need.get(j, 0), kind)
         for (bf, p0, p1, m, wr) in mine:
             old = acc.get(bf, [])
@@ -1071,7 +1148,7 @@ def _emit(g, T, ops, bank):
         k = know[q]
         want = {}
         for j, kind in deps[i].items():
-            if kind == 2 or kind == 1.5 and ops[j]["q"] != q:
+            if kind == 2 or kind == 1.5 and not ops[j]["q"] == q == "V":
                 s, val = tok[j]
                 if k.get(s, 0) < val and (s not in want or want[s][0] < val):
                     want[s] = (val, j)
@@ -1090,6 +1167,9 @@ def _emit(g, T, ops, bank):
             count[s] = count.get(s, 0) + 1
             ins.then_inc(T.sem[s], 1)
             tok[i] = (s, count[s])
+            if o.get("drain"):
+                queue[q].wait_ge(T.sem[s], count[s])
+                k[s] = count[s]
         else:
             tok[i] = (o["sem"], o["val"])
             if q == "D":

from concourse.bass import DstId, RemoteDMATransfer
from concourse.mybir import dt, AluOpType as A, AxisListType, ActivationFunctionType as F

N, W, H, L, CAP, RO, SL = 4, 2048, 2048, 256, 56, 4, 224
DUMP = 256
SW = DUMP + N * 256
PH = 2176
BIG = 67108864.0
NONE = 127 << 17
_B, _F, _H, _I, _U = "bfloat16", "float32", "float16", "int32", "uint16"
_SB = {
    "tab": (3 * H + W + 1024, _B), "xtl": (W + H + L, _I), "xmo": (4096, _B), "sn0": (H, _B), "fm0": (L, _B),
    "fr0": (RO * L, _B), "wk0": (3, _I), "wkf": (4, _F), "frc": (3 * L, _B),
    "win0": (SW, _B), "win1": (SW, _B), "win2": (SW, _B), "win3": (SW, _B), "wint0": (SW, _F), "wint1": (SW, _F),
    "L1": (L, _B), "L2": (L, _B), "L3": (L, _B), "L4": (L, _B), "TR0": (L, _F), "TR1": (L, _F), "TR2": (L, _F),
    "mT": (384, _B), "qT": (L, _B), "au": (64, _I), "am": (64, _I), "up": (64, _F), "ui": (64, _I), "uj": (64, _I),
    "hb": (16, _F), "zm": (16, _F), "capT": (16, _F), "capU": (16, _F), "LO": (W + L, _B), "cT": (256, _F),
    "a12": (64, _H), "ci": (L, _I), "cj": (L, _I), "cf": (L, _H), "MR": (4096, _B), "CL": (L, _U),
    "X": (4096, _B), "E": (4096, _B), "Y": (4096, _B), "P": (2 * PH + 16, _B),
    "NE": (4096, _B), "SX": (4096, _B), "SD": (272, _F), "GV": (272, _H), "GS": (128, _F), "GL": (16, _U), "TG": (L, _U), "xg": (L, _B),
    "hi": (512, _I), "hm": (512, _I), "hp": (256, _I), "hq": (256, _I), "lo": (256, _F), "hh": (256, _H), "uf": (256, _H),
    "hf": (256, _F), "hn": (256, _B), "hr": (256, _I), "hs": (256, _I), "HL": (256, _U), "SC2": (256, _F), "key": (16, _I), "T1": (128, _B),
    "IV": (32, _H), "fp": (16, _I), "XC": (32, _H), "CS": (256, _H), "CHL": (16, _U),
    "CH": (L, _B), "dd": (16, _I), "OH": (80, _B), "S5": (80, _H), "SS": (128, _F), "SLL": (16, _U),
    "TGp": (L, _F), "mk": (L, _F), "CT": (L, _I), "CTm": (L, _I), "t1": (16, _I), "TS": (128, _F),
    "WA": (16, _U), "FT0": (L, _B), "FT1": (L, _B), "EW": (1024, _B), "WL": (16, _U), "WO": (16, _H),
}
_CO = {
    "one": (512, _B), "zero": (272, _B), "I": (128, _B), "nI": (128, _B), "n8": (8, _B), "n32": (128, _B), "If": (128, _F),
    "b8": (8, _B), "t8": (8, _B), "Rep": (512, _B), "R32": (512, _B), "C8": (1024, _B), "i4": (128, _B),
    "TR": (128, _B), "TRB": (128, _B), "JR": (272, _B), "K17": (16, _B), "Et": (96, _B), "Z": (160, _B),
    "EX": (512, _F), "EM": (256, _B), "EA": (512, _B), "Eq": (40, _B),
    "base": (80, _B), "r5": (80, _B), "rm8": (256, _B), "k8": (128, _B), "Mk": (256, _B), "C8p": (1024, _B),
    "mkw": (256, _B), "mki": (128, _B), "sel": (2, _B), "pc": (20, _F), "pi": (8, _I),
    "NP": (16, _B), "PB8": (8, _B), "Wp": (16, _B),
    "lt": (16, _F), "ti": (12, _F), "tj": (12, _F), "tk": (12, _F), "tbl": (4096 + 16, _B),
}
_PACK, _POS = {}, {}
for _k in list(_SB) + list(_CO):
    _n, _t = (_SB.get(_k) or _CO.get(_k))
    if _n <= 64:
        _nn = max(32, (_n + 31) // 32 * 32)
        _o = _PACK.get(_t, 0)
        _POS[_k] = ("pk_" + _t, _o)
        _PACK[_t] = _o + _nn
    else:
        _POS[_k] = ("t_" + _k, 0)
SCRATCH = {}
for _k in list(_SB) + list(_CO):
    _n, _t = (_SB.get(_k) or _CO.get(_k))
    if _n > 64:
        SCRATCH["t_" + _k] = ("sbuf", [128, _n], _t)
for _t, _n in _PACK.items():
    SCRATCH["pk_" + _t] = ("sbuf", [128, _n], _t)
for _k in range(8):
    SCRATCH["ps%d" % _k] = ("psum", [128, 512], "float32")
SEMAPHORES = ["q" + e for e in "VSTG"] + ["ld%d" % i for i in range(54)] + ["st0", "st1"] + \
    ["%s%d" % (p, t) for p in ("arr", "tarr", "rarr", "loc", "tloc", "rloc") for t in range(RO)]

EB0, EB = "AAAXXAXA", "AAAXXAXA"
YQ = "YYQQYQQQ"
SE = "XXVVxVVV"
GD = "XXXXXXXX"
MAGIC = 12582912.0
AOFF = 262144.0
SETS = ({"e": 0.00084, "g": 0.00100, "s": 0.0020, "t": 0.00037}, {"e": 0.00110, "g": 0.00160, "s": 0.0060, "t": 0.00052})
FIX = (0.0, 0.0, 0.0, 0.0)
LOOSE = False
SLOW = 1.2
LAG, TLAG, LAG1, LONGER = 0.26, 0.0, 0.26, 1.3
WEIGH = 1.3
XLAG, CALL, RLAG, FLAG, FCALL = 1.8, 0.6, 5.0, 7.0, 4.0
HF = True
PAR = False
DIRECT = ""
HT = True
CUTS = ((), (96,), (), (96,), (), (96,))
QUART = (True, True)
TWOCALL = True
LOOKS = ((0.2, 2.0, 0.0), (0.2, 2.0, 2.0), (0.25, 1.0, 1.0))
MIX = (0.25,)
SHAKES, SHAKE, SPAN, SEED, SHARE = 50, (0.3, 0.6, 1.2), (2.0, 4.0, 3.0, 7.0), 12345, True
TIE, SKIP = 2, 1
MENDS, HEAT, WIDE, FAR = 6500, (0.9, 0.8, 0.7, 0.6, 0.5, 0.4, 0.3, 0.2, 0.1), 200, (0, 0, 1, 2, 4)
NOTE = {}
PASSES = 6


def rank_program(g, core, T, topo):
    me = T.rank_of(core)
    if me is None:
        return
    others = [(me + 1 + k) % N for k in range(N - 1)]
    ops, bank = [], {}
    main = [False]
    setup = [True]
    turn = [-9]

    def v(name, a=None, b=None, step=1, p0=0, p1=128):
        buf, o = _POS[name]
        n = (_SB.get(name) or _CO.get(name))[0]
        return (buf, p0, p1, o + (a or 0), o + (n if b is None else b), step)

    def ap(x):
        buf = T[bank.get(x[0], x[0])]
        if x[5] == 1:
            return buf[x[1]:x[2], x[3]:x[4]]
        return buf[x[1]:x[2], x[3]:(x[4] if x[4] >= 0 else None):x[5]]

    def ncol(x):
        return len(range(x[3], x[4], x[5]))

    def arg(s):
        return ap(s) if isinstance(s, tuple) else s

    def op(q, fn, rd, wr, cost, sem=None, val=0, lag=LAG, after=None):
        cost = cost if isinstance(cost, tuple) else (cost, 0, "e")
        if isinstance(fn, dict) and cost[2] == "e":
            n = ncol(rd[0])
            cost = vc(n, 0.5 if is2(rd[0]) and is2(wr[0]) else 1.0) + (FIX[2] if inps(rd[0]) else FIX[1], max(64, n), "e")
        ops.append({"q": q, "fn": fn, "rd": rd, "wr": wr, "cost": cost[:3], "costs": cost[-3:],
                    "sem": sem, "val": val, "lag": lag, "after": after, "main": main[0] and len(ops), "round": turn[0]})
        return len(ops) - 1

    def vc(n, f=1.0):
        return (FIX[0], max(64, n * f), "e")

    def inps(x):
        return x[0][:2] == "ps"

    def is2(x):
        return not inps(x) and SCRATCH[x[0]][2] in (_B, _H, _U)

    def tc(out, x):
        f = 0.5 if is2(out) and is2(x) else 1.0
        return op("V", lambda: g.vector.tensor_copy(ap(out), ap(x)), [x], [out], vc(ncol(x), f))

    def tt(out, x, y, o):
        f = 1.0 if inps(x) or inps(y) else 2.0
        return op("V", lambda: g.vector.tensor_tensor(ap(out), ap(x), ap(y), o), [x, y], [out], vc(ncol(x), f))

    def ts(out, x, s1, o1, s2=None, o2=None):
        f = 0.5 if is2(out) and is2(x) else 1.0
        rd = [x] + [s for s in (s1, s2) if isinstance(s, tuple)]
        if o2 is None:
            return op("V", lambda: g.vector.tensor_scalar(ap(out), ap(x), arg(s1), None, o1), rd, [out], vc(ncol(x), f))
        return op("V", lambda: g.vector.tensor_scalar(ap(out), ap(x), arg(s1), arg(s2), o1, o2), rd, [out], vc(ncol(x), f))

    def scan(out, d0, d1, o0, o1=A.max):
        return op("V", lambda: g.vector.tensor_tensor_scan(ap(out), ap(d0), ap(d1), 0.0, o0, o1), [d0, d1], [out], vc(ncol(d1)))

    def vset(out, c):
        return op("V", lambda: g.vector.memset(ap(out), c), [], [out], vc(ncol(out), 0.5))

    def act(out, x, fn=F.Copy, bias=0.0, scale=1.0):
        if setup[0]:
            return move(out, x, bias, scale)
        return op("S", lambda: g.scalar.activation(ap(out), ap(x), fn, bias=arg(bias), scale=arg(scale)),
                  [x] + [s for s in (bias, scale) if isinstance(s, tuple)], [out],
                  (FIX[2] if inps(x) else FIX[1], max(64, ncol(x)), "e"))

    def gather(q, out, win, off, turn=None):
        fn = {"V": lambda: g.vector.tensor_copy(ap(out), ap(win).indirect(ap(off))),
              "S": lambda: g.scalar.activation(ap(out), ap(win).indirect(ap(off)), F.Copy)}
        if turn:
            fn = {"V": lambda: g.vector.tensor_scalar(ap(out), ap(win).indirect(ap(off)), arg(turn[1]), turn[0], A.mult, A.add),
                  "S": lambda: g.scalar.activation(ap(out), ap(win).indirect(ap(off)), F.Identity, bias=turn[0], scale=arg(turn[1]))}
        return op(q, fn, [win, off] + [x for x in turn or () if isinstance(x, tuple)], [out], (0.06, ncol(out), "g"))

    def relu(out, x, c, q):
        return op(q, {"V": lambda: g.vector.tensor_scalar(ap(out), ap(x), c, 0.0, A.add, A.max),
                        "S": lambda: g.scalar.activation(ap(out), ap(x), F.Relu, bias=c)}, [x], [out], (0.1, ncol(x), "e"))

    def under(out, x, q):
        return op(q, {"V": lambda: g.vector.tensor_scalar(ap(out), ap(x), -1.0, 0.0, A.mult, A.max),
                        "S": lambda: g.scalar.activation(ap(out), ap(x), F.Relu, scale=-1.0)}, [x], [out], (0.1, ncol(x), "e"))

    def differs(out, x, q):
        return op(q, {"V": lambda: g.vector.tensor_scalar(ap(out), ap(x), 0.0, None, A.not_equal),
                        "S": lambda: g.scalar.activation(ap(out), ap(x), F.Abs)}, [x], [out], (0.1, ncol(x), "e"))

    def move(out, x, bias=0.0, scale=1.0, q="X"):
        return op(q, {"V": lambda: g.vector.tensor_scalar(ap(out), ap(x), arg(scale), arg(bias), A.mult, A.add),
                        "S": lambda: g.scalar.activation(ap(out), ap(x), F.Identity, bias=arg(bias), scale=arg(scale))},
                  [x] + [s for s in (bias, scale) if isinstance(s, tuple)], [out],
                  (0.1 if inps(x) else 0.05, max(64, ncol(x)), "e"))

    def times(out, x, s):
        return op("X", {"V": lambda: g.vector.tensor_scalar(ap(out), ap(x), ap(s), None, A.mult),
                        "S": lambda: g.scalar.activation(ap(out), ap(x), F.Identity, scale=ap(s))}, [x, s], [out], vc(ncol(x), 0.8))

    def gatherop(out, win, off, y, o):
        return op("V", lambda: g.vector.tensor_tensor(ap(out), ap(win).indirect(ap(off)), ap(y), o), [win, off, y], [out],
                  (0.05, ncol(out), "g"))

    def scatter(win, off, x, y=None, o=A.add):
        c = (0.05, ncol(x), "s")
        if y:
            return op("V", lambda: g.vector.tensor_tensor(ap(win).indirect(ap(off)), ap(x), ap(y), o), [x, y, off], [win], c)
        return op("V", lambda: g.vector.tensor_copy(ap(win).indirect(ap(off)), ap(x)), [x, off], [win], c)

    def mms(calls):
        def fn():
            for out, lhsT, rhs, start, stop in calls:
                ins = g.tensor.matmul(ap(out), ap(lhsT), ap(rhs), start, stop)
            return ins
        n = sum((4 if SCRATCH[x[2][0]][2] == _F else 1) * max(min(64, ncol(x[1])), ncol(x[2])) for x in calls)
        return op("T", fn, [y for x in calls for y in x[1:3]], [x[0] for x in calls], (FIX[3] * len(calls), n, "t"), lag=LAG + TLAG)

    def mm(out, lhsT, rhs, start=True, stop=True):
        return mms([(out, lhsT, rhs, start, stop)])

    def pick(out, x, pattern, cmp, fill, base, cm):
        return op("G", lambda: g.affine_select(ap(out), ap(x), pattern, cmp, fill, base, cm), [x], [out, pool], (0.17, 2 * ncol(out), "e"))

    def iota(out, pattern, base, cm, small=True):
        def fn():
            if small:
                return g.iota(ap(out), pattern, base, cm, allow_small_or_imprecise_dtypes=True)
            return g.iota(ap(out), pattern, base, cm)
        return op("G", fn, [], [out, pool], (0.13, 2 * ncol(out), "e"))
    pool = ("pool", 0, 128, 0, 1, 1)

    nld, nps = [0], [0]

    def load(out, src, cost, rows=None):
        s = "ld%d" % nld[0]
        nld[0] += 1
        rd, wr = ([src, v("sn0", 0, 1)], [out]) if isinstance(src, tuple) else ([], [out, ("order", 0, 128, 0, 1, 2)])
        if rows:
            return op("D", lambda: g.sync.dma_start(T[out[0]][rows[0], out[3]:out[4]], T[src[0]][rows[1], src[3]:src[4]]),
                      rd, wr, 0.08, sem=s, val=16, lag=2.0 + cost)
        return op("D", lambda: g.sync.dma_start(ap(out), arg(src)), rd, wr, 0.08, sem=s, val=16, lag=2.0 + cost)

    def ps(a, b, step=1, p0=0, p1=128, k=0):
        return ("ps%d" % k, p0, p1, a, b, step)

    def nb():
        nps[0] += 1
        return nps[0]

    def masks(s, two):
        od = [(s + 1 + k) % N for k in range(N - 1)]
        eng = topo.engines(T.cores[s], T.cores[od[0]])
        for d in od:
            eng = [e for e in eng if e in topo.engines(T.cores[s], T.cores[d])]
        n = len(eng)
        return dict(zip(od, [eng[:n // 2], eng[n // 2:], eng] if two else [eng[:n // 2:2], eng[n // 2::2], eng[1::2]]))

    def fused(src, dst, sem, loc, two=False, after=None, behind=()):
        parts = masks(me, two)

        def fn():
            for call in ([others[:2], others[2:]] if two else [others]):
                tr = []
                for d in call:
                    rid, pid, _ = topo.addr(T.cores[d])
                    tr.append(RemoteDMATransfer(dst_ids=[DstId(rid=rid, pnc=pid)], dma_engine_mask=sum(1 << e for e in parts[d]),
                                                remote_sem=T.sem[sem], srcs=[ap(src(d))], dsts=[ap(dst(d))], alu_op=0))
                ins = g.remote_dma_fused(tr, local_sem=T.sem[loc])
            return ins
        return op("G", fn, [src(d) for d in others] + list(behind), [], CALL, sem=loc, val=sum(len(x) for x in parts.values()), lag=1.5,
                  after=after)

    def got(sem, wr, after, lag, two=False, rd=()):
        return op("R", None, list(rd), wr, 0.0, sem=sem, val=sum(len(masks(s, two)[me]) for s in others), lag=lag, after=after)

    def slot(d, name, t):
        return v("%s%d" % (name, t), DUMP + 256 * d, DUMP + 256 * d + CAP)

    def halves(name, h, n=128):
        return v(name, h * n, h * n + n)

    def mp(h):
        return v("P", PH * h, PH * h + 128)

    def prod(a, n):
        c = PH * (a // 128) + 128 + 16 * (a % 128)
        return v("P", c, c + 16 * n)

    def chunks(kinds, h):
        return [(kinds[q].upper(), q, 32 * q + a, n) for q in range(4 * h, 4 * h + 4)
                for a, n in (((0, 16), (16, 16)) if kinds[q].islower() else ((0, 32),))]

    def wide(name, a, n):
        return v(name, 16 * a, 16 * (a + n))

    def rep(p, a, n):
        return v("Rep", 16 * (a % 32), 16 * (a % 32 + n), p0=p, p1=p + 32)

    def back(x):
        return x[:3] + (x[4] - 1, x[3] - 1, -1)
    LM, TL = v("tab", 0, W), v("xtl", 0, W)
    copies = (1, 3, 3, 3)

    def again(n):
        for c in range(1, n):
            load(v("tab", W + c * H, W + c * H + H), v("tab", W, W + H), 3.0)
        if HF:
            load(v("tab", W + 3 * H, W + 3 * H + 1024), v("tab", W, W + 1024), 3.5)

    load(v("wk0"), T.wk[:], 0.2)
    load(v("fm0"), T.fm[:], 0.5)
    load(LM, T.lm[:], 2.5 * SLOW)
    load(TL, T.tl[:], 5.0 * SLOW)
    load(v("xmo"), T.mo[:], 8.0 * SLOW)
    load(v("fr0", 0, L), T.fr[:, 0:L], 8.2 * SLOW)
    load(v("sn0"), T.sn[:], 9.7 * SLOW)
    load(v("fr0", L), T.fr[:, L:RO * L], 10.5 * SLOW)
    vset(v("one", 0, 128), 1.0)
    vset(v("one", 128, 512), 1.0)
    vset(v("zero"), 0.0)
    o128 = v("one", 0, 128)
    iota(v("pi", 0, 1), [[0, 1]], 0, 1, False)
    iota(v("ti"), [[1, 12]], 0, 0)
    pick(v("t8"), v("one", 0, 8), [[-16, 8]], A.is_ge, 0.0, 0, 1)
    pick(v("b8"), v("t8"), [[16, 8]], A.is_ge, 0.0, 15, -1)
    pick(v("I"), o128, [[-1, 128]], A.is_equal, 0.0, 0, 1)
    pick(v("R32", p1=32), v("one", 0, 512, p1=32), [[-1, 32], [0, 16]], A.is_equal, 0.0, 0, 1)
    pick(v("JR"), v("one", 0, 272), [[0, 2], [-16, 8], [1, 17]], A.is_equal, 0.0, -16, 1)
    for a in range(2):
        pick(halves("C8", a, 512), v("one"), [[-16, 4], [0, 8], [-1, 16]], A.is_equal, 0.0, -64 * a, 1)
    pick(v("Mk", 0, 128), v("zero", 0, 128), [[0, 16], [-16, 8]], A.is_ge, -16384.0, 0, 1)
    pick(v("Mk", 0, 128), v("Mk", 0, 128), [[0, 16], [16, 8]], A.is_ge, -16384.0, 15, -1)
    act(v("Mk", 128, 256), v("Mk", 0, 128))
    iota(v("lt"), [[128, 2], [0, 8]], 0, 1)
    iota(v("base"), [[0, 16], [256, 5]], DUMP - 256 - 2048, 0)
    pick(v("TR"), o128, [[1, 128]], A.is_gt, 0.0, 0, -1)
    for c in range(8):
        p = 64 * (c // 4)
        load(v("C8p", p0=16 * c, p1=16 * c + 16), v("C8"), 0.5, (slice(16 * c, 16 * c + 16), slice(p + c % 4, p + 64, 4)))
    iota(v("mki"), [[1, 16], [16, 4], [0, 2]], 0, 0)
    for x in range(2):
        for y in range(2):
            vset(v("sel", x, x + 1, p0=64 * y, p1=64 * y + 64), float(x == y))
    for a in range(4):
        act(v("i4", 32 * a, 32 * a + 32, p1=32), v("I", 0, 32, p1=32))
    b = nb()
    mm(ps(0, 512, k=b), v("i4", p1=32), v("R32", p1=32))
    act(v("Rep"), ps(0, 512, k=b))
    act(v("nI"), v("I"), scale=-1.0)
    act(v("If"), v("I"), scale=1 / 32 if HF else 1.0)
    act(v("n32"), v("I"), scale=-1 / 32)
    act(v("n8"), v("b8"), scale=-1.0)
    act(v("NP", 0, 8), v("b8"), scale=-8192.0)
    act(v("NP", 8, 16), v("b8"), scale=8192.0)
    act(v("PB8"), v("b8"), scale=-BIG / 2)
    ts(v("pi", 1, 2), v("pi", 0, 1), 15, A.bitwise_and)
    tc(v("pc", 0, 1), v("pi", 1, 2))
    ts(v("tj"), v("ti"), v("pc", 0, 1), A.is_equal)
    act(v("pc", 1, 2), v("tj", 0, 1), F.Identity, 65536.0 + 2 * AOFF, -65536.0 - 2 * AOFF)
    act(v("pc", 2, 3), v("lt", 0, 1), F.Identity, 128.0 - 2048, 16.0)
    act(v("pc", 3, 4), v("lt", 0, 1), F.Identity, 2048.0 - 128 * 8192, -15.0 * 8192)
    b = nb()
    mms([(ps(0, 1, p0=64 * x, p1=64 * x + 64, k=b), v("mki", 0, 128, 2, p1=1), v("one", 0, 1, p1=1), True, True) for x in range(2)])
    ts(halves("mkw", 0), v("mki"), ps(0, 1, k=b), A.is_le, -131072.0, A.mult)
    act(halves("mkw", 1), halves("mkw", 0))
    for c in range(4):
        act(v("pc", 8 + c, 9 + c), v("pc", 0, 1), F.Identity, 2049.0 + 16 * c)
    vset(v("pc", 4, 5, p1=96), 0.0)
    vset(v("pc", 4, 5, p0=96), 32.0)
    times(v("pc", 13, 14), v("pc", 0, 1), v("pc", 0, 1))
    act(v("pc", 14, 15), v("pc", 13, 14), F.Identity, 2 * AOFF, -2 * AOFF)
    act(v("pc", 15, 16), v("pc", 0, 1), F.Identity, 0.0, 2.0)
    ts(v("pi", 3, 4), v("pi", 0, 1), 4, A.arith_shift_right, 1, A.bitwise_and)
    tc(v("pc", 6, 7), v("pi", 3, 4))
    tc(v("wkf", 0, 3), v("wk0"))
    vset(v("Eq"), 0.0)
    times(v("Eq", 8, 16), v("b8"), v("pc", 15, 16))
    act(v("Eq", 24, 32), v("n8"))
    b = nb()
    for h in range(2):
        mm(ps(128 * h, 128 * h + 128, p1=32, k=b), v("Eq", 8 - 8 * h, 40 - 8 * h), v("I"))
    act(v("EM", p1=32), ps(0, 256, p1=32, k=b))
    for x in range(4):
        times(halves("Wp", x, 4), halves("n8", x // 2, 4), v("wkf", x % 2, x % 2 + 1))
    for name in ("Z", "Et"):
        vset(v(name), 0.0)
    times(v("Z", 24, 32), v("n8"), v("wkf", 0, 1))
    times(v("Z", 56, 64), v("b8"), v("wkf", 0, 1))
    times(v("Z", 88, 96), v("n8"), v("wkf", 1, 2))
    act(v("Et", 24, 32), v("b8"))
    times(v("Et", 56, 64), v("n8"), v("wkf", 2, 3))

    def lanesums(b, xs):
        mms([(ps(0, ncol(x), k=b), v("Z", 24 - 8 * blk, 152 - 8 * blk), x, blk == 0, blk == 3) for blk, x in enumerate(xs)])
    b = nb()
    lanesums(b, [v("one", 0, 2)] * 4)
    act(v("pc", 12, 13), ps(0, 1, k=b), F.Identity, v("pc", 4, 5), -255.0)
    b = nb()
    for blk in range(4):
        mm(ps(128 * blk, 128 * blk + 128, p1=64, k=b), v("Et", 24 - 8 * blk, 88 - 8 * blk), v("I"))
    for x in range(2):
        act(v("EX", 256 * x, 256 * x + 256, p1=64), ps(256 * x, 256 * x + 256, p1=64, k=b))
    pick(v("EA", p1=32), v("one", p1=32), [[-8, 4], [-1, 8], [0, 16]], A.is_equal, 0.0, 0, 1)
    vset(v("EA", p0=32, p1=33), 2048 - AOFF)
    tc(v("a12", p0=32, p1=33), v("one", 0, 64, p0=32, p1=33))
    for x in range(2):
        act(v("JR", 136 * x, 136 * x + 136, 17), v("I", 0, 128, 16))
    vset(v("K17"), -2048.0)
    vset(v("rm8"), BIG)
    vset(v("rm8", 0, None, 8), -BIG)
    vset(v("k8"), 8192.0)
    b = nb()
    mms([(ps(i, 256, 16, k=b), o128, v("Wp"), True, True) for i in range(16)])
    act(v("cT"), ps(0, 256, k=b), scale=-255.0)
    act(v("base", 0, 80, 5), v("lt"))
    vset(v("r5"), 1.0)
    vset(v("r5", 0, 80, 5), 0.0)
    vset(v("OH"), 0.0)
    pick(v("TRB"), v("TR"), [[-1, 128]], A.not_equal, 2048.0, 0, 1)
    act(v("tk"), v("tj"), F.Identity, 1.0, -2.0)
    ts(v("tbl", 0, 1), v("pc", 0, 1), 11.5, A.is_lt, 128.0, A.mult)
    ts(v("tbl", 0, 1), v("tbl", 0, 1), -64.0, A.add)
    vset(v("tbl", 4096, 4112), 64.0)
    vset(v("P", 2 * PH, 2 * PH + 16), 0.0)
    for k in range(12):
        if k >= 10:
            load(v("tbl", 1 << k, 2 << k), v("tbl", 0, 1 << k), 1.5)
            load(v("tbl", 1 << k, 2 << k), v("tbl", 0, 1 << k), 0.5, (slice(k, 128, 16), slice(12, 128, 16)))
            continue
        for c in range(0, 1 << k, 512):
            n = min(1 << k, 512)
            times(v("tbl", (1 << k) + c, (1 << k) + c + n), v("tbl", c, c + n), v("tk", k, k + 1))
    act(v("TR0"), v("one", 0, L), F.Identity, -2 * AOFF, v("pc", 1, 2))
    for t in range(RO - 2):
        load(v("TR%d" % (t + 1), SL, L), v("TR0", SL, L), 1.0)
        for d in range(N):
            load(slot(d, "wint", t), v("TR0", 0, CAP), 1.0)
    for c in range(0, H, 1024):
        move(v("tab", W + c, W + c + 1024), v("sn0", c, c + 1024), 255.0, -1.0)

    move(v("frc", 0, L), v("fr0", 0, L), 255.0, -1.0)
    move(v("frc", L), v("fr0", L, 3 * L), 255.0, -1.0)
    later = {}
    for t in range(RO):
        def fill(a, b, t=t):
            return v("frc" if t < RO - 1 else "fr0", t * L + a, t * L + b)
        load(slot(me, "win", t), fill(me * CAP, me * CAP + CAP), 1.0)
        load(v("L%d" % (t + 1), SL, L), fill(SL, L), 1.0)

        def refills(snd, behind=(), t=t, fill=fill):
            snd = fused(lambda d: fill(d * CAP, d * CAP + CAP), lambda d: slot(me, "win", t), "rarr%d" % t, "rloc%d" % t,
                        after=snd, behind=behind)
            if not t:
                ops[snd]["cost"] = (FCALL, 0, "e")
            got("rarr%d" % t, [slot(s, "win", t) for s in others], snd, RLAG if t else FLAG)
        if not t:
            refills(None)
        else:
            later[t - 1] = refills

    setup[0] = False

    def group(out, lhsT, rhs, parts, by=()):
        mm(out, lhsT, rhs, True, False)
        for n in by:
            mms([x + (False, False) for x in parts[:n]])
            parts = parts[n:]
        if parts[-1][0][2] - parts[-1][0][1] < 128:
            parts = parts + [(out[:4] + (out[3] + 2, 1), v("I"), v("zero", 0, 2))]
        return mms([x + (False, n == len(parts) - 1) for n, x in enumerate(parts)])

    def tolist(name, a, n, step, out, by="C8"):
        b = nb()
        group(ps(0, 8 * n, k=b), v("I"), v("Mk", 0, 8 * n),
              [(ps(n * c, n * c + n, k=b), halves(by, c), v(name, a, a + (n - 1) * step + 1, step)) for c in range(8)])
        scan(out, v("rm8", 0, 8 * n), ps(0, 8 * n, k=b), A.min)

    def ends(name, h):
        return v(name, 8 * h + 7, 128, 16)

    def sums(b, cols, name, c, w, cuts):
        return [(ps(*cols(i), p0=a, p1=e, k=b), v(name, c + 16 * a + i, c + 16 * e, 16), w)
                for a, e in zip((0,) + cuts, cuts + (128,)) for i in range(16)]

    def lowest(shift, own):
        tolist("XC", 16, 16, 1, v("TS"), "C8p")
        for h in range(2):
            ts(halves("WA", h, 8), ends("TS", h), shift, A.add, 4096.0, A.min)
        gather("X", v("FT0"), v("tbl"), v("WA"))
        if PAR:
            gather("X", v("FT1"), v("tbl"), v("WA"), (0.0, v("pc", 6, 7)))
        else:
            times(v("FT1"), v("FT0"), v("pc", 6, 7))
        for pair in range(4):
            b, p = nb(), 32 * pair
            parts = []
            for odd in range(2):
                for lc in range(2):
                    for blk in range(2):
                        c, o, e = lc * 128 + blk * 64, odd * 128, p + 16 + 16 * odd
                        parts.append((ps(o + lc, o + 128, 2, p0=64 * blk, p1=64 * blk + 64, k=b), v("FT%d" % odd, c, c + 64, p0=p, p1=e),
                                      v("FT0", c, c + 64, p0=p, p1=e)))
            group(ps(0, 256, k=b), v("I"), v("mkw"), parts, () if PAR else (4,))
            relu(halves("EW", pair, 256), ps(0, 256, k=b), -57344.0, "X")
        b = nb()
        group(ps(0, 16, k=b), v("I"), v("zero", 0, 16), [(ps(8 * h, 8 * h + 8, k=b), v("I"), own(h)) for h in range(2)] +
              [(ps(8 * lc + c, 8 * lc + 8, 4, k=b), v("EW", 2 * c + lc, 1024, 8), v("sel")) for lc in range(2) for c in range(4)], (2,))
        for c in range(4):
            ts(v("WL", c, 16, 4), ps(c, 16, 4, k=b), v("pc", 8 + c, 9 + c), A.min, shift, A.add)

    mine = (me * CAP, me * CAP + CAP)
    order = (0, 1)
    for t in range(RO):
        last = t == RO - 1
        Lt, Ln = "L%d" % t if t else "fm0", "L%d" % (t + 1)
        main[0], turn[0] = True, t
        if t:
            b = nb()
            mm(ps(0, 128, p1=32, k=b), halves(Lt, 7, 32), v("nI"))
            move(v("mT", 256, 384, p1=32), ps(0, 128, p1=32, k=b), 255.0)
        b = nb()
        lanesums(b, [halves(Lt, blk, 64) for blk in range(4)])
        if t:
            ts(v("au"), ps(0, 64, k=b), v("pc", 12, 13), A.add)
        else:
            ts(v("au"), ps(0, 64, k=b), -1.0, A.mult, v("pc", 4, 5), A.add)
        ts(v("am"), v("au"), 4095, A.bitwise_and)
        o = ops[tt(v("up", p1=64), v("am", p1=64), v("am", p0=64), A.mult)]
        o.update(drain=True, lag=0.01, cost=(LAG,) + o["cost"][1:])
        for h in order:
            b = nb()
            mm(ps(0, 128, k=b), halves(Lt, h), v("nI" if t else "I"))
            move(halves("mT", h), ps(0, 128, k=b), 255.0 if t else 0.0)
            for blks in ((0,), (1,)) if QUART[h] else ((0, 1),):
                b, a, n = nb(), 128 * h + 64 * blks[0], 64 * len(blks)
                mms([(ps(64 * k, 64 * k + 64, k=b), v("EX", 256 * h + 128 * blk, 256 * h + 128 * blk + 128, p1=64), v("up", p1=64),
                      True, True) for k, blk in enumerate(blks)])
                tc(v("ci", a, a + n), ps(0, n, k=b))
                ts(v("cj", a, a + n), v("ci", a, a + n), 5, A.arith_shift_right, 2047, A.bitwise_and)
                tc(v("CL", a, a + n), v("cj", a, a + n))
            ts(halves("cf", h), halves("CL", h), 0.0, A.add)
            move(mp(h), halves(Lt, h), *((255.0, -1.0) if t else ()))
        for h in order:
            for kind, q, a, n in chunks(EB if t else EB0, h):
                p, c = (0, 256) if t and q == 7 else (32 * (q % 4), q // 4 * 128)
                x, e, mr, off = wide("X", a, n), wide("E", a, n), wide("MR", a, n), v("CL", a, a + n)
                mt, rp = v("mT", c, c + 128, p0=p, p1=p + 32), rep(p, a, n)
                b = nb()
                out = ps(0, 16 * n, k=b)
                if kind == "A" and t and str(q) in DIRECT:
                    mms([(ps(j, 16 * n, 16, k=b), v("nI"), v(Lt, a, a + n), True, True) for j in range(16)])
                    move(mr, out, 255.0)
                    gatherop(e, LM, off, mr, A.is_gt)
                elif kind == "A":
                    mm(out, mt, rp)
                    move(mr, out)
                    gatherop(e, LM, off, mr, A.is_gt)
                else:
                    gather(kind, x, LM, off)
                    mm(out, mt, rp, True, False)
                    mm(out, v("nI"), x, False, True)
                    under(e, out, kind)
            b = nb()
            group(ps(0, 272, k=b), halves("cf", h), v("JR"),
                  [(ps(0, 272, 17, k=b), v("I"), v("K17"))] + sums(b, lambda i: (16 - i, 272, 17), "E", 2048 * h, v("NP"), CUTS[h]),
                  (1,) + (16,) * len(CUTS[h]))
            move(halves("SD", h, 136), ps(136, 272, k=b))
            scan(halves("GV", h, 136), ps(0, 136, k=b), halves("SD", h, 136), A.max, A.min)
            tolist("GV", 136 * h + 16, 8, 17, halves("GS", h, 64))
            gl = halves("GL", h, 8)
            ts(gl, v("GS", 64 * h + 7, 64 * h + 64, 8), 0.0, A.max)
            gather("X", halves("xg", h), LM, gl)
            gather("V", halves("TG", h), TL, gl)
            b = nb()
            mm(ps(0, 128, k=b), v("nI"), halves("mT", h), True, False)
            mm(ps(0, 128, k=b), halves("xg", h), v("I"), False, True)
            move(halves("qT", h), ps(0, 128, k=b))
        main[0] = False
        gv = v("GV", 16, 272, 17)
        ts(v("hb"), gv, 0.0, A.is_ge, BIG, A.mult)
        tt(v("zm"), v("hb"), gv, A.add)
        ts(v("capU"), v("zm"), v("pc", 3, 4), A.add, 131072.0, A.min)
        if not last:
            ts(v("capT"), v("zm"), 2048.0, A.min)
        else:
            ts(v("XC", 16, 32), gv, 2048.0, A.add, 2048.0, A.min)
            for h in order:
                ts(halves("WO", h, 8), v("GS", 64 * h + 7, 64 * h + 64, 8), 2048.0, A.add, 2048.0, A.min)
            lowest(0.0, lambda h: halves("WO", h, 8))
            for blk in range(3, -1, -1):
                c = PH * (blk // 2) + 64 * (blk % 2)
                scatter(v("LO"), halves("WL", blk, 4), v("P", c, c + 64))
        if t < RO - 2:
            gather("X", v("TGp"), TL, v("GL"), (-16384.0, 1.0))
        if not last:
            b, b2 = nb(), nb()
            tc(v("ui", p1=32), v("up", p1=32))
            ts(v("uj", p1=32), v("ui", p1=32), 5, A.arith_shift_right, 4095, A.bitwise_and)
            ts(v("a12", p1=32), v("uj", p1=32), -2048.0, A.add)
            mms([(ps(64 * blk, 64 * blk + 64, k=b), v("EA", 128 * blk, 128 * blk + 128, p1=33), v("a12", p1=33), True, True)
                 for blk in range(4)])
            tt(ps(0, 256, k=b2), v("TR%d" % t), ps(0, 256, k=b), A.max)
            tt(v("CT"), v("xtl", 0, L), ps(0, 256, k=b2), A.min)
            ts(v("CTm"), v("CT"), 4095, A.bitwise_and)
        main[0] = True
        for h in order:
            for kind, q, a, n in chunks(GD, h):
                y, p, r = wide("Y", a, n), prod(a, n), 32 * (q % 4)
                gather(kind, y, v("xmo"), v("TG", a, a + n))
                b = nb()
                two = [(v("nI"), y), (v("qT", h * 128, h * 128 + 128, p0=r, p1=r + 32), rep(r, a, n))]
                for k, x in enumerate(two if YQ[q] == "Y" else two[::-1]):
                    mm(ps(0, 16 * n, k=b), x[0], x[1], k == 0, k == 1)
                relu(p, ps(0, 16 * n, k=b), 255.0, kind)
            b = nb()
            parts = sums(b, lambda i: (i, 256, 16), "P", PH * h + 128, v("Wp"), CUTS[2 + h])
            for n in range(0, len(parts), 16):
                mms([x + (True, True) for x in parts[n:n + 16]])
            for z in range(2):
                c = 256 * h + 128 * z
                tt(v("hi", c, c + 128), ps(128 * z, 128 * z + 128, k=b), halves("cT", z), A.add)
                ts(v("hm", c, c + 128), v("hi", c, c + 128), 4095, A.bitwise_and)
                c, u = 2 * h + z, v("hm", c, c + 64)
                if t and HF:
                    tt(halves("hf", c, 64), u, halves("hm", 2 * c + 1, 64), A.mult)
                    ts(halves("hn", c, 64), halves("hf", c, 64), MAGIC * 65536, A.add, -MAGIC * 65536, A.add)
                    ts(halves("uf", c, 64), u, -2048.0, A.add)
                    continue
                tt(halves("hp", c, 64), u, halves("hm", 2 * c + 1, 64), A.mult)
                ts(halves("hq", c, 64), halves("hp", c, 64), 5, A.arith_shift_right, 2047, A.bitwise_and)
                if not t:
                    tt(halves("hr", c, 64), u, halves("hq", c, 64), A.add)
                    ts(halves("hs", c, 64), halves("hr", c, 64), 2047, A.bitwise_and)
                    tc(halves("hh", c, 64), halves("hs", c, 64))
                elif HT:
                    tc(halves("hh", c, 64), halves("hq", c, 64))
                    ts(halves("uf", c, 64), u, -2048.0, A.add)
                else:
                    tt(halves("lo", c, 64), u, halves("hq", c, 64), A.add)
            b = nb()
            if t and HF:
                three = (("hf", "If"), ("hn", "n32"), ("uf", "I"))
                mm(ps(0, 128, k=b), halves("hf", h), v("If"), True, False)
                mms([(ps(0, 128, k=b), halves(x, h), v(y), False, x == "uf") for x, y in three[1:]])
                ts(halves("HL", h), ps(0, 128, k=b), 3072 - 15.5 / 32, A.add)
                b = nb()
                mms([(ps(0, 128, k=b), v(y), halves(x, h), x == "hf", x == "uf") for x, y in three])
                move(halves("lo", h), ps(0, 128, k=b), 4096 - 15.5 / 32)
            elif t and HT:
                mm(ps(0, 128, k=b), halves("uf", h), v("I"), True, False)
                mm(ps(0, 128, k=b), halves("hh", h), v("I"), False, True)
                ts(halves("HL", h), ps(0, 128, k=b), 2048.0, A.add)
                b = nb()
                mm(ps(0, 128, k=b), v("I"), halves("uf", h), True, False)
                mm(ps(0, 128, k=b), v("I"), halves("hh", h), False, True)
                move(halves("lo", h), ps(0, 128, k=b), 2048.0)
            else:
                mm(ps(0, 128, k=b), halves("lo" if t else "hh", h), v("If" if t else "I"))
                tc(halves("HL", h), ps(0, 128, k=b))
        SN = v("tab", W + 1024, W + 7168) if t and HF else v("tab", W, W + copies[t] * H)
        for h in order:
            for kind, q, a, n in chunks(SE, h):
                ne, p, sx, off = wide("NE", a, n), prod(a, n), wide("SX", a, n), v("HL", a, a + n)
                if kind == "V":
                    gatherop(ne, SN, off, p, A.not_equal)
                else:
                    gather(kind, sx, SN, off)
                    b = nb()
                    mm(ps(0, 16 * n, k=b), v("nI"), p, True, False)
                    mm(ps(0, 16 * n, k=b), v("I"), sx, False, True)
                    differs(ne, ps(0, 16 * n, k=b), kind)
            b = nb()
            group(ps(0, 128, k=b), v("I"), v("k8"), sums(b, lambda i: (i, 128, 16), "NE", 2048 * h, v("PB8"), CUTS[4 + h]),
                  (16,) * len(CUTS[4 + h]))
            scan(back(halves("SC2", h)), back(ps(0, 128, k=b)), back(halves("lo" if t else "hh", h)), A.add)
        tt(v("key"), v("SC2", 0, 256, 16), v("capU"), A.min)
        ts(v("dd"), v("key"), (1 << 24) + (1 << 17) + 3, A.bitwise_and)
        for d in range(N):
            ts(v("OH", 1 + d, 80, 5), v("dd"), float(d), A.is_equal)
        b = nb()
        mm(ps(0, 80, k=b), v("I"), v("base"), True, False)
        mm(ps(40, 80, k=b), o128, v("OH", 0, 40), False, False)
        mm(ps(0, 80, k=b), v("TRB"), v("OH"), False, True)
        scan(v("S5"), v("r5"), ps(0, 80, k=b), A.mult)
        tolist("S5", 4, 16, 5, v("SS"))
        for h in range(2):
            tc(halves("SLL", h, 8), ends("SS", h))
        ts(v("fp"), v("key"), 13, A.arith_shift_right)
        ts(v("XC", 0, 16), v("fp"), v("pc", 2, 3), A.add)
        n = 16 if last else 32
        if not last:
            ts(v("t1"), v("key"), (1 << 17) + 2047, A.bitwise_and)
            tt(v("XC", 16, 32), v("t1"), v("capT"), A.min)
        tolist("XC", 0, n, 1, v("CS", 0, 8 * n))
        for h in range(2):
            ts(halves("CHL", h, 8), v("CS", 8 * h + 7, 8 * n, n), 2048.0, A.add)
            gather("X", halves("CH", h), v("P", PH * h, PH * h + PH + 16), halves("CHL", h, 8), last and (255.0, -1.0))
        scatter(v("win%d" % t), v("SLL"), v("CH"))
        snd = fused(lambda d, t=t: slot(d, "win", t), lambda d, Ln=Ln: v(Ln, mine[0], mine[1]), "arr%d" % t, "loc%d" % t, TWOCALL)
        move(v(Ln, mine[0], mine[1]), slot(me, "win", t))
        here = [("here%d" % t, 0, 128, 0, 1, 1)]
        got("arr%d" % t, [v(Ln, s * CAP, s * CAP + CAP) for s in others] + here, snd, XLAG, TWOCALL)
        main[0] = False
        if t < RO - 2:
            TR = "TR%d" % (t + 1)
            ts(halves("IV", 0, 16), v("fp"), 0.0, A.max, 16.0, A.min)
            tt(halves("IV", 1, 16), halves("IV", 0, 16), halves("IV", 0, 16), A.mult)
            b = nb()
            mm(ps(0, 128, p1=32, k=b), v("IV"), v("I"))
            move(v("T1", p1=32), ps(0, 128, p1=32, k=b))
            b = nb()
            mms([(ps(128 * h, 128 * h + 128, k=b), v("EM", 128 * h, 128 * h + 128, p1=32), v("T1", p1=32), True, True) for h in range(2)])
            act(v("mk"), ps(0, 256, k=b), F.Relu, v("pc", 14, 15), 2 * AOFF)
            scatter(v("wint%d" % t), v("SLL"), v("TGp"), v("mk"), A.subtract)
            snd = fused(lambda d, t=t: slot(d, "wint", t), lambda d, TR=TR: v(TR, mine[0], mine[1]), "tarr%d" % t, "tloc%d" % t,
                        behind=here)
            act(v(TR, mine[0], mine[1]), slot(me, "wint", t))
            got("tarr%d" % t, [v(TR, s * CAP, s * CAP + CAP) for s in others], snd, XLAG + 1.0)
        if not last:
            later[t](snd, here)
            main[0] = True
            lowest(2048.0, lambda h: v("CS", 8 * h + 23, 256, 32))
            for blk in range(3, -1, -1):
                scatter(v("tab", 0, W + H + L), halves("WL", blk, 4), halves("CH", blk, 64))
            main[0] = False
            again(copies[t + 1])
            if t == RO - 2:
                load(v("LO", 0, W), LM, 3.0)
            for blk in range(3, -1, -1):
                scatter(v("xtl"), halves("WL", blk, 4), halves("CTm", blk, 64))
    op("D", lambda: g.sync.dma_start(T.yf[:], ap(v("L4"))), [v("L4")], [], 0.08, sem="st0", val=16, lag=2.0)
    out = op("D", lambda: g.sync.dma_start(T.yl[:], ap(v("LO", 0, W))), [v("LO", 0, W)], [], 0.08, sem="st1", val=16, lag=2.0)
    op("R", None, [], [], 0.0, sem="st1", val=16, lag=4.5, after=out)
    _emit(g, T, ops, bank)


def _plan(ops, deps, bank):
    nop = len(ops)
    post = [[] for _ in ops]

    def more(lag):
        return lag + LAG1 - LAG if 0 < lag < 1 else lag * LONGER
    for j in range(nop):
        for i, kind in deps[j].items():
            post[i].append((j, ops[j]["lag"] if ops[j]["q"] == "R" else ops[i]["lag"] if kind > 1 and ops[i]["q"] != "R" else 0.0))
    key = [0.0] * nop
    for i in range(nop - 1, -1, -1):
        key[i] = min([key[j] - 1e-4 for j, _ in post[i]] + [ops[i]["main"] or nop + i])
    uses = {}
    for i, o in enumerate(ops):
        for x in o["rd"] + o["wr"]:
            if x[0][:2] == "ps" and i not in uses.setdefault(x[0], []):
                uses[x[0]].append(i)
    opens, closes, need = {}, {}, [len(d) for d in deps]
    gate = [[] for _ in ops]
    for u, lst in uses.items():
        opens[lst[0]] = u
        closes.setdefault(lst[-1], []).append(u)
        for j in deps[lst[1]]:
            if j != lst[0] and j not in deps[lst[0]]:
                gate[j].append(lst[0])
                need[lst[0]] += 1
    costs = [[o["cost"][0] + o["cost"][1] * z[o["cost"][2]] for o in ops] +
             [o["costs"][0] + o["costs"][1] * z[o["costs"][2]] for o in ops] for z in SETS]

    free_q = [o["q"] for o in ops]

    def forward(key, cost, LOOK, pins=free_q):
        left, est, end, on, banks, after = list(need), [0.0] * nop, [0.0] * nop, list(pins), {}, {}
        ready = {q: [] for q in "VSTGDRX"}
        for i in range(nop):
            if not left[i]:
                ready[on[i]].append(i)
        clock, free, order = {q: 0.0 for q in "VSTGDR"}, [(0.0, k, None) for k in range(8)], []

        def when(i):
            return max(est[i], min(free)[0] if free else 1e9) if i in opens else est[i]
        while len(order) < nop:
            best = None
            for q in clock:
                lst = ready[q] + ready["X"] if q in "VS" else ready[q]
                if lst:
                    s = max(clock[q], min(when(i) for i in lst))
                    if best is None or s < best[0]:
                        best = (s, q, lst)
            s, q, lst = best
            i = min((z for z in lst if when(z) <= s), key=lambda z: key[z] + (LOOK[1 + (ops[z]["cost"][2] == "e")] if q == "V" and on[z] == "X" else 0))
            soon = [when(z) for z in lst if key[z] < key[i] and s < when(z) < s + min(LOOK[0], cost[i])]
            if soon and q != "R":
                clock[q] = min(soon)
                continue
            ready[on[i]].remove(i)
            on[i] = q
            if i in opens:
                f = min(free)
                free.remove(f)
                banks[opens[i]], after[i] = f[1], f[2]
            end[i] = s + cost[i + nop * (q == "S")]
            for u in closes.get(i, ()):
                free.append((end[i] + LAG, banks[u], i))
            if q != "R":
                clock[q] = end[i]
            order.append(i)
            for j, lag in post[i]:
                est[j] = max(est[j], end[i] + lag)
            for j in [j for j, _ in post[i]] + gate[i]:
                left[j] -= 1
                if not left[j]:
                    ready[on[j]].append(j)
        return max(end), order, on, banks, after, end

    def backward(order, on, end, cost):
        late, busy, at = [0.0] * nop, {}, {i: n for n, i in enumerate(order)}
        for i in sorted(order, key=lambda i: (-end[i], -at[i])):
            s = max([late[j] + lag for j, lag in post[i]] + [0.0])
            if on[i] != "R":
                row = busy.setdefault(on[i], [])
                lo = len(row)
                while lo and row[lo - 1][1] > s:
                    lo -= 1
                while lo < len(row) and row[lo][0] < s + cost[i]:
                    s = max(s, row[lo][1])
                    lo += 1
                row.insert(lo, (s, s + cost[i]))
            late[i] = s + cost[i]
        return [-x for x in late]

    def replay(plan, cost):
        est, clock, end = [0.0] * nop, {}, [0.0] * nop
        for i in plan[1]:
            s = max(est[i], clock.get(plan[2][i], 0.0) if plan[2][i] != "R" else 0.0)
            if plan[4].get(i) is not None:
                s = max(s, end[plan[4][i]] + LAG)
            end[i] = clock[plan[2][i]] = s + cost[i + nop * (plan[2][i] == "S")]
            for j, lag in post[i]:
                est[j] = max(est[j], end[i] + lag)
        return max(end)
    best, first = None, key
    for mix in MIX:
        cost = [a + mix * (b - a) for a, b in zip(*costs)]
        for look in LOOKS:
            key = first
            for _ in range(PASSES):
                plan = forward(key, cost, look)
                mark = replay(plan, costs[0]) * 1.5 + replay(plan, costs[1])
                if best is None or mark < best[0]:
                    best = (mark,) + plan[1:] + (key, look, free_q)
                key = backward(plan[1], plan[2], plan[5], cost)
    z = SEED
    cost = [a + MIX[0] * (b - a) for a, b in zip(*costs)]
    shakes = SHAKES
    site, alike = [], {}
    for i, o in enumerate(ops):
        site.append((o["q"],) + tuple((x[0].rstrip("0123456789"), x[1], x[3]) for x in o["wr"][:1] + o["rd"][:2]))
        alike.setdefault(site[i], []).append(i)
    shared = "plan" in NOTE and SHARE
    for n in range(0 if shared else shakes):
        z = (z * 1103515245 + 12345) % 2147483648
        lo, key, pins = z / 2147483648 * max(best[5]), list(best[6]), list(best[8])
        seen = set()
        for i in range(nop):
            if lo <= best[5][i] < lo + SPAN[n % len(SPAN)] and site[i] not in seen:
                seen.add(site[i])
                z = (z * 1103515245 + 12345) % 2147483648
                if z // 4096 % 4 < SKIP:
                    continue
                for j in (alike[site[i]] if n % 5 < TIE else [i]):
                    key[j] += SHAKE[n % len(SHAKE)] * (z / 2147483648 - 0.5)
                    if free_q[j] == "X" and z // 64 % 8 == 0:
                        pins[j] = "VSX"[z // 512 % 3]
        plan = forward(key, cost, best[7], pins)
        mark = replay(plan, costs[0]) * 1.5 + replay(plan, costs[1])
        if mark <= best[0]:
            best = (mark,) + plan[1:] + (key, best[7], pins)
    NOTE["key"] = best[6:9]
    pre = [[] for _ in ops]
    for i in range(nop):
        for j, lag in post[i]:
            pre[j].append((i, lag, deps[j][i] == 1.5, more(lag)))
    above = [0] * nop
    for j in range(nop):
        for x in pre[j]:
            above[j] |= above[x[0]] | 1 << x[0]
        pre[j] = [x for x in pre[j] if x[1] > 1 or not any(above[y[0]] >> x[0] & 1 and not y[2] and y[1] >= x[1] for y in pre[j])]
    c0, c1 = costs
    opn = [opens.get(i) for i in range(nop)]
    cls = [closes.get(i) for i in range(nop)]

    def play(order, on, head=None, tail=None, same=0):
        snaps = []
        if same:
            same -= same % 16
            snaps = head[9][:same // 16]
            (e0, e1), (w0, w1), (last, free) = [[x.copy() for x in y] for y in (head[5], head[6], head[9][same // 16])]
            banks, after = head[3].copy(), head[4].copy()
        elif head:
            (e0, e1), (w0, w1), (last, free), banks, after = [[x.copy() for x in y] for y in head[5:8]] + [head[3].copy(), {}]
        else:
            e0, e1, w0, w1 = [0.0] * nop, [0.0] * nop, [None] * nop, [None] * nop
            last, free, banks, after = {}, [(0.0, k, None) for k in range(8)], {}, {}
        for n in range(same, len(order)):
            i = order[n]
            if not n & 15:
                snaps.append((last.copy(), free.copy()))
            q = on[i]
            s0 = s1 = 0.0
            a = b = None
            if q != "R":
                j = last.get(q)
                if j is not None:
                    s0, s1, a, b = e0[j], e1[j], j, j
                last[q] = i
            for j, lag, soft, lag1 in pre[i]:
                if soft and on[j] == q == "V":
                    continue
                x = e0[j] + lag
                if x > s0:
                    s0, a = x, j
                x = e1[j] + lag1
                if x > s1:
                    s1, b = x, j
            if opn[i] is not None:
                if not free:
                    return None
                f = min(free)
                free.remove(f)
                banks[opn[i]], after[i] = f[1], f[2]
                j = f[2]
                if j is not None:
                    if e0[j] + LAG > s0:
                        s0, a = e0[j] + LAG, j
                    if e1[j] + LAG1 > s1:
                        s1, b = e1[j] + LAG1, j
            k = i + nop if q == "S" else i
            e0[i], e1[i], w0[i], w1[i] = s0 + c0[k], s1 + c1[k], a, b
            if cls[i]:
                for u in cls[i]:
                    free.append((e0[i] + e1[i], banks[u], i))
        ends = []
        for k, e in enumerate((e0, e1)):
            if tail:
                out = [(e[i] + x[k], i) for i, x in tail[0]] + [(e[last[q]] + x[k], last[q]) for q, x in tail[1] if q in last]
                out += [(e[f[2]] + (LAG, LAG1)[k] + x[k], f[2]) for f, x in zip(sorted(free), tail[2]) if f[2] is not None]
                ends.append(max(out))
            else:
                ends.append(max((e[i], i) for i in order[-60:]) if order else (0.0, 0))
        return WEIGH * ends[0][0] + ends[1][0], order, on, banks, after, (e0, e1), (w0, w1), (last, free), ends, snaps

    def rest(p, hi):
        order, on, after = p[1], p[2], p[4]
        t, nxt, takers, later = {}, {}, [], set(order[hi:])
        for i in reversed(order[hi:]):
            q, k = on[i], i + nop * (on[i] == "S")
            x, y = nxt.get(q, (0.0, 0.0)) if q != "R" else (0.0, 0.0), t.pop(i, (0.0, 0.0))
            x = nxt[q] = (max(x[0], y[0]) + c0[k], max(x[1], y[1]) + c1[k])
            arcs = [(j, lag, lag1) for j, lag, soft, lag1 in pre[i] if not (soft and on[j] == q == "V")]
            if after.get(i) in later:
                arcs.append((after[i], LAG, LAG1))
            elif opn[i] is not None:
                takers.append(x)
            for j, lag, lag1 in arcs:
                y = t.get(j, (0.0, 0.0))
                t[j] = (max(y[0], x[0] + lag), max(y[1], x[1] + lag1))
        nxt.pop("R", None)
        return list(t.items()), list(nxt.items()), takers[::-1]

    def chain(p, k, inside):
        w = p[6][k]
        i, out = p[8][k][1], []
        while w[i] in inside:
            if all(x[0] != w[i] or x[2] and p[2][i] == p[2][w[i]] == "V" for x in pre[i]):
                out.append((w[i], i))
            i = w[i]
        return out
    preset = [{x[0] for x in p} for p in pre]
    now = top = play(best[1], best[2])
    twin, count = {}, {}
    for i, o in enumerate(ops):
        k = (site[i], o["round"])
        count[k] = count.get(k, 0) + 1
        site[i] = (site[i], count[k])
        twin[site[i], o["round"]] = i

    def ahead(order, j, i):
        lo, hi = order.index(i), order.index(j)
        if lo > hi:
            return order
        take, keep, need = [j], [], set(preset[j])
        for x in reversed(order[lo:hi]):
            if x in need:
                take.append(x)
                need |= preset[x]
            else:
                keep.append(x)
        return order[:lo] + take[::-1] + keep[::-1] + order[hi + 1:]

    def behind(order, i, j):
        lo, hi = order.index(i), order.index(j)
        if lo > hi:
            return order
        take, keep, gone = [i], [], {i}
        for x in order[lo + 1:hi + 1]:
            if preset[x] & gone:
                take.append(x)
                gone.add(x)
            else:
                keep.append(x)
        return order[:lo] + keep + take + order[hi + 1:]

    def mend(whole, lo, hi, heat, z):
        head, tail = play(whole[1][:lo], whole[2]), rest(whole, hi) if hi < nop else None
        now = top = play(whole[1][lo:hi], whole[2], head, tail)
        arcs, inside = None, set(now[1])
        for n in range(MENDS):
            if arcs is None:
                row = {}
                for i in now[1]:
                    row.setdefault(now[2][i], []).append(i)
                at = {i: k for r in row.values() for k, i in enumerate(r)}
                arcs = chain(now, 0, inside) + chain(now, 1, inside)
                if not arcs:
                    break
            z = (z * 1103515245 + 12345) % 2147483648
            i, j = arcs[(z >> 8) % len(arcs)]
            z = (z * 1103515245 + 12345) % 2147483648
            how, far, order, on = (z >> 8) % 8, FAR[(z >> 14) % len(FAR)], now[1], now[2]
            if how >= 6 and "X" in (free_q[i], free_q[j]):
                i = i if free_q[i] == "X" and (free_q[j] != "X" or how == 6) else j
                on = list(on)
                on[i] = "S" if on[i] == "V" else "V"
            elif how % 2:
                i = row[on[i]][max(0, at[i] - far)]
                order = ahead(order, j, i)
            else:
                order = behind(order, i, row[on[j]][min(len(row[on[j]]) - 1, at[j] + far)])
            if order is now[1] and on is now[2]:
                continue
            same = now[1].index(i)
            p = play(order, on, now, tail, same) if same >= 16 else play(order, on, head, tail)
            z = (z * 1103515245 + 12345) % 2147483648
            if p and p[0] <= now[0] + heat * (1 - n / MENDS) * (z / 2147483648) ** 2:
                now, arcs = p, None
                if p[0] < top[0]:
                    top = p
        return play(whole[1][:lo] + top[1] + whole[1][hi:], top[2])

    def timed(p):
        pos = {i: k for k, i in enumerate(p[1])}
        x = play(sorted(p[1], key=lambda i: (round(p[5][0][i] - c0[i + nop * (p[2][i] == "S")], 6), pos[i])), p[2])
        return x if x and x[0] <= p[0] + 0.2 else p

    def like(p, a, b):
        start = [p[5][0][i] - c0[i + nop * (p[2][i] == "S")] for i in range(nop)]
        pairs = [(i, twin[site[i], a]) for i in range(nop) if ops[i]["round"] == b and (site[i], a) in twin]
        shift = sorted(start[i] - start[j] for i, j in pairs)[len(pairs) // 2]
        key, on = list(start), list(p[2])
        for i, j in pairs:
            key[i], on[i] = start[j] + shift, p[2][j]
        return keyed(key, on)

    def keyed(key, on):
        left, order = [len(x) for x in deps], []
        ready = [i for i in range(nop) if not left[i]]
        while ready:
            i = min(ready, key=lambda z: key[z])
            ready.remove(i)
            order.append(i)
            for j, _ in post[i]:
                left[j] -= 1
                if not left[j]:
                    ready.append(j)
        return play(order, on)
    if shared:
        top = keyed(*NOTE["plan"])
    for sweep, heat in enumerate(() if shared else HEAT):
        for lo in range(-(sweep % 2) * WIDE // 4, nop - WIDE // 2, WIDE // 2):
            z = (z * 1103515245 + 12345) % 2147483648
            p = mend(top, max(lo, 0), min(lo + WIDE, nop), heat, z)
            if p and p[0] <= top[0]:
                top = timed(p)
        for a in range(RO):
            for b in range(1, RO):
                p = like(top, a, b) if a != b else None
                if p and p[0] < top[0]:
                    top = p
    best = top[:5] + best[5:]
    NOTE["plan"] = ({i: k for k, i in enumerate(top[1])}, top[2])
    order, on, banks, after = best[1:5]
    NOTE["mark"] = best[0]
    for i in range(nop):
        ops[i]["q"] = on[i]
    for i, j in after.items():
        if j is not None:
            deps[i][j] = 2
    for u, k in banks.items():
        bank[u] = "ps%d" % k
    return order


def _emit(g, T, ops, bank):
    nop = len(ops)
    acc, deps = {}, [None] * nop

    def mask(x):
        if x[5] == 1:
            return ((1 << (x[4] - x[3])) - 1) << x[3]
        m = 0
        for c in range(x[3], x[4], x[5]):
            m |= 1 << c
        return m
    memo = {}
    for i, o in enumerate(ops):
        need = {}
        mine = []
        for wr, lst in ((0, o["rd"]), (1, o["wr"])):
            for x in lst:
                if x not in memo:
                    memo[x] = mask(x)
                mine.append((x[0], x[1], x[2], memo[x], wr))
        for (bf, p0, p1, m, wr) in mine:
            for (j, q0, q1, mj, wj) in acc.get(bf, ()):
                if j == i:
                    continue
                same = ops[j]["q"] == o["q"] != "X"
                hit = (wr or wj) and (m & mj) and p0 < q1 and q0 < p1
                if bf[:2] == "ps":
                    hit = hit or not same
                    need[j] = max(need.get(j, 0), 1)
                if hit:
                    kind = 1 if same and (o["q"] == "T" or bf == "order") else 2
                    if kind == 2 and wr and not wj and LOOSE and o["q"] in "VSX" and ops[j]["q"] in "VSX":
                        kind = 1 if same and o["q"] == "V" else 1.5
                    need[j] = max(need.get(j, 0), kind)
        for (bf, p0, p1, m, wr) in mine:
            old = acc.get(bf, [])
            if bf[:2] == "ps":
                old = [z for z in old if z[0] == i]
            elif wr:
                old = [z for z in old if not (z[0] != i and (z[3] | m) == m and p0 <= z[1] and z[2] <= p1)]
            acc[bf] = old + [(i, p0, p1, m, wr)]
        if o["after"] is not None:
            need[o["after"]] = max(need.get(o["after"], 0), 1)
        deps[i] = need
    order = _plan(ops, deps, bank)
    queue = {"V": g.vector, "S": g.scalar, "T": g.tensor, "G": g, "D": g.sync}
    count = {}
    know = {q: {} for q in queue}
    tok, kn = [None] * nop, [None] * nop
    for i in order:
        o = ops[i]
        q = o["q"]
        if q == "R":
            tok[i] = (o["sem"], o["val"])
            kn[i] = {o["sem"]: o["val"]}
            continue
        k = know[q]
        want = {}
        for j, kind in deps[i].items():
            if kind == 2 or kind == 1.5 and not ops[j]["q"] == q == "V":
                s, val = tok[j]
                if k.get(s, 0) < val and (s not in want or want[s][0] < val):
                    want[s] = (val, j)
        for s in list(want):
            if any(z != s and kn[want[z][1]].get(s, 0) >= want[s][0] for z in want):
                del want[s]
        for s, (val, j) in want.items():
            queue[q].wait_ge(T.sem[s], val)
        for s, (val, j) in want.items():
            for z, n in kn[j].items():
                if k.get(z, 0) < n:
                    k[z] = n
        ins = o["fn"][q]() if isinstance(o["fn"], dict) else o["fn"]()
        if o["sem"] is None:
            s = "q" + q
            count[s] = count.get(s, 0) + 1
            ins.then_inc(T.sem[s], 1)
            tok[i] = (s, count[s])
            if o.get("drain"):
                queue[q].wait_ge(T.sem[s], count[s])
                k[s] = count[s]
        else:
            tok[i] = (o["sem"], o["val"])
            if q == "D":
                ins.then_inc(T.sem[o["sem"]], 16)
        kn[i] = dict(k)
        kn[i][tok[i][0]] = tok[i][1]
    k = know["G"]
    fin = {}
    for i in range(nop):
        if tok[i][1] > fin.get(tok[i][0], 0):
            fin[tok[i][0]] = tok[i][1]
    for s, n in fin.items():
        if k.get(s, 0) < n:
            g.wait_ge(T.sem[s], n)
